import numpy as np, ml_dtypes
CORES = [5,29,101,125,133,157,229,253]
N = 8
BF = ml_dtypes.bfloat16
def gentries(a):
    return np.ascontiguousarray(a.reshape(8, 16, -1).transpose(0, 2, 1)).reshape(8, -1)
def gtable(e):
    e = np.asarray(e); return np.ascontiguousarray(e.reshape(8, -1, 16).transpose(0, 2, 1)).reshape(128, -1).astype(np.int32)
def f(rng, *shape):
    return (rng.standard_normal(shape, dtype=np.float32) * np.exp2(rng.integers(-2, 3, shape[:-1] + (1,)))).astype(BF)
def wide(rng, *shape):
    v = f(rng, *shape).astype(np.float32); k = shape[:-2] + (1, shape[-1])
    return (v * np.exp2(rng.integers(-6, 7, k)) * (rng.random(k) > 0.0625)).astype(BF)
V, B, CAP, RO, HI, LO, M = 896, 32, 320, 5, 9, 3, 8192
FP = (N - 1) * B
def face(x, y, fs):
    p = np.zeros(4 * V, np.int64); p[x] = y; p[y] = x; p[fs] = 4 * V + np.arange(FP)
    return p
def mate(rng, a):
    a = rng.permutation(a); x, y = a[0::2].copy(), a[1::2].copy()
    for i in np.flatnonzero(x >> 2 == y >> 2):
        if x[i] >> 2 != y[i] >> 2: continue
        j = rng.choice(np.flatnonzero((x >> 2 != x[i] >> 2) & (y >> 2 != x[i] >> 2)))
        y[i], y[j] = int(y[j]), int(y[i])
    return x, y
def wire(rng, half=None, px=(), py=(), must=(), cell=0):
    px, py, must = np.array(px, np.int64), np.array(py, np.int64), np.array(must, np.int64)
    free = np.ones(4 * V, bool); free[px] = False; free[py] = False; free[must] = False
    a = np.flatnonzero(free); a = a[(a >> 2) >= cell]
    if half is None: fs = rng.permutation(a)[:FP - len(must)]
    else:
        h = half[a >> 2]; n = FP // 2 - len(must) // 2
        fs = np.concatenate([rng.permutation(a[h])[:n], rng.permutation(a[~h])[:n]])
    fs = np.concatenate([must[:1], rng.permutation(fs), must[1:]]); free[fs] = False; a = np.flatnonzero(free)
    if half is None: x, y = mate(rng, a)
    else:
        h = half[a >> 2]; c = (a >> 2) < cell
        x = np.concatenate([a[h & c], a[h & ~c]]); y = np.concatenate([rng.permutation(a[~h & c]), rng.permutation(a[~h & ~c])])
    return face(np.concatenate([x, px]), np.concatenate([y, py]), fs), fs
def seeds(rng, m):
    o = rng.permutation(V); st = np.sort(o[:m]); w = np.sort(o[m:]); give = np.zeros(V - m, bool)
    if m > 0:
        give[0] = True; give[1 + rng.permutation(V - m - 1)[:m - 1]] = True
    j = np.flatnonzero(~give); j = j[j > 0]
    px = np.concatenate([4 * rng.permutation(st) + 1, 4 * w[j - 1] + 1]); py = np.concatenate([4 * w[give], 4 * w[j]])
    free = np.ones(4 * V, bool); free[px] = False; free[py] = False
    s = np.flatnonzero(free); first = np.isin(s >> 2, st); a = s[first]; b = rng.permutation(s[~first])
    if m == 0: b = np.concatenate([np.zeros(1, np.int64), b[b != 0]])
    fs = rng.permutation(b[:FP]); b = b[FP:]; x, y = mate(rng, b[len(a):])
    return face(np.concatenate([px, a, x]), np.concatenate([py, b[:len(a)], y]), fs), fs, st
def knit(rng, px, py, fo, st):
    z = rng.integers(0, 2, (FP // 2, 1)); fs = (4 * fo[:, None] + 2 + np.concatenate([z, 1 - z], axis=1)).reshape(-1)
    free = np.ones(4 * V, bool); free[px] = False; free[py] = False; free[fs] = False
    s = np.flatnonzero(free); first = np.isin(s >> 2, st); a = s[first]; b = rng.permutation(s[~first]); x, y = mate(rng, b[len(a):])
    return face(np.concatenate([px, a, x]), np.concatenate([py, b[:len(a)], y]), fs), fs
def chain(rng, st, fo):
    m = len(st); w = np.setdiff1d(np.arange(V), st); give = np.zeros(V - m, bool); give[0] = True; give[1 + rng.permutation(V - m - 1)[:m - 1]] = True
    j = np.flatnonzero(~give)
    return knit(rng, np.concatenate([4 * rng.permutation(st) + 1, 4 * w[j - 1] + 1]), np.concatenate([4 * w[give], 4 * w[j]]), fo, st)
def blank():
    return np.zeros((N, 8, 4 * V), np.int64), np.zeros((N, 8, FP), np.int64), np.zeros((N, 8, V), np.int64), np.ones((N, 8, V), np.int64)
def mixed(rng):
    port, rim, t, d = blank()
    for r in range(N):
        k = rng.permutation(8)
        for g in range(8):
            if k[g] < 4:
                port[r, g], rim[r, g] = wire(rng); t[r, g] = rng.integers(0, 4, V); d[r, g] = 2 ** rng.integers(0, 3, V)
            else:
                half = np.zeros(V, bool); half[rng.permutation(V)[:V // 2]] = True
                port[r, g], rim[r, g] = wire(rng, half)
                t[r, g] = np.where(half, rng.integers(0, 2, V), rng.integers(2, 4, V)); d[r, g] = np.where(half, 2 ** rng.integers(0, 2, V), 2 ** rng.integers(0, 3, V))
    return port, rim, t, d
def limit(x, m):
    return np.clip(np.asarray(x).astype(np.float32), -m, m)
def gates(rng, q):
    z = np.std(q.reshape(N, 8, 16, V), axis=3, keepdims=True) * rng.uniform(0.4, 1.1, (N, 8, 1, 1))
    return np.clip(z, 0.0625, 4)
def sized(x):
    x = np.ascontiguousarray(np.reshape(x, (N, 128, V))).astype(np.float32)
    return np.where(np.abs(x) < np.float32(2.0 ** -40), np.float32(0), x).astype(BF)
def pack(q, v, h, t, d, port, rim):
    return {"q0": sized(q), "q1": sized(v),
            "th": np.ascontiguousarray(np.reshape(h, (N, 128, 1))).astype(np.float32), "t0": t.astype(np.int32), "d0": d.astype(np.int32),
            "port": np.stack([gtable(a) for a in port]), "rim": np.stack([gtable(a) for a in rim])}
def setup_inputs(rng):
    port, rim, t, d = mixed(rng); q = limit(f(rng, N, 128, V), 4); v = limit(0.25 * f(rng, N, 128, V).astype(np.float32), 1)
    return pack(q, v, gates(rng, q), t, d, port, rim)
def setup_inputs_spread(rng):
    port, rim, t, d = mixed(rng); q = limit(wide(rng, N, 128, V), 4); v = limit(0.25 * wide(rng, N, 128, V).astype(np.float32), 1)
    q = np.where(q == 0, np.float32(2.0 ** -12), q)
    h = np.clip(np.exp2(rng.uniform(-4, 2, (N, 8, 16, 1))), 0.0625, 4)
    t = np.minimum((4 * rng.random((N, 8, V)) ** 3).astype(np.int64), 3); d = 2 ** np.minimum((3 * rng.random((N, 8, V)) ** 0.5).astype(np.int64), 2)
    return pack(q, v, h, t, d, port, rim)
def setup_inputs_ends(rng):
    port, rim, t, d = blank(); t = 3 * rng.integers(0, 2, (N, 8, V)); d = 1 + 3 * rng.integers(0, 2, (N, 8, V))
    q = 8 * rng.integers(0, 2, (N, 8, 16, V)) - 4; v = 2 * rng.integers(0, 2, (N, 8, 16, V)) - 1
    h = np.where(rng.random((N, 8, 16, 1)) < 0.5, 0.0625, 4.0); half = np.arange(V) < V // 2
    for r in range(N):
        k = rng.permutation(8)
        if r == N - 1:
            i = int(np.flatnonzero(k == 4)[0]); k[i], k[7] = int(k[7]), 4
        for g in range(8):
            odd = (r + g) % 2 == 1
            px, py, must = ((), (), (0, 4 * V - 1)) if odd else ((0,), (4 * V - 1,), ())
            if k[g] < 4:
                low = rng.permutation(16) < (0, LO, LO + 1, HI - 1)[k[g]]
                h[r, g, :, 0] = np.where(low, 0.0625, 4.0); q[r, g] = np.where(low[:, None], q[r, g], np.where(half, -4, 4)[None, :])
                port[r, g], rim[r, g] = wire(rng, half, px, py, must)
            else:
                if k[g] == 4: h[r, g] = 0.0625
                port[r, g], rim[r, g] = wire(rng, None, px, py, must)
            late = (r + g) % 2 == (N + 6) % 2
            t[r, g, V - 2:] = (0, 3) if late else (3, 0); d[r, g, V - 2:] = (1, 4) if late else (4, 1)
    return pack(q, v, h, t, d, port, rim)
def setup_inputs_corners(rng):
    port, rim, t, d = blank(); most = (2 * V - FP) // 4 - 4
    for r in range(N):
        k = rng.permutation(np.array([1, CAP - 1, CAP, CAP, CAP + 1, CAP + 1, most])); k = np.concatenate([k[:5], np.zeros(1, np.int64), k[5:]])
        for g in range(8):
            port[r, g], rim[r, g], st = seeds(rng, int(k[g]))
            i = rng.integers(0, 3, V); t[r, g] = np.array([0, 2, 3])[i]; d[r, g] = np.array([4, 2, 1])[i]
            t[r, g, st] = 0; d[r, g, st] = 1
            if k[g] == 0: t[r, g] = 3; d[r, g] = 4
    q = limit(f(rng, N, 128, V), 4); v = limit(0.25 * f(rng, N, 128, V).astype(np.float32), 1)
    return pack(q, v, gates(rng, q), t, d, port, rim)
def setup_inputs_calm(rng):
    port, rim, t, d = blank(); e = np.arange(V); half = (e < CAP // 2) | ((e >= CAP) & (e < CAP + (V - CAP) // 2))
    q = np.zeros((N, 8, 16, V), np.float32); v = np.zeros((N, 8, 16, V), np.float32); h = np.zeros((N, 8, 16, 1), np.float32)
    kinds = ((LO, 3, 4), (LO, 2, 4), (LO, 0, 4), (HI, 0, 1), (HI, 1, 1), (HI - 1, 0, 2), (LO + 1, 3, 2), (HI - 1, 2, 2))
    for r in range(N):
        k = rng.permutation(8)
        for g in range(8):
            n, a, b = kinds[k[g]]; low = (rng.permutation(16) < n)[:, None]
            z = (0.5 + 2.5 * rng.random((16, 1))).astype(np.float32).astype(BF).astype(np.float32); sg = np.where(half, -1, 1)[None, :]
            any_ = 2 * rng.integers(0, 2, (16, V)) - 1
            q[r, g] = np.where(low, any_ * (1 + 2 * rng.random((16, V))), sg * z)
            v[r, g] = np.where(low, 2 * rng.random((16, V)) - 1, sg * rng.random((16, V)))
            h[r, g] = np.where(low, 0.0625, z); t[r, g] = a; d[r, g] = b
            port[r, g], rim[r, g] = wire(rng, half, (), (), (), CAP)
    return pack(q, v, h, t, d, port, rim)
def setup_inputs_knots(rng):
    port, rim, t, d = blank(); q = limit(f(rng, N, 128, V), 4).reshape(N, 8, 16, V); v = limit(0.25 * f(rng, N, 128, V).astype(np.float32), 1).reshape(N, 8, 16, V)
    h = gates(rng, q); tm = rng.permutation(16)[:2]; nt = np.setdiff1d(np.arange(16), tm); sg = 2 * rng.integers(0, 2, (N, 8, 2, V)) - 1
    q[:, :, tm] = sg * np.exp2(rng.integers(-40, -33, sg.shape).astype(np.float64)) * (1 + 0.0078125 * rng.integers(0, 128, sg.shape))
    v[:, :, tm] = sg * np.exp2(rng.integers(-40, -35, sg.shape).astype(np.float64))
    off = int(rng.integers(0, 2)); ne = (V - FP // 4) // 2; none = np.zeros(0, np.int64)
    for r in range(N):
        k = rng.permutation(4)
        for g in range(8):
            kind = int(k[g // 2])
            if (g + off) % 2 == 0:
                fo = rng.permutation(V)[:FP // 2]; st = np.sort(fo); port[r, g], rim[r, g] = chain(rng, st, fo)
                i = rng.integers(0, 3, V); t[r, g] = np.array([0, 2, 3])[i]; d[r, g] = np.array([4, 2, 1])[i]
                t[r, g, st] = rng.integers(0, 2, FP // 2); d[r, g, st] = 2 - t[r, g, st]
            elif kind == 0:
                fo = rng.permutation(V)[:FP // 2]; i = int(rng.integers(0, FP // 2)); st = fo[i:i + 1]; port[r, g], rim[r, g] = chain(rng, st, fo)
                t[r, g] = 3; d[r, g] = 4; t[r, g, st] = 0; d[r, g, st] = 1; q[r, g] = np.clip(q[r, g], -3, 3); h[r, g] = 4
            elif kind == 1:
                o = 1 + rng.permutation(V - 2); n = FP // 2; fo = o[:n]
                ea = np.concatenate([np.array([0]), o[n:n + 15]]); eb = np.concatenate([np.array([V - 1]), o[n + 15:n + 30]])
                px = (4 * ea[:, None] + np.arange(4)).reshape(-1); py = (4 * eb[:, None] + np.argsort(rng.random((16, 4)), axis=1)).reshape(-1)
                port[r, g], rim[r, g] = knit(rng, px, py, fo, none)
                t[r, g] = rng.integers(0, 4, V); d[r, g] = 2 ** rng.integers(0, 3, V); t[r, g, fo] = rng.integers(0, 2, n); d[r, g, fo] = 4
                t[r, g, ea] = 0; t[r, g, eb] = 0; d[r, g, ea] = 2 ** rng.integers(0, 3, 16); d[r, g, eb] = d[r, g, ea]
            else:
                up = kind == 2; e = np.arange(V); first = (e >= V - ne) if up else (e < ne); s = 1 if up else -1
                fo = rng.permutation(np.flatnonzero(~first))[:FP // 2]; port[r, g], rim[r, g] = knit(rng, none, none, fo, np.flatnonzero(first))
                t[r, g] = 0; d[r, g] = np.where(first, 2, 4)
                o = rng.permutation(nt); n = (LO, HI - 1)[(r + kind) % 2]; lo, ex = o[:n], o[n:]
                z = (1 + 0.9 * rng.random((len(ex), 1))).astype(np.float32).astype(BF).astype(np.float32)
                q[r, g][ex] = s * np.where(first[None, :], z, 2.0 ** -8 * (0.75 + 0.6 * rng.random((len(ex), V))))
                v[r, g][ex] = s * np.where(first[None, :], rng.random((len(ex), V)), 0); h[r, g][ex] = z
                q[r, g][lo] = (2 * rng.integers(0, 2, (n, V)) - 1) * (1 + 2 * rng.random((n, V))); h[r, g][lo] = 0.0625
    return pack(q, v, h, t, d, port, rim)
def check_inputs(d):
    bad = []
    for k, lo, hi in (("q0", -4, 4), ("q1", -1, 1), ("th", 0.0625, 4), ("t0", 0, 3), ("d0", 1, 4), ("port", 0, 4 * V + FP - 1), ("rim", 0, 4 * V - 1)):
        x = np.asarray(d[k]).astype(np.float64)
        if not np.all((x >= lo) & (x <= hi)): bad.append("range of " + k)
        if k in ("q0", "q1") and np.any((x != 0) & (np.abs(x) < 2.0 ** -40)): bad.append(k + " is under 2**-40 in size somewhere and not 0")
    if np.any(np.asarray(d["d0"]) == 3): bad.append("d0 is 3 somewhere")
    if bad: return bad
    p = np.stack([gentries(a) for a in d["port"]]).astype(np.int64); m = np.stack([gentries(a) for a in d["rim"]]).astype(np.int64)
    s = np.arange(4 * V); own = p < 4 * V; back = np.take_along_axis(p, np.where(own, p, 0), 2)
    if np.any(own & (back != s)): bad.append("port: facing slots don't face each other")
    if np.any(own & ((p >> 2) == (s >> 2))): bad.append("port: an element faces itself")
    if np.any(np.add.reduce((~own).astype(np.int64), axis=2) != FP) or np.any(np.take_along_axis(p, m, 2) != 4 * V + np.arange(FP)): bad.append("port and rim: foreign ports")
    return bad
def swap(x):
    y = np.zeros_like(x)
    for r in range(N):
        for d in range(1, N):
            s = (r + d) % N; gs = (np.arange(8) + (1 if r < s else 7)) % 8
            y[r][..., (d - 1) * B:d * B] = x[s][gs][..., (N - d - 1) * B:(N - d) * B]
    return y
def around(x, e):
    b = np.take_along_axis(x, e[:, :, None, :], 3) if x.ndim == 4 else np.take_along_axis(x, e, 2)
    return np.concatenate([x, swap(b)], axis=-1)
def overlap(x0, x1, a, b, tau):
    u = (b - a).astype(np.float32) * x0
    w = (np.float32(0.5) * ((b - tau) ** 2 - (a - tau) ** 2).astype(np.float32)) * x1
    return np.float32(0.03125) * (u + w)
def reference(q0, q1, th, t0, d0, port, rim):
    s0 = q0.astype(np.float32).reshape(N, 8, 16, V); s1 = q1.astype(np.float32).reshape(N, 8, 16, V); h = th.astype(np.float32).reshape(N, 8, 16, 1)
    t = t0.astype(np.int64); dt = d0.astype(np.int64)
    p = np.stack([gentries(a) for a in port]).astype(np.int64); m = np.stack([gentries(a) for a in rim]).astype(np.int64)
    col = np.where(p < 4 * V, p >> 2, p - 3 * V); e = m >> 2
    num = np.zeros((N, 8, V), np.int64) + np.arange(N)[:, None, None] * V + np.arange(V); nx = around(num, e)
    fm = np.zeros((N, 8, 16, 4 * V + FP), np.float32); inv = np.array([0, 1, 0.5, 0, 0.25], np.float32)
    for rnd in range(RO):
        key = M * (t + dt) + num; kn = np.take_along_axis(around(key, e), col, 2).reshape(N, 8, V, 4)
        can = np.all(key[..., None] < kn, axis=3); act = can & (np.add.accumulate(can.astype(np.int64), axis=2) <= CAP)
        x0, x1, tx = around(s0, e), around(s1, e), around(t, e)
        for r in range(N):
            for g in range(8):
                a = np.flatnonzero(act[r, g]); sl = 4 * a[:, None] + np.arange(4); c = p[r, g][sl]; n = col[r, g][sl]
                te = tx[r, g][a][:, None]; tn = tx[r, g][n]; de = dt[r, g][a]; tb = te + de[:, None]; ta = np.minimum(np.maximum(te, tn), tb)
                old = x0[r, g][:, a]
                ie = overlap(old[:, :, None], x1[r, g][:, a][:, :, None], ta, tb, te); ni = overlap(x0[r, g][:, n], x1[r, g][:, n], ta, tb, tn)
                left = nx[r, g][a][:, None] < nx[r, g][n]
                up = np.maximum(np.where(left, ie, ni), np.float32(0)); dn = np.minimum(np.where(left, ni, ie), np.float32(0))
                ph = np.float32(0.5) * (up * up + dn * dn); own = np.where(left, -ph, ph)
                new = old
                for i in range(4): new = new + (fm[r, g][:, sl[:, i]] + own[:, :, i])
                fm[r, g][:, sl] = 0
                fm[r, g][:, c] = fm[r, g][:, c] - own
                s0[r, g][:, a] = new; s1[r, g][:, a] = (new - old) * inv[de]
                cnt = np.add.reduce((np.abs(new) > h[r, g]).astype(np.int64), axis=0)
                t[r, g][a] = tb[:, 0]; dt[r, g][a] = np.where(cnt >= HI, 1, np.where(cnt <= LO, 4, 2))
        come = swap(fm[..., 4 * V:])
        for r in range(N):
            for g in range(8): fm[r, g][:, m[r, g]] = fm[r, g][:, m[r, g]] + come[r, g]
        fm[..., 4 * V:] = 0
    k = fm[..., :4 * V].reshape(N, 8, 16, V, 4)
    ym = ((k[..., 0] + k[..., 1]) + k[..., 2]) + k[..., 3]
    return {"y0": s0.reshape(N, 128, V), "y1": s1.reshape(N, 128, V), "ym": np.ascontiguousarray(ym).reshape(N, 128, V), "yt": np.concatenate([t, dt], axis=2).astype(np.float32)}

@@ -1,0 +1,701 @@
+from concourse.bass import DstId, RemoteDMATransfer
+from concourse.mybir import AluOpType as A, ActivationFunctionType as AF
+
+V, FP, CAP, RO, BLKW = 896, 224, 320, 5, 1504
+F, H, I, U = "float32", "bfloat16", "int32", "uint16"
+fA, fB, fNLO, fNHI, fT, fM, fD, fR, fJLO, fJHI = 0, 4, 8, 9, 10, 11, 12, 13, 14, 15
+NW = 26
+Q_ON_PE = False
+J_ON_PE = False
+MSG = [(w_, m_) for m_ in range(RO + 1) for w_ in (1, 2, 3) if not (w_ == 3 and m_ == 0) and not (w_ == 2 and m_ == RO)]
+
+
+def sb(n, t):
+    return ("sbuf", [128, n], t)
+
+
+SCRATCH = {
+    "ST": sb(1440, H), "C": sb(3456, H), "G": sb(3584, H), "GN": sb(1280, H), "GO": sb(320, H),
+    "QA": sb(1440, F), "QB": sb(1440, F), "LG": sb(6 * BLKW, F), "YM": sb(V, F), "YT": sb(2 * V, F),
+    "snd1": sb(6 * FP, H), "lnd1": sb(6 * FP, H), "hb1": sb(6 * 96, H),
+    "snd2": ("sbuf", [128, 35, 64], F), "lnd2": ("sbuf", [128, 35, 64], F), "hb2": ("sbuf", [128, 15, 64], F),
+    "snd3": sb(6 * FP, F), "hb3": sb(6 * 96, F),
+    "qa": sb(V, H), "qb": sb(V, H), "TD": sb(V, I), "TB": sb(V, H), "TH": sb(8, F), "NTH": sb(8, F),
+    "PI": sb(FP, I), "RI": sb(16, I), "RJ": sb(32, I), "rimU": sb(16, U), "rimS": sb(16, U), "rimK": sb(16, F), "ryF": sb(16, F), "ryU": sb(16, U),
+    "s0": sb(FP, I), "s1": sb(FP, I), "s2": sb(FP, I), "s3": sb(FP, I), "s4": sb(FP, I), "s5": sb(FP, I), "SI": sb(FP, F),
+    "colU": sb(FP, U), "KN": sb(FP, F), "AB": sb(2 * FP, H), "PE": sb(FP, F), "fa": sb(FP, F), "fb": sb(FP, F), "adU": sb(FP, U),
+    "Pi": sb(8, I), "CI": sb(8, I), "CF": sb(24, F), "MK": sb(8, F), "BR": sb(8, F), "RW": sb(16 * NW, H), "E1": sb(144, H),
+    "WS": sb(32, F), "X": sb(240, F), "XB": sb(256, H), "XQ": sb(144, F), "X16": sb(128, F), "CR": sb(512, H),
+    "HI": sb(V + 64, H), "Wt": sb(128, H), "Wc": sb(32, H), "ZI": sb(240, H), "ZF": sb(240, F), "NI": sb(128, F),
+    "ZE0": sb(144, H), "ZO0": sb(144, H), "ZA0": sb(144, H),
+    "ZE": sb(144, H), "ZT": sb(144, H), "ZP": sb(144, H), "ZO": sb(144, H), "ZQ": sb(144, H), "Z2": sb(144, H), "ZA": sb(4 * 144, H),
+    "BK": sb(128, H), "TR": sb(128, H), "Wb1": sb(128, H), "Wb2": sb(128, H), "Wy": sb(16, H), "CH": sb(FP, H),
+    "TRE": sb(56, F), "JX": sb(24, F), "TRJ": sb(24, F), "K3": sb(80, F), "ONE": sb(56, F), "SX": sb(64, F),
+    "L1": sb(384, F), "L2": sb(384, F), "L3": sb(384, F), "LS": sb(256, F), "LI": sb(8, F),
+    "bit": sb(FP, H), "can": sb(56, H), "v0": sb(56, F), "v1": sb(56, F), "posU": sb(56, U),
+    "UU": sb(200, U), "sm": sb(720, F), "si": sb(160, I), "su": sb(280, U),
+    "qe": sb(960, F), "cq": sb(3 * 1280, F), "w": sb(4 * 640, F), "r": sb(3 * 640, F), "FF": sb(1280, F), "xx": sb(640, F),
+    "po": sb(640, F), "gb": sb(4 * 320, H), "pk1": sb(FP, H), "pk2": sb(3 * FP, F),
+}
+for _k in range(8):
+    SCRATCH["P%d" % _k] = ("psum", [128, 512], F)
+SEMAPHORES = (["v", "a", "p", "g", "loc", "out"] + ["in%d" % k for k in range(8)]
+              + ["ar%d" % k for k in range(len(MSG))] + ["hs%d" % k for k in range(len(MSG))])
+
+
+def routes(T, topo):
+    plan = []
+    n = len(T.cores)
+    for r, c in enumerate(T.cores):
+        direct = [d - 1 for d in range(1, n) if topo.may_write(c, T.cores[(r + d) % n])]
+        far = [d - 1 for d in range(1, n) if d - 1 not in direct]
+        able = [h for h in topo.cores_of(c) if T.rank_of(h) is None
+                and all(topo.may_write(h, T.cores[(r + b + 1) % n]) for b in far)]
+        able.sort(key=lambda h: topo.die(h) != topo.die(c))
+        half = len(far) // 2
+        plan.append((direct, [(able[0], far[:half]), (able[1], far[half:])]))
+    return plan
+
+
+def shares(engs, n):
+    size = [1] * n
+    while True:
+        k = size.index(min(size))
+        if sum(size) + size[k] > len(engs):
+            break
+        size[k] *= 2
+    out, at = [], 0
+    for s in size:
+        out.append((sum(1 << e for e in engs[at:at + s]), s))
+        at += s
+    return out
+
+
+def piece(T, kind, which, m, a, n):
+    per = 3 if kind == "hb" else 7
+    if which == 2:
+        return T[kind + "2"][:, m * per + a:m * per + a + n, :]
+    if which == 3 and kind == "lnd":
+        return T.LG[:, BLKW * m + 1280 + 32 * a:BLKW * m + 1280 + 32 * (a + n)]
+    return T[kind + str(which)][:, (m * per + a) * 32:(m * per + a + n) * 32]
+
+
+def forward(g, T, topo, src, r, blocks, kind, first, which, m):
+    n = len(T.cores)
+    sh = shares(topo.engines(src, T.cores[(r + blocks[0] + 1) % n]), len(blocks))
+    tr = []
+    for b, (mask, _) in zip(blocks, sh):
+        rid, pid = topo.addr(T.cores[(r + b + 1) % n], src)
+        tr.append(RemoteDMATransfer(dst_ids=[DstId(rid=rid, pnc=pid)], dma_engine_mask=mask, remote_sem=T.sem["ar%d" % MSG.index((which, m))],
+                                    src=piece(T, kind, which, m, b - first, 1), dst=piece(T, "lnd", which, m, n - 2 - b, 1)))
+    g.remote_dma_fused(tr, local_sem=T.sem.loc)
+    return sum(s for _, s in sh)
+
+
+def rank_program(g, core, T, topo):
+    plan = routes(T, topo)
+    n = len(T.cores)
+    rank = T.rank_of(core)
+    if rank is None:
+        for r in range(n):
+            hs = shares(topo.engines(T.cores[r], plan[r][1][0][0]), 2)
+            for k, (h, blocks) in enumerate(plan[r][1]):
+                if h != core:
+                    continue
+                sent = 0
+                for j, (which, m) in enumerate(MSG):
+                    g.wait_ge(T.sem["hs%d" % j], hs[k][1])
+                    sent += forward(g, T, topo, core, r, blocks, "hb", blocks[0], which, m)
+                g.wait_ge(T.sem.loc, sent)
+        return
+    arrive = 0
+    for r in range(n):
+        for src, blocks in [(T.cores[r], plan[r][0])] + plan[r][1]:
+            sh = shares(topo.engines(src, T.cores[(r + blocks[0] + 1) % n]), len(blocks))
+            arrive += sum(s for b, (_, s) in zip(blocks, sh) if (r + b + 1) % n == rank)
+
+    Q = {"v": g.vector, "a": g.scalar, "p": g.tensor, "g": g, "s": g.sync}
+    cnt = {"v": 0, "a": 0, "p": 0, "g": 0, "loc": 0, "out": 0}
+    seen = {e: {} for e in Q}
+    wr, rd = {}, {}
+
+    def need(e, toks):
+        top = {}
+        for s, val in toks:
+            if not (e == "p" and s == "p"):
+                top[s] = max(top.get(s, 0), val)
+        for s, val in top.items():
+            if seen[e].get(s, 0) < val:
+                Q[e].wait_ge(T.sem[s], val)
+                seen[e][s] = val
+
+    def deps(e, reads, writes):
+        toks = []
+        for x in reads:
+            if x in wr:
+                toks.append(wr[x])
+            if x[0] == "P" and x[1:].isdigit():
+                toks += [t for t in rd.get(x, []) if t[0] != e]
+        for x in writes:
+            if x in wr:
+                toks.append(wr[x])
+            toks += rd.get(x, [])
+        return toks
+
+    def op(e, fn, reads, writes):
+        need(e, deps(e, reads, writes))
+        fn().then_inc(T.sem[e], 1)
+        cnt[e] += 1
+        tok = (e, cnt[e])
+        for x in reads:
+            rd.setdefault(x, []).append(tok)
+        for x in writes:
+            wr[x] = tok
+            rd[x] = []
+        return tok
+
+    vec, act, pe = g.vector, g.scalar, g.tensor
+
+    def tt(out, a, b, o, reads, writes):
+        return op("v", lambda: vec.tensor_tensor(out, a, b, o), reads, writes)
+
+    def ts(out, a, s1, o1, reads, writes, s2=None, o2=None):
+        if o2 is None:
+            return op("v", lambda: vec.tensor_scalar(out, a, s1, None, o1), reads, writes)
+        return op("v", lambda: vec.tensor_scalar(out, a, s1, s2, o1, o2), reads, writes)
+
+    def cp(out, a, reads, writes):
+        return op("v", lambda: vec.tensor_copy(out, a), reads, writes)
+
+    def ms(out, c, writes, reads=()):
+        return op("v", lambda: vec.memset(out, c), reads, writes)
+
+    def ac(out, a, reads, writes, func=AF.Identity, bias=0.0, scale=1.0):
+        return op("a", lambda: act.activation(out, a, func, bias=bias, scale=scale), reads, writes)
+
+    def mm(out, l, r, start, stop, reads, writes):
+        return op("p", lambda: pe.matmul(out, l, r, start, stop), reads, writes)
+
+    def iota(out, pat, base, cm, writes, exact=False):
+        if exact:
+            return op("g", lambda: g.iota(out, pat, base, cm), [], writes)
+        return op("g", lambda: g.iota(out, pat, base, cm, allow_small_or_imprecise_dtypes=True), [], writes)
+
+    def sel(out, a, cmp, fill, base, cm, reads, writes):
+        return op("g", lambda: g.affine_select(out, a, [[1, 128]], cmp, fill, base, cm), reads, writes)
+
+    def load(e, k, out, src, name):
+        Q[e].dma_start(out, src).then_inc(T.sem["in%d" % k], 16)
+        wr[name] = ("in%d" % k, 16)
+
+    def store(out, src, reads):
+        need("s", deps("s", reads, []))
+        g.sync.dma_start(out, src).then_inc(T.sem.out, 16)
+        cnt["out"] += 16
+
+    def send(which, m, reads, lands):
+        need("g", deps("g", reads, []))
+        hs = shares(topo.engines(core, plan[rank][1][0][0]), 2)
+        tr = []
+        for (h, blocks), (mask, s) in zip(plan[rank][1], hs):
+            rid, pid = topo.addr(h, core)
+            tr.append(RemoteDMATransfer(dst_ids=[DstId(rid=rid, pnc=pid)], dma_engine_mask=mask, remote_sem=T.sem["hs%d" % MSG.index((which, m))],
+                                        src=piece(T, "snd", which, m, blocks[0], 3), dst=piece(T, "hb", which, m, 0, 3)))
+            cnt["loc"] += s
+        g.remote_dma_fused(tr, local_sem=T.sem.loc)
+        cnt["loc"] += forward(g, T, topo, core, rank, plan[rank][0], "snd", 0, which, m)
+        wr[lands] = ("ar%d" % MSG.index((which, m)), arrive)
+
+    P = [T["P%d" % k] for k in range(8)]
+    ST, QA, QB, LG, WS, CF = T.ST, T.QA, T.QB, T.LG, T.WS, T.CF
+    STw, QAw, QBw = ["STl", "STh"], ["QAl", "QAh"], ["QBl", "QBh"]
+
+    def wcol(k):
+        return WS[:, k:k + 1]
+
+    def W1(f):
+        return T.E1[0:1, 15 - f:143 - f]
+
+    cI, cG, cQ, cK, cP, cM, cE, nE, cO, c320, n320, n336, c12, c4, c2, cA, nK = [CF[:, k:k + 1] for k in range(17)]
+
+    load("s", 0, T.TD[0:8, :], T.t0[:], "TD0")
+    load("a", 1, T.TD[8:16, :], T.d0[:], "TD1")
+    load("s", 2, T.TD[16:24, :], T.d0[:], "TD2")
+    load("a", 3, T.RI[:, 0:14], T.rim[:], "RI")
+    load("s", 4, T.qa[:], T.q0[:], "qa")
+    load("a", 5, T.qb[:], T.q1[:], "qb")
+    load("s", 6, T.PI[:], T.port[:], "PI")
+    load("s", 7, T.TH[:, 0:1], T.th[:], "TH")
+
+    ms(T.Wt[0:24, :], 0.0, ["Wt"])
+    ms(T.RW[0:1, :], 0.0, ["RW0"])
+    ms(T.E1[0:1, :], 0.0, ["E1"])
+    iota(cP, [[0, 1]], 0, 1, ["cP"])
+    iota(T.XB[0:1, :], [[1, 256]], 0, 0, ["XB"])
+    for base, fill in ((-fT, 1.0), (128 - fD, -1.0), (256 - fD, 1.0), (256 - fM, 1.0)):
+        sel(T.Wt[0:24, :], T.Wt[0:24, :], A.not_equal, fill, base, -16, ["Wt"], ["Wt"])
+    iota(T.X[:], [[1, 240]], 0, 0, ["X"])
+    iota(T.Pi[:, 0:1], [[0, 1]], 0, 1, ["Pi"], True)
+    iota(T.XQ[:], [[1, 36], [0, 4]], 0, 0, ["XQ"])
+    iota(T.X16[:], [[1, 8], [0, 16]], 0, 0, ["X16"])
+    iota(T.SI[:], [[16, FP]], 15, 1, ["SI"])
+    iota(T.TRE[:], [[16, 56]], 2560, 1, ["TRE"])
+    ms(T.CR[0:1, :], float(7 * rank), ["CR"])
+    ms(T.E1[0:1, 15:144:16], 1.0, ["E1"])
+    ts(cM, cP, 16.0, A.is_ge, ["cP"], ["cM"], 2.0, A.mult)
+    for k in range(7):
+        wr["HI"] = ac(T.HI[0:1, 128 * k:128 * k + 128], T.XB[0:1, 0:128], ["XB"], [], bias=float(k), scale=0.0)
+    for k in range(2):
+        wr["HI"] = ac(T.HI[0:1, V + 32 * k:V + 32 * k + 32], T.XB[0:1, 0:32], ["XB"], [], bias=float(9 + k), scale=0.0)
+    terms = [(fA, 0, 0.25, 4, NW + 1), (fB, 0, 32, 4, NW + 1), (fA, 4, 1, 4, NW + 1), (fM, 8, 1, 2, NW),
+             (fNLO, 9, 1, 2, 9), (fNHI, 9, 128, 2, 9), (fT, 10, -1, 4, 1), (fM, 10, -32, 4, 1), (fD, 10, 64, 4, 1),
+             (fR, 14, BLKW, 4, 1), (fJLO, 14, 1, 4, 1), (fJHI, 14, 128, 4, 1), (fT, 18, 8192, 2, NW), (fD, 18, -8192, 1, 1),
+             (fT, 19, 1, 1, 1), (fM, 20, 3.5, 1, 1), (fD, 20, 8.5, 1, 1), (fM, 21, -2, 1, 1), (fD, 21, 1, 1, 1),
+             (0, 22, 1, 11, NW), (fM, 23, 1, 1, 1), (fD, 23, -1, 1, 1), (fM, 24, 4, 1, 1), (fR, 25, 1, 1, 1)]
+    for j, (f, col, c, count, step) in enumerate(terms):
+        a = NW * f + col
+        x = T.RW[0:1, a:a + (count - 1) * step + 1:step]
+        if j % 2:
+            wr["RWa"] = ac(x, x, ["RW0"], [], bias=float(c), scale=0.0)
+        else:
+            wr["RWv"] = ms(x, float(c), [], ["RW0"])
+    ts(T.TB[0:24, :], T.TD[0:24, :], CF[0:24, 5:6], A.max, ["TD0", "TD1", "TD2", "cM"], ["TB"])
+    ts(T.RJ[:, 0:14], T.RI[:, 0:14], 2, A.arith_shift_right, ["RI"], ["RJ0"])
+    ts(T.ZI[:, 0:128], T.X[:, 0:128], cP, A.is_equal, ["X", "cP"], ["ZI0"])
+    ts(T.ZI[:, 128:240], T.X[:, 0:112], cP, A.is_equal, ["X", "cP"], ["ZI"])
+    cp(T.rimU[:, 0:14], T.RJ[:, 0:14], ["RJ0"], ["rimU"])
+    halves = ((0, 512), (512, V))
+    for k, (a, b) in enumerate(halves):
+        mm(P[k][:, 0:b - a], W1(fNHI), T.HI[0:1, a:b], True, False, ["E1", "HI"], ["P%d" % k])
+        mm(P[k][:, 0:b - a], W1(fNHI), T.CR[0:1, 0:b - a], False, False, ["E1", "CR"], ["P%d" % k])
+        for c in range(a, b, 128):
+            mm(P[k][:, c - a:c - a + 128], W1(fNLO), T.XB[0:1, 0:128], False, False, ["E1", "XB"], ["P%d" % k])
+    for k, (a, b) in enumerate(halves):
+        mm(P[k][:, 0:b - a], T.Wt[0:24, :], T.TB[0:24, a:b], False, True, ["Wt", "TB"], ["P%d" % k])
+    ac(ST[:, 0:512], P[0][:, 0:512], ["P0"], ["ST0"])
+    cp(ST[:, 512:V], P[1][:, 0:V - 512], ["P1"], ["STl"])
+    for b in range(7):
+        j0 = (6 - b) * 32
+        mm(P[4][:, 32 * b:32 * b + 32], W1(fJLO), T.XB[0:1, 128 + j0 % 128:160 + j0 % 128], True, False, ["E1", "XB"], ["P4"])
+        mm(P[4][:, 32 * b:32 * b + 32], W1(fJHI), T.HI[0:1, V + 32 * (j0 // 128):V + 32 * (j0 // 128) + 32], False, True, ["E1", "HI"], ["P4"])
+    ac(T.CH[:], P[4][:, 0:FP], ["P4"], ["CH"])
+    for f in range(16):
+        mm(P[5][:, 0:NW], W1(f), T.RW[0:1, NW * f:NW * f + NW], f == 0, f == 15, ["E1", "RWa", "RWv"], ["P5"])
+    up = 32 * (n - 1 - rank)
+
+    def shift(bank, src, a, Z, reads):
+        for lo, hi, o in ((0, up, 112), (up, FP, 16)):
+            if hi > lo:
+                mm(P[bank][:, lo:hi], Z[:, o:o + 128], src[:, a + lo:a + hi], True, True, reads, ["P%d" % bank])
+
+    def message1(m, fill=None):
+        cp(T.pk1[:], ST[:, 0:V].indirect(T.rimU[:, 0:14]), ["STl", "ST0", "rimU"], ["pk1"])
+        shift(2, T.pk1, 0, T.ZI, ["pk1", "ZI", "ZI0"])
+        if fill:
+            fill()
+        tt(T.snd1[:, m * FP:(m + 1) * FP], P[2][:, 0:FP], T.CH[:], A.max, ["P2", "CH"], ["snd1_%d" % m])
+        send(1, m, ["snd1_%d" % m], "lnd1_%d" % m)
+
+    def pack_q(m, fill=None):
+        for k, (W, nm) in enumerate(((QA, "QAl"), (QB, "QBl"))):
+            ac(T.pk2[:, k * FP:(k + 1) * FP], W[:, 0:V].indirect(T.rimU[:, 0:14]), [nm, "rimU"], ["pk2_%d" % k])
+            shift(2 + k, T.pk2, k * FP, T.ZF, ["pk2_%d" % k, "ZF"])
+            if fill and k == 0:
+                fill()
+        for k in range(2):
+            ac(T.snd2[:, 7 * m:7 * m + 7, 32 * k:32 * k + 32], P[2 + k][:, 0:FP], ["P%d" % (2 + k)], ["snd2_%d_%d" % (m, k)])
+        send(2, m, ["snd2_%d_0" % m, "snd2_%d_1" % m], "lnd2_%d" % m)
+
+    def columns():
+        ts(T.CI[:, 0:1], T.Pi[:, 0:1], 15, A.bitwise_and, ["Pi"], ["CI0"])
+        ts(T.CI[:, 1:2], T.Pi[:, 0:1], 4, A.arith_shift_right, ["Pi"], ["CI1"])
+        ts(T.CI[:, 2:3], T.Pi[:, 0:1], 2, A.arith_shift_right, ["Pi"], ["CI2"], 3, A.bitwise_and)
+        ts(T.CI[:, 3:4], T.Pi[:, 0:1], 3, A.bitwise_and, ["Pi"], ["CI3"])
+
+    message1(0, columns)
+    cp(CF[:, 0:4], T.CI[:, 0:4], ["CI0", "CI1", "CI2", "CI3"], ["CF"])
+    ac(WS[:, 0:NW], P[5][:, 0:NW], ["P5"], ["WS"])
+    ac(QA[:, 0:V], T.qa[:], ["qa"], ["QAl"])
+    for x, sc, bi, nm in ((cE, 16, 15, "cE"), (nE, -16, -15, "nE"), (cO, 4, 3, "cO"), (c12, 16, 12, "c12"), (c4, 16, 4, "c4"),
+                          (c320, 320, 0, "c320"), (n320, -320, 0, "n320"), (n336, -336, 0, "n336")):
+        ac(x, cG, ["CF"], [nm], bias=float(bi), scale=float(sc))
+    ac(T.SI[:], T.SI[:], ["SI", "nE"], ["SI"], bias=nE)
+    ac(c2, cQ, ["CF", "c12"], ["c2"], bias=c12)
+    ac(cA, cK, ["CF", "c4"], ["cA"], bias=c4)
+    ac(nK, wcol(18), ["WS"], ["nK"], scale=-1.0)
+    ac(QB[:, 0:V], T.qb[:], ["qb"], ["QBl"])
+    ac(T.ZF[:], T.ZI[:], ["ZI", "ZI0"], ["ZF"])
+    pack_q(0)
+
+    c = T.PI[:]
+    ts(T.s1[:], c, 4.0, A.mult, ["PI"], ["s1"], -10752.0, A.add)
+    ts(T.s3[:], c, float(3584 + up), A.is_ge, ["PI"], ["s3"])
+    tt(T.s0[:], T.s1[:], c, A.max, ["s1", "PI"], ["s0"])
+    tt(T.s2[:], T.SI[:], c, A.is_lt, ["SI", "PI"], ["s2"])
+    ts(T.colU[:], T.s0[:], 0.25, A.mult, ["s0"], ["colU"], -0.375, A.add)
+    tt(T.s2[:], T.s2[:], T.s3[:], A.subtract, ["s2", "s3"], ["s2"])
+    ts(T.s4[:], T.s0[:], 127, A.bitwise_and, ["s0"], ["s4"])
+    ts(T.s5[:], T.s0[:], 7, A.arith_shift_right, ["s0"], ["s5"])
+    ts(T.s3[:], T.s2[:], 128.0, A.mult, ["s2"], ["s3"])
+    ts(T.MK[:, 0:4], T.X[:, 0:4], cQ, A.is_equal, ["X", "CF"], ["MK"])
+    ts(T.ZA0[:], T.X[:, 0:144], cA, A.is_equal, ["X", "cA"], ["ZA0"])
+    ts(T.ZO0[:], T.XQ[:], cO, A.is_equal, ["XQ", "cO"], ["ZO0"])
+    ts(T.ZE0[:], T.X[:, 0:144], cE, A.is_equal, ["X", "cE"], ["ZE0"])
+    tt(T.AB[:, FP:2 * FP], T.s5[:], T.s2[:], A.subtract, ["s5", "s2"], ["ABb"])
+    tt(T.AB[:, 0:FP], T.s4[:], T.s3[:], A.add, ["s4", "s3"], ["ABa"])
+    for m in range(4):
+        wr["ZA"] = ac(T.ZA[:, 144 * m:144 * m + 144], T.ZA0[:], ["ZA0", "MK"], [], scale=T.MK[:, m:m + 1])
+    ac(T.ZO[:], T.ZO0[:], ["ZO0", "nK"], ["ZO"], scale=nK)
+    ac(T.ZE[:], T.ZE0[:], ["ZE0", "WS"], ["ZE"], scale=wcol(18))
+    ac(T.TRE[:], T.TRE[:], ["TRE", "n336"], ["TRE"], bias=n336)
+    ts(T.BK[:], T.X16[:], cG, A.is_equal, ["X16", "CF"], ["BK"])
+    ts(T.Z2[:], T.X[:, 0:144], c2, A.is_equal, ["X", "c2"], ["Z2"])
+    sel(T.TR[:], T.BK[:], A.is_gt, 0.0, 0, -1, ["BK"], ["TR"])
+    sel(T.TR[:], T.TR[:], A.not_equal, -1024.0, 0, -1, ["TR"], ["TR"])
+    iota(T.C[:, 0:2560], [[0, 2560]], 0, 0, ["C"])
+    iota(T.JX[:, 0:20], [[1, 20]], 1024, 20, ["JX"])
+    iota(T.TRJ[:, 0:20], [[16, 20]], 1120 + V * rank + 15, 1, ["TRJ"])
+    iota(T.K3[:], [[320, 4], [0, 20]], 0, 0, ["K3"])
+    iota(LG[:, 0:BLKW], [[0, BLKW]], 0, 0, ["LG0"])
+    for k, (a, b) in enumerate(halves):
+        mm(P[k][:, 0:b - a], T.ZI[:, 0:128], ST[:, a:b], True, False, ["ZI0", "STl", "ST0"], ["P%d" % k])
+        for m in range(4):
+            mm(P[k][:, m:b - a:4], T.ZA[:, 144 * m:144 * m + 128], T.AB[:, FP + a // 4:FP + b // 4], False, False, ["ZA", "ABb"], ["P%d" % k])
+            mm(P[k][:, m:b - a:4], T.ZA[:, 144 * m + 4:144 * m + 132], T.AB[:, a // 4:b // 4], False, m == 3, ["ZA", "ABa"], ["P%d" % k])
+    ms(T.ONE[:], 1.0, ["ONE"])
+    ms(ST[:, V:V + FP], 0.0, ["STh"])
+    cp(T.rimS[:, 0:14], T.RI[:, 0:14], ["RI"], ["rimS"])
+    ms(T.SX[:, 0:1], 1024.0, ["SX0"])
+    cp(T.Wc[:, 0:18], WS[:, 0:18], ["WS"], ["Wc"])
+    ts(T.NTH[:, 0:1], T.TH[:, 0:1], -1.0, A.mult, ["TH"], ["NTH"])
+    ts(T.RJ[:, 16:30], T.RI[:, 0:14], 3, A.bitwise_and, ["RI"], ["RJ1"])
+    ts(T.s1[:], T.s0[:], 3, A.bitwise_and, ["s0"], ["s1"])
+    ts(T.rimK[:, 0:14], T.RJ[:, 16:30], 320.0, A.mult, ["RJ1"], ["rimK"])
+    ts(T.KN[:], T.s1[:], 320.0, A.mult, ["s1"], ["KN"])
+    ac(ST[:, 0:512], P[0][:, 0:512], ["P0"], ["ST0", "STl"])
+    ac(ST[:, 512:V], P[1][:, 0:V - 512], ["P1"], ["STl"])
+
+    def later_constants():
+        ac(T.JX[:, 0:20], T.JX[:, 0:20], ["JX", "n320"], ["JX"], bias=n320)
+        ac(T.TRJ[:, 0:20], T.TRJ[:, 0:20], ["TRJ", "nE"], ["TRJ"], bias=nE)
+        ac(T.ZT[:], T.ZE0[:], ["ZE0", "WS"], ["ZT"], scale=wcol(19))
+        for x in ("L1", "L2", "L3"):
+            ac(T[x][:, 0:192], T.X[:, 0:192], ["X"], [x + "z"], scale=0.0)
+
+        def put(x, a, b, val):
+            wr[x] = ac(T[x][:, a:b], T.X[:, 0:b - a], ["X", "L3z"], [], bias=val, scale=0.0)
+
+        put("LS", 0, 128, 0.5)
+        put("LS", 128, 256, -0.5)
+        for di, d in enumerate((4, 2, 1)):
+            o = 64 * di + 32
+            for a in range(d):
+                lo = o - 3 if a == 0 else o + a
+                put("L1", lo, o + a + 1, -(d - a) / 32.0)
+                put("L2", lo, o + a + 1, -(d * d - a * a) / 64.0)
+            for a in range(d - 4, d):
+                put("L3", o + a, o + a + 1, ((d - a) ** 2 - (max(a, 0) - a) ** 2) / 64.0)
+        for x in ("L1", "L2", "L3"):
+            ac(T[x][:, 192:384], T[x][:, 0:192], [x], [x], scale=-1.0)
+        ac(T.NI[:], T.ZI[:, 0:128], ["ZI0"], ["NI"], scale=-1.0)
+
+    def last_constants():
+        for a, b, val in ((0, 3, 0.5), (3, 4, 1.0), (4, 5, 0.25)):
+            wr["LI"] = ac(T.LI[:, a:b], T.X[:, 0:b - a], ["X"], [], bias=val, scale=0.0)
+        ac(T.Wb1[:], T.ZI[:, 0:128], ["ZI0", "WS"], ["Wb1"], scale=wcol(22))
+        ac(T.Wb2[:], T.ZE0[:, 15 - fT:143 - fT], ["ZE0", "WS"], ["Wb2"], scale=wcol(23))
+        for r in range(1, RO + 1):
+            wr["BR"] = ac(T.BR[:, r:r + 1], wcol(25), ["WS"], [], bias=wcol(24), scale=float(r))
+        ac(T.ZP[:], T.ZE0[:], ["ZE0", "WS"], ["ZP"], scale=wcol(14))
+        ac(T.ZQ[:], T.ZO0[:], ["ZO0", "WS"], ["ZQ"], scale=wcol(14))
+        ac(T.Wy[:, 0:8], T.BK[:, 0:128:16], ["BK", "WS"], ["Wy0"], scale=wcol(19))
+        ac(T.Wy[:, 8:16], T.BK[:, 0:128:16], ["BK", "WS"], ["Wy1"], scale=wcol(23))
+
+    def slots_a(a, b, s):
+        ac(T.G[:, 16 * a:16 * b], ST[:, 0:V + FP].indirect(T.colU[:, a:b]), STw + ["colU"], ["G%d" % s])
+
+    def slots_v(a, b, s):
+        cp(T.G[:, 16 * a:16 * b], ST[:, 0:V + FP].indirect(T.colU[:, a:b]), STw + ["colU"], ["G%d" % s])
+
+    def all_slots(m, bank, Z, zn):
+        Gs = ["G0", "G1", "G2"]
+        cp(T.G[:, 0:4 * V].indirect(T.rimS[:, 0:14]), T.lnd1[:, m * FP:(m + 1) * FP], ["lnd1_%d" % m, "rimS"], Gs)
+        for i in range(16):
+            mm(P[bank][:, 0:FP], Z[:, 15 - i:143 - i], T.G[:, i:4 * V:16], False, i == 15, Gs + [zn], ["P%d" % bank])
+
+    def lgw(r):
+        return ["LG0"] + ["LGl%d_%d" % (k, j) for k in range(1, r) for j in range(4)] + ["LGh%d" % k for k in range(1, r)]
+
+    UU, sm, si, su, qe, cq, w, rr, FF, xx, po, gb = T.UU, T.sm, T.si, T.su, T.qe, T.cq, T.w, T.r, T.FF, T.xx, T.po, T.gb
+    eU, caseU, takeU, keepU, eS = UU[:, 180:200], su[:, 0:80], su[:, 80:160], su[:, 160:240], su[:, 240:260]
+    pre, knf, Pk, zz, own, t0, t1, t3 = [sm[:, 80 * k:80 * k + 80] for k in range(8)]
+    t2 = sm[:, 640:660]
+    L1, L2, L3, LS, LGall = T.L1[:, 0:384], T.L2[:, 0:384], T.L3[:, 0:384], T.LS[:, 0:256], LG[:, 0:6 * BLKW]
+    q0e, q1e, inv = qe[:, 0:320], qe[:, 320:640], qe[:, 640:960]
+    qf, dq = po[:, 0:320], po[:, 320:640]
+    g1, g2, nn, base = [gb[:, 320 * k:320 * k + 320] for k in range(4)]
+
+    def sums(r, a, b):
+        out, names = LG[:, BLKW * r + 320 * a:BLKW * r + 320 * b], ["LGl%d_%d" % (r, k) for k in range(a, b)]
+        fs = ["F%d" % k for k in range(a, b)]
+        if r == 1:
+            ac(out, FF[:, 320 * a:320 * b], fs, names, scale=-1.0)
+        else:
+            tt(out, LG[:, 0:BLKW * r].indirect(su[:, 160 + 20 * a:160 + 20 * b]), FF[:, 320 * a:320 * b], A.subtract, lgw(r) + ["keepU"] + fs, names)
+
+    def rim_a():
+        tt(T.ryF[:, 0:14], P[4][:, 0:14], T.rimK[:, 0:14], A.add, ["P4", "rimK"], ["ryF"])
+
+    def rim_b():
+        cp(T.ryU[:, 0:14], T.ryF[:, 0:14], ["ryF"], ["ryU"])
+
+    def pack_y(r):
+        ac(T.pk2[:, 2 * FP:3 * FP], LG[:, 0:BLKW * r + 1280].indirect(T.ryU[:, 0:14]),
+           lgw(r) + ["LGl%d_%d" % (r, k) for k in range(4)] + ["ryU"], ["pk2_2"])
+        shift(3, T.pk2, 2 * FP, T.ZF, ["pk2_2", "ZF"])
+        ac(T.snd3[:, r * FP:(r + 1) * FP], P[3][:, 0:FP], ["P3"], ["snd3_%d" % r])
+        send(3, r, ["snd3_%d" % r], "LGh%d" % r)
+
+    for r in range(1, RO + 1):
+        for m in range(4):
+            mm(P[5][:, 0:FP], T.ZO[:, 12 - 4 * m:140 - 4 * m], ST[:, m:V:4], m == 0, False, ["ZO", "STl"], ["P5"])
+        if r == 1:
+            slots_a(0, 56, 0)
+            slots_v(112, FP, 2)
+            slots_a(56, 112, 1)
+            later_constants()
+            last_constants()
+        all_slots(r - 1, 5, T.ZE, "ZE")
+        ac(ST[:, V:V + FP], T.lnd1[:, (r - 1) * FP:r * FP], ["lnd1_%d" % (r - 1)], ["STh"])
+        if r > 1:
+            sums(r - 1, 1 if r > 2 else 0, 4)
+        ts(T.bit[:], P[5][:, 0:FP], 0.0, A.is_gt, ["P5"], ["bit"])
+        for h in range(4):
+            mm(P[6][:, 0:56], T.Z2[:, 12 - 4 * h:140 - 4 * h], T.bit[:, h:FP:4], h == 0, h == 3, ["Z2", "bit"], ["P6"])
+        if r > 1:
+            rim_a()
+        ts(T.can[:], P[6][:, 0:56], 3.5, A.is_ge, ["P6"], ["can"])
+        mm(P[1][:, 0:56], T.BK[:], T.can[:], True, True, ["BK", "can"], ["P1"])
+        mm(P[0][:, 0:56], T.TR[:], T.can[:], True, True, ["TR", "can"], ["P0"])
+        if r > 1:
+            rim_b()
+            pack_y(r - 1)
+        op("v", lambda: vec.tensor_tensor_scan(T.SX[:, 1:57], T.ONE[:], P[1][:, 0:56], 1024.0, A.mult, A.add), ["ONE", "P1"], ["SX"])
+        tt(T.v0[:], P[0][:, 0:56], T.SX[:, 0:56], A.add, ["P0", "SX", "SX0"], ["v0"])
+        ts(T.v1[:], T.v0[:], float(CAP), A.is_ge, ["v0"], ["v1"], 8192.0, A.mult)
+        tt(T.v0[:], T.v0[:], T.v1[:], A.add, ["v0", "v1"], ["v0"])
+        tt(T.v0[:], T.v0[:], T.TRE[:], A.min, ["v0", "TRE"], ["v0"])
+        ts(T.posU[:], T.v0[:], c320, A.add, ["v0", "c320"], ["posU"])
+        cp(T.C[:, 0:3456].indirect(T.posU[:, 0:56]), ST[:, 0:V], ["posU", "STl"], ["C"])
+        ac(QB[:, V:V + FP], T.lnd2[:, 7 * r - 7:7 * r, 32:64], ["lnd2_%d" % (r - 1)], ["QBh"])
+        ac(QA[:, V:V + FP], T.lnd2[:, 7 * r - 7:7 * r, 0:32], ["lnd2_%d" % (r - 1)], ["QAh"])
+        for b in range(20):
+            mm(P[7][:, b:360:20], T.C[:, b:2560:20], T.Wc[:, 0:18], True, True, ["C", "Wc"], ["P7"])
+        ts(t2, T.JX[:, 0:20], T.SX[:, 56:57], A.is_ge, ["JX", "SX"], ["t2"], 16384.0, A.mult)
+        ts(UU[:, 0:180], P[7][:, 0:180], -0.375, A.add, ["P7"], ["UU"])
+        ts(eU, P[7][:, 180:200], float(-V * rank), A.add, ["P7"], ["eU"])
+        cp(T.GN[:, 0:640], ST[:, 0:V + FP].indirect(UU[:, 0:40]), STw + ["UU"], ["GNv"])
+        ac(T.GN[:, 640:1280], ST[:, 0:V + FP].indirect(UU[:, 40:80]), STw + ["UU"], ["GNa"])
+        for i in range(16):
+            mm(P[4][:, 0:80], T.ZT[:, 15 - i:143 - i], T.GN[:, i:1280:16], i == 0, i == 15, ["GNv", "GNa", "ZT"], ["P4"])
+        if r > 1:
+            for i in range(16):
+                mm(P[5][:, 0:80], T.ZP[:, 15 - i:143 - i], T.GN[:, i:1280:16], i == 0, i == 15, ["GNv", "GNa", "ZP"], ["P5"])
+        ts(pre, P[7][:, 80:160], 128.0, A.is_ge, ["P7"], ["pre"], 192.0, A.mult)
+        tt(t2, P[7][:, 180:200], t2, A.add, ["P7", "t2"], ["t2"])
+        tt(pre, P[7][:, 200:280], pre, A.add, ["P7", "pre"], ["pre"])
+        tt(t2, t2, T.TRJ[:, 0:20], A.min, ["t2", "TRJ"], ["t2"])
+        if r > 1:
+            cp(si[:, 0:80], P[7][:, 80:160], ["P7"], ["si0"])
+        tt(t0, P[4][:, 0:80], pre, A.add, ["P4", "pre"], ["t0"])
+        ts(eS, t2, float(-V * rank), A.add, ["t2"], ["eS"])
+        ts(caseU, t0, 160.0, A.add, ["t0"], ["caseU"])
+
+        def cut(buf, a, k, per=4):
+            o = 320 * (per * a + k % per)
+            return buf[:, o:o + 320]
+
+        def lst(x, k, o=0):
+            return x[:, o + 20 * k:o + 20 * k + 20]
+
+        def a_pre(k):
+            ac(cut(cq, 0, k), QB[:, 0:V + FP].indirect(lst(UU, k)), QBw + ["UU"], ["q1n%d" % k])
+            ac(cut(cq, 1, k), L1.indirect(lst(su, k)), ["L1", "caseU"], ["c1%d" % k])
+
+        def a_sgn(k):
+            ac(cut(cq, 2, k), LS.indirect(lst(UU, k, 80)), ["LS", "UU"], ["sg%d" % k])
+
+        def v_a(k):
+            b = k % 2
+            we, un, wn, je = [cut(w, a, k, 2) for a in range(4)]
+
+            def o_wn():
+                tt(wn, L3.indirect(lst(su, k)), cut(cq, 0, k), A.mult, ["L3", "caseU", "q1n%d" % k], ["wn%d" % b])
+
+            def o_un():
+                tt(un, QA[:, 0:V + FP].indirect(lst(UU, k)), cut(cq, 1, k), A.mult, QAw + ["UU", "c1%d" % k], ["un%d" % b])
+                mm(P[2 + b][:, 0:320], T.ZF[:, 0:128], wn, True, False, ["ZF", "wn%d" % b], ["P%d" % (2 + b)])
+                mm(P[2 + b][:, 0:320], T.NI[:], un, False, True, ["NI", "un%d" % b], ["P%d" % (2 + b)])
+
+            def o_we():
+                tt(we, L2.indirect(lst(su, k)), q1e, A.mult, ["L2", "caseU", "q1e"], ["we%d" % b])
+
+            def o_ue():
+                if J_ON_PE:
+                    tt(je, P[0][:, 0:320], cut(cq, 1, k), A.mult, ["P0", "c1%d" % k], ["je%d" % b])
+                    mm(P[1][:, 0:320], T.ZF[:, 0:128], we, True, False, ["ZF", "we%d" % b], ["P1"])
+                    mm(P[1][:, 0:320], T.ZF[:, 0:128], je, False, True, ["ZF", "je%d" % b], ["P1"])
+                else:
+                    tt(P[1][:, 0:320], P[0][:, 0:320], cut(cq, 1, k), A.mult, ["P0", "c1%d" % k], ["P1"])
+
+            def o_je():
+                if not J_ON_PE:
+                    tt(je, P[1][:, 0:320], we, A.add, ["P1", "we%d" % b], ["je%d" % b])
+
+            return [o_we, o_wn, o_un, o_ue, o_je] if k == 0 else [o_wn, o_un, o_we, o_ue, o_je]
+
+        def a_sq(k):
+            b = k % 2
+            re, rn, sq = [cut(rr, a, k, 2) for a in range(3)]
+            ac(rn, P[2 + b][:, 0:320], ["P%d" % (2 + b)], ["rn%d" % b], AF.Relu)
+            if J_ON_PE:
+                ac(re, P[1][:, 0:320], ["P1"], ["re%d" % b], AF.Relu)
+            else:
+                ac(re, cut(w, 3, k, 2), ["je%d" % b], ["re%d" % b], AF.Relu)
+            ac(sq, rn, ["rn%d" % b], ["sq%d" % b], AF.Square)
+            ac(P[4 + b][:, 0:320], re, ["re%d" % b], ["P%d" % (4 + b)], AF.Square)
+
+        def v_b(k):
+            b = k % 2
+            pb, nm = P[4 + b][:, 0:320], "P%d" % (4 + b)
+            x, xn = (cut(xx, 0, k, 2), "x%d" % b) if r > 1 else (cut(FF, 0, k), "F%d" % k)
+
+            def o_s():
+                tt(pb, pb, cut(rr, 2, k, 2), A.add, [nm, "sq%d" % b], [nm])
+
+            def o_f():
+                tt(cut(FF, 0, k), pb, cut(cq, 2, k), A.mult, [nm, "sg%d" % k], ["F%d" % k])
+
+            def o_x():
+                if r > 1:
+                    tt(x, LG[:, 0:BLKW * r].indirect(lst(su, k, 80)), cut(FF, 0, k), A.add, lgw(r) + ["takeU", "F%d" % k], [xn])
+
+            def o_q():
+                if Q_ON_PE and k < 3:
+                    if k == 0:
+                        mm(P[6][:, 0:320], T.ZF[:, 0:128], q0e, True, False, ["ZF", "q0e"], ["P6"])
+                    mm(P[6][:, 0:320], T.ZF[:, 0:128], x, False, k == 2, ["ZF", xn], ["P6"])
+                    return
+                src, sn = (P[0], "P0") if k == 0 else (P[6], "P6")
+                if k < 3:
+                    tt(P[6][:, 0:320], src[:, 0:320], x, A.add, [sn, xn], ["P6"])
+                else:
+                    tt(qf, src[:, 0:320], x, A.add, [sn, xn], ["qf"])
+
+            return [o_s, o_f, o_x, o_q]
+
+        def take():
+            return [lambda: ts(si[:, 80:160], si[:, 0:80], 3, A.bitwise_and, ["si0"], ["si2"]),
+                    lambda: tt(Pk, P[7][:, 280:360], T.K3[:], A.add, ["P7", "K3"], ["Pk"]),
+                    lambda: ts(knf, si[:, 80:160], 320.0, A.mult, ["si2"], ["knf"]),
+                    lambda: tt(zz, P[5][:, 0:80], knf, A.add, ["P5", "knf"], ["zz"]),
+                    lambda: tt(own, zz, Pk, A.is_gt, ["zz", "Pk"], ["own"]),
+                    lambda: tt(t1, own, zz, A.mult, ["own", "zz"], ["t1"]),
+                    lambda: cp(takeU, t1, ["t1"], ["takeU"])]
+
+        def keep():
+            return [lambda: tt(t3, own, Pk, A.mult, ["own", "Pk"], ["t3"]),
+                    lambda: tt(t3, Pk, t3, A.subtract, ["Pk", "t3"], ["t3"]),
+                    lambda: cp(keepU, t3, ["t3"], ["keepU"])]
+
+        def run(a, b=(), order=None):
+            both = {"a": list(a), "b": list(b)}
+            for ch in order or "a" * len(a):
+                if both[ch]:
+                    both[ch].pop(0)()
+
+        ac(q1e, QB[:, 0:V].indirect(eU), ["QBl", "eU"], ["q1e"])
+        a_pre(0)
+        ac(q0e, QA[:, 0:V].indirect(eU), ["QAl", "eU"], ["q0e"])
+        ac(P[0][:, 0:320], q0e, ["q0e"], ["P0"])
+        a_pre(1)
+        run(v_a(0), take()[:4] if r > 1 else (), "abbababaa")
+        a_sq(0)
+        a_sgn(0)
+        a_pre(2)
+        run(v_a(1), take()[4:] if r > 1 else (), "babababaa")
+        a_sq(1)
+        a_sgn(1)
+        a_pre(3)
+        run(v_a(2), v_b(0), "bababaaba")
+        a_sq(2)
+        a_sgn(2)
+        a_sgn(3)
+        ac(T.GO[:], ST[:, 0:V].indirect(eU), ["STl", "eU"], ["GO"])
+        run(v_a(3), v_b(1), "bababaaba")
+        mm(P[7][:, 0:320], T.Wb1[:], T.GO[:], True, False, ["Wb1", "GO"], ["P7"])
+        mm(P[7][:, 0:320], T.Wb2[:], T.GO[:], False, False, ["Wb2", "GO"], ["P7"])
+        for c0 in range(0, 320, 128):
+            c1 = min(c0 + 128, 320)
+            mm(P[7][:, c0:c1], W1(fJLO), T.XB[0:1, 0:c1 - c0], False, False, ["E1", "XB"], ["P7"])
+        mm(P[7][:, 0:320], W1(fJHI), T.HI[0:1, 0:320], False, True, ["E1", "HI"], ["P7"])
+        a_sq(3)
+        ac(base, P[7][:, 0:320], ["P7", "BR"], ["base"], bias=T.BR[:, r:r + 1])
+        ac(inv, T.LI[:, 0:5].indirect(UU[:, 160:180]), ["LI", "UU"], ["inv"])
+        run(v_b(2))
+        run(v_b(3))
+        ts(g1, qf, T.TH[:, 0:1], A.is_gt, ["qf", "TH"], ["g1"])
+        mm(P[1][:, 0:320], T.BK[:], g1, True, False, ["BK", "g1"], ["P1"])
+        ts(g2, qf, T.NTH[:, 0:1], A.is_lt, ["qf", "NTH"], ["g2"])
+        mm(P[1][:, 0:320], T.BK[:], g2, False, True, ["BK", "g2"], ["P1"])
+        tt(dq, qf, P[0][:, 0:320], A.subtract, ["qf", "P0"], ["dq"])
+        ts(nn, P[1][:, 0:320], wcol(20), A.is_ge, ["P1", "WS"], ["nn"], wcol(21), A.mult)
+        tt(ST[:, 0:1440].indirect(eS), nn, base, A.add, ["nn", "base", "eS"], STw)
+        slots_a(0, 104, 0)
+        message1(r, keep()[0] if r > 1 else None)
+        for i in range(16):
+            mm(P[4][:, 0:14], T.ZP[:, 15 - i:143 - i], T.pk1[:, i:FP:16], i == 0, i == 15, ["pk1", "ZP"], ["P4"])
+        if r == RO:
+            run(keep()[1:])
+            sums(r, 0, 4)
+            rim_a()
+            rim_b()
+            pack_y(r)
+            slots_a(104, 196, 1)
+            slots_v(196, FP, 2)
+        cp(QA[:, 0:1440].indirect(eS), qf, ["qf", "eS"], QAw)
+        tt(QB[:, 0:1440].indirect(eS), dq, inv, A.mult, ["dq", "inv", "eS"], QBw)
+        if r < RO:
+            slots_v(160, FP, 2)
+            pack_q(r, lambda: slots_a(104, 160, 1))
+            if r > 1:
+                run(keep()[1:])
+                sums(r, 0, 1)
+
+    store(T.y0[:], QA[:, 0:V], ["QAl"])
+    store(T.y1[:], QB[:, 0:V], ["QBl"])
+    for m in range(4):
+        mm(P[6][:, 0:FP], T.ZQ[:, 12 - 4 * m:140 - 4 * m], ST[:, m:V:4], m == 0, m == 3, ["ZQ", "STl"], ["P6"])
+    mm(P[5][:, 0:FP], T.ZF[:, 0:128], T.KN[:], True, False, ["ZF", "KN"], ["P5"])
+    ac(T.PE[:], P[6][:, 0:FP], ["P6"], ["PE"])
+    for j in range(2):
+        for k, (a, b) in enumerate(halves):
+            mm(P[2 * j + k][0:8, 0:b - a], T.Wy[:, 8 * j:8 * j + 8], ST[:, a:b], True, True, ["Wy%d" % j, "STl"], ["P%d" % (2 * j + k)])
+            wr["YT"] = ac(T.YT[0:8, j * V + a:j * V + b], P[2 * j + k][0:8, 0:b - a], ["P%d" % (2 * j + k)], [])
+    store(T.yt[:], T.YT[0:8, :], ["YT"])
+    all_slots(RO, 5, T.ZP, "ZP")
+    tt(T.fa[:], P[5][:, 0:FP], T.PE[:], A.is_gt, ["P5", "PE"], ["fa"])
+    tt(T.fb[:], P[5][:, 0:FP], T.fa[:], A.mult, ["P5", "fa"], ["fb"])
+    cp(T.adU[:], T.fb[:], ["fb"], ["adU"])
+    full = lgw(RO + 1) + ["adU"]
+    M = cq
+    cp(M[:, 0:V], LGall.indirect(T.adU[:, 0:56]), full, ["M0"])
+    for k in range(1, 4):
+        ac(M[:, V * k:V * k + V], LGall.indirect(T.adU[:, 56 * k:56 * k + 56]), full, ["M%d" % k])
+    for k in range(4):
+        a, pb, nm = V * k, P[6 + k % 2][:, 0:FP], "P%d" % (6 + k % 2)
+        tt(pb, M[:, a:a + V:4], M[:, a + 1:a + V:4], A.add, ["M%d" % k], [nm])
+        tt(pb, pb, M[:, a + 2:a + V:4], A.add, ["M%d" % k, nm], [nm])
+        tt(T.YM[:, FP * k:FP * k + FP], pb, M[:, a + 3:a + V:4], A.add, ["M%d" % k, nm], ["YM%d" % k])
+        store(T.ym[:, FP * k:FP * (k + 1)], T.YM[:, FP * k:FP * (k + 1)], ["YM%d" % k])
+    need("g", [(s, c_) for s, c_ in cnt.items()])

@@ -2,12 +2,23 @@ from concourse.bass import DstId, RemoteDMATransfer
 from concourse.mybir import AluOpType as A, ActivationFunctionType as AF
 
 V, FP, CAP, RO, BLKW = 896, 224, 320, 5, 1504
+NR = CAP - FP
 F, H, I, U = "float32", "bfloat16", "int32", "uint16"
 fA, fB, fNLO, fNHI, fT, fM, fD, fR, fJLO, fJHI = 0, 4, 8, 9, 10, 11, 12, 13, 14, 15
-NW = 26
-Q_ON_PE = False
-J_ON_PE = False
-MSG = [(w_, m_) for m_ in range(RO + 1) for w_ in (1, 2, 3) if not (w_ == 3 and m_ == 0) and not (w_ == 2 and m_ == RO)]
+NW = 34
+GW = 4800
+LO, QS = 640, CAP + FP
+TW = 1472
+MSG = [(w_, m_) for m_ in range(RO + 1) for w_ in (1, 2, 3) if (m_ > 0 if w_ == 3 else m_ < RO)]
+CYC, PCYC, GA, SC, LAT, DMA, HOP = 0.83, 0.42, 1.56, 3.8, 100.0, 2000.0, 4500.0
+MARGIN, TURNS, WAIT, SLACK = 1500.0, 10, 100.0, 4.0
+JV = (1, 3, 5)
+CUT = (4, 4)
+VADD, VMIN, AADD, PFIX, CROSS = 0.0, 53.0, 66.0, 10.0, 120.0
+SGV, ABS, SND, QV = (0, 1, 2, 3, 4, 5), (), "a", ()
+URGE = 1500.0
+LATE, PK, WIDE, FIRST, T2, T3 = ["G7"], "a", 4000.0, 1.8, 2.0, 3.0
+ORDER = "f0 f1 m0 f2 m1 b0 f3 m2 b1 f4 m3 b2 b3 out f5 m4 m5 b4 b5"
 
 
 def sb(n, t):
@@ -15,27 +26,27 @@ def sb(n, t):
 
 
 SCRATCH = {
-    "ST": sb(1440, H), "C": sb(3456, H), "G": sb(3584, H), "GN": sb(1280, H), "GO": sb(320, H),
-    "QA": sb(1440, F), "QB": sb(1440, F), "LG": sb(6 * BLKW, F), "YM": sb(V, F), "YT": sb(2 * V, F),
-    "snd1": sb(6 * FP, H), "lnd1": sb(6 * FP, H), "hb1": sb(6 * 96, H),
-    "snd2": ("sbuf", [128, 35, 64], F), "lnd2": ("sbuf", [128, 35, 64], F), "hb2": ("sbuf", [128, 15, 64], F),
-    "snd3": sb(6 * FP, F), "hb3": sb(6 * 96, F),
-    "qa": sb(V, H), "qb": sb(V, H), "TD": sb(V, I), "TB": sb(V, H), "TH": sb(8, F), "NTH": sb(8, F),
-    "PI": sb(FP, I), "RI": sb(16, I), "RJ": sb(32, I), "rimU": sb(16, U), "rimS": sb(16, U), "rimK": sb(16, F), "ryF": sb(16, F), "ryU": sb(16, U),
-    "s0": sb(FP, I), "s1": sb(FP, I), "s2": sb(FP, I), "s3": sb(FP, I), "s4": sb(FP, I), "s5": sb(FP, I), "SI": sb(FP, F),
-    "colU": sb(FP, U), "KN": sb(FP, F), "AB": sb(2 * FP, H), "PE": sb(FP, F), "fa": sb(FP, F), "fb": sb(FP, F), "adU": sb(FP, U),
-    "Pi": sb(8, I), "CI": sb(8, I), "CF": sb(24, F), "MK": sb(8, F), "BR": sb(8, F), "RW": sb(16 * NW, H), "E1": sb(144, H),
-    "WS": sb(32, F), "X": sb(240, F), "XB": sb(256, H), "XQ": sb(144, F), "X16": sb(128, F), "CR": sb(512, H),
-    "HI": sb(V + 64, H), "Wt": sb(128, H), "Wc": sb(32, H), "ZI": sb(240, H), "ZF": sb(240, F), "NI": sb(128, F),
+    "ST": sb(TW, H), "C": sb(3456, H), "CT": sb(2560, H), "G": sb(GW, H), "GN": sb(1280, H), "GO": sb(320, H),
+    "QA": sb(LO + RO * QS + CAP, F), "QB": sb(LO + RO * QS + CAP, F), "LG": sb(LO + 6 * BLKW, F),
+    "snd1": sb(5 * FP, H), "lnd1": sb(5 * FP, H),
+    "snd2": ("sbuf", [128, 35, 64], F), "lnd2": ("sbuf", [128, 35, 64], F),
+    "snd3": sb(6 * FP, F),
+    "qa": sb(V, H), "qb": sb(V, H), "TD": sb(V, I), "TB": sb(V, H), "TH": sb(8, F),
+    "PI": sb(FP, I), "RI": sb(16, I), "RJ": sb(32, I), "rimU": sb(16, U), "rimS": sb(16, U), "rimK": sb(32, F), "ryF": sb(16, F), "ryU": sb(32, U), "qU": sb(240, U), "ZR": sb(144, H),
+    "s0": sb(6 * FP, I), "SI": sb(FP, F),
+    "colU": sb(FP, U), "KN": sb(FP, F), "AB": sb(2 * FP, H), "PE": sb(3 * FP, F), "adU": sb(FP, U),
+    "Pi": sb(8, I), "CI": sb(8, I), "CF": sb(32, F), "MK": sb(32, F), "BR": sb(8, F), "RW": sb(16 * NW, H), "E1": sb(144, H),
+    "WS": sb(40, F), "X": sb(240, F), "XB": sb(256, H), "XQ": sb(144, F), "X16": sb(128, F), "CR": sb(512, H),
+    "HI": sb(V + 64, H), "Wt": sb(128, H), "Wc": sb(112, H), "ZJ": sb(240, H), "ZI": sb(240, H), "ZF": sb(240, F), "NI": sb(128, F),
     "ZE0": sb(144, H), "ZO0": sb(144, H), "ZA0": sb(144, H),
     "ZE": sb(144, H), "ZT": sb(144, H), "ZP": sb(144, H), "ZO": sb(144, H), "ZQ": sb(144, H), "Z2": sb(144, H), "ZA": sb(4 * 144, H),
-    "BK": sb(128, H), "TR": sb(128, H), "Wb1": sb(128, H), "Wb2": sb(128, H), "Wy": sb(16, H), "CH": sb(FP, H),
-    "TRE": sb(56, F), "JX": sb(24, F), "TRJ": sb(24, F), "K3": sb(80, F), "ONE": sb(56, F), "SX": sb(64, F),
-    "L1": sb(384, F), "L2": sb(384, F), "L3": sb(384, F), "LS": sb(256, F), "LI": sb(8, F),
-    "bit": sb(FP, H), "can": sb(56, H), "v0": sb(56, F), "v1": sb(56, F), "posU": sb(56, U),
-    "UU": sb(200, U), "sm": sb(720, F), "si": sb(160, I), "su": sb(280, U),
-    "qe": sb(960, F), "cq": sb(3 * 1280, F), "w": sb(4 * 640, F), "r": sb(3 * 640, F), "FF": sb(1280, F), "xx": sb(640, F),
-    "po": sb(640, F), "gb": sb(4 * 320, H), "pk1": sb(FP, H), "pk2": sb(3 * FP, F),
+    "BK": sb(128, H), "TR": sb(7 * 128, H), "Wb": sb(128, H), "Wy": sb(16, H), "CH": sb(FP, H), "ZB": sb(176, H), "KI": sb(504, H),
+    "TRE": sb(56, F), "ONE": sb(176, F), "SX": sb(176, F), "IN": sb(176, F),
+    "L1": sb(384, F), "L2": sb(384, F), "L3": sb(384, F), "LS": sb(384, F), "LI": sb(384, F),
+    "bit": sb(FP, H), "can": sb(112, H), "THR": sb(112, F), "v0": sb(176, F), "v1": sb(4 * 56, F), "posU": sb(56, U),
+    "UU": sb(104, U), "sm": sb(720, F), "su": sb(240, U),
+    "qe": sb(960, F), "cq": sb(1280, F), "cb": sb(2 * 1280, H), "WK": sb(5 * 832, F), "r": sb(2 * 832, F), "FF": sb(1288, F), "xx": sb(832, F),
+    "po": sb(960, F), "gb": sb(4 * 320, H), "NT": sb(8, F), "pk1": sb(FP, H), "pk2": sb(3 * FP, F),
 }
 for _k in range(8):
     SCRATCH["P%d" % _k] = ("psum", [128, 512], F)
@@ -72,11 +83,11 @@ def shares(engs, n):
 
 
 def piece(T, kind, which, m, a, n):
-    per = 3 if kind == "hb" else 7
+    per, kind = (3, "snd") if kind == "hb" else (7, kind)
     if which == 2:
         return T[kind + "2"][:, m * per + a:m * per + a + n, :]
     if which == 3 and kind == "lnd":
-        return T.LG[:, BLKW * m + 1280 + 32 * a:BLKW * m + 1280 + 32 * (a + n)]
+        return T.LG[:, LO + BLKW * m + 1280 + 32 * a:LO + BLKW * m + 1280 + 32 * (a + n)]
     return T[kind + str(which)][:, (m * per + a) * 32:(m * per + a + n) * 32]
 
 
@@ -90,6 +101,61 @@ def forward(g, T, topo, src, r, blocks, kind, first, which, m):
                                     src=piece(T, kind, which, m, b - first, 1), dst=piece(T, "lnd", which, m, n - 2 - b, 1)))
     g.remote_dma_fused(tr, local_sem=T.sem.loc)
     return sum(s for _, s in sh)
+
+
+def place(nodes, rank, before, after, urge=0.0):
+    left, at = [len(x) for x in before], {}
+    pool, free, due = {e: [] for e in "vapgsx"}, {e: 0.0 for e in "vapgsx"}, {e: [0.0] * len(nodes) for e in "vapgsx"}
+    for k, nd in enumerate(nodes):
+        for e in nd["ns"] if not left[k] else ():
+            pool[e].append(k)
+    while len(at) < len(nodes):
+        t, e = min((max(free[e], min(due[e][k] for k in row)), e) for e, row in pool.items() if row)
+        ready = due[e]
+        row = sorted(pool[e], key=lambda k: ((MARGIN if e == "v" and len(nodes[k]["ns"]) > 1 else 0) - rank[k], k))
+        k, soon = None, []
+        for j in row:
+            if ready[j] > t:
+                soon.append(j)
+            elif e == "x" or all(t + nodes[j]["ns"][e] <= ready[i] + WAIT or rank[i] - rank[j] < SLACK * (ready[i] - t + nodes[i]["ns"][e]) for i in soon):
+                k = j
+                break
+        if k is None:
+            free[e] = min(t + 50.0, min(ready[i] for i in soon))
+            continue
+        at[k] = (e, t, t + nodes[k]["ns"][e] + (urge if nodes[k]["out"][0:1] and nodes[k]["out"][0][0:4] == "lnd1" else 0.0))
+        if e != "x":
+            free[e] = at[k][2]
+        for e2 in nodes[k]["ns"]:
+            pool[e2].remove(k)
+        for j, lat in after[k]:
+            for e2 in nodes[j]["ns"]:
+                due[e2][j] = max(due[e2][j], at[k][2] + lat + (CROSS if lat == LAT and e2 != e else 0.0))
+            left[j] -= 1
+            for e2 in nodes[j]["ns"] if not left[j] else ():
+                pool[e2].append(j)
+    return at
+
+
+def arrange(nodes):
+    n = len(nodes)
+    pre, post = [[] for nd in nodes], [[] for nd in nodes]
+    for k, nd in enumerate(nodes):
+        for j in sorted(nd["pre"] | nd["soft"]):
+            lat = 0.0 if j in nd["soft"] or nd["tok"] is False or list(nd["ns"]) == list(nodes[j]["ns"]) == ["p"] else nodes[j]["lat"]
+            pre[k].append((j, lat))
+            post[j].append((k, lat))
+    rank, best = [float(-k) for k in range(n)], None
+    for turn in range(TURNS):
+        at = place(nodes, rank, pre, post)
+        span = max(at[k][2] + nodes[k]["lat"] for k in range(n))
+        if best is None or span < best[0]:
+            best = (span, at)
+        back = place(nodes, [at[k][2] for k in range(n)], post, pre, URGE)
+        rank = [back[k][2] for k in range(n)]
+    for k in range(n):
+        nodes[k]["e"], nodes[k]["at"] = best[1][k][0:2]
+    return sorted(range(n), key=lambda k: (nodes[k]["at"], k))
 
 
 def rank_program(g, core, T, topo):
@@ -116,8 +182,657 @@ def rank_program(g, core, T, topo):
 
     Q = {"v": g.vector, "a": g.scalar, "p": g.tensor, "g": g, "s": g.sync}
     cnt = {"v": 0, "a": 0, "p": 0, "g": 0, "loc": 0, "out": 0}
+    nodes, wr, rd = [], {}, {}
+
+    def op(ns, fn, reads, writes, lat=LAT, tok=True):
+        k, pre = len(nodes), set()
+        ns = {e: x if x > 0 else max(VADD - x, VMIN) if e == "v" else AADD - x for e, x in ns.items()}
+        for x in reads:
+            if x in wr:
+                pre.add(wr[x])
+            if x[0] == "P" and x[1:].isdigit():
+                pre.update(j for j in rd.get(x, []) if len(ns) > 1 or list(nodes[j]["ns"]) != list(ns))
+        for x in writes:
+            if x in wr:
+                pre.add(wr[x])
+            pre.update(rd.get(x, []))
+        nodes.append({"ns": ns, "fn": fn, "pre": pre, "lat": lat, "tok": tok, "out": writes, "soft": set()})
+        for x in reads:
+            rd.setdefault(x, []).append(k)
+        for x in writes:
+            wr[x] = k
+            rd[x] = []
+
+    vec, act, pe = g.vector, g.scalar, g.tensor
+    either = [""]
+
+    def cyc(c):
+        return -1.0 - c * CYC
+
+    def ind(c, rate=GA):
+        return 60 + rate * c * CYC
+
+    def tt(out, a, b, o, reads, writes, ns=cyc(0)):
+        op({"v": ns}, lambda e: vec.tensor_tensor(out, a, b, o), reads, writes)
+
+    def ts(out, a, s1, o1, reads, writes, s2=None, o2=None, ns=cyc(0)):
+        if o2 is None:
+            op({"v": ns}, lambda e: vec.tensor_scalar(out, a, s1, None, o1), reads, writes)
+        else:
+            op({"v": ns}, lambda e: vec.tensor_scalar(out, a, s1, s2, o1, o2), reads, writes)
+
+    def cp(out, a, reads, writes, ns=cyc(0), on="v"):
+        op({e: ns for e in (either[0] or on)}, lambda e: vec.tensor_copy(out, a) if e == "v" else act.activation(out, a, AF.Identity), reads, writes)
+
+    def ms(out, c, writes, ns=cyc(0)):
+        op({"v": ns}, lambda e: vec.memset(out, c), [], writes)
+
+    def ac(out, a, reads, writes, func=AF.Identity, bias=0.0, scale=1.0, ns=cyc(0)):
+        op({e: ns for e in (either[0] or "a")},
+           lambda e: act.activation(out, a, func, bias=bias, scale=scale) if e == "a" else vec.tensor_scalar(out, a, scale, bias, A.mult, A.add), reads, writes)
+
+    def fills(on, parts, reads, writes):
+        def fn(e):
+            for out, src, val in parts:
+                last = vec.memset(out, float(val)) if e == "v" else act.activation(out, src, AF.Identity, bias=float(val), scale=0.0)
+            return last
+        op({e: (VMIN if e == "v" else AADD + 10) * len(parts) for e in on}, fn, reads, writes)
+
+    def mm(parts, reads, bank, cols, wide=1, start=True, stop=True, calls=None):
+        def fn(_):
+            for j, (out, l, r) in enumerate(parts):
+                last = pe.matmul(out, l, r, start == "each" or (start and j == 0), stop == "each" or (stop and j == len(parts) - 1))
+            return last
+        op({"p": cols * wide * PCYC + PFIX * (calls or len(parts))}, fn, reads, ["P%d" % bank])
+
+    def iota(out, pat, base, cm, writes, exact=False, c=64):
+        if exact:
+            op({"g": 130 + 2 * c * CYC}, lambda e: g.iota(out, pat, base, cm), [], writes)
+        else:
+            op({"g": 130 + 2 * c * CYC}, lambda e: g.iota(out, pat, base, cm, allow_small_or_imprecise_dtypes=True), [], writes)
+
+    def sel(out, a, cmp, fill, base, cm, reads, writes):
+        op({"g": 170 + 256 * CYC}, lambda e: g.affine_select(out, a, [[1, 128]], cmp, fill, base, cm), reads, writes)
+
+    def load(e, k, out, src, name, turn=1):
+        def fn(_):
+            Q[e].dma_start(out, src).then_inc(T.sem["in%d" % k], 16)
+        op({e: 60.0}, fn, ["issued"], [name], DMA * turn, ("in%d" % k, 16))
+        op({"x": 1.0}, None, [], ["issued"], 1.0, False)
+
+    def store(e, out, src, reads):
+        def fn(_):
+            Q[e].dma_start(out, src).then_inc(T.sem.out, 16)
+            cnt["out"] += 16
+        op({e: 60.0}, fn, reads, [], DMA, None)
+
+    def send(which, m, reads, lands):
+        def fn(_):
+            hs = shares(topo.engines(core, plan[rank][1][0][0]), 2)
+            tr = []
+            for (h, blocks), (mask, s) in zip(plan[rank][1], hs):
+                rid, pid = topo.addr(h, core)
+                tr.append(RemoteDMATransfer(dst_ids=[DstId(rid=rid, pnc=pid)], dma_engine_mask=mask, remote_sem=T.sem["hs%d" % MSG.index((which, m))],
+                                            src=piece(T, "snd", which, m, blocks[0], 3), dst=piece(T, "hb", which, m, 0, 3)))
+                cnt["loc"] += s
+            g.remote_dma_fused(tr, local_sem=T.sem.loc)
+            cnt["loc"] += forward(g, T, topo, core, rank, plan[rank][0], "snd", 0, which, m)
+        op({"g": 1000.0}, fn, reads, ["sent"], 1.0, None)
+        op({"x": HOP * (FIRST if m == 0 else 1) - 1000.0 + (WIDE if which > 1 and m < RO else 0.0)}, None, ["sent"], [lands], 1.0, ("ar%d" % MSG.index((which, m)), arrive))
+        rd["sent"] = []
+
+    P = [T["P%d" % k] for k in range(8)]
+    ST, QA, QB, LG, WS, CF = T.ST, T.QA, T.QB, T.LG, T.WS, T.CF
+    STw = ["STl", "STh"]
+
+    def qw(x, r):
+        return [x + "0", x + "z"] + ["%s%d_%d" % (x, k, j) for k in range(1, r + 1) for j in range(2)] + ["%sh%d" % (x, k) for k in range(r + 1)]
+
+    def wcol(k):
+        return WS[:, k:k + 1]
+
+    def W1(f):
+        return T.E1[0:1, 15 - f:143 - f]
+
+    cI, cG, cQ, cK, cP, cM, cE, nE, cO, n16, cF1, cF2, c12, c4, c2, cA, nK = [CF[:, k:k + 1] for k in range(17)]
+    s0, s1, s2, s3, s4, s5 = [T.s0[:, FP * k:FP * k + FP] for k in range(6)]
+    TRs, TRi, TRa, TRb, TRc, NBK, BK8 = [T.TR[:, 128 * k:128 * k + 128] for k in range(7)]
+    ZF = T.ZF[:, 0:128]
+
+    load("s", 0, T.TD[0:8, :], T.t0[:], "TD0")
+    load("a", 1, T.TD[8:16, :], T.d0[:], "TD1")
+    load("s", 2, T.TD[16:24, :], T.d0[:], "TD2")
+    load("a", 3, T.RI[:, 0:14], T.rim[:], "RI")
+    load("s", 6, T.PI[:], T.port[:], "PI", T2)
+    load("s", 4, T.qa[:], T.q0[:], "qa", T3)
+    load("s", 5, T.qb[:], T.q1[:], "qb", T3)
+    load("s", 7, T.TH[:, 0:1], T.th[:], "TH", T3)
+
+    ms(T.Wt[0:24, :], 0.0, ["Wt"])
+    ms(T.RW[0:1, :], 0.0, ["RW0"], cyc(8 * NW))
+    ms(T.E1[0:1, :], 0.0, ["E1"])
+    iota(cP, [[0, 1]], 0, 1, ["cP"], c=1)
+    iota(T.XB[0:1, :], [[1, 256]], 0, 0, ["XB"], c=256)
+    for base, fill in ((-fT, 1.0), (128 - fD, -1.0), (256 - fD, 1.0), (256 - fM, 1.0)):
+        sel(T.Wt[0:24, :], T.Wt[0:24, :], A.not_equal, fill, base, -16, ["Wt"], ["Wt"])
+    iota(T.X[:], [[1, 240]], 0, 0, ["X"], c=240)
+    iota(T.Pi[:, 0:1], [[0, 1]], 0, 1, ["Pi"], True, 1)
+    iota(T.XQ[:], [[1, 36], [0, 4]], 0, 0, ["XQ"], c=144)
+    iota(T.X16[:], [[1, 8], [0, 16]], 0, 0, ["X16"], c=128)
+    iota(T.SI[:], [[16, FP]], 15, 1, ["SI"], c=FP)
+    iota(T.TRE[:], [[16, 56]], 2560, 1, ["TRE"])
+    ms(T.CR[0:1, :], float(7 * rank), ["CR"], cyc(256))
+    ms(T.E1[0:1, 15:144:16], 1.0, ["E1"])
+    ts(cM, cP, 16.0, A.is_ge, ["cP"], ["cM"], 2.0, A.mult)
+    fills("v", [(T.HI[0:1, 128 * k:128 * k + 128], None, k) for k in range(7)], [], ["HI"])
+    terms = [(fA, 0, 0.25, 4, NW + 1), (fB, 0, 32, 4, NW + 1), (fA, 4, 1, 4, NW + 1), (fA, 26, 320, 4, NW + 1), (fB, 26, 40960, 4, NW + 1), (0, 30, 1, 14, NW),
+             (fA, 8, 1, 4, NW), (fNLO, 8, 1, 1, 1), (fB, 32, 35, 4, NW), (fB, 33, 35, 4, NW), (fNHI, 32, 7 * rank + 9, 1, 1), (fNHI, 33, 7 * rank + 10, 1, 1),
+             (fR, 31, QS, 1, 1), (fJLO, 31, 1, 1, 1), (fJHI, 31, 128, 1, 1),
+             (fNLO, 9, 1, 2, 9), (fNHI, 9, 128, 2, 9), (fT, 10, -1, 4, 1), (fM, 10, -32, 4, 1), (fD, 10, 64, 4, 1),
+             (fR, 14, BLKW, 4, 1), (fJLO, 14, 1, 4, 1), (fJHI, 14, 128, 4, 1), (fT, 18, 8192, 2, NW), (fD, 18, -8192, 1, 1),
+             (fT, 19, 1, 1, 1), (fM, 20, 3.5, 1, 1), (fD, 20, 8.5, 1, 1), (fM, 21, -2, 1, 1), (fD, 21, 1, 1, 1),
+             (0, 22, 1, 11, NW), (fM, 23, 1, 1, 1), (fD, 23, -1, 1, 1), (fM, 24, 4, 1, 1), (fR, 25, 1, 1, 1)]
+    places = [T.RW[0:1, NW * f + col:NW * f + col + (count - 1) * step + 1:step] for f, col, c, count, step in terms]
+    fills("a", [(x, x, t[2]) for x, t in zip(places[1::2], terms[1::2])], ["RW0"], ["RWa"])
+    fills("v", [(x, x, t[2]) for x, t in zip(places[0::2], terms[0::2])], ["RW0"], ["RWv"])
+    ts(T.TB[0:24, :], T.TD[0:24, :], CF[0:24, 5:6], A.max, ["TD0", "TD1", "TD2", "cM"], ["TB"], ns=cyc(V))
+    ts(T.RJ[:, 0:14], T.RI[:, 0:14], 2, A.arith_shift_right, ["RI"], ["RJ0"])
+    ts(T.ZI[:, 0:128], T.X[:, 0:128], cP, A.is_equal, ["X", "cP"], ["ZI0"], ns=cyc(128))
+    ts(T.ZI[:, 128:240], T.X[:, 0:112], cP, A.is_equal, ["X", "cP"], ["ZI"], ns=cyc(112))
+    cp(T.rimU[:, 0:14], T.RJ[:, 0:14], ["RJ0"], ["rimU"])
+    halves = ((0, 512), (512, V))
+    for k, (a, b) in enumerate(halves):
+        mm([(P[k][:, 0:b - a], W1(fNHI), T.HI[0:1, a:b]), (P[k][:, 0:b - a], W1(fNHI), T.CR[0:1, 0:b - a])]
+           + [(P[k][:, c - a:c - a + 128], W1(fNLO), T.XB[0:1, 0:128]) for c in range(a, b, 128)], ["E1", "HI", "CR", "XB"], k, 3 * (b - a), stop=False)
+    for k, (a, b) in enumerate(halves):
+        mm([(P[k][:, 0:b - a], T.Wt[0:24, :], T.TB[0:24, a:b])], ["Wt", "TB"], k, b - a, start=False)
+    cp(ST[:, 0:512], P[0][:, 0:512], ["P0"], ["ST0"], cyc(512), "a")
+    cp(ST[:, 512:V], P[1][:, 0:V - 512], ["P1"], ["STl"], cyc(384))
+    for b in range(7):
+        j0 = (6 - b) * 32
+        mm([(P[4][:, 32 * b:32 * b + 32], W1(fJLO), T.XB[0:1, 64 + j0 % 128:96 + j0 % 128]),
+            (P[4][:, 32 * b:32 * b + 32], W1(fJHI), T.HI[0:1, 128 * (2 + j0 // 128):128 * (2 + j0 // 128) + 32])], ["E1", "XB", "HI"], 4, 128)
+    cp(T.CH[:], P[4][:, 0:FP], ["P4"], ["CH"], cyc(FP), "a")
+    mm([(P[5][:, 0:NW], W1(f), T.RW[0:1, NW * f:NW * f + NW]) for f in range(16)], ["E1", "RWa", "RWv"], 5, 1024)
+    up = 32 * (n - 1 - rank)
+
+    def shift(bank, o_, src, a, Z, reads, wide, fresh=True):
+        mm([(P[bank][:, o_ + lo:o_ + hi], Z[:, o:o + 128], src[:, a + lo:a + hi]) for lo, hi, o in ((0, up, 112), (up, FP, 16)) if hi > lo],
+           reads, bank, FP + 32, wide, "each" if fresh else False, "each" if fresh else True, 2)
+
+    def message1(m):
+        cp(T.pk1[:], ST[:, 0:V].indirect(T.rimU[:, 0:14]), ["STl", "ST0", "rimU"], ["pk1"], ind(FP), PK)
+        if m == 0:
+            shift(7, 0, T.pk1, 0, T.ZI, ["pk1", "ZI", "ZI0"], 1)
+            tt(T.snd1[:, 0:FP], P[7][:, 0:FP], T.CH[:], A.add, ["P7", "CH"], ["snd1_0"], cyc(FP))
+        else:
+            mm([(P[7][:, 0:FP], T.ZI[:, 0:128], T.CH[:])], ["ZI0", "CH"], 7, FP, stop=False)
+            shift(7, 0, T.pk1, 0, T.ZJ, ["pk1", "ZJ"], 1, False)
+            cp(T.snd1[:, m * FP:(m + 1) * FP], P[7][:, 0:FP], ["P7"], ["snd1_%d" % m], cyc(FP), SND)
+        send(1, m, ["snd1_%d" % m], "lnd1_%d" % m)
+
+    def pack_q(m):
+        if m > 0:
+            mm([(P[6][:, 0:14], T.ZR[:, 15 - i:143 - i], T.pk1[:, i:FP:16]) for i in range(16)], ["pk1", "ZR"], 6, 1024)
+            ts(T.ryU[:, 16:30], P[6][:, 0:14], float(LO), A.add, ["P6"], ["rqU"])
+        for k, (W, nm) in enumerate(((QA, "QA"), (QB, "QB"))):
+            if m == 0:
+                cp(T.pk2[:, k * FP:(k + 1) * FP], W[:, 0:V].indirect(T.rimU[:, 0:14]), [nm + "0", "rimU"], ["pk2_%d" % k], ind(FP), "a")
+            else:
+                cp(T.pk2[:, k * FP:(k + 1) * FP], W[:, 0:LO + QS * m + FP].indirect(T.ryU[:, 16:30]), qw(nm, m - 1) + ["%s%d_0" % (nm, m), "rqU"],
+                   ["pk2_%d" % k], ind(FP), "a")
+        for k in range(2):
+            shift(6, FP * k, T.pk2, k * FP, T.ZF, ["pk2_%d" % k, "ZF"], 4)
+        for k in range(2):
+            cp(T.snd2[:, 7 * m:7 * m + 7, 32 * k:32 * k + 32], P[6][:, FP * k:FP * k + FP], ["P6"], ["snd2_%d_%d" % (m, k)], cyc(FP), "a")
+        send(2, m, ["snd2_%d_0" % m, "snd2_%d_1" % m], "lnd2_%d" % m)
+
+    message1(0)
+    ts(T.CI[:, 0:1], T.Pi[:, 0:1], 15, A.bitwise_and, ["Pi"], ["CI0"])
+    ts(T.CI[:, 1:2], T.Pi[:, 0:1], 4, A.arith_shift_right, ["Pi"], ["CI1"])
+    ts(T.CI[:, 2:3], T.Pi[:, 0:1], 2, A.arith_shift_right, ["Pi"], ["CI2"], 3, A.bitwise_and)
+    ts(T.CI[:, 3:4], T.Pi[:, 0:1], 3, A.bitwise_and, ["Pi"], ["CI3"])
+    cp(CF[:, 0:4], T.CI[:, 0:4], ["CI0", "CI1", "CI2", "CI3"], ["CF"])
+    either[0] = "av"
+    cp(WS[:, 0:NW], P[5][:, 0:NW], ["P5"], ["WS"], on="a")
+    cp(QA[:, 0:V], T.qa[:], ["qa"], ["QA0"], cyc(V), "a")
+    for x, sc, bi, nm in ((cE, 16, 15, "cE"), (nE, -16, -15, "nE"), (cO, 4, 3, "cO"), (c12, 16, 12, "c12"), (c4, 16, 4, "c4"), (n16, -16, 0, "n16"),
+                          (cF1, FP, FP, "cF1"), (cF2, NR - FP, 7 * FP, "cF2")):
+        ac(x, cG, ["CF"], [nm], bias=float(bi), scale=float(sc))
+    ac(T.SI[:], T.SI[:], ["SI", "nE"], ["SI"], bias=nE, ns=cyc(FP))
+    ac(c2, cQ, ["CF", "c12"], ["c2"], bias=c12)
+    ac(cA, cK, ["CF", "c4"], ["cA"], bias=c4)
+    ac(nK, wcol(18), ["WS"], ["nK"], scale=-1.0)
+    cp(QB[:, 0:V], T.qb[:], ["qb"], ["QB0"], cyc(V), "a")
+    cp(T.ZF[:], T.ZI[:], ["ZI", "ZI0"], ["ZF"], cyc(240), "a")
+    pack_q(0)
+
+    c = T.PI[:]
+    ts(s1, c, 4.0, A.mult, ["PI"], ["s1"], -10749.0, A.add, cyc(FP))
+    ts(s3, c, float(3584 + up), A.is_ge, ["PI"], ["s3"], ns=cyc(FP))
+    tt(s0, s1, c, A.max, ["s1", "PI"], ["s0"], cyc(2 * FP))
+    tt(s2, T.SI[:], c, A.is_lt, ["SI", "PI"], ["s2"], cyc(2 * FP))
+    ts(T.colU[:], s0, 0.25, A.mult, ["s0"], ["colU"], -0.375, A.add, cyc(FP))
+    tt(s2, s2, s3, A.subtract, ["s2", "s3"], ["s2"], cyc(2 * FP))
+    ts(s4, s0, 127, A.bitwise_and, ["s0"], ["s4"], ns=cyc(FP))
+    ts(s5, s0, 7, A.arith_shift_right, ["s0"], ["s5"], ns=cyc(FP))
+    ts(s3, s2, 128.0, A.mult, ["s2"], ["s3"], ns=cyc(FP))
+    ts(T.MK[:, 0:4], T.X[:, 0:4], cQ, A.is_equal, ["X", "CF"], ["MK"])
+    ts(T.ZA0[:], T.X[:, 0:144], cA, A.is_equal, ["X", "cA"], ["ZA0"], ns=cyc(144))
+    ts(T.ZO0[:], T.XQ[:], cO, A.is_equal, ["XQ", "cO"], ["ZO0"], ns=cyc(144))
+    ts(T.ZE0[:], T.X[:, 0:144], cE, A.is_equal, ["X", "cE"], ["ZE0"], ns=cyc(144))
+    tt(T.AB[:, FP:2 * FP], s5, s2, A.subtract, ["s5", "s2"], ["ABb"], cyc(2 * FP))
+    tt(T.AB[:, 0:FP], s4, s3, A.add, ["s4", "s3"], ["ABa"], cyc(2 * FP))
+    for m in range(4):
+        ac(T.ZA[:, 144 * m:144 * m + 144], T.ZA0[:], ["ZA0", "MK"], ["ZA%d" % m], scale=T.MK[:, m:m + 1], ns=cyc(144))
+    ac(T.ZO[:], T.ZO0[:], ["ZO0", "nK"], ["ZO"], scale=nK, ns=cyc(144))
+    ac(T.ZE[:], T.ZE0[:], ["ZE0", "WS"], ["ZE"], scale=wcol(18), ns=cyc(144))
+    ac(T.TRE[:], T.TRE[:], ["TRE", "n16"], ["TRE"], bias=n16)
+    ts(T.BK[:], T.X16[:], cG, A.is_equal, ["X16", "CF"], ["BK"], ns=cyc(128))
+    ts(T.Z2[:], T.X[:, 0:144], c2, A.is_equal, ["X", "c2"], ["Z2"], ns=cyc(144))
+    sel(TRs, T.BK[:], A.is_gt, 0.0, 0, -1, ["BK"], ["TRs"])
+    sel(TRi, T.BK[:], A.is_ge, 0.0, 0, -1, ["BK"], ["TRi"])
+    sel(TRa, TRs, A.not_equal, -4096.0, 0, -1, ["TRs"], ["TRa"])
+    ac(TRb, TRs, ["TRs"], ["TRb"], scale=-1.0, ns=cyc(128))
+    sel(TRb, TRb, A.not_equal, -4096.0, 0, -1, ["TRb"], ["TRb"])
+    ac(TRc, TRi, ["TRi"], ["TRc"], scale=8192.0, ns=cyc(128))
+    ac(NBK, T.BK[:], ["BK"], ["NBK"], scale=-1.0, ns=cyc(128))
+    ac(BK8, T.BK[:], ["BK"], ["BK8"], scale=8192.0, ns=cyc(128))
+    for j, (col, nm) in enumerate(((8, "MKa"), (32, "MKb"), (33, "MKc"))):
+        ac(T.MK[:, 8 + 8 * j:16 + 8 * j], T.BK[:, 0:128:16], ["BK", "WS"], [nm], scale=wcol(col))
+    ms(T.G[:, 4 * V:GW], 0.0, ["Gz"], cyc(608))
+    for j in range(8):
+        ac(T.CT[:, FP * j:FP * j + FP], T.X[:, 0:FP], ["X", "MKa", "MKb"], ["CT%d" % j], bias=T.MK[:, 16 + j:17 + j], scale=T.MK[:, 8 + j:9 + j], ns=cyc(FP))
+        ac(T.CT[:, 8 * FP + NR * j:8 * FP + NR * j + NR], T.X[:, NR:2 * NR], ["X", "MKa", "MKc"], ["CT%d" % (8 + j)],
+           bias=T.MK[:, 24 + j:25 + j], scale=T.MK[:, 8 + j:9 + j], ns=cyc(NR))
+    op({"g": 130 + 2 * (LO + BLKW) * CYC}, lambda e: g.iota(LG[:, 0:LO + BLKW], [[0, LO + BLKW]], 0, 0, allow_small_or_imprecise_dtypes=True), ["sent"], ["LG0"])
+    ms(T.CR[0:1, :], -LO / 128.0, ["CR"], cyc(256))
+    for k, (a, b) in enumerate(halves):
+        parts = [(P[k][:, 0:b - a], T.ZI[:, 0:128], ST[:, a:b]), (P[k][:, 0:b - a], W1(fJHI), T.HI[0:1, a:b]), (P[k][:, 0:b - a], W1(fJHI), T.CR[0:1, 0:b - a])]
+        parts += [(P[k][:, c_ - a:c_ - a + 128], W1(fJLO), T.XB[0:1, 0:128]) for c_ in range(a, b, 128)]
+        for m in range(4):
+            parts.append((P[k][:, m:b - a:4], T.ZA[:, 144 * m:144 * m + 128], T.AB[:, FP + a // 4:FP + b // 4]))
+            parts.append((P[k][:, m:b - a:4], T.ZA[:, 144 * m + 4:144 * m + 132], T.AB[:, a // 4:b // 4]))
+        mm(parts, ["ZI0", "STl", "ST0", "ZA0", "ZA1", "ZA2", "ZA3", "ABa", "ABb", "E1", "HI", "CR", "XB"], k, 6 * (b - a))
+    ms(T.ONE[:], 1.0, ["ONE"], cyc(176))
+    ms(T.ONE[:, 0:171:57], 0.0, ["ONE"])
+    ms(T.IN[:], 0.0, ["IN"], cyc(176))
+    ac(T.IN[:, 0:1], cG, ["CF", "IN"], ["IN0"], bias=4096.0, scale=float(FP))
+    ac(T.IN[:, 57:58], cG, ["CF", "IN"], ["IN1"], bias=4096.0 + CAP - 1, scale=float(FP))
+    ac(T.IN[:, 114:115], cG, ["CF", "IN"], ["IN2"], bias=-8192.0 * CAP, scale=0.0)
+    ms(T.ZB[:], 0.0, ["ZB"], cyc(88))
+    ms(T.KI[:], 0.0, ["KI"], cyc(252))
+    fills("v", [(T.KI[:, 0:80], None, -0.375), (T.KI[:, 168:248], None, 160), (T.KI[:, 462:482], None, -V * rank),
+                (T.KI[:, 420:434], None, LO), (T.KI[:, 482:488], None, LO)]
+          + [(T.KI[:, 252 + 14 * k:266 + 14 * k], None, LO + 320 * k) for k in range(4)]
+          + [(T.KI[:, 308 + 6 * k:314 + 6 * k], None, LO + 320 * k) for k in range(4)], [], ["KI"])
+    ac(T.ZJ[:], T.ZI[:], ["ZI", "ZI0", "WS"], ["ZJ"], scale=wcol(30), ns=cyc(240))
+    for W, nm in ((QA, "QAz"), (QB, "QBz")):
+        ms(W[:, V:LO + CAP], 0.0, [nm])
+    ac(T.ZR[:], T.ZE0[:], ["ZE0", "WS"], ["ZR"], scale=wcol(31), ns=cyc(144))
+    ms(T.FF[:, 0:8], 0.0, ["FF0"])
+    ts(T.NT[:, 0:1], T.TH[:, 0:1], -1.0, A.mult, ["TH"], ["NTH"])
+    ms(ST[:, V:TW], 0.0, ["STh"], cyc(288))
+    ms(T.Wc[:], 0.0, ["Wc"])
+    for j, col in enumerate((0, 4, 10, 14, 26)):
+        cp(T.Wc[:, 6 * j:6 * j + 4], WS[:, col:col + 4], ["WS", "Wc"], ["WcF%d" % j], on="a")
+        cp(T.Wc[:, 40 + 14 * j:44 + 14 * j], WS[:, col:col + 4], ["WS", "Wc"], ["WcN%d" % j], on="a")
+    cp(T.Wc[:, 33:34], wcol(9), ["WS", "Wc"], ["WcF5"], on="a")
+    cp(T.Wc[:, 110:111], wcol(9), ["WS", "Wc"], ["WcN5"], on="a")
+    cp(T.Wc[:, 30:31], wcol(31), ["WS", "Wc"], ["WcF6"], on="a")
+    cp(T.Wc[:, 111:112], wcol(31), ["WS", "Wc"], ["WcN6"], on="a")
+    Wcs = ["WcF%d" % j for j in range(7)] + ["WcN%d" % j for j in range(7)]
+    ts(T.RJ[:, 16:30], T.RI[:, 0:14], 3, A.bitwise_and, ["RI"], ["RJ1"])
+    ts(s1, s0, 3, A.bitwise_and, ["s0"], ["s1"], ns=cyc(FP))
+    ts(T.rimK[:, 0:14], T.RJ[:, 16:30], 320.0, A.mult, ["RJ1"], ["rimK"], float(LO), A.add)
+    ts(T.rimK[:, 16:30], T.RJ[:, 16:30], float(FP), A.mult, ["RJ1"], ["rimL"], 8.0 - BLKW * RO, A.add)
+    ts(T.KN[:], s1, 320.0, A.mult, ["s1"], ["KN"], float(LO), A.add, cyc(FP))
+    cp(ST[:, 0:512], P[0][:, 0:512], ["P0"], ["ST0", "STl"], cyc(512), "a")
+    cp(ST[:, 512:V], P[1][:, 0:V - 512], ["P1"], ["STl"], cyc(384), "a")
+    ts(T.bit[:], c, 3584.0, A.is_ge, ["PI"], ["bit"], ns=cyc(FP))
+    mm([(P[4][:, 0:56], T.Z2[:, 12 - 4 * h:140 - 4 * h], T.bit[:, h:FP:4]) for h in range(4)], ["Z2", "bit"], 4, 256)
+    ts(T.THR[:, 0:56], P[4][:, 0:56], 0.5, A.is_lt, ["P4"], ["THa"], 64.0, A.mult)
+    ts(T.THR[:, 56:112], P[4][:, 0:56], 0.5, A.is_ge, ["P4"], ["THb"], 64.0, A.mult)
+    ts(T.THR[:], T.THR[:], 3.5, A.add, ["THa", "THb"], ["THa", "THb"], ns=cyc(112))
+    ac(T.ZT[:], T.ZE0[:], ["ZE0", "WS"], ["ZT"], scale=wcol(19), ns=cyc(144))
+    tabs = {"L1": [], "L2": [], "L3": []}
+    for di, d in enumerate((4, 2, 1)):
+        o = 64 * di + 32
+        for a in range(d):
+            lo = o - 3 if a == 0 else o + a
+            tabs["L1"].append((lo, o + a + 1, -(d - a) / 32.0))
+            tabs["L2"].append((lo, o + a + 1, -(d * d - a * a) / 64.0))
+        for a in range(d - 4, d):
+            tabs["L3"].append((o + a, o + a + 1, ((d - a) ** 2 - (max(a, 0) - a) ** 2) / 64.0))
+    for x, rows in tabs.items():
+        ac(T[x][:, 0:192], T.X[:, 0:192], ["X"], [x], scale=0.0, ns=cyc(192))
+        fills("av", [(T[x][:, a:b], T.X[:, 0:b - a], val) for a, b, val in rows], ["X"], [x])
+        ac(T[x][:, 192:384], T[x][:, 0:192], [x], [x + "n"], scale=-1.0, ns=cyc(192))
+    fills("a", [(T.LS[:, 0:192], T.X[:, 0:192], 0.5), (T.LS[:, 192:384], T.X[:, 0:192], -0.5)], ["X"], ["LS"])
+    fills("a", [(T.LI[:, 64 * j:64 * j + 64], T.X[:, 0:64], (0.25, 0.5, 1.0)[j % 3]) for j in range(6)], ["X"], ["LI"])
+    ac(T.NI[:], T.ZI[:, 0:128], ["ZI0"], ["NI"], scale=-1.0, ns=cyc(128))
+    ac(T.Wb[:], T.ZE0[:, 15 - fT:143 - fT], ["ZE0", "WS"], ["Wb"], scale=wcol(23), ns=cyc(128))
+    ts(TRi, T.ZI[:, 0:128], wcol(22), A.mult, ["ZI0", "WS"], ["TRi"])
+    tt(T.Wb[:], T.Wb[:], TRi, A.add, ["Wb", "TRi"], ["Wb"], cyc(256))
+    for r in range(1, RO + 1):
+        ac(T.BR[:, r:r + 1], wcol(25), ["WS"], ["BR%d" % r], bias=wcol(24), scale=float(r))
+    ac(T.ZP[:], T.ZE0[:], ["ZE0", "WS"], ["ZP"], scale=wcol(14), ns=cyc(144))
+    ac(T.ZQ[:], T.ZO0[:], ["ZO0", "WS"], ["ZQ"], scale=wcol(14), ns=cyc(144))
+    ac(T.Wy[:, 0:8], T.BK[:, 0:128:16], ["BK", "WS"], ["Wy0"], scale=wcol(19))
+    ac(T.Wy[:, 8:16], T.BK[:, 0:128:16], ["BK", "WS"], ["Wy1"], scale=wcol(23))
+
+    either[0] = ""
+    cp(T.rimS[:, 0:14], T.RI[:, 0:14], ["RI"], ["rimS"])
+    NG = 8
+    Gs = ["G%d" % k for k in range(NG)]
+
+    def neighbours():
+        w_ = FP // NG
+        for k in range(NG):
+            cp(T.G[:, 16 * w_ * k:16 * w_ * (k + 1)], ST[:, 0:V + FP].indirect(T.colU[:, w_ * k:w_ * (k + 1)]), STw + ["colU"], [Gs[k]], ind(16 * w_), "av")
+
+    def by_slot(bank, Z, zn, cut=CUT):
+        at = 0
+        for j, k in enumerate(cut):
+            a, b = at * FP // NG, (at + k) * FP // NG
+            mm([(P[bank][:, a:b], Z[:, 15 - i:143 - i], T.G[:, 16 * a + i:16 * b:16]) for i in range(16)], Gs[at:at + k] + [zn], bank,
+               16 * max(b - a, 64), start=False, stop=j == len(cut) - 1)
+            at += k
+
+    def lgw(r):
+        return ["LG0"] + ["LG%d_%d" % (k, j) for k in range(1, r) for j in range(8)] + ["LGh%d" % k for k in range(1, r)]
+
+    UU, sm, su, qe, cq, WK, rr, FF, xx, po, gb = T.UU, T.sm, T.su, T.qe, T.cq, T.WK, T.r, T.FF, T.xx, T.po, T.gb
+    eU, caseU, takeU, keepU = UU[:, 80:100], su[:, 0:80], su[:, 80:160], su[:, 160:240]
+    qnU, qeU, qyU, faceU = T.qU[:, 0:80], T.qU[:, 80:100], T.qU[:, 100:156], T.qU[:, 160:240]
+    pre, knf, mine, zz, own, t0, t1, t3 = [sm[:, 80 * k:80 * k + 80] for k in range(8)]
+    m0, m1, m2, m3 = [T.v1[:, 56 * k:56 * k + 56] for k in range(4)]
+    L1, L2, L3, LS = T.L1[:, 0:384], T.L2[:, 0:384], T.L3[:, 0:384], T.LS[:, 0:384]
+    TH, base = T.TH[:, 0:1], gb[:, 640:960]
+    PARTS = ((0, FP, 0, 14), (FP, CAP, 14, 20))
+    PORTS = [(FP * k, FP, 14 * k) for k in range(4)] + [(4 * FP + NR * k, NR, 56 + 6 * k) for k in range(4)]
+
+    def rim_address(bank, extra, name):
+        mm([(P[bank][:, 0:14], T.ZP[:, 15 - i:143 - i], T.pk1[:, i:FP:16]) for i in range(16)], ["pk1", "ZP"], bank, 1024)
+        tt(T.ryF[:, 0:14], P[bank][:, 0:14], extra, A.add, ["P%d" % bank, name], ["ryF"])
+        cp(T.ryU[:, 0:14], T.ryF[:, 0:14], ["ryF"], ["ryU"])
+
+    def pack_y(bank, r, window, reads, scale):
+        ac(T.pk2[:, 2 * FP:3 * FP], window.indirect(T.ryU[:, 0:14]), reads + ["ryU"], ["pk2_2"], scale=scale, ns=ind(FP))
+        shift(bank, 0, T.pk2, 2 * FP, T.ZF, ["pk2_2", "ZF"], 4)
+        cp(T.snd3[:, r * FP:(r + 1) * FP], P[bank][:, 0:FP], ["P%d" % bank], ["snd3_%d" % r], cyc(FP), "a")
+        send(3, r, ["snd3_%d" % r], "LGh%d" % r)
+
+    def who_acts(r):
+        mm([(P[5][:, 0:FP], T.ZO[:, 12 - 4 * m:140 - 4 * m], ST[:, m:V:4]) for m in range(4)], ["ZO", "STl"], 5, 4 * FP, stop=False)
+        mm([(P[1][:, 0:171], ZF, T.IN[:, 0:171])], ["ZF", "IN0", "IN1", "IN2"], 1, 171, 4, stop=False)
+        mm([(P[0][:, 0:171], T.ZI[:, 0:128], T.ZB[:, 0:171])], ["ZI0", "ZB"], 0, 171, stop=False)
+        mm([(P[6][:, 0:504], T.ZI[:, 0:128], T.KI[:])], ["ZI0", "KI"], 6, 504, stop=False)
+        if r == 1:
+            cp(T.C[:, 0:2560], T.CT[:], ["CT%d" % j for j in range(16)], ["C"], cyc(1280))
+        else:
+            op({"g": 170 + 2 * 2560 * CYC}, lambda e: g.affine_select(T.C[:, 0:2560], T.CT[:], [[0, 2560]], A.is_ge, 0.0, 0, 0), ["CT%d" % j for j in range(16)], ["C"])
+        lnd, ln = T.lnd1[:, (r - 1) * FP:r * FP], "lnd1_%d" % (r - 1)
+        if r == 1:
+            neighbours()
+        cp(T.G[:, 0:4 * V].indirect(T.rimS[:, 0:14]), lnd, [ln, "rimS"], Gs, ind(FP, SC))
+        cp(ST[:, V:V + FP], lnd, [ln], ["STh"], cyc(FP), "a")
+        by_slot(5, T.ZE, "ZE", (NG,))
+        marks[r] = {wr[x] for x in LATE}
+        ts(T.bit[:], P[5][:, 0:FP], 0.0, A.is_gt, ["P5"], ["bit"], ns=cyc(FP))
+        mm([(P[4][:, 0:56], T.Z2[:, 12 - 4 * h:140 - 4 * h], T.bit[:, h:FP:4]) for h in range(4)], ["Z2", "bit"], 4, 256)
+        cf, cn = T.can[:, 0:56], T.can[:, 56:112]
+        tt(cf, P[4][:, 0:56], T.THR[:, 0:56], A.is_ge, ["P4", "THa"], ["cf"])
+        tt(cn, P[4][:, 0:56], T.THR[:, 56:112], A.is_ge, ["P4", "THb"], ["cn"])
+        mm([(P[1][:, 1:57], T.BK[:], cf), (P[1][:, 115:171], BK8, cf)], ["BK", "BK8", "cf"], 1, 128, start=False, stop=False)
+        mm([(P[1][:, 58:114], NBK, cn), (P[1][:, 115:171], BK8, cn)], ["NBK", "BK8", "cn"], 1, 128, start=False)
+        mm([(P[0][:, 0:56], TRa, cf), (P[0][:, 114:170], TRc, cf), (P[0][:, 57:113], TRb, cn), (P[0][:, 114:170], TRc, cn)],
+           ["TRa", "TRb", "TRc", "cf", "cn"], 0, 256, start=False)
+        op({"v": cyc(171)}, lambda e: vec.tensor_tensor_scan(T.SX[:, 0:171], T.ONE[:, 0:171], P[1][:, 0:171], 0.0, A.mult, A.add), ["ONE", "P1"], ["SX"])
+        tt(T.v0[:, 0:171], P[0][:, 0:171], T.SX[:, 0:171], A.add, ["P0", "SX"], ["v0"], cyc(171))
+        tt(m0, T.v0[:, 0:56], T.v0[:, 57:113], A.min, ["v0"], ["m0"], cyc(112))
+        ts(m1, m0, cF1, A.is_ge, ["m0", "cF1", "cF2"], ["m1"], cF2, A.mult)
+        tt(m2, m0, T.v0[:, 114:170], A.max, ["m0", "v0"], ["m2"], cyc(112))
+        tt(m3, m1, m2, A.add, ["m1", "m2"], ["m3"], cyc(112))
+        tt(m0, m3, T.TRE[:], A.min, ["m3", "TRE"], ["m0"], cyc(112))
+        cp(T.posU[:], m0, ["m0"], ["posU"])
+        cp(T.C[:, 0:3456].indirect(T.posU[:, 0:56]), ST[:, 0:V], ["posU", "STl"], ["C"], ind(V, SC))
+        mm([(P[6][:, b:504:14], T.C[:, b:8 * FP:14], T.Wc[:, 0:36]) for b in range(14)]
+           + [(P[6][:, 56 + b:56 + b + 6 * 71 + 1:6], T.C[:, 8 * FP + b:2560:6], T.Wc[:, 40:112]) for b in range(6)], ["C"] + Wcs, 6, 20 * 66, start=False)
+        for W, o, nm in ((QB, 32, "QBh"), (QA, 0, "QAh")):
+            cp(W[:, LO + QS * r - FP:LO + QS * r], T.lnd2[:, 7 * r - 7:7 * r, o:o + 32], ["lnd2_%d" % (r - 1)], [nm + str(r - 1)], cyc(FP), "a")
+        cp(UU[:, 0:80], P[6][:, 0:80], ["P6"], ["UU"], cyc(80))
+        cp(eU, P[6][:, 462:482], ["P6"], ["eU"])
+        for k in range(2):
+            cp(T.GN[:, 640 * k:640 * k + 640], ST[:, 0:GW // 4].indirect(UU[:, 40 * k:40 * k + 40]), STw + ["UU"], ["GN%d" % k], ind(640), "va"[k])
+        mm([(P[2][:, 0:80], T.ZT[:, 15 - i:143 - i], T.GN[:, i:1280:16]) for i in range(16)], ["GN0", "GN1", "ZT"], 2, 1280)
+        ts(pre, P[6][:, 84:164], 128.0, A.is_ge, ["P6"], ["pre"], 192.0, A.mult, cyc(80))
+        tt(pre, P[6][:, 168:248], pre, A.add, ["P6", "pre"], ["pre"], cyc(80))
+        tt(t0, P[2][:, 0:80], pre, A.add, ["P2", "pre"], ["t0"], cyc(80))
+        cp(caseU, t0, ["t0"], ["caseU"], cyc(80))
+        mm([(P[4][:, 0:80], T.ZR[:, 15 - i:143 - i], T.GN[:, i:1280:16]) for i in range(16)], ["GN0", "GN1", "ZR"], 4, 1280)
+        ts(qnU, P[4][:, 0:80], float(LO), A.add, ["P4"], ["qnU"], ns=cyc(80))
+        if r < RO:
+            ts(faceU, P[6][:, 0:80], 0.375, A.add, ["P6"], ["faceU"], 4.0, A.mult, cyc(80))
+        cp(qeU[:, 0:14], P[6][:, 420:434], ["P6"], ["qeU0"])
+        cp(qeU[:, 14:20], P[6][:, 482:488], ["P6"], ["qeU1"])
+        if r > 1:
+            mm([(P[3][:, 0:80], T.ZP[:, 15 - i:143 - i], T.GN[:, i:1280:16]) for i in range(16)], ["GN0", "GN1", "ZP"], 3, 1280)
+            Pk = P[6][:, 252:332]
+            ts(knf, UU[:, 0:80], -1280.0, A.mult, ["UU"], ["knf"], float(LO), A.add, cyc(80))
+            tt(knf, P[6][:, 336:416], knf, A.add, ["P6", "knf"], ["knf"], cyc(80))
+            tt(zz, P[3][:, 0:80], knf, A.add, ["P3", "knf"], ["zz"], cyc(80))
+            tt(own, Pk, zz, A.is_lt, ["zz", "P6"], ["own"], cyc(80))
+            tt(mine, Pk, zz, A.is_ge, ["zz", "P6"], ["mine"], cyc(80))
+            tt(t1, own, zz, A.mult, ["own", "zz"], ["t1"], cyc(160))
+            tt(t3, Pk, mine, A.mult, ["mine", "P6"], ["t3"], cyc(80))
+            cp(takeU, t1, ["t1"], ["takeU"], cyc(80))
+            cp(keepU, t3, ["t3"], ["keepU"], cyc(80))
+        for p_, (a, b, c0, c1) in enumerate(PARTS):
+            cp(qe[:, 320 + a:320 + b], QB[:, 0:LO + QS * r - FP].indirect(qeU[:, c0:c1]), qw("QB", r - 1)[:-1] + ["qeU%d" % p_], ["q1e%d" % p_], ind(b - a), "a")
+            cp(qe[:, a:b], QA[:, 0:LO + QS * r - FP].indirect(qeU[:, c0:c1]), qw("QA", r - 1)[:-1] + ["qeU%d" % p_], ["q0e%d" % p_], ind(b - a), "a")
+        cp(P[0][:, 0:CAP], qe[:, 0:CAP], ["q0e0", "q0e1"], ["P0"], cyc(CAP), "a")
+        cp(T.GO[:], ST[:, 0:TW].indirect(eU), STw + ["eU"], ["GO"], ind(CAP), "a")
+        mm([(P[6][:, 0:CAP], T.Wb[:], T.GO[:]), (P[6][:, 0:CAP], W1(fJHI), T.HI[0:1, 0:CAP])]
+           + [(P[6][:, c0:min(c0 + 128, CAP)], W1(fJLO), T.XB[0:1, 0:min(128, CAP - c0)]) for c0 in range(0, CAP, 128)],
+           ["Wb", "GO", "E1", "XB", "HI"], 6, 3 * CAP)
+        ac(base, P[6][:, 0:CAP], ["P6", "BR%d" % r], ["base"], bias=T.BR[:, r:r + 1], ns=cyc(CAP))
+        for p_, (a, b, c0, c1) in enumerate(PARTS):
+            l0 = PORTS[4 * p_][2]
+            cp(qe[:, 640 + a:640 + b], T.LI[:, 0:384].indirect(caseU[:, l0:l0 + c1 - c0]), ["LI", "caseU"], ["inv%d" % p_], ind(b - a), "a")
+
+    def flux(r, s, step):
+        ports = [s] if s < 4 else [2 * s - 4, 2 * s - 3]
+        part = s // 4
+        a, b = PARTS[part][0:2]
+        lo, l0 = PORTS[ports[0]][0], PORTS[ports[0]][2]
+        wd = sum(PORTS[k][1] for k in ports)
+        l1, h, hb = l0 + wd // 16, (0, 1, 0, 1, 2, 3)[s], s % 2
+        at = (0, FP, 2 * FP, 2 * FP + 2 * NR)[h]
+        q1n, c1, sg = cq[:, lo:lo + wd], T.cb[:, lo:lo + wd], T.cb[:, 1280 + lo:1280 + lo + wd]
+        wn, un, we, ue, sq = [WK[:, 832 * j + at:832 * j + at + wd] for j in range(5)]
+        nm = {x: "%s%d" % (x, h) for x in ("wn", "un", "we", "ue", "sq", "r", "x")}
+        bj, bs = 1 + hb, 3 + hb
+        pn, pj, ps, nj, ns_ = P[bj][:, 0:wd], P[bj][:, wd:2 * wd], P[bs][:, 0:wd], "P%d" % bj, "P%d" % bs
+        if step == "f":
+            def each(f):
+                def fn(_):
+                    for k in ports:
+                        last = f(PORTS[k][0] - lo, PORTS[k][1], PORTS[k][2])
+                    return last
+                return fn
+            cp(c1, L1.indirect(caseU[:, l0:l1]), ["L1", "L1n", "caseU"], ["c1%d" % s], ind(wd), "a")
+            cp(q1n, QB[:, 0:LO + QS * r].indirect(qnU[:, l0:l1]), qw("QB", r - 1) + ["qnU"], ["q1n%d" % s], ind(wd), "a")
+            op({"v": len(ports) * ind(b - a)},
+               each(lambda o, w_, c0: vec.tensor_tensor(we[:, o:o + w_], L2.indirect(caseU[:, c0:c0 + w_ // 16]), qe[:, 320 + a:320 + b], A.mult)),
+               ["L2", "L2n", "caseU", "q1e%d" % part], [nm["we"]])
+            tt(wn, L3.indirect(caseU[:, l0:l1]), q1n, A.mult, ["L3", "L3n", "caseU", "q1n%d" % s], [nm["wn"]], ind(wd))
+            tt(un, QA[:, 0:LO + QS * r].indirect(qnU[:, l0:l1]), c1, A.mult, qw("QA", r - 1) + ["qnU", "c1%d" % s], [nm["un"]], ind(wd))
+            to, tn = (pj, nj) if s in JV else (ue, nm["ue"])
+            op({"v": cyc(wd)}, each(lambda o, w_, c0: vec.tensor_tensor(to[:, o:o + w_], P[0][:, a:b], c1[:, o:o + w_], A.mult)), ["P0", "c1%d" % s], [tn])
+            if s in JV:
+                tt(pj, pj, we, A.add, [nj, nm["we"]], [nj], cyc(wd))
+            mm([(pn, ZF, wn), (pn, T.NI[:], un)], ["ZF", "NI", nm["wn"], nm["un"]], bj, 2 * wd, 4)
+            if s not in JV:
+                mm([(pj, ZF, we), (pj, ZF, ue)], ["ZF", nm["we"], nm["ue"]], bj, 2 * wd, 4)
+        elif step == "m":
+            ac(rr[:, 2 * at:2 * at + 2 * wd], P[bj][:, 0:2 * wd], [nj], [nm["r"]], AF.Relu, ns=cyc(2 * wd))
+            ac(sq, rr[:, 2 * at:2 * at + wd], [nm["r"]], [nm["sq"]], AF.Square, ns=cyc(wd))
+            ac(ps, rr[:, 2 * at + wd:2 * at + 2 * wd], [nm["r"]], [ns_], AF.Square, ns=cyc(wd))
+        else:
+            f = FF[:, 8 + lo:8 + lo + wd]
+            if s in SGV:
+                ts(sg, c1, 0.0, A.is_lt, ["c1%d" % s], ["sg%d" % s], 0.5, A.subtract, cyc(wd // 2))
+            else:
+                cp(sg, LS.indirect(caseU[:, l0:l1]), ["LS", "caseU"], ["sg%d" % s], ind(wd), "a")
+            tt(ps, ps, sq, A.add, [ns_, nm["sq"]], [ns_], cyc(wd))
+            tt(f, ps, sg, A.mult, [ns_, "sg%d" % s], ["F%d" % s], cyc(wd))
+            x, xn = f, "F%d" % s
+            if r > 1:
+                x, xn = xx[:, at:at + wd], nm["x"]
+                tt(x, LG[:, 0:LO + BLKW * r].indirect(takeU[:, l0:l1]), f, A.add, lgw(r) + ["takeU", "F%d" % s], [xn], ind(wd))
+            pq, qf = P[5][:, a:b], QA[:, LO + QS * r + a:LO + QS * r + b]
+            if s == 0:
+                mm([(pq, ZF, qe[:, a:b])], ["ZF", "q0e0"], 5, wd, 4, stop=False)
+            if s < 3:
+                mm([(pq, ZF, x)], ["ZF", xn], 5, wd, 4, start=False, stop=s == 2)
+            elif s == 3:
+                tt(qf, pq, x, A.add, ["P5", xn], ["QA%d_0" % r], cyc(wd))
+            elif QV:
+                for j in range(2):
+                    last = s == 5 and j == 1
+                    tt(qf if last else pq, P[0][:, a:b] if s == 4 and j == 0 else pq, x[:, NR * j:NR * j + NR], A.add, ["P0", "P5", xn],
+                       ["QA%d_1" % r] if last else ["P5"], cyc(NR))
+            elif s == 4:
+                mm([(pq, ZF, qe[:, a:b]), (pq, ZF, x[:, 0:NR]), (pq, ZF, x[:, NR:2 * NR])], ["ZF", "q0e1", xn], 5, 3 * NR, 4, stop=False)
+            else:
+                mm([(pq, ZF, x[:, 0:NR])], ["ZF", xn], 5, NR, 4, start=False)
+                tt(qf, pq, x[:, NR:2 * NR], A.add, ["P5", xn], ["QA%d_1" % r], cyc(NR))
+
+    def sums(r, part):
+        a, b = PARTS[part][0:2]
+        for k in range(4):
+            lo, wd, l0 = PORTS[4 * part + k]
+            out, f, fn = LG[:, LO + BLKW * r + 320 * k + a:LO + BLKW * r + 320 * k + b], FF[:, 8 + lo:8 + lo + wd], "F%d" % (4 + k // 2 if part else k)
+            if r == 1:
+                ac(out, f, [fn], ["LG%d_%d" % (r, 4 * part + k)], scale=-1.0, ns=cyc(wd))
+            else:
+                tt(out, LG[:, 0:LO + BLKW * r].indirect(keepU[:, l0:l0 + wd // 16]), f, A.subtract, lgw(r) + ["keepU", fn], ["LG%d_%d" % (r, 4 * part + k)], ind(wd))
+
+    def new_fields(r, part):
+        a, b, c0, c1 = PARTS[part]
+        g1, nn = [gb[:, 320 * k + a:320 * k + b] for k in range(2)]
+        size, qf, qn = po[:, a:b], QA[:, LO + QS * r + a:LO + QS * r + b], "QA%d_%d" % (r, part)
+        if part in ABS:
+            ac(size, qf, [qn], ["size%d" % part], AF.Abs, ns=cyc(b - a))
+            ts(g1, size, TH, A.is_gt, ["size%d" % part, "TH"], ["g%d" % part], ns=cyc(b - a))
+            mm([(P[7][:, 0:b - a], T.BK[:], g1)], ["BK", "g%d" % part], 7, b - a)
+        else:
+            g2 = gb[:, 960 + a:960 + b]
+            ts(g1, qf, TH, A.is_gt, [qn, "TH"], ["g%d" % part], ns=cyc(b - a))
+            ts(g2, qf, T.NT[:, 0:1], A.is_lt, [qn, "NTH"], ["h%d" % part], ns=cyc(b - a))
+            mm([(P[7][:, 0:b - a], T.BK[:], g1), (P[7][:, 0:b - a], T.BK[:], g2)], ["BK", "g%d" % part, "h%d" % part], 7, 2 * (b - a))
+        ts(nn, P[7][:, 0:b - a], wcol(20), A.is_ge, ["P7", "WS"], ["nn%d" % part], wcol(21), A.mult, cyc(b - a))
+        tt(ST[:, 0:TW].indirect(eU[:, c0:c1]), nn, base[:, a:b], A.add, ["nn%d" % part, "base", "eU"], STw, ind(b - a, SC))
+
+    def tell(part):
+        a, b = PARTS[part][0:2]
+        for k in range(4):
+            l0 = PORTS[4 * part + k][2]
+            tt(T.G[:, 0:GW].indirect(faceU[:, l0:l0 + (b - a) // 16]), gb[:, 320 + a:320 + b], base[:, a:b], A.add,
+               ["nn%d" % part, "base", "faceU", "Gz"], Gs, ind(b - a, SC))
+
+    def new_q(r, part):
+        a, b = PARTS[part][0:2]
+        o = LO + QS * r
+        tt(P[0][:, a:b], QA[:, o + a:o + b], P[0][:, a:b], A.subtract, ["QA%d_%d" % (r, part), "P0"], ["P0"], cyc(b - a))
+        tt(QB[:, o + a:o + b], P[0][:, a:b], qe[:, 640 + a:640 + b], A.mult, ["P0", "inv%d" % part], ["QB%d_%d" % (r, part)], cyc(b - a))
+
+    def last_addresses():
+        cp(ST[:, 0:TW].indirect(eU), base, ["base", "eU"], STw, ind(CAP, SC))
+        cp(T.pk1[:], ST[:, 0:V].indirect(T.rimU[:, 0:14]), ["STl", "rimU"], ["pk1"], ind(FP), "a")
+        rim_address(7, T.rimK[:, 16:30], "rimL")
+        own_a, fa, fb = [T.PE[:, FP * k:FP * k + FP] for k in range(3)]
+        mm([(P[7][:, 0:FP], T.ZQ[:, 12 - 4 * m:140 - 4 * m], ST[:, m:V:4]) for m in range(4)], ["ZQ", "STl"], 7, 4 * FP)
+        ac(own_a, P[7][:, 0:FP], ["P7"], ["PE"], bias=float(LO), ns=cyc(FP))
+        mm([(P[7][:, 0:56], T.ZR[:, 15 - i:143 - i], ST[:, i:V:16]) for i in range(16)], ["ZR", "STl"], 7, 1024)
+        ts(qyU, P[7][:, 0:56], float(LO), A.add, ["P7"], ["qyU"])
+        neighbours()
+        mm([(P[6][:, 0:FP], ZF, T.KN[:])], ["ZF", "KN"], 6, FP, 4, stop=False)
+        by_slot(6, T.ZP, "ZP")
+        tt(fa, P[6][:, 0:FP], own_a, A.is_gt, ["P6", "PE"], ["fa"], cyc(FP))
+        tt(fb, P[6][:, 0:FP], fa, A.mult, ["P6", "fa"], ["fb"], cyc(FP))
+        cp(T.adU[:], fb, ["fb"], ["adU"], cyc(FP))
+
+    late, marks = [], {}
+    for r in range(1, RO + 1):
+        who_acts(r)
+        if r == RO:
+            last_addresses()
+        for step in ORDER.split():
+            if step != "out":
+                flux(r, int(step[1]), step[0])
+                continue
+            if r == RO:
+                pack_y(7, r, FF[:, 0:8 + 4 * FP], ["FF0", "F0", "F1", "F2", "F3"], -1.0)
+            new_fields(r, 0)
+            if r < RO:
+                message1(r)
+                neighbours()
+        new_fields(r, 1)
+        if r < RO:
+            tell(1)
+        new_q(r, 0)
+        if r < RO:
+            pack_q(r)
+            rim_address(6, T.rimK[:, 0:14], "rimK")
+        new_q(r, 1)
+        first = len(nodes)
+        sums(r, 0)
+        sums(r, 1)
+        late.append((first, len(nodes), r + 1))
+        if r < RO:
+            pack_y(6, r, LG[:, 0:LO + BLKW * r + 1280], lgw(r) + ["LG%d_%d" % (r, j) for j in range(8)], 1.0)
+
+    for W, nm, y, to, names in ((QA, "QA", T.y0, qe, ["q0e0", "q0e1", "q1e0", "q1e1", "inv0", "inv1"]), (QB, "QB", T.y1, cq, ["q1n%d" % s for s in range(6)])):
+        op({"x": 1.0}, None, [], names + [nm + "y0", nm + "y1"], 1.0, None)
+        for k in range(2):
+            cp(to[:, 448 * k:448 * k + 448], W[:, 0:LO + QS * RO + CAP].indirect(qyU[:, 28 * k:28 * k + 28]),
+               qw(nm, RO - 1) + ["%s%d_%d" % (nm, RO, j) for j in range(2)] + ["qyU"], [nm + "y%d" % k], ind(448), "av")
+        store("s", y[:], to[:, 0:V], [nm + "y0", nm + "y1"])
+    op({"x": 1.0}, None, [], ["r%d" % h for h in range(4)] + ["YT0", "YT1"], 1.0, None)
+    for k, (a, b) in enumerate(halves):
+        mm([(P[1 + k][0:16, 0:b - a], T.Wy[:, 0:16], ST[:, a:b])], ["Wy0", "Wy1", "STl"], 1 + k, b - a)
+        cp(rr[0:16, a:b], P[1 + k][0:16, 0:b - a], ["P%d" % (1 + k)], ["YT%d" % k], cyc(b - a), "a")
+    for j in range(2):
+        store("s", T.yt[:, V * j:V * j + V], rr[8 * j:8 * j + 8, 0:V], ["YT0", "YT1"])
+    M = WK
+    used = [x + h for x in ("wn", "un", "we", "ue", "sq") for h in "0123"]
+    Ms = ["M%d" % k for k in range(NG)]
+    full = lgw(RO) + ["LG%d_%d" % (RO, j) for j in range(8)] + ["adU"]
+    op({"x": 1.0}, None, [], used + Ms, 1.0, None)
+    op({"x": 1.0}, None, [], ["size0", "size1"] + ["YM%d" % k for k in range(4)], 1.0, None)
+    for k in range(NG):
+        w_ = FP // NG
+        cp(M[:, 16 * w_ * k:16 * w_ * (k + 1)], LG[:, 0:LO + BLKW * RO + 1280].indirect(T.adU[:, w_ * k:w_ * (k + 1)]), full, [Ms[k]], ind(16 * w_), "av")
+    Mr = T.pk2[:, 0:FP]
+    cp(Mr, M[:, 0:4 * V].indirect(T.rimS[:, 0:14]), Ms + ["rimS"], ["pk2_0"], ind(FP), "av")
+    tt(M[:, 0:4 * V].indirect(T.rimS[:, 0:14]), Mr, LG[:, LO + BLKW * RO + 1280:LO + BLKW * (RO + 1)], A.add, ["pk2_0", "LGh%d" % RO, "rimS"], Ms, ind(FP, SC))
+    for k in range(4):
+        a, pb, nm, ms_ = V * k, P[3 + k % 2][:, 0:FP], "P%d" % (3 + k % 2), Ms[2 * k:2 * k + 2]
+        if k == 3:
+            mm([(P[5][:, 0:FP], ZF, M[:, a + j:a + V:4]) for j in range(4)], ["ZF"] + ms_, 5, V, 4)
+            cp(po[:, FP * k:FP * k + FP], P[5][:, 0:FP], ["P5"], ["YM%d" % k], cyc(FP), "a")
+        else:
+            tt(pb, M[:, a:a + V:4], M[:, a + 1:a + V:4], A.add, ms_, [nm], cyc(2 * FP))
+            tt(pb, pb, M[:, a + 2:a + V:4], A.add, ms_ + [nm], [nm], cyc(FP))
+            tt(po[:, FP * k:FP * k + FP], pb, M[:, a + 3:a + V:4], A.add, ms_ + [nm], ["YM%d" % k], cyc(FP))
+        store("sa"[k % 2], T.ym[:, FP * k:FP * (k + 1)], po[:, FP * k:FP * (k + 1)], ["YM%d" % k])
+
+    for a, b, r in late:
+        for nd in nodes[a:b]:
+            nd["soft"] = marks.get(r, set())
     seen = {e: {} for e in Q}
-    wr, rd = {}, {}
 
     def need(e, toks):
         top = {}
@@ -129,573 +844,19 @@ def rank_program(g, core, T, topo):
                 Q[e].wait_ge(T.sem[s], val)
                 seen[e][s] = val
 
-    def deps(e, reads, writes):
-        toks = []
-        for x in reads:
-            if x in wr:
-                toks.append(wr[x])
-            if x[0] == "P" and x[1:].isdigit():
-                toks += [t for t in rd.get(x, []) if t[0] != e]
-        for x in writes:
-            if x in wr:
-                toks.append(wr[x])
-            toks += rd.get(x, [])
-        return toks
-
-    def op(e, fn, reads, writes):
-        need(e, deps(e, reads, writes))
-        fn().then_inc(T.sem[e], 1)
-        cnt[e] += 1
-        tok = (e, cnt[e])
-        for x in reads:
-            rd.setdefault(x, []).append(tok)
-        for x in writes:
-            wr[x] = tok
-            rd[x] = []
-        return tok
-
-    vec, act, pe = g.vector, g.scalar, g.tensor
-
-    def tt(out, a, b, o, reads, writes):
-        return op("v", lambda: vec.tensor_tensor(out, a, b, o), reads, writes)
-
-    def ts(out, a, s1, o1, reads, writes, s2=None, o2=None):
-        if o2 is None:
-            return op("v", lambda: vec.tensor_scalar(out, a, s1, None, o1), reads, writes)
-        return op("v", lambda: vec.tensor_scalar(out, a, s1, s2, o1, o2), reads, writes)
-
-    def cp(out, a, reads, writes):
-        return op("v", lambda: vec.tensor_copy(out, a), reads, writes)
-
-    def ms(out, c, writes, reads=()):
-        return op("v", lambda: vec.memset(out, c), reads, writes)
-
-    def ac(out, a, reads, writes, func=AF.Identity, bias=0.0, scale=1.0):
-        return op("a", lambda: act.activation(out, a, func, bias=bias, scale=scale), reads, writes)
-
-    def mm(out, l, r, start, stop, reads, writes):
-        return op("p", lambda: pe.matmul(out, l, r, start, stop), reads, writes)
-
-    def iota(out, pat, base, cm, writes, exact=False):
-        if exact:
-            return op("g", lambda: g.iota(out, pat, base, cm), [], writes)
-        return op("g", lambda: g.iota(out, pat, base, cm, allow_small_or_imprecise_dtypes=True), [], writes)
-
-    def sel(out, a, cmp, fill, base, cm, reads, writes):
-        return op("g", lambda: g.affine_select(out, a, [[1, 128]], cmp, fill, base, cm), reads, writes)
-
-    def load(e, k, out, src, name):
-        Q[e].dma_start(out, src).then_inc(T.sem["in%d" % k], 16)
-        wr[name] = ("in%d" % k, 16)
-
-    def store(out, src, reads):
-        need("s", deps("s", reads, []))
-        g.sync.dma_start(out, src).then_inc(T.sem.out, 16)
-        cnt["out"] += 16
-
-    def send(which, m, reads, lands):
-        need("g", deps("g", reads, []))
-        hs = shares(topo.engines(core, plan[rank][1][0][0]), 2)
-        tr = []
-        for (h, blocks), (mask, s) in zip(plan[rank][1], hs):
-            rid, pid = topo.addr(h, core)
-            tr.append(RemoteDMATransfer(dst_ids=[DstId(rid=rid, pnc=pid)], dma_engine_mask=mask, remote_sem=T.sem["hs%d" % MSG.index((which, m))],
-                                        src=piece(T, "snd", which, m, blocks[0], 3), dst=piece(T, "hb", which, m, 0, 3)))
-            cnt["loc"] += s
-        g.remote_dma_fused(tr, local_sem=T.sem.loc)
-        cnt["loc"] += forward(g, T, topo, core, rank, plan[rank][0], "snd", 0, which, m)
-        wr[lands] = ("ar%d" % MSG.index((which, m)), arrive)
-
-    P = [T["P%d" % k] for k in range(8)]
-    ST, QA, QB, LG, WS, CF = T.ST, T.QA, T.QB, T.LG, T.WS, T.CF
-    STw, QAw, QBw = ["STl", "STh"], ["QAl", "QAh"], ["QBl", "QBh"]
-
-    def wcol(k):
-        return WS[:, k:k + 1]
-
-    def W1(f):
-        return T.E1[0:1, 15 - f:143 - f]
-
-    cI, cG, cQ, cK, cP, cM, cE, nE, cO, c320, n320, n336, c12, c4, c2, cA, nK = [CF[:, k:k + 1] for k in range(17)]
-
-    load("s", 0, T.TD[0:8, :], T.t0[:], "TD0")
-    load("a", 1, T.TD[8:16, :], T.d0[:], "TD1")
-    load("s", 2, T.TD[16:24, :], T.d0[:], "TD2")
-    load("a", 3, T.RI[:, 0:14], T.rim[:], "RI")
-    load("s", 4, T.qa[:], T.q0[:], "qa")
-    load("a", 5, T.qb[:], T.q1[:], "qb")
-    load("s", 6, T.PI[:], T.port[:], "PI")
-    load("s", 7, T.TH[:, 0:1], T.th[:], "TH")
-
-    ms(T.Wt[0:24, :], 0.0, ["Wt"])
-    ms(T.RW[0:1, :], 0.0, ["RW0"])
-    ms(T.E1[0:1, :], 0.0, ["E1"])
-    iota(cP, [[0, 1]], 0, 1, ["cP"])
-    iota(T.XB[0:1, :], [[1, 256]], 0, 0, ["XB"])
-    for base, fill in ((-fT, 1.0), (128 - fD, -1.0), (256 - fD, 1.0), (256 - fM, 1.0)):
-        sel(T.Wt[0:24, :], T.Wt[0:24, :], A.not_equal, fill, base, -16, ["Wt"], ["Wt"])
-    iota(T.X[:], [[1, 240]], 0, 0, ["X"])
-    iota(T.Pi[:, 0:1], [[0, 1]], 0, 1, ["Pi"], True)
-    iota(T.XQ[:], [[1, 36], [0, 4]], 0, 0, ["XQ"])
-    iota(T.X16[:], [[1, 8], [0, 16]], 0, 0, ["X16"])
-    iota(T.SI[:], [[16, FP]], 15, 1, ["SI"])
-    iota(T.TRE[:], [[16, 56]], 2560, 1, ["TRE"])
-    ms(T.CR[0:1, :], float(7 * rank), ["CR"])
-    ms(T.E1[0:1, 15:144:16], 1.0, ["E1"])
-    ts(cM, cP, 16.0, A.is_ge, ["cP"], ["cM"], 2.0, A.mult)
-    for k in range(7):
-        wr["HI"] = ac(T.HI[0:1, 128 * k:128 * k + 128], T.XB[0:1, 0:128], ["XB"], [], bias=float(k), scale=0.0)
-    for k in range(2):
-        wr["HI"] = ac(T.HI[0:1, V + 32 * k:V + 32 * k + 32], T.XB[0:1, 0:32], ["XB"], [], bias=float(9 + k), scale=0.0)
-    terms = [(fA, 0, 0.25, 4, NW + 1), (fB, 0, 32, 4, NW + 1), (fA, 4, 1, 4, NW + 1), (fM, 8, 1, 2, NW),
-             (fNLO, 9, 1, 2, 9), (fNHI, 9, 128, 2, 9), (fT, 10, -1, 4, 1), (fM, 10, -32, 4, 1), (fD, 10, 64, 4, 1),
-             (fR, 14, BLKW, 4, 1), (fJLO, 14, 1, 4, 1), (fJHI, 14, 128, 4, 1), (fT, 18, 8192, 2, NW), (fD, 18, -8192, 1, 1),
-             (fT, 19, 1, 1, 1), (fM, 20, 3.5, 1, 1), (fD, 20, 8.5, 1, 1), (fM, 21, -2, 1, 1), (fD, 21, 1, 1, 1),
-             (0, 22, 1, 11, NW), (fM, 23, 1, 1, 1), (fD, 23, -1, 1, 1), (fM, 24, 4, 1, 1), (fR, 25, 1, 1, 1)]
-    for j, (f, col, c, count, step) in enumerate(terms):
-        a = NW * f + col
-        x = T.RW[0:1, a:a + (count - 1) * step + 1:step]
-        if j % 2:
-            wr["RWa"] = ac(x, x, ["RW0"], [], bias=float(c), scale=0.0)
+    for k in arrange(nodes):
+        nd = nodes[k]
+        toks = [t for j in nd["pre"] for t in nodes[j]["done"]]
+        if nd["fn"] is None:
+            nd["done"] = [nd["tok"]] if nd["tok"] else toks if nd["tok"] is None else []
+            continue
+        e = nd["e"]
+        need(e, toks)
+        last = nd["fn"](e)
+        if nd["tok"] is True:
+            last.then_inc(T.sem[e], 1)
+            cnt[e] += 1
+            nd["done"] = [(e, cnt[e])]
         else:
-            wr["RWv"] = ms(x, float(c), [], ["RW0"])
-    ts(T.TB[0:24, :], T.TD[0:24, :], CF[0:24, 5:6], A.max, ["TD0", "TD1", "TD2", "cM"], ["TB"])
-    ts(T.RJ[:, 0:14], T.RI[:, 0:14], 2, A.arith_shift_right, ["RI"], ["RJ0"])
-    ts(T.ZI[:, 0:128], T.X[:, 0:128], cP, A.is_equal, ["X", "cP"], ["ZI0"])
-    ts(T.ZI[:, 128:240], T.X[:, 0:112], cP, A.is_equal, ["X", "cP"], ["ZI"])
-    cp(T.rimU[:, 0:14], T.RJ[:, 0:14], ["RJ0"], ["rimU"])
-    halves = ((0, 512), (512, V))
-    for k, (a, b) in enumerate(halves):
-        mm(P[k][:, 0:b - a], W1(fNHI), T.HI[0:1, a:b], True, False, ["E1", "HI"], ["P%d" % k])
-        mm(P[k][:, 0:b - a], W1(fNHI), T.CR[0:1, 0:b - a], False, False, ["E1", "CR"], ["P%d" % k])
-        for c in range(a, b, 128):
-            mm(P[k][:, c - a:c - a + 128], W1(fNLO), T.XB[0:1, 0:128], False, False, ["E1", "XB"], ["P%d" % k])
-    for k, (a, b) in enumerate(halves):
-        mm(P[k][:, 0:b - a], T.Wt[0:24, :], T.TB[0:24, a:b], False, True, ["Wt", "TB"], ["P%d" % k])
-    ac(ST[:, 0:512], P[0][:, 0:512], ["P0"], ["ST0"])
-    cp(ST[:, 512:V], P[1][:, 0:V - 512], ["P1"], ["STl"])
-    for b in range(7):
-        j0 = (6 - b) * 32
-        mm(P[4][:, 32 * b:32 * b + 32], W1(fJLO), T.XB[0:1, 128 + j0 % 128:160 + j0 % 128], True, False, ["E1", "XB"], ["P4"])
-        mm(P[4][:, 32 * b:32 * b + 32], W1(fJHI), T.HI[0:1, V + 32 * (j0 // 128):V + 32 * (j0 // 128) + 32], False, True, ["E1", "HI"], ["P4"])
-    ac(T.CH[:], P[4][:, 0:FP], ["P4"], ["CH"])
-    for f in range(16):
-        mm(P[5][:, 0:NW], W1(f), T.RW[0:1, NW * f:NW * f + NW], f == 0, f == 15, ["E1", "RWa", "RWv"], ["P5"])
-    up = 32 * (n - 1 - rank)
-
-    def shift(bank, src, a, Z, reads):
-        for lo, hi, o in ((0, up, 112), (up, FP, 16)):
-            if hi > lo:
-                mm(P[bank][:, lo:hi], Z[:, o:o + 128], src[:, a + lo:a + hi], True, True, reads, ["P%d" % bank])
-
-    def message1(m, fill=None):
-        cp(T.pk1[:], ST[:, 0:V].indirect(T.rimU[:, 0:14]), ["STl", "ST0", "rimU"], ["pk1"])
-        shift(2, T.pk1, 0, T.ZI, ["pk1", "ZI", "ZI0"])
-        if fill:
-            fill()
-        tt(T.snd1[:, m * FP:(m + 1) * FP], P[2][:, 0:FP], T.CH[:], A.max, ["P2", "CH"], ["snd1_%d" % m])
-        send(1, m, ["snd1_%d" % m], "lnd1_%d" % m)
-
-    def pack_q(m, fill=None):
-        for k, (W, nm) in enumerate(((QA, "QAl"), (QB, "QBl"))):
-            ac(T.pk2[:, k * FP:(k + 1) * FP], W[:, 0:V].indirect(T.rimU[:, 0:14]), [nm, "rimU"], ["pk2_%d" % k])
-            shift(2 + k, T.pk2, k * FP, T.ZF, ["pk2_%d" % k, "ZF"])
-            if fill and k == 0:
-                fill()
-        for k in range(2):
-            ac(T.snd2[:, 7 * m:7 * m + 7, 32 * k:32 * k + 32], P[2 + k][:, 0:FP], ["P%d" % (2 + k)], ["snd2_%d_%d" % (m, k)])
-        send(2, m, ["snd2_%d_0" % m, "snd2_%d_1" % m], "lnd2_%d" % m)
-
-    def columns():
-        ts(T.CI[:, 0:1], T.Pi[:, 0:1], 15, A.bitwise_and, ["Pi"], ["CI0"])
-        ts(T.CI[:, 1:2], T.Pi[:, 0:1], 4, A.arith_shift_right, ["Pi"], ["CI1"])
-        ts(T.CI[:, 2:3], T.Pi[:, 0:1], 2, A.arith_shift_right, ["Pi"], ["CI2"], 3, A.bitwise_and)
-        ts(T.CI[:, 3:4], T.Pi[:, 0:1], 3, A.bitwise_and, ["Pi"], ["CI3"])
-
-    message1(0, columns)
-    cp(CF[:, 0:4], T.CI[:, 0:4], ["CI0", "CI1", "CI2", "CI3"], ["CF"])
-    ac(WS[:, 0:NW], P[5][:, 0:NW], ["P5"], ["WS"])
-    ac(QA[:, 0:V], T.qa[:], ["qa"], ["QAl"])
-    for x, sc, bi, nm in ((cE, 16, 15, "cE"), (nE, -16, -15, "nE"), (cO, 4, 3, "cO"), (c12, 16, 12, "c12"), (c4, 16, 4, "c4"),
-                          (c320, 320, 0, "c320"), (n320, -320, 0, "n320"), (n336, -336, 0, "n336")):
-        ac(x, cG, ["CF"], [nm], bias=float(bi), scale=float(sc))
-    ac(T.SI[:], T.SI[:], ["SI", "nE"], ["SI"], bias=nE)
-    ac(c2, cQ, ["CF", "c12"], ["c2"], bias=c12)
-    ac(cA, cK, ["CF", "c4"], ["cA"], bias=c4)
-    ac(nK, wcol(18), ["WS"], ["nK"], scale=-1.0)
-    ac(QB[:, 0:V], T.qb[:], ["qb"], ["QBl"])
-    ac(T.ZF[:], T.ZI[:], ["ZI", "ZI0"], ["ZF"])
-    pack_q(0)
-
-    c = T.PI[:]
-    ts(T.s1[:], c, 4.0, A.mult, ["PI"], ["s1"], -10752.0, A.add)
-    ts(T.s3[:], c, float(3584 + up), A.is_ge, ["PI"], ["s3"])
-    tt(T.s0[:], T.s1[:], c, A.max, ["s1", "PI"], ["s0"])
-    tt(T.s2[:], T.SI[:], c, A.is_lt, ["SI", "PI"], ["s2"])
-    ts(T.colU[:], T.s0[:], 0.25, A.mult, ["s0"], ["colU"], -0.375, A.add)
-    tt(T.s2[:], T.s2[:], T.s3[:], A.subtract, ["s2", "s3"], ["s2"])
-    ts(T.s4[:], T.s0[:], 127, A.bitwise_and, ["s0"], ["s4"])
-    ts(T.s5[:], T.s0[:], 7, A.arith_shift_right, ["s0"], ["s5"])
-    ts(T.s3[:], T.s2[:], 128.0, A.mult, ["s2"], ["s3"])
-    ts(T.MK[:, 0:4], T.X[:, 0:4], cQ, A.is_equal, ["X", "CF"], ["MK"])
-    ts(T.ZA0[:], T.X[:, 0:144], cA, A.is_equal, ["X", "cA"], ["ZA0"])
-    ts(T.ZO0[:], T.XQ[:], cO, A.is_equal, ["XQ", "cO"], ["ZO0"])
-    ts(T.ZE0[:], T.X[:, 0:144], cE, A.is_equal, ["X", "cE"], ["ZE0"])
-    tt(T.AB[:, FP:2 * FP], T.s5[:], T.s2[:], A.subtract, ["s5", "s2"], ["ABb"])
-    tt(T.AB[:, 0:FP], T.s4[:], T.s3[:], A.add, ["s4", "s3"], ["ABa"])
-    for m in range(4):
-        wr["ZA"] = ac(T.ZA[:, 144 * m:144 * m + 144], T.ZA0[:], ["ZA0", "MK"], [], scale=T.MK[:, m:m + 1])
-    ac(T.ZO[:], T.ZO0[:], ["ZO0", "nK"], ["ZO"], scale=nK)
-    ac(T.ZE[:], T.ZE0[:], ["ZE0", "WS"], ["ZE"], scale=wcol(18))
-    ac(T.TRE[:], T.TRE[:], ["TRE", "n336"], ["TRE"], bias=n336)
-    ts(T.BK[:], T.X16[:], cG, A.is_equal, ["X16", "CF"], ["BK"])
-    ts(T.Z2[:], T.X[:, 0:144], c2, A.is_equal, ["X", "c2"], ["Z2"])
-    sel(T.TR[:], T.BK[:], A.is_gt, 0.0, 0, -1, ["BK"], ["TR"])
-    sel(T.TR[:], T.TR[:], A.not_equal, -1024.0, 0, -1, ["TR"], ["TR"])
-    iota(T.C[:, 0:2560], [[0, 2560]], 0, 0, ["C"])
-    iota(T.JX[:, 0:20], [[1, 20]], 1024, 20, ["JX"])
-    iota(T.TRJ[:, 0:20], [[16, 20]], 1120 + V * rank + 15, 1, ["TRJ"])
-    iota(T.K3[:], [[320, 4], [0, 20]], 0, 0, ["K3"])
-    iota(LG[:, 0:BLKW], [[0, BLKW]], 0, 0, ["LG0"])
-    for k, (a, b) in enumerate(halves):
-        mm(P[k][:, 0:b - a], T.ZI[:, 0:128], ST[:, a:b], True, False, ["ZI0", "STl", "ST0"], ["P%d" % k])
-        for m in range(4):
-            mm(P[k][:, m:b - a:4], T.ZA[:, 144 * m:144 * m + 128], T.AB[:, FP + a // 4:FP + b // 4], False, False, ["ZA", "ABb"], ["P%d" % k])
-            mm(P[k][:, m:b - a:4], T.ZA[:, 144 * m + 4:144 * m + 132], T.AB[:, a // 4:b // 4], False, m == 3, ["ZA", "ABa"], ["P%d" % k])
-    ms(T.ONE[:], 1.0, ["ONE"])
-    ms(ST[:, V:V + FP], 0.0, ["STh"])
-    cp(T.rimS[:, 0:14], T.RI[:, 0:14], ["RI"], ["rimS"])
-    ms(T.SX[:, 0:1], 1024.0, ["SX0"])
-    cp(T.Wc[:, 0:18], WS[:, 0:18], ["WS"], ["Wc"])
-    ts(T.NTH[:, 0:1], T.TH[:, 0:1], -1.0, A.mult, ["TH"], ["NTH"])
-    ts(T.RJ[:, 16:30], T.RI[:, 0:14], 3, A.bitwise_and, ["RI"], ["RJ1"])
-    ts(T.s1[:], T.s0[:], 3, A.bitwise_and, ["s0"], ["s1"])
-    ts(T.rimK[:, 0:14], T.RJ[:, 16:30], 320.0, A.mult, ["RJ1"], ["rimK"])
-    ts(T.KN[:], T.s1[:], 320.0, A.mult, ["s1"], ["KN"])
-    ac(ST[:, 0:512], P[0][:, 0:512], ["P0"], ["ST0", "STl"])
-    ac(ST[:, 512:V], P[1][:, 0:V - 512], ["P1"], ["STl"])
-
-    def later_constants():
-        ac(T.JX[:, 0:20], T.JX[:, 0:20], ["JX", "n320"], ["JX"], bias=n320)
-        ac(T.TRJ[:, 0:20], T.TRJ[:, 0:20], ["TRJ", "nE"], ["TRJ"], bias=nE)
-        ac(T.ZT[:], T.ZE0[:], ["ZE0", "WS"], ["ZT"], scale=wcol(19))
-        for x in ("L1", "L2", "L3"):
-            ac(T[x][:, 0:192], T.X[:, 0:192], ["X"], [x + "z"], scale=0.0)
-
-        def put(x, a, b, val):
-            wr[x] = ac(T[x][:, a:b], T.X[:, 0:b - a], ["X", "L3z"], [], bias=val, scale=0.0)
-
-        put("LS", 0, 128, 0.5)
-        put("LS", 128, 256, -0.5)
-        for di, d in enumerate((4, 2, 1)):
-            o = 64 * di + 32
-            for a in range(d):
-                lo = o - 3 if a == 0 else o + a
-                put("L1", lo, o + a + 1, -(d - a) / 32.0)
-                put("L2", lo, o + a + 1, -(d * d - a * a) / 64.0)
-            for a in range(d - 4, d):
-                put("L3", o + a, o + a + 1, ((d - a) ** 2 - (max(a, 0) - a) ** 2) / 64.0)
-        for x in ("L1", "L2", "L3"):
-            ac(T[x][:, 192:384], T[x][:, 0:192], [x], [x], scale=-1.0)
-        ac(T.NI[:], T.ZI[:, 0:128], ["ZI0"], ["NI"], scale=-1.0)
-
-    def last_constants():
-        for a, b, val in ((0, 3, 0.5), (3, 4, 1.0), (4, 5, 0.25)):
-            wr["LI"] = ac(T.LI[:, a:b], T.X[:, 0:b - a], ["X"], [], bias=val, scale=0.0)
-        ac(T.Wb1[:], T.ZI[:, 0:128], ["ZI0", "WS"], ["Wb1"], scale=wcol(22))
-        ac(T.Wb2[:], T.ZE0[:, 15 - fT:143 - fT], ["ZE0", "WS"], ["Wb2"], scale=wcol(23))
-        for r in range(1, RO + 1):
-            wr["BR"] = ac(T.BR[:, r:r + 1], wcol(25), ["WS"], [], bias=wcol(24), scale=float(r))
-        ac(T.ZP[:], T.ZE0[:], ["ZE0", "WS"], ["ZP"], scale=wcol(14))
-        ac(T.ZQ[:], T.ZO0[:], ["ZO0", "WS"], ["ZQ"], scale=wcol(14))
-        ac(T.Wy[:, 0:8], T.BK[:, 0:128:16], ["BK", "WS"], ["Wy0"], scale=wcol(19))
-        ac(T.Wy[:, 8:16], T.BK[:, 0:128:16], ["BK", "WS"], ["Wy1"], scale=wcol(23))
-
-    def slots_a(a, b, s):
-        ac(T.G[:, 16 * a:16 * b], ST[:, 0:V + FP].indirect(T.colU[:, a:b]), STw + ["colU"], ["G%d" % s])
-
-    def slots_v(a, b, s):
-        cp(T.G[:, 16 * a:16 * b], ST[:, 0:V + FP].indirect(T.colU[:, a:b]), STw + ["colU"], ["G%d" % s])
-
-    def all_slots(m, bank, Z, zn):
-        Gs = ["G0", "G1", "G2"]
-        cp(T.G[:, 0:4 * V].indirect(T.rimS[:, 0:14]), T.lnd1[:, m * FP:(m + 1) * FP], ["lnd1_%d" % m, "rimS"], Gs)
-        for i in range(16):
-            mm(P[bank][:, 0:FP], Z[:, 15 - i:143 - i], T.G[:, i:4 * V:16], False, i == 15, Gs + [zn], ["P%d" % bank])
-
-    def lgw(r):
-        return ["LG0"] + ["LGl%d_%d" % (k, j) for k in range(1, r) for j in range(4)] + ["LGh%d" % k for k in range(1, r)]
-
-    UU, sm, si, su, qe, cq, w, rr, FF, xx, po, gb = T.UU, T.sm, T.si, T.su, T.qe, T.cq, T.w, T.r, T.FF, T.xx, T.po, T.gb
-    eU, caseU, takeU, keepU, eS = UU[:, 180:200], su[:, 0:80], su[:, 80:160], su[:, 160:240], su[:, 240:260]
-    pre, knf, Pk, zz, own, t0, t1, t3 = [sm[:, 80 * k:80 * k + 80] for k in range(8)]
-    t2 = sm[:, 640:660]
-    L1, L2, L3, LS, LGall = T.L1[:, 0:384], T.L2[:, 0:384], T.L3[:, 0:384], T.LS[:, 0:256], LG[:, 0:6 * BLKW]
-    q0e, q1e, inv = qe[:, 0:320], qe[:, 320:640], qe[:, 640:960]
-    qf, dq = po[:, 0:320], po[:, 320:640]
-    g1, g2, nn, base = [gb[:, 320 * k:320 * k + 320] for k in range(4)]
-
-    def sums(r, a, b):
-        out, names = LG[:, BLKW * r + 320 * a:BLKW * r + 320 * b], ["LGl%d_%d" % (r, k) for k in range(a, b)]
-        fs = ["F%d" % k for k in range(a, b)]
-        if r == 1:
-            ac(out, FF[:, 320 * a:320 * b], fs, names, scale=-1.0)
-        else:
-            tt(out, LG[:, 0:BLKW * r].indirect(su[:, 160 + 20 * a:160 + 20 * b]), FF[:, 320 * a:320 * b], A.subtract, lgw(r) + ["keepU"] + fs, names)
-
-    def rim_a():
-        tt(T.ryF[:, 0:14], P[4][:, 0:14], T.rimK[:, 0:14], A.add, ["P4", "rimK"], ["ryF"])
-
-    def rim_b():
-        cp(T.ryU[:, 0:14], T.ryF[:, 0:14], ["ryF"], ["ryU"])
-
-    def pack_y(r):
-        ac(T.pk2[:, 2 * FP:3 * FP], LG[:, 0:BLKW * r + 1280].indirect(T.ryU[:, 0:14]),
-           lgw(r) + ["LGl%d_%d" % (r, k) for k in range(4)] + ["ryU"], ["pk2_2"])
-        shift(3, T.pk2, 2 * FP, T.ZF, ["pk2_2", "ZF"])
-        ac(T.snd3[:, r * FP:(r + 1) * FP], P[3][:, 0:FP], ["P3"], ["snd3_%d" % r])
-        send(3, r, ["snd3_%d" % r], "LGh%d" % r)
-
-    for r in range(1, RO + 1):
-        for m in range(4):
-            mm(P[5][:, 0:FP], T.ZO[:, 12 - 4 * m:140 - 4 * m], ST[:, m:V:4], m == 0, False, ["ZO", "STl"], ["P5"])
-        if r == 1:
-            slots_a(0, 56, 0)
-            slots_v(112, FP, 2)
-            slots_a(56, 112, 1)
-            later_constants()
-            last_constants()
-        all_slots(r - 1, 5, T.ZE, "ZE")
-        ac(ST[:, V:V + FP], T.lnd1[:, (r - 1) * FP:r * FP], ["lnd1_%d" % (r - 1)], ["STh"])
-        if r > 1:
-            sums(r - 1, 1 if r > 2 else 0, 4)
-        ts(T.bit[:], P[5][:, 0:FP], 0.0, A.is_gt, ["P5"], ["bit"])
-        for h in range(4):
-            mm(P[6][:, 0:56], T.Z2[:, 12 - 4 * h:140 - 4 * h], T.bit[:, h:FP:4], h == 0, h == 3, ["Z2", "bit"], ["P6"])
-        if r > 1:
-            rim_a()
-        ts(T.can[:], P[6][:, 0:56], 3.5, A.is_ge, ["P6"], ["can"])
-        mm(P[1][:, 0:56], T.BK[:], T.can[:], True, True, ["BK", "can"], ["P1"])
-        mm(P[0][:, 0:56], T.TR[:], T.can[:], True, True, ["TR", "can"], ["P0"])
-        if r > 1:
-            rim_b()
-            pack_y(r - 1)
-        op("v", lambda: vec.tensor_tensor_scan(T.SX[:, 1:57], T.ONE[:], P[1][:, 0:56], 1024.0, A.mult, A.add), ["ONE", "P1"], ["SX"])
-        tt(T.v0[:], P[0][:, 0:56], T.SX[:, 0:56], A.add, ["P0", "SX", "SX0"], ["v0"])
-        ts(T.v1[:], T.v0[:], float(CAP), A.is_ge, ["v0"], ["v1"], 8192.0, A.mult)
-        tt(T.v0[:], T.v0[:], T.v1[:], A.add, ["v0", "v1"], ["v0"])
-        tt(T.v0[:], T.v0[:], T.TRE[:], A.min, ["v0", "TRE"], ["v0"])
-        ts(T.posU[:], T.v0[:], c320, A.add, ["v0", "c320"], ["posU"])
-        cp(T.C[:, 0:3456].indirect(T.posU[:, 0:56]), ST[:, 0:V], ["posU", "STl"], ["C"])
-        ac(QB[:, V:V + FP], T.lnd2[:, 7 * r - 7:7 * r, 32:64], ["lnd2_%d" % (r - 1)], ["QBh"])
-        ac(QA[:, V:V + FP], T.lnd2[:, 7 * r - 7:7 * r, 0:32], ["lnd2_%d" % (r - 1)], ["QAh"])
-        for b in range(20):
-            mm(P[7][:, b:360:20], T.C[:, b:2560:20], T.Wc[:, 0:18], True, True, ["C", "Wc"], ["P7"])
-        ts(t2, T.JX[:, 0:20], T.SX[:, 56:57], A.is_ge, ["JX", "SX"], ["t2"], 16384.0, A.mult)
-        ts(UU[:, 0:180], P[7][:, 0:180], -0.375, A.add, ["P7"], ["UU"])
-        ts(eU, P[7][:, 180:200], float(-V * rank), A.add, ["P7"], ["eU"])
-        cp(T.GN[:, 0:640], ST[:, 0:V + FP].indirect(UU[:, 0:40]), STw + ["UU"], ["GNv"])
-        ac(T.GN[:, 640:1280], ST[:, 0:V + FP].indirect(UU[:, 40:80]), STw + ["UU"], ["GNa"])
-        for i in range(16):
-            mm(P[4][:, 0:80], T.ZT[:, 15 - i:143 - i], T.GN[:, i:1280:16], i == 0, i == 15, ["GNv", "GNa", "ZT"], ["P4"])
-        if r > 1:
-            for i in range(16):
-                mm(P[5][:, 0:80], T.ZP[:, 15 - i:143 - i], T.GN[:, i:1280:16], i == 0, i == 15, ["GNv", "GNa", "ZP"], ["P5"])
-        ts(pre, P[7][:, 80:160], 128.0, A.is_ge, ["P7"], ["pre"], 192.0, A.mult)
-        tt(t2, P[7][:, 180:200], t2, A.add, ["P7", "t2"], ["t2"])
-        tt(pre, P[7][:, 200:280], pre, A.add, ["P7", "pre"], ["pre"])
-        tt(t2, t2, T.TRJ[:, 0:20], A.min, ["t2", "TRJ"], ["t2"])
-        if r > 1:
-            cp(si[:, 0:80], P[7][:, 80:160], ["P7"], ["si0"])
-        tt(t0, P[4][:, 0:80], pre, A.add, ["P4", "pre"], ["t0"])
-        ts(eS, t2, float(-V * rank), A.add, ["t2"], ["eS"])
-        ts(caseU, t0, 160.0, A.add, ["t0"], ["caseU"])
-
-        def cut(buf, a, k, per=4):
-            o = 320 * (per * a + k % per)
-            return buf[:, o:o + 320]
-
-        def lst(x, k, o=0):
-            return x[:, o + 20 * k:o + 20 * k + 20]
-
-        def a_pre(k):
-            ac(cut(cq, 0, k), QB[:, 0:V + FP].indirect(lst(UU, k)), QBw + ["UU"], ["q1n%d" % k])
-            ac(cut(cq, 1, k), L1.indirect(lst(su, k)), ["L1", "caseU"], ["c1%d" % k])
-
-        def a_sgn(k):
-            ac(cut(cq, 2, k), LS.indirect(lst(UU, k, 80)), ["LS", "UU"], ["sg%d" % k])
-
-        def v_a(k):
-            b = k % 2
-            we, un, wn, je = [cut(w, a, k, 2) for a in range(4)]
-
-            def o_wn():
-                tt(wn, L3.indirect(lst(su, k)), cut(cq, 0, k), A.mult, ["L3", "caseU", "q1n%d" % k], ["wn%d" % b])
-
-            def o_un():
-                tt(un, QA[:, 0:V + FP].indirect(lst(UU, k)), cut(cq, 1, k), A.mult, QAw + ["UU", "c1%d" % k], ["un%d" % b])
-                mm(P[2 + b][:, 0:320], T.ZF[:, 0:128], wn, True, False, ["ZF", "wn%d" % b], ["P%d" % (2 + b)])
-                mm(P[2 + b][:, 0:320], T.NI[:], un, False, True, ["NI", "un%d" % b], ["P%d" % (2 + b)])
-
-            def o_we():
-                tt(we, L2.indirect(lst(su, k)), q1e, A.mult, ["L2", "caseU", "q1e"], ["we%d" % b])
-
-            def o_ue():
-                if J_ON_PE:
-                    tt(je, P[0][:, 0:320], cut(cq, 1, k), A.mult, ["P0", "c1%d" % k], ["je%d" % b])
-                    mm(P[1][:, 0:320], T.ZF[:, 0:128], we, True, False, ["ZF", "we%d" % b], ["P1"])
-                    mm(P[1][:, 0:320], T.ZF[:, 0:128], je, False, True, ["ZF", "je%d" % b], ["P1"])
-                else:
-                    tt(P[1][:, 0:320], P[0][:, 0:320], cut(cq, 1, k), A.mult, ["P0", "c1%d" % k], ["P1"])
-
-            def o_je():
-                if not J_ON_PE:
-                    tt(je, P[1][:, 0:320], we, A.add, ["P1", "we%d" % b], ["je%d" % b])
-
-            return [o_we, o_wn, o_un, o_ue, o_je] if k == 0 else [o_wn, o_un, o_we, o_ue, o_je]
-
-        def a_sq(k):
-            b = k % 2
-            re, rn, sq = [cut(rr, a, k, 2) for a in range(3)]
-            ac(rn, P[2 + b][:, 0:320], ["P%d" % (2 + b)], ["rn%d" % b], AF.Relu)
-            if J_ON_PE:
-                ac(re, P[1][:, 0:320], ["P1"], ["re%d" % b], AF.Relu)
-            else:
-                ac(re, cut(w, 3, k, 2), ["je%d" % b], ["re%d" % b], AF.Relu)
-            ac(sq, rn, ["rn%d" % b], ["sq%d" % b], AF.Square)
-            ac(P[4 + b][:, 0:320], re, ["re%d" % b], ["P%d" % (4 + b)], AF.Square)
-
-        def v_b(k):
-            b = k % 2
-            pb, nm = P[4 + b][:, 0:320], "P%d" % (4 + b)
-            x, xn = (cut(xx, 0, k, 2), "x%d" % b) if r > 1 else (cut(FF, 0, k), "F%d" % k)
-
-            def o_s():
-                tt(pb, pb, cut(rr, 2, k, 2), A.add, [nm, "sq%d" % b], [nm])
-
-            def o_f():
-                tt(cut(FF, 0, k), pb, cut(cq, 2, k), A.mult, [nm, "sg%d" % k], ["F%d" % k])
-
-            def o_x():
-                if r > 1:
-                    tt(x, LG[:, 0:BLKW * r].indirect(lst(su, k, 80)), cut(FF, 0, k), A.add, lgw(r) + ["takeU", "F%d" % k], [xn])
-
-            def o_q():
-                if Q_ON_PE and k < 3:
-                    if k == 0:
-                        mm(P[6][:, 0:320], T.ZF[:, 0:128], q0e, True, False, ["ZF", "q0e"], ["P6"])
-                    mm(P[6][:, 0:320], T.ZF[:, 0:128], x, False, k == 2, ["ZF", xn], ["P6"])
-                    return
-                src, sn = (P[0], "P0") if k == 0 else (P[6], "P6")
-                if k < 3:
-                    tt(P[6][:, 0:320], src[:, 0:320], x, A.add, [sn, xn], ["P6"])
-                else:
-                    tt(qf, src[:, 0:320], x, A.add, [sn, xn], ["qf"])
-
-            return [o_s, o_f, o_x, o_q]
-
-        def take():
-            return [lambda: ts(si[:, 80:160], si[:, 0:80], 3, A.bitwise_and, ["si0"], ["si2"]),
-                    lambda: tt(Pk, P[7][:, 280:360], T.K3[:], A.add, ["P7", "K3"], ["Pk"]),
-                    lambda: ts(knf, si[:, 80:160], 320.0, A.mult, ["si2"], ["knf"]),
-                    lambda: tt(zz, P[5][:, 0:80], knf, A.add, ["P5", "knf"], ["zz"]),
-                    lambda: tt(own, zz, Pk, A.is_gt, ["zz", "Pk"], ["own"]),
-                    lambda: tt(t1, own, zz, A.mult, ["own", "zz"], ["t1"]),
-                    lambda: cp(takeU, t1, ["t1"], ["takeU"])]
-
-        def keep():
-            return [lambda: tt(t3, own, Pk, A.mult, ["own", "Pk"], ["t3"]),
-                    lambda: tt(t3, Pk, t3, A.subtract, ["Pk", "t3"], ["t3"]),
-                    lambda: cp(keepU, t3, ["t3"], ["keepU"])]
-
-        def run(a, b=(), order=None):
-            both = {"a": list(a), "b": list(b)}
-            for ch in order or "a" * len(a):
-                if both[ch]:
-                    both[ch].pop(0)()
-
-        ac(q1e, QB[:, 0:V].indirect(eU), ["QBl", "eU"], ["q1e"])
-        a_pre(0)
-        ac(q0e, QA[:, 0:V].indirect(eU), ["QAl", "eU"], ["q0e"])
-        ac(P[0][:, 0:320], q0e, ["q0e"], ["P0"])
-        a_pre(1)
-        run(v_a(0), take()[:4] if r > 1 else (), "abbababaa")
-        a_sq(0)
-        a_sgn(0)
-        a_pre(2)
-        run(v_a(1), take()[4:] if r > 1 else (), "babababaa")
-        a_sq(1)
-        a_sgn(1)
-        a_pre(3)
-        run(v_a(2), v_b(0), "bababaaba")
-        a_sq(2)
-        a_sgn(2)
-        a_sgn(3)
-        ac(T.GO[:], ST[:, 0:V].indirect(eU), ["STl", "eU"], ["GO"])
-        run(v_a(3), v_b(1), "bababaaba")
-        mm(P[7][:, 0:320], T.Wb1[:], T.GO[:], True, False, ["Wb1", "GO"], ["P7"])
-        mm(P[7][:, 0:320], T.Wb2[:], T.GO[:], False, False, ["Wb2", "GO"], ["P7"])
-        for c0 in range(0, 320, 128):
-            c1 = min(c0 + 128, 320)
-            mm(P[7][:, c0:c1], W1(fJLO), T.XB[0:1, 0:c1 - c0], False, False, ["E1", "XB"], ["P7"])
-        mm(P[7][:, 0:320], W1(fJHI), T.HI[0:1, 0:320], False, True, ["E1", "HI"], ["P7"])
-        a_sq(3)
-        ac(base, P[7][:, 0:320], ["P7", "BR"], ["base"], bias=T.BR[:, r:r + 1])
-        ac(inv, T.LI[:, 0:5].indirect(UU[:, 160:180]), ["LI", "UU"], ["inv"])
-        run(v_b(2))
-        run(v_b(3))
-        ts(g1, qf, T.TH[:, 0:1], A.is_gt, ["qf", "TH"], ["g1"])
-        mm(P[1][:, 0:320], T.BK[:], g1, True, False, ["BK", "g1"], ["P1"])
-        ts(g2, qf, T.NTH[:, 0:1], A.is_lt, ["qf", "NTH"], ["g2"])
-        mm(P[1][:, 0:320], T.BK[:], g2, False, True, ["BK", "g2"], ["P1"])
-        tt(dq, qf, P[0][:, 0:320], A.subtract, ["qf", "P0"], ["dq"])
-        ts(nn, P[1][:, 0:320], wcol(20), A.is_ge, ["P1", "WS"], ["nn"], wcol(21), A.mult)
-        tt(ST[:, 0:1440].indirect(eS), nn, base, A.add, ["nn", "base", "eS"], STw)
-        slots_a(0, 104, 0)
-        message1(r, keep()[0] if r > 1 else None)
-        for i in range(16):
-            mm(P[4][:, 0:14], T.ZP[:, 15 - i:143 - i], T.pk1[:, i:FP:16], i == 0, i == 15, ["pk1", "ZP"], ["P4"])
-        if r == RO:
-            run(keep()[1:])
-            sums(r, 0, 4)
-            rim_a()
-            rim_b()
-            pack_y(r)
-            slots_a(104, 196, 1)
-            slots_v(196, FP, 2)
-        cp(QA[:, 0:1440].indirect(eS), qf, ["qf", "eS"], QAw)
-        tt(QB[:, 0:1440].indirect(eS), dq, inv, A.mult, ["dq", "inv", "eS"], QBw)
-        if r < RO:
-            slots_v(160, FP, 2)
-            pack_q(r, lambda: slots_a(104, 160, 1))
-            if r > 1:
-                run(keep()[1:])
-                sums(r, 0, 1)
-
-    store(T.y0[:], QA[:, 0:V], ["QAl"])
-    store(T.y1[:], QB[:, 0:V], ["QBl"])
-    for m in range(4):
-        mm(P[6][:, 0:FP], T.ZQ[:, 12 - 4 * m:140 - 4 * m], ST[:, m:V:4], m == 0, m == 3, ["ZQ", "STl"], ["P6"])
-    mm(P[5][:, 0:FP], T.ZF[:, 0:128], T.KN[:], True, False, ["ZF", "KN"], ["P5"])
-    ac(T.PE[:], P[6][:, 0:FP], ["P6"], ["PE"])
-    for j in range(2):
-        for k, (a, b) in enumerate(halves):
-            mm(P[2 * j + k][0:8, 0:b - a], T.Wy[:, 8 * j:8 * j + 8], ST[:, a:b], True, True, ["Wy%d" % j, "STl"], ["P%d" % (2 * j + k)])
-            wr["YT"] = ac(T.YT[0:8, j * V + a:j * V + b], P[2 * j + k][0:8, 0:b - a], ["P%d" % (2 * j + k)], [])
-    store(T.yt[:], T.YT[0:8, :], ["YT"])
-    all_slots(RO, 5, T.ZP, "ZP")
-    tt(T.fa[:], P[5][:, 0:FP], T.PE[:], A.is_gt, ["P5", "PE"], ["fa"])
-    tt(T.fb[:], P[5][:, 0:FP], T.fa[:], A.mult, ["P5", "fa"], ["fb"])
-    cp(T.adU[:], T.fb[:], ["fb"], ["adU"])
-    full = lgw(RO + 1) + ["adU"]
-    M = cq
-    cp(M[:, 0:V], LGall.indirect(T.adU[:, 0:56]), full, ["M0"])
-    for k in range(1, 4):
-        ac(M[:, V * k:V * k + V], LGall.indirect(T.adU[:, 56 * k:56 * k + 56]), full, ["M%d" % k])
-    for k in range(4):
-        a, pb, nm = V * k, P[6 + k % 2][:, 0:FP], "P%d" % (6 + k % 2)
-        tt(pb, M[:, a:a + V:4], M[:, a + 1:a + V:4], A.add, ["M%d" % k], [nm])
-        tt(pb, pb, M[:, a + 2:a + V:4], A.add, ["M%d" % k, nm], [nm])
-        tt(T.YM[:, FP * k:FP * k + FP], pb, M[:, a + 3:a + V:4], A.add, ["M%d" % k, nm], ["YM%d" % k])
-        store(T.ym[:, FP * k:FP * (k + 1)], T.YM[:, FP * k:FP * (k + 1)], ["YM%d" % k])
+            nd["done"] = [nd["tok"]] if nd["tok"] else []
     need("g", [(s, c_) for s, c_ in cnt.items()])

@@ -1,24 +1,34 @@
+import math
 from concourse.bass import DstId, RemoteDMATransfer
 from concourse.mybir import AluOpType as A, ActivationFunctionType as AF
 
-V, FP, CAP, RO, BLKW = 896, 224, 320, 5, 1504
+V, FP, CAP, RO = 896, 224, 320, 5
 NR = CAP - FP
 F, H, I, U = "float32", "bfloat16", "int32", "uint16"
-fA, fB, fNLO, fNHI, fT, fM, fD, fR, fJLO, fJHI = 0, 4, 8, 9, 10, 11, 12, 13, 14, 15
-NW = 34
-GW = 4800
-LO, QS = 640, CAP + FP
-TW = 1472
-MSG = [(w_, m_) for m_ in range(RO + 1) for w_ in (1, 2, 3) if (m_ > 0 if w_ == 3 else m_ < RO)]
-CYC, PCYC, GA, SC, LAT, DMA, HOP = 0.83, 0.42, 1.56, 3.8, 100.0, 2000.0, 4500.0
-MARGIN, TURNS, WAIT, SLACK = 1500.0, 10, 100.0, 4.0
+fS, fEL, fEH, fT, fM, fD, fR, fJL, fJH, fP, fQ = 0, 4, 5, 6, 7, 8, 9, 10, 11, 12, 13
+BL, LND, ZC = 2688, 1920, 2592
+SL = V + CAP
+CF0, CB0 = V, V + 8 * FP
+BIG, B2 = 4096.0, 8192.0
+NW = 77
+cWO, cWN, cWF = 22, 38, 54
+cS, cX, cZJ, cTH, cNN, cKP, cD, cB4, cR, cT, cEL, cPL, cQ4, cXR = range(63, NW)
+MSG = [(1, m_) for m_ in range(RO)] + [(2, m_) for m_ in range(RO)] + [(3, RO)]
+MSG.sort(key=lambda x: (x[1], x[0]))
+CYC, PCYC, GA, SC, LAT, DMA, HOP = 0.83, 0.42, 1.5, 3.6, 100.0, 2000.0, 4800.0
+MARGIN, TURNS, WAIT, SLACK, AHEAD = 1500.0, 3, 100.0, 3.0, 0.0
 JV = (1, 3, 5)
+GV = 34
 CUT = (4, 4)
-VADD, VMIN, AADD, PFIX, CROSS = 0.0, 53.0, 66.0, 10.0, 120.0
-SGV, ABS, SND, QV = (0, 1, 2, 3, 4, 5), (), "a", ()
+VADD, VMIN, AADD, PFIX, CROSS = 0.0, 53.0, 66.0, 20.0, 120.0
 URGE = 1500.0
-LATE, PK, WIDE, FIRST, T2, T3 = ["G7"], "a", 4000.0, 1.8, 2.0, 3.0
-ORDER = "f0 f1 m0 f2 m1 b0 f3 m2 b1 f4 m3 b2 b3 out f5 m4 m5 b4 b5"
+WIDE, FIRST, T2, T3, ONCE = 4000.0, 1.4, 1.5, 2.0, 3000.0
+MOVES = ((None, 1, 26000), (1, 3, 36000), (4, None, 15000))
+STEP, HEAT, SEED = (0.0, 300.0, 600.0, 2500.0), 120.0, 1
+GFQ = "av"
+ORDER = "a1 e1 g4 g5 x a0 f4 f5 g0 e0 g1 m4 g2 m5 g3 f0 f1 b4 o1 b5 m0 q f2 m1 f3 b0 m2 b1 m3 s o0 b2 n b3 l"
+SNQ = "av"
+SA = (2, 3, 4, 5)
 
 
 def sb(n, t):
@@ -26,27 +36,23 @@ def sb(n, t):
 
 
 SCRATCH = {
-    "ST": sb(TW, H), "C": sb(3456, H), "CT": sb(2560, H), "G": sb(GW, H), "GN": sb(1280, H), "GO": sb(320, H),
-    "QA": sb(LO + RO * QS + CAP, F), "QB": sb(LO + RO * QS + CAP, F), "LG": sb(LO + 6 * BLKW, F),
-    "snd1": sb(5 * FP, H), "lnd1": sb(5 * FP, H),
-    "snd2": ("sbuf", [128, 35, 64], F), "lnd2": ("sbuf", [128, 35, 64], F),
-    "snd3": sb(6 * FP, F),
+    "ST": sb(SL + RO * FP, H), "C": sb(3456, H), "TK": sb(2560, F), "G": sb(FP + 4 * V, H), "GF": sb(V + 2 * FP, H), "GO": sb(CAP, H),
+    "RR": sb(V, H), "RF": sb(FP, H), "FT": sb(V, H), "LG": sb(RO * BL + LND, F),
+    "snd1": sb(5 * FP, H), "snd2": sb(5 * 3 * FP, F), "snd3": sb(FP, F), "lnd3": sb(FP, F),
     "qa": sb(V, H), "qb": sb(V, H), "TD": sb(V, I), "TB": sb(V, H), "TH": sb(8, F),
-    "PI": sb(FP, I), "RI": sb(16, I), "RJ": sb(32, I), "rimU": sb(16, U), "rimS": sb(16, U), "rimK": sb(32, F), "ryF": sb(16, F), "ryU": sb(32, U), "qU": sb(240, U), "ZR": sb(144, H),
-    "s0": sb(6 * FP, I), "SI": sb(FP, F),
-    "colU": sb(FP, U), "KN": sb(FP, F), "AB": sb(2 * FP, H), "PE": sb(3 * FP, F), "adU": sb(FP, U),
-    "Pi": sb(8, I), "CI": sb(8, I), "CF": sb(32, F), "MK": sb(32, F), "BR": sb(8, F), "RW": sb(16 * NW, H), "E1": sb(144, H),
-    "WS": sb(40, F), "X": sb(240, F), "XB": sb(256, H), "XQ": sb(144, F), "X16": sb(128, F), "CR": sb(512, H),
-    "HI": sb(V + 64, H), "Wt": sb(128, H), "Wc": sb(112, H), "ZJ": sb(240, H), "ZI": sb(240, H), "ZF": sb(240, F), "NI": sb(128, F),
-    "ZE0": sb(144, H), "ZO0": sb(144, H), "ZA0": sb(144, H),
-    "ZE": sb(144, H), "ZT": sb(144, H), "ZP": sb(144, H), "ZO": sb(144, H), "ZQ": sb(144, H), "Z2": sb(144, H), "ZA": sb(4 * 144, H),
-    "BK": sb(128, H), "TR": sb(7 * 128, H), "Wb": sb(128, H), "Wy": sb(16, H), "CH": sb(FP, H), "ZB": sb(176, H), "KI": sb(504, H),
-    "TRE": sb(56, F), "ONE": sb(176, F), "SX": sb(176, F), "IN": sb(176, F),
-    "L1": sb(384, F), "L2": sb(384, F), "L3": sb(384, F), "LS": sb(384, F), "LI": sb(384, F),
-    "bit": sb(FP, H), "can": sb(112, H), "THR": sb(112, F), "v0": sb(176, F), "v1": sb(4 * 56, F), "posU": sb(56, U),
-    "UU": sb(104, U), "sm": sb(720, F), "su": sb(240, U),
-    "qe": sb(960, F), "cq": sb(1280, F), "cb": sb(2 * 1280, H), "WK": sb(5 * 832, F), "r": sb(2 * 832, F), "FF": sb(1288, F), "xx": sb(832, F),
-    "po": sb(960, F), "gb": sb(4 * 320, H), "NT": sb(8, F), "pk1": sb(FP, H), "pk2": sb(3 * FP, F),
+    "PI": sb(FP, I), "RI": sb(32, I), "RJ": sb(32, I), "rimU": sb(16, U), "rimS": sb(16, U), "rimK": sb(32, F), "ryF": sb(16, F), "ryU": sb(48, U),
+    "s0": sb(6 * FP, I), "SI": sb(FP, F), "colU": sb(2 * FP, U), "KN": sb(FP, F), "AB": sb(8 * FP + 16, H), "PE": sb(3 * FP, F), "adU": sb(FP, U),
+    "Pi": sb(8, I), "CI": sb(8, I), "CF": sb(32, F), "MK": sb(32, F), "BR": sb(8, F), "RW": sb(16 * NW, H), "E1": sb(144 + 256, H),
+    "WS": sb(80, F), "WB": sb(80, H), "X": sb(256, F), "XB": sb(256, H), "XQ": sb(144, F), "X16": sb(128, F), "CR": sb(512, H), "PT": sb(256 + 3 * CAP, H),
+    "HI": sb(V + 64, H), "Wt": sb(128, H), "Wo": sb(128, H), "WN": sb(144, H), "ZJ": sb(240, H), "ZI": sb(256, H), "ZF": sb(240, F), "NI": sb(128, F),
+    "ZE0": sb(144, H), "ZO0": sb(144, H), "ZA0": sb(144, H), "ZE": sb(144, H), "ZX": sb(144, H), "ZP": sb(144, H), "ZO": sb(144, H), "ZQ": sb(144, H),
+    "Z2": sb(144, H), "ZA": sb(4 * 144, H), "BK": sb(128, H), "TR": sb(13 * 128, H), "Wb": sb(128, H), "Wy": sb(16, H), "CH": sb(FP, H), "JR": sb(CAP, H),
+    "TRE": sb(56, F), "ONE": sb(56, F), "SX": sb(240, F), "LT": sb(4 * 256, F), "LW": sb(7 * 64, F), "KE": sb(80, F),
+    "bit": sb(FP, H), "can": sb(112, H), "THR": sb(56, F), "v1": sb(4 * 56, F), "posU": sb(72, U), "MF": sb(FP, H), "NB": sb(FP, H),
+    "FN": sb(5 * 56 + 32, U), "FW": sb(2 * 56, F), "FI": sb(32, I), "THF": sb(84, H), "bf": sb(70, F),
+    "UA": sb(180, U), "UB": sb(100, U), "UC": sb(160, U), "eU": sb(20, U), "qyU": sb(112, U), "ki": sb(80, I), "sm": sb(320, F),
+    "qe": sb(960, F), "cq": sb(1280, F), "cb": sb(2688, H), "WK": sb(5 * 832, F), "r": sb(2 * 832, F), "FF": sb(1288, F), "xx": sb(832, F),
+    "po": sb(V, F), "gb": sb(4 * 320, H), "NT": sb(8, F), "pk1": sb(FP, H), "pk2": sb(3 * FP, F),
 }
 for _k in range(8):
     SCRATCH["P%d" % _k] = ("psum", [128, 512], F)
@@ -64,7 +70,7 @@ def routes(T, topo):
                 and all(topo.may_write(h, T.cores[(r + b + 1) % n]) for b in far)]
         able.sort(key=lambda h: topo.die(h) != topo.die(c))
         half = len(far) // 2
-        plan.append((direct, [(able[0], far[:half]), (able[1], far[half:])]))
+        plan.append((direct[::-1], [(able[0], far[:half]), (able[1], far[half:])]))
     return plan
 
 
@@ -83,22 +89,22 @@ def shares(engs, n):
 
 
 def piece(T, kind, which, m, a, n):
-    per, kind = (3, "snd") if kind == "hb" else (7, kind)
-    if which == 2:
-        return T[kind + "2"][:, m * per + a:m * per + a + n, :]
-    if which == 3 and kind == "lnd":
-        return T.LG[:, LO + BLKW * m + 1280 + 32 * a:LO + BLKW * m + 1280 + 32 * (a + n)]
-    return T[kind + str(which)][:, (m * per + a) * 32:(m * per + a + n) * 32]
+    w = 96 if which == 2 else 32
+    if kind == "lnd":
+        buf, at = ((T.ST, SL + FP * m), (T.LG, BL * m + LND), (T.lnd3, 0))[which - 1]
+    else:
+        buf, at = T["snd%d" % which], (m % RO) * 7 * w
+    return buf[:, at + w * a:at + w * (a + n)]
 
 
 def forward(g, T, topo, src, r, blocks, kind, first, which, m):
     n = len(T.cores)
     sh = shares(topo.engines(src, T.cores[(r + blocks[0] + 1) % n]), len(blocks))
     tr = []
-    for b, (mask, _) in zip(blocks, sh):
+    for j, (b, (mask, _)) in enumerate(zip(blocks, sh)):
         rid, pid = topo.addr(T.cores[(r + b + 1) % n], src)
         tr.append(RemoteDMATransfer(dst_ids=[DstId(rid=rid, pnc=pid)], dma_engine_mask=mask, remote_sem=T.sem["ar%d" % MSG.index((which, m))],
-                                    src=piece(T, kind, which, m, b - first, 1), dst=piece(T, "lnd", which, m, n - 2 - b, 1)))
+                                    src=piece(T, kind, which, m, first + j, 1), dst=piece(T, "lnd", which, m, n - 2 - b, 1)))
     g.remote_dma_fused(tr, local_sem=T.sem.loc)
     return sum(s for _, s in sh)
 
@@ -113,15 +119,18 @@ def place(nodes, rank, before, after, urge=0.0):
         t, e = min((max(free[e], min(due[e][k] for k in row)), e) for e, row in pool.items() if row)
         ready = due[e]
         row = sorted(pool[e], key=lambda k: ((MARGIN if e == "v" and len(nodes[k]["ns"]) > 1 else 0) - rank[k], k))
-        k, soon = None, []
+        k = None
+        soon = [(j, ready[j]) for j in row if ready[j] > t]
+        for e2 in "vapg" if e != "x" else "":
+            for j in pool[e2] if e2 != e else ():
+                end = max(free[e2], due[e2][j], t) + nodes[j]["ns"][e2]
+                soon += [(i, max(ready[i], end + lat + CROSS)) for i, lat in after[j] if left[i] == 1 and e in nodes[i]["ns"] and end < t + AHEAD]
         for j in row:
-            if ready[j] > t:
-                soon.append(j)
-            elif e == "x" or all(t + nodes[j]["ns"][e] <= ready[i] + WAIT or rank[i] - rank[j] < SLACK * (ready[i] - t + nodes[i]["ns"][e]) for i in soon):
+            if ready[j] <= t and (e == "x" or all(t + nodes[j]["ns"][e] <= w + WAIT or rank[i] - rank[j] < SLACK * (w - t + nodes[i]["ns"][e]) for i, w in soon)):
                 k = j
                 break
         if k is None:
-            free[e] = min(t + 50.0, min(ready[i] for i in soon))
+            free[e] = t + 50.0
             continue
         at[k] = (e, t, t + nodes[k]["ns"][e] + (urge if nodes[k]["out"][0:1] and nodes[k]["out"][0][0:4] == "lnd1" else 0.0))
         if e != "x":
@@ -137,25 +146,124 @@ def place(nodes, rank, before, after, urge=0.0):
     return at
 
 
+def polish(nodes, pre, post, at):
+    n, seed = len(nodes), [SEED]
+
+    def draw():
+        seed[0] = (seed[0] * 1103515245 + 12345) % 2147483648
+        return (seed[0] + 0.5) / 2147483648
+
+    kin, ends = {}, {nd["ends"]: k for k, nd in enumerate(nodes) if "ends" in nd}
+    for k, nd in enumerate(nodes):
+        kin.setdefault(nd["twin"][1] if nd["twin"] else -1 - k, []).append(k)
+    alike = [kin[nd["twin"][1] if nd["twin"] else -1 - k] for k, nd in enumerate(nodes)]
+    key, on = [at[k][1] for k in range(n)], [at[k][0] for k in range(n)]
+    length = (key[kin[0][2]] - key[kin[0][0]]) / 2
+    for row in kin.values():
+        for i, k in enumerate(row):
+            key[k], on[k] = at[row[len(row) // 2]][1] + (i - len(row) // 2) * length, at[row[len(row) // 2]][0]
+
+    def move(k, d, undo, most):
+        todo = [(k, d)]
+        while todo and len(undo) <= most:
+            a, d = todo.pop()
+            for i in alike[a]:
+                undo.append((i, key[i]))
+                key[i] += d
+            for i in alike[a]:
+                todo += [(j, key[i] - key[j] + math.copysign(0.01, d)) for j, lat in (post if d > 0 else pre)[i] if (key[i] - key[j]) * d >= 0]
+        return not todo
+
+    for k in range(n):
+        late = max([key[j] - key[k] for j, lat in pre[k]] + [-1.0])
+        if late >= 0:
+            move(k, late + 0.01, [], n * n)
+
+    def times(first, end, why, goal):
+        order = sorted(range(n), key=lambda k: key[k])
+        last, span, who = {}, 0.0, 0
+        for k in order:
+            if goal is not None and key[k] > key[goal]:
+                return end[goal], end, why, goal
+            e = on[k]
+            if key[k] >= first:
+                t, w = 0.0, None
+                for j, lat in pre[k]:
+                    x = end[j] + lat + (CROSS if lat == LAT and on[j] != e else 0.0)
+                    if x > t:
+                        t, w = x, (j, False)
+                j = last.get(e)
+                if j is not None and end[j] >= t and e != "x":
+                    t, w = end[j], (j, True)
+                end[k], why[k] = t + nodes[k]["ns"][e], w
+                if end[k] + nodes[k]["lat"] > span:
+                    span, who = end[k] + nodes[k]["lat"], k
+            last[e] = k
+        return span, end, why, who
+
+    for start, goal, moves in MOVES:
+        start, goal = ends.get(start), ends.get(goal)
+        now = times(-1e30, [0.0] * n, [None] * n, goal)
+        best = (now[0], list(key), list(on))
+        for turn in range(moves):
+            span, end, why, k = now
+            links = []
+            while why[k] and (start is None or key[k] > key[start]):
+                if why[k][1]:
+                    links.append((why[k][0], k))
+                k = why[k][0]
+            u, v = links[int(draw() * len(links))]
+            z, undo, both = draw(), [], [k for k in (u, v) if len(nodes[k]["ns"]) > 1]
+            turned = both[int(draw() * len(both))] if both and z < 0.15 else None
+            if turned is not None:
+                was = on[turned]
+                for i in alike[turned]:
+                    undo.append((i, key[i]))
+                    on[i] = "v" if was == "a" else "a"
+                ok = True
+            elif z < 0.55:
+                ok = move(v, key[u] - key[v] - 0.01 + STEP[int(draw() * len(STEP))] * math.log(draw()), undo, 60)
+            else:
+                ok = move(u, key[v] - key[u] + 0.01 - STEP[int(draw() * len(STEP))] * math.log(draw()), undo, 60)
+            new = times(min(min(x, key[i]) for i, x in undo), list(end), list(why), goal) if ok else None
+            if ok and new[0] - span <= -math.log(draw()) * (HEAT * (1 - turn / moves) + 2):
+                now = new
+                if new[0] < best[0]:
+                    best = (new[0], list(key), list(on))
+            else:
+                for i, x in reversed(undo):
+                    key[i] = x
+                    if turned is not None:
+                        on[i] = was
+        key[:], on[:] = best[1], best[2]
+    return best
+
+
+PLACED = {}
+
+
 def arrange(nodes):
     n = len(nodes)
-    pre, post = [[] for nd in nodes], [[] for nd in nodes]
+    if n not in PLACED:
+        pre, post = [[] for nd in nodes], [[] for nd in nodes]
+        for k, nd in enumerate(nodes):
+            for j in sorted(nd["pre"]):
+                lat = 0.0 if nd["tok"] is False or list(nd["ns"]) == list(nodes[j]["ns"]) == ["p"] else nodes[j]["lat"]
+                pre[k].append((j, lat))
+                post[j].append((k, lat))
+        rank, best = [-nd["key"] for nd in nodes], None
+        for turn in range(TURNS):
+            at = place(nodes, rank, pre, post)
+            span = max(at[k][2] + nodes[k]["lat"] for k in range(n))
+            if best is None or span < best[0]:
+                best = (span, at)
+            back = place(nodes, [at[k][2] for k in range(n)], post, pre)
+            rank = [back[k][2] for k in range(n)]
+        PLACED[n] = polish(nodes, pre, post, best[1])
+    span, key, on = PLACED[n]
     for k, nd in enumerate(nodes):
-        for j in sorted(nd["pre"] | nd["soft"]):
-            lat = 0.0 if j in nd["soft"] or nd["tok"] is False or list(nd["ns"]) == list(nodes[j]["ns"]) == ["p"] else nodes[j]["lat"]
-            pre[k].append((j, lat))
-            post[j].append((k, lat))
-    rank, best = [float(-k) for k in range(n)], None
-    for turn in range(TURNS):
-        at = place(nodes, rank, pre, post)
-        span = max(at[k][2] + nodes[k]["lat"] for k in range(n))
-        if best is None or span < best[0]:
-            best = (span, at)
-        back = place(nodes, [at[k][2] for k in range(n)], post, pre, URGE)
-        rank = [back[k][2] for k in range(n)]
-    for k in range(n):
-        nodes[k]["e"], nodes[k]["at"] = best[1][k][0:2]
-    return sorted(range(n), key=lambda k: (nodes[k]["at"], k))
+        nd["e"] = on[k]
+    return sorted(range(n), key=lambda k: key[k])
 
 
 def rank_program(g, core, T, topo):
@@ -171,7 +279,7 @@ def rank_program(g, core, T, topo):
                 sent = 0
                 for j, (which, m) in enumerate(MSG):
                     g.wait_ge(T.sem["hs%d" % j], hs[k][1])
-                    sent += forward(g, T, topo, core, r, blocks, "hb", blocks[0], which, m)
+                    sent += forward(g, T, topo, core, r, blocks, "hb", 0, which, m)
                 g.wait_ge(T.sem.loc, sent)
         return
     arrive = 0
@@ -180,6 +288,7 @@ def rank_program(g, core, T, topo):
             sh = shares(topo.engines(src, T.cores[(r + blocks[0] + 1) % n]), len(blocks))
             arrive += sum(s for b, (_, s) in zip(blocks, sh) if (r + b + 1) % n == rank)
 
+    lay = plan[rank][1][0][1] + plan[rank][1][1][1] + plan[rank][0]
     Q = {"v": g.vector, "a": g.scalar, "p": g.tensor, "g": g, "s": g.sync}
     cnt = {"v": 0, "a": 0, "p": 0, "g": 0, "loc": 0, "out": 0}
     nodes, wr, rd = [], {}, {}
@@ -196,12 +305,19 @@ def rank_program(g, core, T, topo):
             if x in wr:
                 pre.add(wr[x])
             pre.update(rd.get(x, []))
-        nodes.append({"ns": ns, "fn": fn, "pre": pre, "lat": lat, "tok": tok, "out": writes, "soft": set()})
+        nodes.append({"ns": ns, "fn": fn, "pre": pre, "lat": lat, "tok": tok, "out": writes, "soft": set(), "key": k})
         for x in reads:
             rd.setdefault(x, []).append(k)
         for x in writes:
             wr[x] = k
             rd[x] = []
+
+    soft, marks = [], {}
+
+    def behind(mark, fn, *args):
+        first = len(nodes)
+        fn(*args)
+        soft.append((first, len(nodes), mark))
 
     vec, act, pe = g.vector, g.scalar, g.tensor
     either = [""]
@@ -222,13 +338,14 @@ def rank_program(g, core, T, topo):
             op({"v": ns}, lambda e: vec.tensor_scalar(out, a, s1, s2, o1, o2), reads, writes)
 
     def cp(out, a, reads, writes, ns=cyc(0), on="v"):
-        op({e: ns for e in (either[0] or on)}, lambda e: vec.tensor_copy(out, a) if e == "v" else act.activation(out, a, AF.Identity), reads, writes)
+        op({e: ns for e in (on if on == "v" else either[0] or on)}, lambda e: vec.tensor_copy(out, a) if e == "v" else act.activation(out, a, AF.Identity), reads, writes)
 
     def ms(out, c, writes, ns=cyc(0)):
         op({"v": ns}, lambda e: vec.memset(out, c), [], writes)
 
-    def ac(out, a, reads, writes, func=AF.Identity, bias=0.0, scale=1.0, ns=cyc(0)):
-        op({e: ns for e in (either[0] or "a")},
+    def ac(out, a, reads, writes, func=AF.Identity, bias=0.0, scale=1.0, ns=cyc(0), on="a", narrow=False):
+        narrow = narrow or writes[0][0:2] in ("aF", "aS", "SG", "ZA", "ZO", "ZE", "BQ", "ZJ", "ZX", "Wb", "tm", "ZP", "ZQ")
+        op({e: ns / 2 if narrow and e == "v" else ns for e in (either[0] or on)},
            lambda e: act.activation(out, a, func, bias=bias, scale=scale) if e == "a" else vec.tensor_scalar(out, a, scale, bias, A.mult, A.add), reads, writes)
 
     def fills(on, parts, reads, writes):
@@ -245,14 +362,17 @@ def rank_program(g, core, T, topo):
             return last
         op({"p": cols * wide * PCYC + PFIX * (calls or len(parts))}, fn, reads, ["P%d" % bank])
 
-    def iota(out, pat, base, cm, writes, exact=False, c=64):
-        if exact:
-            op({"g": 130 + 2 * c * CYC}, lambda e: g.iota(out, pat, base, cm), [], writes)
-        else:
-            op({"g": 130 + 2 * c * CYC}, lambda e: g.iota(out, pat, base, cm, allow_small_or_imprecise_dtypes=True), [], writes)
+    def scan(out, first, bank, o, w, reads, writes):
+        op({"v": cyc(w)}, lambda e: vec.tensor_tensor_scan(out, T.ONE[:, 0:w], P[bank][:, o:o + w], first, A.mult, A.add), reads + ["ONE", "P%d" % bank], writes)
 
-    def sel(out, a, cmp, fill, base, cm, reads, writes):
-        op({"g": 170 + 256 * CYC}, lambda e: g.affine_select(out, a, [[1, 128]], cmp, fill, base, cm), reads, writes)
+    def iota(out, pat, base, cm, writes, exact=False, c=64, reads=()):
+        if exact:
+            op({"g": 130 + 2 * c * CYC}, lambda e: g.iota(out, pat, base, cm), list(reads), writes)
+        else:
+            op({"g": 130 + 2 * c * CYC}, lambda e: g.iota(out, pat, base, cm, allow_small_or_imprecise_dtypes=True), list(reads), writes)
+
+    def sel(out, a, cmp, fill, base, cm, reads, writes, step=1):
+        op({"g": 170 + 256 * CYC}, lambda e: g.affine_select(out, a, [[step, 128]], cmp, fill, base, cm), reads, writes)
 
     def load(e, k, out, src, name, turn=1):
         def fn(_):
@@ -273,20 +393,23 @@ def rank_program(g, core, T, topo):
             for (h, blocks), (mask, s) in zip(plan[rank][1], hs):
                 rid, pid = topo.addr(h, core)
                 tr.append(RemoteDMATransfer(dst_ids=[DstId(rid=rid, pnc=pid)], dma_engine_mask=mask, remote_sem=T.sem["hs%d" % MSG.index((which, m))],
-                                            src=piece(T, "snd", which, m, blocks[0], 3), dst=piece(T, "hb", which, m, 0, 3)))
+                                            src=piece(T, "snd", which, m, lay.index(blocks[0]), len(blocks)), dst=piece(T, "hb", which, m, 0, len(blocks))))
                 cnt["loc"] += s
             g.remote_dma_fused(tr, local_sem=T.sem.loc)
-            cnt["loc"] += forward(g, T, topo, core, rank, plan[rank][0], "snd", 0, which, m)
-        op({"g": 1000.0}, fn, reads, ["sent"], 1.0, None)
-        op({"x": HOP * (FIRST if m == 0 else 1) - 1000.0 + (WIDE if which > 1 and m < RO else 0.0)}, None, ["sent"], [lands], 1.0, ("ar%d" % MSG.index((which, m)), arrive))
+            cnt["loc"] += forward(g, T, topo, core, rank, plan[rank][0], "snd", lay.index(plan[rank][0][0]), which, m)
+        op({"g": ONCE if (which, m) == (1, 0) else 1000.0}, fn, reads, ["sent"], 1.0, None)
+        op({"x": HOP * (FIRST if m == 0 else 1) - 1000.0 + (WIDE if which == 2 else 0.0)}, None, ["sent"], [lands], 1.0, ("ar%d" % MSG.index((which, m)), arrive))
         rd["sent"] = []
 
     P = [T["P%d" % k] for k in range(8)]
-    ST, QA, QB, LG, WS, CF = T.ST, T.QA, T.QB, T.LG, T.WS, T.CF
-    STw = ["STl", "STh"]
+    ST, LG, WS, WB, CF = T.ST, T.LG, T.WS, T.WB, T.CF
 
-    def qw(x, r):
-        return [x + "0", x + "z"] + ["%s%d_%d" % (x, k, j) for k in range(1, r + 1) for j in range(2)] + ["%sh%d" % (x, k) for k in range(r + 1)]
+    def log(r, landed):
+        return (["T0a", "T0b", "TZ"] + ["TZ%d" % k for k in range(r)] + ["%s%d_%d" % (x, k, j) for k in range(1, r + 1) for x, c_ in (("QA", 2), ("QB", 2), ("LG", 8)) for j in range(c_)]
+                + ["lnd2_%d" % k for k in range(r + landed)])
+
+    def upto(r, landed, first=0):
+        return LG[:, first:BL * r + (ZC if landed else LND)]
 
     def wcol(k):
         return WS[:, k:k + 1]
@@ -294,530 +417,624 @@ def rank_program(g, core, T, topo):
     def W1(f):
         return T.E1[0:1, 15 - f:143 - f]
 
-    cI, cG, cQ, cK, cP, cM, cE, nE, cO, n16, cF1, cF2, c12, c4, c2, cA, nK = [CF[:, k:k + 1] for k in range(17)]
+    cI, cG, cQ, cK, cP, cM, cE, nE, cO, n16, cF1, cF2, c12, c8, c2, cA, nS, c16, cF3, cF4, cF5 = [CF[:, k:k + 1] for k in range(21)]
     s0, s1, s2, s3, s4, s5 = [T.s0[:, FP * k:FP * k + FP] for k in range(6)]
-    TRs, TRi, TRa, TRb, TRc, NBK, BK8 = [T.TR[:, 128 * k:128 * k + 128] for k in range(7)]
-    ZF = T.ZF[:, 0:128]
+    TRs, TRg, Na, nNa, Pa, nPa, Ka, Kb, NBK, NBI, BQ, tmp, Z128 = [T.TR[:, 128 * k:128 * k + 128] for k in range(13)]
+    ZF, ZI = T.ZF[:, 0:128], T.ZI[:, 0:128]
+    EA, EB = T.E1[0:1, 144:272], T.E1[0:1, 272:400]
+    halves, wide = ((0, V // 2), (V // 2, V)), ((0, 512), (512, V))
 
-    load("s", 0, T.TD[0:8, :], T.t0[:], "TD0")
-    load("a", 1, T.TD[8:16, :], T.d0[:], "TD1")
-    load("s", 2, T.TD[16:24, :], T.d0[:], "TD2")
-    load("a", 3, T.RI[:, 0:14], T.rim[:], "RI")
     load("s", 6, T.PI[:], T.port[:], "PI", T2)
+    load("a", 1, T.TD[8:16, :], T.d0[:], "TD1")
+    load("s", 0, T.TD[0:8, :], T.t0[:], "TD0")
+    load("a", 3, T.RI[:, 0:14], T.rim[:], "RI")
+    load("s", 2, T.TD[16:24, :], T.d0[:], "TD2")
     load("s", 4, T.qa[:], T.q0[:], "qa", T3)
     load("s", 5, T.qb[:], T.q1[:], "qb", T3)
     load("s", 7, T.TH[:, 0:1], T.th[:], "TH", T3)
 
     ms(T.Wt[0:24, :], 0.0, ["Wt"])
     ms(T.RW[0:1, :], 0.0, ["RW0"], cyc(8 * NW))
-    ms(T.E1[0:1, :], 0.0, ["E1"])
+    ms(T.E1[0:1, :], 0.0, ["E1"], cyc(200))
     iota(cP, [[0, 1]], 0, 1, ["cP"], c=1)
-    iota(T.XB[0:1, :], [[1, 256]], 0, 0, ["XB"], c=256)
     for base, fill in ((-fT, 1.0), (128 - fD, -1.0), (256 - fD, 1.0), (256 - fM, 1.0)):
         sel(T.Wt[0:24, :], T.Wt[0:24, :], A.not_equal, fill, base, -16, ["Wt"], ["Wt"])
-    iota(T.X[:], [[1, 240]], 0, 0, ["X"], c=240)
+    iota(T.X[:], [[1, 256]], 0, 0, ["X"], c=256)
+    iota(T.PT[0:1, 0:128], [[-96, 4], [3, 32]], 64, 0, ["PT0"], c=128)
     iota(T.Pi[:, 0:1], [[0, 1]], 0, 1, ["Pi"], True, 1)
     iota(T.XQ[:], [[1, 36], [0, 4]], 0, 0, ["XQ"], c=144)
     iota(T.X16[:], [[1, 8], [0, 16]], 0, 0, ["X16"], c=128)
     iota(T.SI[:], [[16, FP]], 15, 1, ["SI"], c=FP)
-    iota(T.TRE[:], [[16, 56]], 2560, 1, ["TRE"])
-    ms(T.CR[0:1, :], float(7 * rank), ["CR"], cyc(256))
-    ms(T.E1[0:1, 15:144:16], 1.0, ["E1"])
+    iota(T.TRE[:], [[16, 56]], 0, 1, ["TRE"])
+    iota(T.PT[0:1, 128:256], [[0, 8], [1, 16]], 0, 0, ["PT1"], c=128)
+    fills("v", [(T.E1[0:1, 15:144:16], None, 1), (EA[:, fEL:128:16], None, 1), (EA[:, fJL:128:16], None, 2),
+                (EB[:, fEH:128:16], None, 1), (EB[:, fJH:128:16], None, 2)], [], ["E1"])
     ts(cM, cP, 16.0, A.is_ge, ["cP"], ["cM"], 2.0, A.mult)
-    fills("v", [(T.HI[0:1, 128 * k:128 * k + 128], None, k) for k in range(7)], [], ["HI"])
-    terms = [(fA, 0, 0.25, 4, NW + 1), (fB, 0, 32, 4, NW + 1), (fA, 4, 1, 4, NW + 1), (fA, 26, 320, 4, NW + 1), (fB, 26, 40960, 4, NW + 1), (0, 30, 1, 14, NW),
-             (fA, 8, 1, 4, NW), (fNLO, 8, 1, 1, 1), (fB, 32, 35, 4, NW), (fB, 33, 35, 4, NW), (fNHI, 32, 7 * rank + 9, 1, 1), (fNHI, 33, 7 * rank + 10, 1, 1),
-             (fR, 31, QS, 1, 1), (fJLO, 31, 1, 1, 1), (fJHI, 31, 128, 1, 1),
-             (fNLO, 9, 1, 2, 9), (fNHI, 9, 128, 2, 9), (fT, 10, -1, 4, 1), (fM, 10, -32, 4, 1), (fD, 10, 64, 4, 1),
-             (fR, 14, BLKW, 4, 1), (fJLO, 14, 1, 4, 1), (fJHI, 14, 128, 4, 1), (fT, 18, 8192, 2, NW), (fD, 18, -8192, 1, 1),
-             (fT, 19, 1, 1, 1), (fM, 20, 3.5, 1, 1), (fD, 20, 8.5, 1, 1), (fM, 21, -2, 1, 1), (fD, 21, 1, 1, 1),
-             (0, 22, 1, 11, NW), (fM, 23, 1, 1, 1), (fD, 23, -1, 1, 1), (fM, 24, 4, 1, 1), (fR, 25, 1, 1, 1)]
-    places = [T.RW[0:1, NW * f + col:NW * f + col + (count - 1) * step + 1:step] for f, col, c, count, step in terms]
-    fills("a", [(x, x, t[2]) for x, t in zip(places[1::2], terms[1::2])], ["RW0"], ["RWa"])
-    fills("v", [(x, x, t[2]) for x, t in zip(places[0::2], terms[0::2])], ["RW0"], ["RWv"])
+    fills("v", [(T.HI[0:1, V:V + 32], None, 19), (T.HI[0:1, V + 32:V + 64], None, 16)], [], ["HJ"])
     ts(T.TB[0:24, :], T.TD[0:24, :], CF[0:24, 5:6], A.max, ["TD0", "TD1", "TD2", "cM"], ["TB"], ns=cyc(V))
-    ts(T.RJ[:, 0:14], T.RI[:, 0:14], 2, A.arith_shift_right, ["RI"], ["RJ0"])
+    def relay(e):
+        for j, b in enumerate(lay):
+            last = vec.tensor_copy(T.RI[:, 16 + 2 * j:18 + 2 * j], T.RI[:, 2 * b:2 * b + 2])
+        return last
+    op({"v": 7 * VMIN}, relay, ["RI"], ["RP"])
+    ts(T.RJ[:, 0:14], T.RI[:, 16:30], 2, A.arith_shift_right, ["RP"], ["RJ0"])
     ts(T.ZI[:, 0:128], T.X[:, 0:128], cP, A.is_equal, ["X", "cP"], ["ZI0"], ns=cyc(128))
-    ts(T.ZI[:, 128:240], T.X[:, 0:112], cP, A.is_equal, ["X", "cP"], ["ZI"], ns=cyc(112))
+    ts(T.ZI[:, 128:256], T.X[:, 0:128], cP, A.is_equal, ["X", "cP"], ["ZI"], ns=cyc(128))
     cp(T.rimU[:, 0:14], T.RJ[:, 0:14], ["RJ0"], ["rimU"])
-    halves = ((0, 512), (512, V))
-    for k, (a, b) in enumerate(halves):
-        mm([(P[k][:, 0:b - a], W1(fNHI), T.HI[0:1, a:b]), (P[k][:, 0:b - a], W1(fNHI), T.CR[0:1, 0:b - a])]
-           + [(P[k][:, c - a:c - a + 128], W1(fNLO), T.XB[0:1, 0:128]) for c in range(a, b, 128)], ["E1", "HI", "CR", "XB"], k, 3 * (b - a), stop=False)
-    for k, (a, b) in enumerate(halves):
-        mm([(P[k][:, 0:b - a], T.Wt[0:24, :], T.TB[0:24, a:b])], ["Wt", "TB"], k, b - a, start=False)
-    cp(ST[:, 0:512], P[0][:, 0:512], ["P0"], ["ST0"], cyc(512), "a")
-    cp(ST[:, 512:V], P[1][:, 0:V - 512], ["P1"], ["STl"], cyc(384))
-    for b in range(7):
-        j0 = (6 - b) * 32
-        mm([(P[4][:, 32 * b:32 * b + 32], W1(fJLO), T.XB[0:1, 64 + j0 % 128:96 + j0 % 128]),
-            (P[4][:, 32 * b:32 * b + 32], W1(fJHI), T.HI[0:1, 128 * (2 + j0 // 128):128 * (2 + j0 // 128) + 32])], ["E1", "XB", "HI"], 4, 128)
+    for k, (a, b) in enumerate(wide):
+        mm([(P[k][:, 0:b - a], T.Wt[0:24, :], T.TB[0:24, a:b])], ["Wt", "TB"], k, b - a)
+        cp(ST[:, a:b], P[k][:, 0:b - a], ["P%d" % k], ["ST%d" % k], cyc(b - a), "av"[k])
+    for j, b in enumerate(lay):
+        mm([(P[4][:, 32 * j:32 * j + 32], W1(fJL), T.PT[0:1, 32 * (b % 4):32 * (b % 4) + 32]),
+            (P[4][:, 32 * j:32 * j + 32], W1(fJH), T.HI[0:1, V + 32 * (b // 4):V + 32 * (b // 4) + 32])], ["E1", "PT0", "HJ"], 4, 128)
     cp(T.CH[:], P[4][:, 0:FP], ["P4"], ["CH"], cyc(FP), "a")
-    mm([(P[5][:, 0:NW], W1(f), T.RW[0:1, NW * f:NW * f + NW]) for f in range(16)], ["E1", "RWa", "RWv"], 5, 1024)
-    up = 32 * (n - 1 - rank)
+    up, runs = 32 * (n - 1 - rank), []
+    for j, b in enumerate(lay):
+        o = 112 if 32 * b < up else 16
+        runs = runs[:-1] + [(runs[-1][0], 32 * j + 32, o)] if runs and runs[-1][2] == o else runs + [(32 * j, 32 * j + 32, o)]
+    STs = ["ST0", "ST1"]
 
     def shift(bank, o_, src, a, Z, reads, wide, fresh=True):
-        mm([(P[bank][:, o_ + lo:o_ + hi], Z[:, o:o + 128], src[:, a + lo:a + hi]) for lo, hi, o in ((0, up, 112), (up, FP, 16)) if hi > lo],
-           reads, bank, FP + 32, wide, "each" if fresh else False, "each" if fresh else True, 2)
+        mm([(P[bank][:, o_ + lo:o_ + hi], Z[:, o:o + 128], src[:, a + lo:a + hi]) for lo, hi, o in runs],
+           reads, bank, FP + 32, wide, "each" if fresh else False, "each" if fresh else True, 3)
 
     def message1(m):
-        cp(T.pk1[:], ST[:, 0:V].indirect(T.rimU[:, 0:14]), ["STl", "ST0", "rimU"], ["pk1"], ind(FP), PK)
+        cp(T.pk1[:], ST[:, 0:V].indirect(T.rimU[:, 0:14]), STs + ["rimU"], ["pk1"], ind(FP), "a")
         if m == 0:
             shift(7, 0, T.pk1, 0, T.ZI, ["pk1", "ZI", "ZI0"], 1)
             tt(T.snd1[:, 0:FP], P[7][:, 0:FP], T.CH[:], A.add, ["P7", "CH"], ["snd1_0"], cyc(FP))
         else:
-            mm([(P[7][:, 0:FP], T.ZI[:, 0:128], T.CH[:])], ["ZI0", "CH"], 7, FP, stop=False)
+            mm([(P[7][:, 0:FP], ZI, T.CH[:])], ["ZI0", "CH"], 7, FP, stop=False)
             shift(7, 0, T.pk1, 0, T.ZJ, ["pk1", "ZJ"], 1, False)
-            cp(T.snd1[:, m * FP:(m + 1) * FP], P[7][:, 0:FP], ["P7"], ["snd1_%d" % m], cyc(FP), SND)
-        send(1, m, ["snd1_%d" % m], "lnd1_%d" % m)
+            cp(T.snd1[:, m * FP:(m + 1) * FP], P[7][:, 0:FP], ["P7"], ["snd1_%d" % m], cyc(FP), "a")
+        send(1, m, ["snd1_%d" % m, "Pa", "TRg", "nNa"], "lnd1_%d" % m)
 
-    def pack_q(m):
-        if m > 0:
-            mm([(P[6][:, 0:14], T.ZR[:, 15 - i:143 - i], T.pk1[:, i:FP:16]) for i in range(16)], ["pk1", "ZR"], 6, 1024)
-            ts(T.ryU[:, 16:30], P[6][:, 0:14], float(LO), A.add, ["P6"], ["rqU"])
-        for k, (W, nm) in enumerate(((QA, "QA"), (QB, "QB"))):
-            if m == 0:
-                cp(T.pk2[:, k * FP:(k + 1) * FP], W[:, 0:V].indirect(T.rimU[:, 0:14]), [nm + "0", "rimU"], ["pk2_%d" % k], ind(FP), "a")
-            else:
-                cp(T.pk2[:, k * FP:(k + 1) * FP], W[:, 0:LO + QS * m + FP].indirect(T.ryU[:, 16:30]), qw(nm, m - 1) + ["%s%d_0" % (nm, m), "rqU"],
-                   ["pk2_%d" % k], ind(FP), "a")
-        for k in range(2):
-            shift(6, FP * k, T.pk2, k * FP, T.ZF, ["pk2_%d" % k, "ZF"], 4)
-        for k in range(2):
-            cp(T.snd2[:, 7 * m:7 * m + 7, 32 * k:32 * k + 32], P[6][:, FP * k:FP * k + FP], ["P6"], ["snd2_%d_%d" % (m, k)], cyc(FP), "a")
-        send(2, m, ["snd2_%d_0" % m, "snd2_%d_1" % m], "lnd2_%d" % m)
+    def listed(bank, o, Z, src, w, reads, start=True, stop=True):
+        if start:
+            mm([(P[bank][:, o:o + w], Z[:, 15 - i:143 - i], src[:, i:16 * w:16]) for i in range(16)], reads, bank, 16 * max(w, 64), stop=stop)
+        else:
+            mm([(P[bank][:, o:o + w], Z[:, 15 - i:143 - i], src[:, i:16 * w:16]) for i in range(16)], reads, bank, 16 * max(w, 64), start=False, stop=stop)
 
-    message1(0)
+    def message2(m):
+        ry = [T.ryU[:, 16 * k:16 * k + 14] for k in range(3)]
+        if m == 0:
+            for k in range(2):
+                ts(ry[k], T.RJ[:, 0:14], 2.0, A.mult, ["RJ0"], ["ry%d" % k], float(k), A.add)
+        else:
+            for k in range(2):
+                ts(ry[k], P[3][:, 0:14], float(k), A.add, ["P3"], ["ry%d" % k])
+            tt(T.ryF[:, 0:14], P[3][:, 0:14], T.rimK[:, 0:14], A.add, ["P3", "rimK"], ["ryF"])
+            cp(ry[2], T.ryF[:, 0:14], ["ryF"], ["ry2"])
+        for k in range(3):
+            j = k if m else k % 2
+            if j == k:
+                cp(T.pk2[:, k * FP:(k + 1) * FP], upto(m, 0).indirect(ry[k]), log(m, 0) + ["ry%d" % k], ["pk2_%d" % k], ind(FP), "a")
+            bank, o = (5, 5, 6)[k], (0, FP, 0)[k]
+            shift(bank, o, T.pk2, j * FP, T.ZF, ["pk2_%d" % j, "ZF"], 4)
+        for k in range(3):
+            bank, o = (5, 5, 6)[k], (0, FP, 0)[k]
+            cp(T.snd2[:, 3 * FP * m + k:3 * FP * (m + 1):3], P[bank][:, o:o + FP], ["P%d" % bank], ["snd2_%d_%d" % (m, k)], cyc(FP), SNQ)
+        send(2, m, ["snd2_%d_%d" % (m, k) for k in range(3)], "lnd2_%d" % m)
+
     ts(T.CI[:, 0:1], T.Pi[:, 0:1], 15, A.bitwise_and, ["Pi"], ["CI0"])
     ts(T.CI[:, 1:2], T.Pi[:, 0:1], 4, A.arith_shift_right, ["Pi"], ["CI1"])
     ts(T.CI[:, 2:3], T.Pi[:, 0:1], 2, A.arith_shift_right, ["Pi"], ["CI2"], 3, A.bitwise_and)
     ts(T.CI[:, 3:4], T.Pi[:, 0:1], 3, A.bitwise_and, ["Pi"], ["CI3"])
     cp(CF[:, 0:4], T.CI[:, 0:4], ["CI0", "CI1", "CI2", "CI3"], ["CF"])
+    ts(T.BK[:], T.X16[:], cG, A.is_equal, ["X16", "CF"], ["BK"], ns=cyc(128))
+    sel(TRs, T.BK[:], A.is_gt, 0.0, 0, -1, ["BK"], ["TRs"])
+    sel(Pa, TRs, A.not_equal, BIG, 0, -1, ["TRs"], ["Pa"])
+    sel(TRg, T.BK[:], A.is_ge, 0.0, 0, 1, ["BK"], ["TRg"], -1)
+    sel(nNa, TRs, A.not_equal, -BIG, 0, -1, ["TRs"], ["nNa"])
+    message1(0)
+    iota(T.C[:, CF0:3456], [[0, 2560]], 0, 0, ["C", "late"], c=2560, reads=["sent"])
+
+    d3 = 3 * NW + 1
+    terms = [(12, 0, 1, 2, 2 * NW + 9), (13, 0, 128, 2, 2 * NW + 9), (0, 1, 1, 4, d3), (1, 1, 128, 4, d3), (2, 5, 1, 4, d3),
+             (0, 10, 256, 4, d3), (1, 10, 32768, 4, d3), (12, 10, -256, 4, 1), (13, 10, -32768, 4, 1), (12, 18, 1, 4, 1), (13, 18, 128, 4, 1),
+             (fJL, cWO + 12, 1, 2, NW + 1), (fR, cWO + 13, 21, 2, 4), (fEL, cWO + 14, 1, 2, NW + 1), (fS, cWO + 2, 1, 4, NW + 3),
+             (fT, cWO + 2, 1, 4, 3), (fM, cWO + 2, 9, 4, 3), (fD, cWO + 2, -9, 4, 3), (fJL, cWN, 1, 2, NW + 1), (fT, cWN + 2, -1, 1, 1),
+             (0, cWF, 1, 4, NW + 1), (4, cWF, 128, 4, NW + 1), (8, cWF + 4, 1, 4, NW + 1), (12, cWF + 4, BIG, 4, 1), (14, cWF + 8, 1, 1, 1), (15, cWF + 8, 128, 1, 1),
+             (fT, cS, 2, 2, NW), (fD, cS, -2, 1, 1), (fR, cX, BL, 1, 1), (fJL, cX, 1, 1, 1), (fJH, cX, 128, 1, 1), (fT, cZJ, 1, 4, NW),
+             (fM, cTH, 3.5, 1, 1), (fD, cTH, 8.5, 1, 1), (fM, cNN, -2, 1, 1), (fD, cNN, 1, 1, 1), (0, cKP, 1, 7, NW), (fM, cD, 1, 1, 1), (fD, cD, -1, 1, 1),
+             (fM, cB4, 4, 1, 1), (fR, cR, 1, 1, 1), (fT, cT, 1, 1, 1), (15, cEL, -BIG / 128, 1, 1),
+             (fP, cPL, 1, 2, NW + 1), (fR, cPL, BIG, 1, 1), (fT, cXR, 0.5, 1, 1), (fM, cXR, 64, 1, 1)]
+    places = [T.RW[0:1, NW * f + col:NW * f + col + (count - 1) * step + 1:step] for f, col, c, count, step in terms]
+    fills("a", [(x, x, t[2]) for x, t in zip(places[1::2], terms[1::2])], ["RW0"], ["RWa"])
+    fills("v", [(x, x, t[2]) for x, t in zip(places[0::2], terms[0::2])], ["RW0"], ["RWv"])
+    mm([(P[5][:, 0:NW], W1(f), T.RW[0:1, NW * f:NW * f + NW]) for f in range(16)], ["E1", "RWa", "RWv"], 5, 16 * NW)
     either[0] = "av"
-    cp(WS[:, 0:NW], P[5][:, 0:NW], ["P5"], ["WS"], on="a")
-    cp(QA[:, 0:V], T.qa[:], ["qa"], ["QA0"], cyc(V), "a")
-    for x, sc, bi, nm in ((cE, 16, 15, "cE"), (nE, -16, -15, "nE"), (cO, 4, 3, "cO"), (c12, 16, 12, "c12"), (c4, 16, 4, "c4"), (n16, -16, 0, "n16"),
-                          (cF1, FP, FP, "cF1"), (cF2, NR - FP, 7 * FP, "cF2")):
+    cp(WS[:, 0:NW], P[5][:, 0:NW], ["P5"], ["WS"], cyc(NW), "a")
+    cp(WB[:, 0:NW], WS[:, 0:NW], ["WS"], ["WB0"], cyc(NW), "a")
+    ac(WB[:, 14:18], WS[:, 10:14], ["WS", "WB0"], ["WB"], scale=-1.0)
+    for x, sc, bi, nm in ((cE, 16, 15, "cE"), (nE, -16, -15, "nE"), (cO, 4, 3, "cO"), (c12, 16, 12, "c12"), (c8, 16, 8, "c8"), (n16, -16, 0, "n16"),
+                          (cF1, FP, CF0 + CAP - NR - 0.5, "cF1"), (cF2, NR - FP, 7 * FP, "cF2"), (c16, 16, CF0, "c16"),
+                          (cF3, FP, CF0 + CAP - 210.5, "cF3"), (cF4, FP, CF0 + CAP - 1 - BIG, "cF4"), (cF5, FP, CF0 - BIG, "cF5")):
         ac(x, cG, ["CF"], [nm], bias=float(bi), scale=float(sc))
     ac(T.SI[:], T.SI[:], ["SI", "nE"], ["SI"], bias=nE, ns=cyc(FP))
     ac(c2, cQ, ["CF", "c12"], ["c2"], bias=c12)
-    ac(cA, cK, ["CF", "c4"], ["cA"], bias=c4)
-    ac(nK, wcol(18), ["WS"], ["nK"], scale=-1.0)
-    cp(QB[:, 0:V], T.qb[:], ["qb"], ["QB0"], cyc(V), "a")
-    cp(T.ZF[:], T.ZI[:], ["ZI", "ZI0"], ["ZF"], cyc(240), "a")
-    pack_q(0)
+    ac(cA, cK, ["CF", "c8"], ["cA"], bias=c8)
+    ac(nS, wcol(cS), ["WS"], ["nS"], scale=-1.0)
+    cp(T.XB[0:1, :], T.X[0:1, :], ["X"], ["XB"], cyc(256), "a")
+    cp(LG[:, 0:2 * V:2], T.qa[:], ["qa"], ["T0a"], cyc(V), "a")
+    cp(LG[:, 1:2 * V:2], T.qb[:], ["qb"], ["T0b"], cyc(V), "a")
+    iota(LG[:, 2 * V:LND], [[0, LND - 2 * V]], 0, 0, ["TZ"], c=LND - 2 * V)
+    for k in range(RO):
+        iota(LG[:, BL * k + ZC:BL * (k + 1)], [[0, BL - ZC]], 0, 0, ["TZ%d" % k], c=BL - ZC, reads=["late"])
+    cp(T.ZF[:], T.ZI[:, 0:240], ["ZI", "ZI0"], ["ZF"], cyc(240), "a")
 
     c = T.PI[:]
+    aL, aH, aF, aS, aK, aS2, aF2 = [T.AB[:, FP * k:FP * k + FP] for k in range(7)]
+    SG = T.AB[:, 7 * FP + 14:8 * FP + 14]
+    ms(T.AB[:, 7 * FP:7 * FP + 14], 0.0, ["SGz"])
     ts(s1, c, 4.0, A.mult, ["PI"], ["s1"], -10749.0, A.add, cyc(FP))
-    ts(s3, c, float(3584 + up), A.is_ge, ["PI"], ["s3"], ns=cyc(FP))
+    ts(s3, c, float(4 * V + up), A.is_ge, ["PI"], ["s3"], ns=cyc(FP))
+    ts(T.bit[:], c, float(4 * V), A.is_ge, ["PI"], ["bit"], ns=cyc(FP))
     tt(s0, s1, c, A.max, ["s1", "PI"], ["s0"], cyc(2 * FP))
     tt(s2, T.SI[:], c, A.is_lt, ["SI", "PI"], ["s2"], cyc(2 * FP))
-    ts(T.colU[:], s0, 0.25, A.mult, ["s0"], ["colU"], -0.375, A.add, cyc(FP))
-    tt(s2, s2, s3, A.subtract, ["s2", "s3"], ["s2"], cyc(2 * FP))
-    ts(s4, s0, 127, A.bitwise_and, ["s0"], ["s4"], ns=cyc(FP))
-    ts(s5, s0, 7, A.arith_shift_right, ["s0"], ["s5"], ns=cyc(FP))
-    ts(s3, s2, 128.0, A.mult, ["s2"], ["s3"], ns=cyc(FP))
+    ts(T.colU[:, 0:FP], s0, 0.25, A.mult, ["s0"], ["colU"], -0.375, A.add, cyc(FP))
+    tt(aS, s2, s3, A.subtract, ["s2", "s3"], ["aS"], cyc(2 * FP))
+    ts(s1, s0, 3, A.bitwise_and, ["s0"], ["s1"], ns=cyc(FP))
+    ts(s4, s0, 2, A.arith_shift_right, ["s0"], ["s4"], 127, A.bitwise_and, cyc(FP))
+    ts(s5, s0, 9, A.arith_shift_right, ["s0"], ["s5"], ns=cyc(FP))
+    ts(aK, s1, 64.0, A.mult, ["s1"], ["aK"], -6.0, A.add, cyc(FP))
+    cp(aL, s4, ["s4"], ["aL"], cyc(FP))
+    cp(aH, s5, ["s5"], ["aH"], cyc(FP))
+    ac(aF, T.bit[:], ["bit"], ["aF"], scale=2.5, ns=cyc(FP))
+    ac(aF2, T.bit[:], ["bit"], ["aF2"], scale=-192.0, ns=cyc(FP))
+    ac(aS2, aS, ["aS"], ["aS2"], scale=32.0, ns=cyc(FP))
+    ac(SG, aS, ["aS"], ["SG"], bias=-0.5, ns=cyc(FP))
     ts(T.MK[:, 0:4], T.X[:, 0:4], cQ, A.is_equal, ["X", "CF"], ["MK"])
     ts(T.ZA0[:], T.X[:, 0:144], cA, A.is_equal, ["X", "cA"], ["ZA0"], ns=cyc(144))
     ts(T.ZO0[:], T.XQ[:], cO, A.is_equal, ["XQ", "cO"], ["ZO0"], ns=cyc(144))
     ts(T.ZE0[:], T.X[:, 0:144], cE, A.is_equal, ["X", "cE"], ["ZE0"], ns=cyc(144))
-    tt(T.AB[:, FP:2 * FP], s5, s2, A.subtract, ["s5", "s2"], ["ABb"], cyc(2 * FP))
-    tt(T.AB[:, 0:FP], s4, s3, A.add, ["s4", "s3"], ["ABa"], cyc(2 * FP))
     for m in range(4):
         ac(T.ZA[:, 144 * m:144 * m + 144], T.ZA0[:], ["ZA0", "MK"], ["ZA%d" % m], scale=T.MK[:, m:m + 1], ns=cyc(144))
-    ac(T.ZO[:], T.ZO0[:], ["ZO0", "nK"], ["ZO"], scale=nK, ns=cyc(144))
-    ac(T.ZE[:], T.ZE0[:], ["ZE0", "WS"], ["ZE"], scale=wcol(18), ns=cyc(144))
+    ZAs = ["ZA%d" % m for m in range(4)]
+    ac(T.ZO[:], T.ZO0[:], ["ZO0", "nS"], ["ZO"], scale=nS, ns=cyc(144))
+    ac(T.ZE[:], T.ZE0[:], ["ZE0", "WS"], ["ZE"], scale=wcol(cS), ns=cyc(144))
     ac(T.TRE[:], T.TRE[:], ["TRE", "n16"], ["TRE"], bias=n16)
-    ts(T.BK[:], T.X16[:], cG, A.is_equal, ["X16", "CF"], ["BK"], ns=cyc(128))
     ts(T.Z2[:], T.X[:, 0:144], c2, A.is_equal, ["X", "c2"], ["Z2"], ns=cyc(144))
-    sel(TRs, T.BK[:], A.is_gt, 0.0, 0, -1, ["BK"], ["TRs"])
-    sel(TRi, T.BK[:], A.is_ge, 0.0, 0, -1, ["BK"], ["TRi"])
-    sel(TRa, TRs, A.not_equal, -4096.0, 0, -1, ["TRs"], ["TRa"])
-    ac(TRb, TRs, ["TRs"], ["TRb"], scale=-1.0, ns=cyc(128))
-    sel(TRb, TRb, A.not_equal, -4096.0, 0, -1, ["TRb"], ["TRb"])
-    ac(TRc, TRi, ["TRi"], ["TRc"], scale=8192.0, ns=cyc(128))
-    ac(NBK, T.BK[:], ["BK"], ["NBK"], scale=-1.0, ns=cyc(128))
-    ac(BK8, T.BK[:], ["BK"], ["BK8"], scale=8192.0, ns=cyc(128))
-    for j, (col, nm) in enumerate(((8, "MKa"), (32, "MKb"), (33, "MKc"))):
-        ac(T.MK[:, 8 + 8 * j:16 + 8 * j], T.BK[:, 0:128:16], ["BK", "WS"], [nm], scale=wcol(col))
-    ms(T.G[:, 4 * V:GW], 0.0, ["Gz"], cyc(608))
-    for j in range(8):
-        ac(T.CT[:, FP * j:FP * j + FP], T.X[:, 0:FP], ["X", "MKa", "MKb"], ["CT%d" % j], bias=T.MK[:, 16 + j:17 + j], scale=T.MK[:, 8 + j:9 + j], ns=cyc(FP))
-        ac(T.CT[:, 8 * FP + NR * j:8 * FP + NR * j + NR], T.X[:, NR:2 * NR], ["X", "MKa", "MKc"], ["CT%d" % (8 + j)],
-           bias=T.MK[:, 24 + j:25 + j], scale=T.MK[:, 8 + j:9 + j], ns=cyc(NR))
-    op({"g": 130 + 2 * (LO + BLKW) * CYC}, lambda e: g.iota(LG[:, 0:LO + BLKW], [[0, LO + BLKW]], 0, 0, allow_small_or_imprecise_dtypes=True), ["sent"], ["LG0"])
-    ms(T.CR[0:1, :], -LO / 128.0, ["CR"], cyc(256))
-    for k, (a, b) in enumerate(halves):
-        parts = [(P[k][:, 0:b - a], T.ZI[:, 0:128], ST[:, a:b]), (P[k][:, 0:b - a], W1(fJHI), T.HI[0:1, a:b]), (P[k][:, 0:b - a], W1(fJHI), T.CR[0:1, 0:b - a])]
-        parts += [(P[k][:, c_ - a:c_ - a + 128], W1(fJLO), T.XB[0:1, 0:128]) for c_ in range(a, b, 128)]
-        for m in range(4):
-            parts.append((P[k][:, m:b - a:4], T.ZA[:, 144 * m:144 * m + 128], T.AB[:, FP + a // 4:FP + b // 4]))
-            parts.append((P[k][:, m:b - a:4], T.ZA[:, 144 * m + 4:144 * m + 132], T.AB[:, a // 4:b // 4]))
-        mm(parts, ["ZI0", "STl", "ST0", "ZA0", "ZA1", "ZA2", "ZA3", "ABa", "ABb", "E1", "HI", "CR", "XB"], k, 6 * (b - a))
-    ms(T.ONE[:], 1.0, ["ONE"], cyc(176))
-    ms(T.ONE[:, 0:171:57], 0.0, ["ONE"])
-    ms(T.IN[:], 0.0, ["IN"], cyc(176))
-    ac(T.IN[:, 0:1], cG, ["CF", "IN"], ["IN0"], bias=4096.0, scale=float(FP))
-    ac(T.IN[:, 57:58], cG, ["CF", "IN"], ["IN1"], bias=4096.0 + CAP - 1, scale=float(FP))
-    ac(T.IN[:, 114:115], cG, ["CF", "IN"], ["IN2"], bias=-8192.0 * CAP, scale=0.0)
-    ms(T.ZB[:], 0.0, ["ZB"], cyc(88))
-    ms(T.KI[:], 0.0, ["KI"], cyc(252))
-    fills("v", [(T.KI[:, 0:80], None, -0.375), (T.KI[:, 168:248], None, 160), (T.KI[:, 462:482], None, -V * rank),
-                (T.KI[:, 420:434], None, LO), (T.KI[:, 482:488], None, LO)]
-          + [(T.KI[:, 252 + 14 * k:266 + 14 * k], None, LO + 320 * k) for k in range(4)]
-          + [(T.KI[:, 308 + 6 * k:314 + 6 * k], None, LO + 320 * k) for k in range(4)], [], ["KI"])
-    ac(T.ZJ[:], T.ZI[:], ["ZI", "ZI0", "WS"], ["ZJ"], scale=wcol(30), ns=cyc(240))
-    for W, nm in ((QA, "QAz"), (QB, "QBz")):
-        ms(W[:, V:LO + CAP], 0.0, [nm])
-    ac(T.ZR[:], T.ZE0[:], ["ZE0", "WS"], ["ZR"], scale=wcol(31), ns=cyc(144))
+    iota(T.HI[0:1, 0:V], [[1, 7], [0, 128]], 0, 0, ["HI"], c=V)
+    ms(T.CR[0:1, :], 1.0, ["CR"], cyc(256))
+
+    def by_port(k, a, b, lists):
+        return [(P[k][:, m:b - a:4], T.ZA[:, 144 * m + 8 - f:144 * m + 136 - f], x[:, a // 4:b // 4]) for f, x in lists for m in range(4)]
+
+    for k, (a, b) in enumerate(wide):
+        parts = [(P[k][:, 0:b - a], ZI, ST[:, a:b]), (P[k][:, 0:b - a], EB, T.HI[0:1, a:b])]
+        parts += [(P[k][:, c_ - a:c_ - a + 128], l_, r_) for c_ in range(a, b, 128) for l_, r_ in ((EA, T.XB[0:1, 0:128]), (W1(fQ), T.PT[0:1, 128:256]))]
+        mm(parts, ["ZI0", "E1", "HI", "XB", "PT1", STs[k]], k, 4 * (b - a), stop=False)
+        mm(by_port(k, a, b, ((0, aK), (0, aS2), (0, aF2))), ["aK", "aS2", "aF2"] + ZAs, k, 3 * (b - a), start=False)
+        cp(ST[:, a:b], P[k][:, 0:b - a], ["P%d" % k], [STs[k]], cyc(b - a), "a")
+    iota(ST[:, V:SL], [[0, CAP]], 0, 0, ["STz"], c=CAP)
+    STw = STs + ["STz"]
+    for k, (a, b) in enumerate(wide):
+        parts = [(P[2 + k][:, 0:b - a], W1(15), T.HI[0:1, a:b]), (P[2 + k][:, 0:b - a], W1(12), T.CR[0:1, 0:b - a])]
+        parts += [(P[2 + k][:, c_ - a:c_ - a + 128], W1(14), T.XB[0:1, 0:128]) for c_ in range(a, b, 128)]
+        mm(parts, ["E1", "HI", "XB", "CR"], 2 + k, 3 * (b - a), stop=False)
+        mm(by_port(2 + k, a, b, ((0, aL), (4, aH), (4, aF), (8, aS))), ["aL", "aH", "aF", "aS"] + ZAs, 2 + k, 4 * (b - a), start=False)
+        cp(T.FT[:, a:b], P[2 + k][:, 0:b - a], ["P%d" % (2 + k)], ["FT%d" % k], cyc(b - a), "a")
+    for x, y, sc, nm, src in ((nPa, Pa, -1.0, "nPa", "Pa"), (Na, nNa, -1.0, "Na", "nNa"), (Ka, TRs, -B2, "Ka", "TRs"), (Kb, TRg, -B2, "Kb", "TRg"),
+                              (NBK, T.BK[:], -1.0, "NBK", "BK"), (T.NI[:], ZI, -1.0, "NI", "ZI0")):
+        ac(x, y, [src], [nm], scale=sc, ns=cyc(128), narrow=nm != "NI")
+    ms(T.ONE[:], 1.0, ["ONE"])
+    mm([(P[4][:, 0:56], T.Z2[:, 12 - 4 * h:140 - 4 * h], T.bit[:, h:FP:4]) for h in range(4)], ["Z2", "bit"], 4, 256)
+    isf = T.can[:, 56:112]
+    ts(isf, P[4][:, 0:56], 0.5, A.is_ge, ["P4"], ["isf"])
+    ac(T.THR[:], isf, ["isf"], ["THR"], bias=3.5, scale=64.0)
+    mm([(P[5][:, 0:56], Pa, isf), (P[5][:, 1:56], T.BK[:], isf[:, 0:55]), (P[5][:, 1:56], nPa, isf[:, 0:55])], ["Pa", "nPa", "BK", "isf"], 5, 3 * 64)
+    m0, m1, m2, m3 = [T.v1[:, 56 * k:56 * k + 56] for k in range(4)]
+    scan(m0, -BIG, 5, 0, 56, [], ["m0"])
+    ts(T.ki[:, 0:56], m0, 0.0625, A.mult, ["m0"], ["ki"], -0.47, A.add)
+    ts(m1, T.ki[:, 0:56], 112.0, A.mult, ["ki", "c16"], ["m1"], c16, A.add)
+    tt(m2, m0, m1, A.add, ["m0", "m1"], ["m2"], cyc(112))
+    tt(m3, m2, T.TRE[:], A.max, ["m2", "TRE"], ["m3"], cyc(112))
+    cp(T.posU[:, 0:56], m3, ["m3"], ["posU"])
+    ms(T.cb[:, CF0:CB0], 0.0, ["FZ"], cyc(4 * FP))
+    cp(T.cb[:, 0:CB0].indirect(T.posU[:, 0:56]), T.FT[:], ["posU", "FT0", "FT1"], ["FZ"], ind(V, SC))
+    mm([(P[6][:, b:126:14], T.cb[:, CF0 + 128 * b:CF0 + 128 * b + 128], WB[:, cWF:cWF + 9]) for b in range(14)], ["FZ", "WB0"], 6, 14 * 64, start="each", stop="each")
+    eF, cF = T.FN[:, 280:294], T.FN[:, 296:310]
+    cp(T.FN[:, 0:56], P[6][:, 0:56], ["P6"], ["FN0"])
+    cp(eF, P[6][:, 112:126], ["P6"], ["eF"])
+    ts(T.THF[:, 0:56], P[6][:, 56:112], -0.5 - BIG, A.add, ["P6"], ["THF"])
+    ms(T.THF[:, 56:84], 0.0, ["THz"])
+    ts(cF, P[6][:, 112:126], 0.0625, A.mult, ["P6"], ["cF"], -0.47, A.add)
+    ts(T.FW[:, 0:56], P[6][:, 0:56], SL - 0.5, A.is_ge, ["P6"], ["FW0"], float(FP), A.mult)
+    cp(T.FW[:, 56:112], P[6][:, 0:56], ["P6"], ["FW1"])
+    for r in range(1, RO):
+        tt(T.FW[:, 56:112], T.FW[:, 56:112], T.FW[:, 0:56], A.add, ["FW0", "FW1"], ["FW1"], cyc(112))
+        cp(T.FN[:, 56 * r:56 * r + 56], T.FW[:, 56:112], ["FW1"], ["FN%d" % r])
+    message2(0)
+    ac(BQ, T.BK[:], ["BK", "WS"], ["BQ"], scale=wcol(cQ4), ns=cyc(128))
+    ac(T.MK[:, 8:28], T.TRE[:, 0:20], ["TRE"], ["TRX"], bias=V - BIG)
+    mm([(P[4][:, 16 * (8 * h + j):16 * (8 * h + j) + 16], T.ZI[0:16, 128 - 16 * j:256 - 16 * j], WB[0:16, cWO + 16 * h:cWO + 16 * h + 16]) for h in range(2) for j in range(8)],
+       ["ZI", "ZI0", "WB0"], 4, 16 * 64, start="each", stop="each")
+    ms(T.WN[:, 0:16], 0.0, ["WN0"])
+    cp(T.Wo[:], P[4][:, 0:128], ["P4"], ["Wo"], cyc(128), "a")
+    cp(T.WN[:, 9:137], P[4][:, 128:256], ["P4", "WN0"], ["WN"], cyc(128), "a")
+    ac(T.ZJ[:], T.ZI[:, 0:240], ["ZI", "ZI0", "WS"], ["ZJ"], scale=wcol(cZJ), ns=cyc(240))
+    ac(T.ZX[:], T.ZE0[:], ["ZE0", "WS"], ["ZX"], scale=wcol(cX), ns=cyc(144))
     ms(T.FF[:, 0:8], 0.0, ["FF0"])
     ts(T.NT[:, 0:1], T.TH[:, 0:1], -1.0, A.mult, ["TH"], ["NTH"])
-    ms(ST[:, V:TW], 0.0, ["STh"], cyc(288))
-    ms(T.Wc[:], 0.0, ["Wc"])
-    for j, col in enumerate((0, 4, 10, 14, 26)):
-        cp(T.Wc[:, 6 * j:6 * j + 4], WS[:, col:col + 4], ["WS", "Wc"], ["WcF%d" % j], on="a")
-        cp(T.Wc[:, 40 + 14 * j:44 + 14 * j], WS[:, col:col + 4], ["WS", "Wc"], ["WcN%d" % j], on="a")
-    cp(T.Wc[:, 33:34], wcol(9), ["WS", "Wc"], ["WcF5"], on="a")
-    cp(T.Wc[:, 110:111], wcol(9), ["WS", "Wc"], ["WcN5"], on="a")
-    cp(T.Wc[:, 30:31], wcol(31), ["WS", "Wc"], ["WcF6"], on="a")
-    cp(T.Wc[:, 111:112], wcol(31), ["WS", "Wc"], ["WcN6"], on="a")
-    Wcs = ["WcF%d" % j for j in range(7)] + ["WcN%d" % j for j in range(7)]
-    ts(T.RJ[:, 16:30], T.RI[:, 0:14], 3, A.bitwise_and, ["RI"], ["RJ1"])
-    ts(s1, s0, 3, A.bitwise_and, ["s0"], ["s1"], ns=cyc(FP))
-    ts(T.rimK[:, 0:14], T.RJ[:, 16:30], 320.0, A.mult, ["RJ1"], ["rimK"], float(LO), A.add)
-    ts(T.rimK[:, 16:30], T.RJ[:, 16:30], float(FP), A.mult, ["RJ1"], ["rimL"], 8.0 - BLKW * RO, A.add)
-    ts(T.KN[:], s1, 320.0, A.mult, ["s1"], ["KN"], float(LO), A.add, cyc(FP))
-    cp(ST[:, 0:512], P[0][:, 0:512], ["P0"], ["ST0", "STl"], cyc(512), "a")
-    cp(ST[:, 512:V], P[1][:, 0:V - 512], ["P1"], ["STl"], cyc(384), "a")
-    ts(T.bit[:], c, 3584.0, A.is_ge, ["PI"], ["bit"], ns=cyc(FP))
-    mm([(P[4][:, 0:56], T.Z2[:, 12 - 4 * h:140 - 4 * h], T.bit[:, h:FP:4]) for h in range(4)], ["Z2", "bit"], 4, 256)
-    ts(T.THR[:, 0:56], P[4][:, 0:56], 0.5, A.is_lt, ["P4"], ["THa"], 64.0, A.mult)
-    ts(T.THR[:, 56:112], P[4][:, 0:56], 0.5, A.is_ge, ["P4"], ["THb"], 64.0, A.mult)
-    ts(T.THR[:], T.THR[:], 3.5, A.add, ["THa", "THb"], ["THa", "THb"], ns=cyc(112))
-    ac(T.ZT[:], T.ZE0[:], ["ZE0", "WS"], ["ZT"], scale=wcol(19), ns=cyc(144))
-    tabs = {"L1": [], "L2": [], "L3": []}
-    for di, d in enumerate((4, 2, 1)):
-        o = 64 * di + 32
-        for a in range(d):
-            lo = o - 3 if a == 0 else o + a
-            tabs["L1"].append((lo, o + a + 1, -(d - a) / 32.0))
-            tabs["L2"].append((lo, o + a + 1, -(d * d - a * a) / 64.0))
-        for a in range(d - 4, d):
-            tabs["L3"].append((o + a, o + a + 1, ((d - a) ** 2 - (max(a, 0) - a) ** 2) / 64.0))
-    for x, rows in tabs.items():
-        ac(T[x][:, 0:192], T.X[:, 0:192], ["X"], [x], scale=0.0, ns=cyc(192))
-        fills("av", [(T[x][:, a:b], T.X[:, 0:b - a], val) for a, b, val in rows], ["X"], [x])
-        ac(T[x][:, 192:384], T[x][:, 0:192], [x], [x + "n"], scale=-1.0, ns=cyc(192))
-    fills("a", [(T.LS[:, 0:192], T.X[:, 0:192], 0.5), (T.LS[:, 192:384], T.X[:, 0:192], -0.5)], ["X"], ["LS"])
-    fills("a", [(T.LI[:, 64 * j:64 * j + 64], T.X[:, 0:64], (0.25, 0.5, 1.0)[j % 3]) for j in range(6)], ["X"], ["LI"])
-    ac(T.NI[:], T.ZI[:, 0:128], ["ZI0"], ["NI"], scale=-1.0, ns=cyc(128))
-    ac(T.Wb[:], T.ZE0[:, 15 - fT:143 - fT], ["ZE0", "WS"], ["Wb"], scale=wcol(23), ns=cyc(128))
-    ts(TRi, T.ZI[:, 0:128], wcol(22), A.mult, ["ZI0", "WS"], ["TRi"])
-    tt(T.Wb[:], T.Wb[:], TRi, A.add, ["Wb", "TRi"], ["Wb"], cyc(256))
+    iota(T.KE[:, 0:56], [[1, 4], [0, 14]], 2 - ZC, 0, ["KE0"], c=56, reads=["late"])
+    iota(T.KE[:, 56:80], [[1, 4], [0, 6]], 2 - ZC, 0, ["KE1"], c=24, reads=["late"])
+    ts(T.RJ[:, 16:30], T.RI[:, 16:30], 3, A.bitwise_and, ["RP"], ["RJ1"])
+    ts(T.rimK[:, 0:14], T.RJ[:, 16:30], 2.0, A.add, ["RJ1"], ["rimK"])
+    ts(T.rimK[:, 16:30], T.RJ[:, 16:30], float(FP), A.mult, ["RJ1"], ["rimL"], 8.0 + 160 - BIG * RO, A.add)
+    ty, td, tg, tm, th_, ta, tb = [T.LW[:, 64 * k:64 * k + 64] for k in range(7)]
+    L1, L2, L3, LI = [T.LT[:, 256 * k:256 * k + 256] for k in range(4)]
+    iota(ty, [[0, 8], [1, 8]], -2, 0, ["ty"], reads=["late"])
+    iota(td, [[0, 2], [1, 4], [0, 8]], 1, 0, ["td"], reads=["late"])
+    iota(tg, [[2, 2], [0, 32]], -1, 0, ["tg"], reads=["late"])
+    ts(tm, ty, 0.0, A.max, ["ty"], ["tm"])
+    tt(tm, tm, td, A.min, ["tm", "td"], ["tm"], cyc(128))
+    ac(tg, tg, ["tg"], ["tg"], scale=1.0 / 32, ns=cyc(64))
+    ac(th_, tm, ["tm"], ["th_"], scale=-0.5, ns=cyc(64))
+    tt(L1[:, 0:64], tm, tg, A.mult, ["tm", "tg"], ["L0a"], cyc(128))
+    tt(ta, th_, td, A.add, ["th_", "td"], ["ta"], cyc(128))
+    tt(tb, th_, ty, A.add, ["th_", "ty"], ["tb"], cyc(128))
+    tt(L2[:, 0:64], L1[:, 0:64], ta, A.mult, ["L0a", "ta"], ["L1a"], cyc(128))
+    tt(L3[:, 0:64], L1[:, 0:64], tb, A.mult, ["L0a", "tb"], ["L2a"], cyc(128))
+    fills("av", [(LI[:, a:b], T.X[:, 0:b - a], val) for o in (0, 32) for a, b, val in ((o, o + 8, 1.0), (o + 8, o + 16, 0.5), (o + 16, o + 32, 0.25))], ["X"], ["L3a"])
+    for k, x in enumerate((L1, L2, L3, LI)):
+        cp(x[:, 64:128], x[:, 0:64], ["L%da" % k], ["L%db" % k], cyc(64), "a")
+        cp(x[:, 128:256], x[:, 0:128], ["L%da" % k, "L%db" % k], ["L%d" % k], cyc(128), "a")
+    ac(T.Wb[:], T.ZE0[:, 15 - fT:143 - fT], ["ZE0", "WS"], ["Wb"], scale=wcol(cD), ns=cyc(128))
+    ac(tmp, ZI, ["ZI0", "WS"], ["tmp"], scale=wcol(cKP), ns=cyc(128))
+    tt(T.Wb[:], T.Wb[:], tmp, A.add, ["Wb", "tmp"], ["Wb"], cyc(256))
     for r in range(1, RO + 1):
-        ac(T.BR[:, r:r + 1], wcol(25), ["WS"], ["BR%d" % r], bias=wcol(24), scale=float(r))
-    ac(T.ZP[:], T.ZE0[:], ["ZE0", "WS"], ["ZP"], scale=wcol(14), ns=cyc(144))
-    ac(T.ZQ[:], T.ZO0[:], ["ZO0", "WS"], ["ZQ"], scale=wcol(14), ns=cyc(144))
-    ac(T.Wy[:, 0:8], T.BK[:, 0:128:16], ["BK", "WS"], ["Wy0"], scale=wcol(19))
-    ac(T.Wy[:, 8:16], T.BK[:, 0:128:16], ["BK", "WS"], ["Wy1"], scale=wcol(23))
+        ac(T.BR[:, r:r + 1], wcol(cR), ["WS"], ["BR%d" % r], bias=wcol(cB4), scale=float(r))
+    for k, (pat, base) in enumerate((([[-16, 8], [6, 40]], 0), ([[2, 8], [0, 40]], 0), ([[1, CAP]], -160))):
+        iota(T.PT[0:1, 256 + CAP * k:256 + CAP * (k + 1)], pat, base, 0, ["PJ%d" % k], c=CAP, reads=["late"])
+    ac(T.ZP[:], T.ZE0[:], ["ZE0", "WS"], ["ZP"], scale=wcol(cPL), ns=cyc(144))
+    ac(T.ZQ[:], T.ZO0[:], ["ZO0", "WS"], ["ZQ"], scale=wcol(cX), ns=cyc(144))
+    ac(T.Wy[:, 0:8], T.BK[:, 0:128:16], ["BK", "WS"], ["Wy0"], scale=wcol(cT))
+    ac(T.Wy[:, 8:16], T.BK[:, 0:128:16], ["BK", "WS"], ["Wy1"], scale=wcol(cD))
+    ac(Z128, ZI, ["ZI0"], ["Z128"], scale=128.0, ns=cyc(128), narrow=True)
+    ac(NBI, ZI, ["ZI0"], ["Z64"], scale=1.0 / 64, ns=cyc(128), narrow=True)
+    ac(aS2, aF, ["aF"], ["aS2"], scale=(SL + (RO - 1) * FP - V) / 320.0, ns=cyc(FP), narrow=True)
 
     either[0] = ""
     cp(T.rimS[:, 0:14], T.RI[:, 0:14], ["RI"], ["rimS"])
     NG = 8
     Gs = ["G%d" % k for k in range(NG)]
+    edge = [56 * (k // 2) + GV * (k % 2) for k in range(NG + 1)]
+    OF = T.GF[:, V + FP:V + 2 * FP]
 
-    def neighbours():
-        w_ = FP // NG
+    def neighbours(last, free):
+        o = FP * last
+        win, reads = (ST[:], STw + ["colL"] + ["lnd1_%d" % m for m in range(RO)]) if last else (ST[:, 0:SL], STw + ["colU"])
         for k in range(NG):
-            cp(T.G[:, 16 * w_ * k:16 * w_ * (k + 1)], ST[:, 0:V + FP].indirect(T.colU[:, w_ * k:w_ * (k + 1)]), STw + ["colU"], [Gs[k]], ind(16 * w_), "av")
+            a, b = edge[k], edge[k + 1]
+            cp(T.G[:, FP + 16 * a:FP + 16 * b], win.indirect(T.colU[:, o + a:o + b]), reads, [Gs[k]], ind(16 * (b - a)), "av" if free else "va"[k % 2])
 
-    def by_slot(bank, Z, zn, cut=CUT):
+    def by_slot(bank, Z, zn, more=False):
         at = 0
-        for j, k in enumerate(cut):
-            a, b = at * FP // NG, (at + k) * FP // NG
-            mm([(P[bank][:, a:b], Z[:, 15 - i:143 - i], T.G[:, 16 * a + i:16 * b:16]) for i in range(16)], Gs[at:at + k] + [zn], bank,
-               16 * max(b - a, 64), start=False, stop=j == len(cut) - 1)
+        for j, k in enumerate(CUT):
+            a, b = 14 + edge[at] - (14 if more and j == 0 else 0), 14 + edge[at + k]
+            mm([(P[bank][:, a:b], Z[:, 15 - i:143 - i], T.G[:, 16 * a + i:16 * b:16]) for i in range(16)], Gs[at:at + k] + [zn] + ["XR"] * (a == 0), bank,
+               16 * max(b - a, 64), start=False, stop=j == len(CUT) - 1)
             at += k
 
-    def lgw(r):
-        return ["LG0"] + ["LG%d_%d" % (k, j) for k in range(1, r) for j in range(8)] + ["LGh%d" % k for k in range(1, r)]
-
-    UU, sm, su, qe, cq, WK, rr, FF, xx, po, gb = T.UU, T.sm, T.su, T.qe, T.cq, T.WK, T.r, T.FF, T.xx, T.po, T.gb
-    eU, caseU, takeU, keepU = UU[:, 80:100], su[:, 0:80], su[:, 80:160], su[:, 160:240]
-    qnU, qeU, qyU, faceU = T.qU[:, 0:80], T.qU[:, 80:100], T.qU[:, 100:156], T.qU[:, 160:240]
-    pre, knf, mine, zz, own, t0, t1, t3 = [sm[:, 80 * k:80 * k + 80] for k in range(8)]
-    m0, m1, m2, m3 = [T.v1[:, 56 * k:56 * k + 56] for k in range(4)]
-    L1, L2, L3, LS = T.L1[:, 0:384], T.L2[:, 0:384], T.L3[:, 0:384], T.LS[:, 0:384]
+    qe, cq, WK, rr, FF, xx, po, gb, eU = T.qe, T.cq, T.WK, T.r, T.FF, T.xx, T.po, T.gb, T.eU
     TH, base = T.TH[:, 0:1], gb[:, 640:960]
     PARTS = ((0, FP, 0, 14), (FP, CAP, 14, 20))
-    PORTS = [(FP * k, FP, 14 * k) for k in range(4)] + [(4 * FP + NR * k, NR, 56 + 6 * k) for k in range(4)]
+    PORTS = [(FP * k, FP) for k in range(4)] + [(4 * FP + NR * k, NR) for k in range(4)]
+    APART = [(r, s) for r in range(2, RO + 1) for s in SA if r < RO or s > 3]
+    OWN, ACC = ((0, 0), (4, 0)), ((5, 0), (4, NR))
 
-    def rim_address(bank, extra, name):
-        mm([(P[bank][:, 0:14], T.ZP[:, 15 - i:143 - i], T.pk1[:, i:FP:16]) for i in range(16)], ["pk1", "ZP"], bank, 1024)
-        tt(T.ryF[:, 0:14], P[bank][:, 0:14], extra, A.add, ["P%d" % bank, name], ["ryF"])
-        cp(T.ryU[:, 0:14], T.ryF[:, 0:14], ["ryF"], ["ryU"])
+    def lists(part, what, k0=0, k1=4):
+        w = (14, 6)[part]
+        if what in ("q0e", "q1e"):
+            k0, k1 = -1, 0
+        buf, o = {"q0e": (T.UA, 9), "q0n": (T.UA, 9), "case": (T.UA, 9), "q1e": (T.UB, 5), "q1n": (T.UB, 5), "take": (T.UC, 8), "keep": (T.UC, 8)}[what]
+        at = 14 * o * part + w * {"case": 5, "take": 0, "keep": 4}.get(what, 1)
+        return buf[:, at + w * k0:at + w * k1]
 
-    def pack_y(bank, r, window, reads, scale):
-        ac(T.pk2[:, 2 * FP:3 * FP], window.indirect(T.ryU[:, 0:14]), reads + ["ryU"], ["pk2_2"], scale=scale, ns=ind(FP))
-        shift(bank, 0, T.pk2, 2 * FP, T.ZF, ["pk2_2", "ZF"], 4)
-        cp(T.snd3[:, r * FP:(r + 1) * FP], P[bank][:, 0:FP], ["P%d" % bank], ["snd3_%d" % r], cyc(FP), "a")
-        send(3, r, ["snd3_%d" % r], "LGh%d" % r)
-
-    def who_acts(r):
-        mm([(P[5][:, 0:FP], T.ZO[:, 12 - 4 * m:140 - 4 * m], ST[:, m:V:4]) for m in range(4)], ["ZO", "STl"], 5, 4 * FP, stop=False)
-        mm([(P[1][:, 0:171], ZF, T.IN[:, 0:171])], ["ZF", "IN0", "IN1", "IN2"], 1, 171, 4, stop=False)
-        mm([(P[0][:, 0:171], T.ZI[:, 0:128], T.ZB[:, 0:171])], ["ZI0", "ZB"], 0, 171, stop=False)
-        mm([(P[6][:, 0:504], T.ZI[:, 0:128], T.KI[:])], ["ZI0", "KI"], 6, 504, stop=False)
-        if r == 1:
-            cp(T.C[:, 0:2560], T.CT[:], ["CT%d" % j for j in range(16)], ["C"], cyc(1280))
-        else:
-            op({"g": 170 + 2 * 2560 * CYC}, lambda e: g.affine_select(T.C[:, 0:2560], T.CT[:], [[0, 2560]], A.is_ge, 0.0, 0, 0), ["CT%d" % j for j in range(16)], ["C"])
-        lnd, ln = T.lnd1[:, (r - 1) * FP:r * FP], "lnd1_%d" % (r - 1)
-        if r == 1:
-            neighbours()
-        cp(T.G[:, 0:4 * V].indirect(T.rimS[:, 0:14]), lnd, [ln, "rimS"], Gs, ind(FP, SC))
-        cp(ST[:, V:V + FP], lnd, [ln], ["STh"], cyc(FP), "a")
-        by_slot(5, T.ZE, "ZE", (NG,))
-        marks[r] = {wr[x] for x in LATE}
-        ts(T.bit[:], P[5][:, 0:FP], 0.0, A.is_gt, ["P5"], ["bit"], ns=cyc(FP))
-        mm([(P[4][:, 0:56], T.Z2[:, 12 - 4 * h:140 - 4 * h], T.bit[:, h:FP:4]) for h in range(4)], ["Z2", "bit"], 4, 256)
-        cf, cn = T.can[:, 0:56], T.can[:, 56:112]
-        tt(cf, P[4][:, 0:56], T.THR[:, 0:56], A.is_ge, ["P4", "THa"], ["cf"])
-        tt(cn, P[4][:, 0:56], T.THR[:, 56:112], A.is_ge, ["P4", "THb"], ["cn"])
-        mm([(P[1][:, 1:57], T.BK[:], cf), (P[1][:, 115:171], BK8, cf)], ["BK", "BK8", "cf"], 1, 128, start=False, stop=False)
-        mm([(P[1][:, 58:114], NBK, cn), (P[1][:, 115:171], BK8, cn)], ["NBK", "BK8", "cn"], 1, 128, start=False)
-        mm([(P[0][:, 0:56], TRa, cf), (P[0][:, 114:170], TRc, cf), (P[0][:, 57:113], TRb, cn), (P[0][:, 114:170], TRc, cn)],
-           ["TRa", "TRb", "TRc", "cf", "cn"], 0, 256, start=False)
-        op({"v": cyc(171)}, lambda e: vec.tensor_tensor_scan(T.SX[:, 0:171], T.ONE[:, 0:171], P[1][:, 0:171], 0.0, A.mult, A.add), ["ONE", "P1"], ["SX"])
-        tt(T.v0[:, 0:171], P[0][:, 0:171], T.SX[:, 0:171], A.add, ["P0", "SX"], ["v0"], cyc(171))
-        tt(m0, T.v0[:, 0:56], T.v0[:, 57:113], A.min, ["v0"], ["m0"], cyc(112))
-        ts(m1, m0, cF1, A.is_ge, ["m0", "cF1", "cF2"], ["m1"], cF2, A.mult)
-        tt(m2, m0, T.v0[:, 114:170], A.max, ["m0", "v0"], ["m2"], cyc(112))
-        tt(m3, m1, m2, A.add, ["m1", "m2"], ["m3"], cyc(112))
-        tt(m0, m3, T.TRE[:], A.min, ["m3", "TRE"], ["m0"], cyc(112))
-        cp(T.posU[:], m0, ["m0"], ["posU"])
-        cp(T.C[:, 0:3456].indirect(T.posU[:, 0:56]), ST[:, 0:V], ["posU", "STl"], ["C"], ind(V, SC))
-        mm([(P[6][:, b:504:14], T.C[:, b:8 * FP:14], T.Wc[:, 0:36]) for b in range(14)]
-           + [(P[6][:, 56 + b:56 + b + 6 * 71 + 1:6], T.C[:, 8 * FP + b:2560:6], T.Wc[:, 40:112]) for b in range(6)], ["C"] + Wcs, 6, 20 * 66, start=False)
-        for W, o, nm in ((QB, 32, "QBh"), (QA, 0, "QAh")):
-            cp(W[:, LO + QS * r - FP:LO + QS * r], T.lnd2[:, 7 * r - 7:7 * r, o:o + 32], ["lnd2_%d" % (r - 1)], [nm + str(r - 1)], cyc(FP), "a")
-        cp(UU[:, 0:80], P[6][:, 0:80], ["P6"], ["UU"], cyc(80))
-        cp(eU, P[6][:, 462:482], ["P6"], ["eU"])
-        for k in range(2):
-            cp(T.GN[:, 640 * k:640 * k + 640], ST[:, 0:GW // 4].indirect(UU[:, 40 * k:40 * k + 40]), STw + ["UU"], ["GN%d" % k], ind(640), "va"[k])
-        mm([(P[2][:, 0:80], T.ZT[:, 15 - i:143 - i], T.GN[:, i:1280:16]) for i in range(16)], ["GN0", "GN1", "ZT"], 2, 1280)
-        ts(pre, P[6][:, 84:164], 128.0, A.is_ge, ["P6"], ["pre"], 192.0, A.mult, cyc(80))
-        tt(pre, P[6][:, 168:248], pre, A.add, ["P6", "pre"], ["pre"], cyc(80))
-        tt(t0, P[2][:, 0:80], pre, A.add, ["P2", "pre"], ["t0"], cyc(80))
-        cp(caseU, t0, ["t0"], ["caseU"], cyc(80))
-        mm([(P[4][:, 0:80], T.ZR[:, 15 - i:143 - i], T.GN[:, i:1280:16]) for i in range(16)], ["GN0", "GN1", "ZR"], 4, 1280)
-        ts(qnU, P[4][:, 0:80], float(LO), A.add, ["P4"], ["qnU"], ns=cyc(80))
-        if r < RO:
-            ts(faceU, P[6][:, 0:80], 0.375, A.add, ["P6"], ["faceU"], 4.0, A.mult, cyc(80))
-        cp(qeU[:, 0:14], P[6][:, 420:434], ["P6"], ["qeU0"])
-        cp(qeU[:, 14:20], P[6][:, 482:488], ["P6"], ["qeU1"])
+    def own_control(r):
         if r > 1:
-            mm([(P[3][:, 0:80], T.ZP[:, 15 - i:143 - i], T.GN[:, i:1280:16]) for i in range(16)], ["GN0", "GN1", "ZP"], 3, 1280)
-            Pk = P[6][:, 252:332]
-            ts(knf, UU[:, 0:80], -1280.0, A.mult, ["UU"], ["knf"], float(LO), A.add, cyc(80))
-            tt(knf, P[6][:, 336:416], knf, A.add, ["P6", "knf"], ["knf"], cyc(80))
-            tt(zz, P[3][:, 0:80], knf, A.add, ["P3", "knf"], ["zz"], cyc(80))
-            tt(own, Pk, zz, A.is_lt, ["zz", "P6"], ["own"], cyc(80))
-            tt(mine, Pk, zz, A.is_ge, ["zz", "P6"], ["mine"], cyc(80))
-            tt(t1, own, zz, A.mult, ["own", "zz"], ["t1"], cyc(160))
-            tt(t3, Pk, mine, A.mult, ["mine", "P6"], ["t3"], cyc(80))
-            cp(takeU, t1, ["t1"], ["takeU"], cyc(80))
-            cp(keepU, t3, ["t3"], ["keepU"], cyc(80))
-        for p_, (a, b, c0, c1) in enumerate(PARTS):
-            cp(qe[:, 320 + a:320 + b], QB[:, 0:LO + QS * r - FP].indirect(qeU[:, c0:c1]), qw("QB", r - 1)[:-1] + ["qeU%d" % p_], ["q1e%d" % p_], ind(b - a), "a")
-            cp(qe[:, a:b], QA[:, 0:LO + QS * r - FP].indirect(qeU[:, c0:c1]), qw("QA", r - 1)[:-1] + ["qeU%d" % p_], ["q0e%d" % p_], ind(b - a), "a")
-        cp(P[0][:, 0:CAP], qe[:, 0:CAP], ["q0e0", "q0e1"], ["P0"], cyc(CAP), "a")
-        cp(T.GO[:], ST[:, 0:TW].indirect(eU), STw + ["eU"], ["GO"], ind(CAP), "a")
-        mm([(P[6][:, 0:CAP], T.Wb[:], T.GO[:]), (P[6][:, 0:CAP], W1(fJHI), T.HI[0:1, 0:CAP])]
-           + [(P[6][:, c0:min(c0 + 128, CAP)], W1(fJLO), T.XB[0:1, 0:min(128, CAP - c0)]) for c0 in range(0, CAP, 128)],
-           ["Wb", "GO", "E1", "XB", "HI"], 6, 3 * CAP)
-        ac(base, P[6][:, 0:CAP], ["P6", "BR%d" % r], ["base"], bias=T.BR[:, r:r + 1], ns=cyc(CAP))
-        for p_, (a, b, c0, c1) in enumerate(PARTS):
-            l0 = PORTS[4 * p_][2]
-            cp(qe[:, 640 + a:640 + b], T.LI[:, 0:384].indirect(caseU[:, l0:l0 + c1 - c0]), ["LI", "caseU"], ["inv%d" % p_], ind(b - a), "a")
+            iota(T.C[:, CF0:3456], [[0, 2560]], 0, 0, ["C"], c=2560)
+        mm([(P[3][:, 0:FP + 14], ZI, T.AB[:, 7 * FP:8 * FP + 14])] + [(P[3][:, 14:FP + 14], T.ZO[:, 12 - 4 * m:140 - 4 * m], ST[:, m:V:4]) for m in range(4)],
+           ["ZI0", "SG", "SGz", "ZO"] + STs, 3, 5 * FP, stop=False)
+        if r > 1:
+            mm([(P[6][:, 0:FP], T.WN[:, 9 - fT:137 - fT], T.pk1[:])], ["WN", "pk1"], 6, FP)
+            ac(T.G[:, 0:FP], P[6][:, 0:FP], ["P6", "WS"], ["XR"], scale=wcol(cXR), ns=cyc(FP), on="av")
+        neighbours(False, r == 1)
+        marks["G", r] = len(nodes) - 1
+        by_slot(3, T.ZE, "ZE", r > 1)
+        ts(T.bit[:], P[3][:, 14:FP + 14], 0.0, A.is_gt, ["P3"], ["bit"], ns=cyc(FP))
+        if r > 1:
+            message2(r - 1)
+        mm([(P[4][:, 0:56], T.Z2[:, 12 - 4 * h:140 - 4 * h], T.bit[:, h:FP:4]) for h in range(4)], ["Z2", "bit"], 4, 256)
+        cn, cb_ = T.can[:, 0:56], T.can[:, 0:55]
+        tt(cn, P[4][:, 0:56], T.THR[:], A.is_ge, ["P4", "THR"], ["cn"])
+        mm([(P[0][:, 0:56], Na, cn), (P[0][:, 1:56], NBK, cb_), (P[0][:, 1:56], nNa, cb_)], ["Na", "NBK", "nNa", "cn"], 0, 3 * 64)
+        mm([(P[0][:, 56:112], Ka, cn), (P[0][:, 57:112], Kb, cb_)], ["Ka", "Kb", "cn"], 0, 2 * 64)
+        mm([(P[4][:, 0:56], TRs, cn), (P[4][:, 1:56], TRg, cb_)], ["TRs", "TRg", "cn"], 4, 2 * 64)
+        scan(T.SX[:, 0:56], cF4, 0, 0, 56, ["cF4"], ["SX0"])
+        scan(T.SX[:, 56:112], B2 * (CAP - 0.5), 0, 56, 56, [], ["SX1"])
+        scan(T.SX[:, 112:168], -210.0, 4, 0, 56, [], ["SX"])
+        tt(m0, T.SX[:, 0:56], T.SX[:, 56:112], A.min, ["SX0", "SX1"], ["m0"], cyc(112))
+        ts(m1, T.SX[:, 0:56], cF1, A.is_ge, ["SX0", "cF1", "cF2"], ["m1"], cF2, A.mult)
+        tt(m2, m0, T.TRE[:], A.max, ["m0", "TRE"], ["m2"], cyc(112))
+        tt(m3, m1, m2, A.add, ["m1", "m2"], ["m3"], cyc(112))
+        cp(T.posU[:, 0:56], m3, ["m3"], ["posU"])
+        for k, (a, b) in enumerate(halves):
+            for j in range(4):
+                if j == 0:
+                    mm([(P[1 + k][:, 0:b - a], T.Wo[:], ST[:, a:b])], ["Wo"] + STs, 1 + k, b - a, stop=False)
+                mm([(P[1 + k][:, 0:b - a], T.WN[:, 9 - 3 * j:137 - 3 * j], T.G[:, FP + 4 * a + j:FP + 4 * b:4])], ["WN"] + Gs[4 * k:4 * k + 4], 1 + k, b - a, 1, False, j == 3)
+            ac(T.RR[:, a:b], P[1 + k][:, 0:b - a], ["P%d" % (1 + k), "WS"], ["RR%d" % k], bias=wcol(cEL), ns=cyc(b - a), on="av")
+            marks["rows%d" % k, r] = len(nodes) - 1
+        cp(OF, ST[:, 0:V].indirect(eF), STs + ["eF"], ["OF"], ind(FP), "a")
+        if r == 1:
+            mm([(P[7][:, 0:FP], BQ, OF)], ["BQ", "OF"], 7, FP)
+            ts(T.MF[:], P[7][:, 0:FP], cI, A.is_equal, ["P7", "CF"], ["MF"], ns=cyc(FP))
+        mm([(P[0][:, 0:84], ZI, T.THF[:])], ["ZI0", "THF", "THz"], 0, 84, stop=False)
+        tt(T.NB[:], T.SX[:, 112:168].indirect(cF), T.MF[:], A.mult, ["SX", "cF", "MF"], ["NB"], ind(FP))
+        for k, (a, b) in enumerate(halves):
+            cp(T.C[:].indirect(T.posU[:, a // 16:b // 16]), T.RR[:, a:b], ["posU", "RR%d" % k], ["C"], ind(b - a, SC))
+        mm([(P[7][:, 0:FP], T.ZE0[:, 15 - fT:143 - fT], T.NB[:])], ["ZE0", "NB"], 7, FP)
+        ac(T.GF[:, V:V + FP], P[7][:, 0:FP], ["P7"], ["GF4"], scale=0.5, ns=cyc(FP))
+
+    def far_control(r):
+        for k in range(4):
+            cp(T.GF[:, FP * k:FP * k + FP], ST[:, 0:SL + FP * r].indirect(T.FN[:, 56 * (r - 1) + 14 * k:56 * (r - 1) + 14 * k + 14]),
+               STw + ["FN%d" % (r - 1)] + ["lnd1_%d" % m for m in range(r)], ["GF%d" % k], ind(FP), GFQ)
+        GFs = ["GF%d" % k for k in range(4)]
+        listed(0, 0, T.ZE, T.GF, 84, ["ZE", "GF4", "OF"] + GFs, start=False)
+        f0, f1, f2, f3, f4 = [T.SX[:, 168 + 14 * k:182 + 14 * k] for k in range(5)]
+        cp(T.bf[:, 0:28], P[0][:, 0:28], ["P0"], ["bf0"])
+        ts(f1, P[0][:, 56:70], -1.0, A.mult, ["P0", "cF3"], ["f1"], cF3, A.add)
+        tt(T.bf[:, 28:56], P[0][:, 28:56], T.bf[:, 0:28], A.min, ["P0", "bf0"], ["bf1"])
+        tt(T.bf[:, 56:70], T.bf[:, 28:42], T.bf[:, 42:56], A.min, ["bf1"], ["bf2"])
+        cf, cb_ = T.can[:, 56:70], T.can[:, 56:69]
+        tt(cf, P[0][:, 70:84], T.bf[:, 56:70], A.is_lt, ["P0", "bf2", "THR"], ["cf", "isf"])
+        mm([(P[5][:, 0:14], Pa, cf), (P[5][:, 1:14], T.BK[:], cb_), (P[5][:, 1:14], nPa, cb_)], ["Pa", "BK", "nPa", "cf"], 5, 3 * 64)
+        scan(f0, cF5, 5, 0, 14, ["cF5"], ["f0"])
+        tt(f2, f0, f1, A.is_lt, ["f0", "f1"], ["f2"])
+        tt(f3, f0, f2, A.mult, ["f0", "f2"], ["f3"])
+        tt(f4, f3, T.TRE[:, 0:14], A.max, ["f3", "TRE"], ["f4"])
+        cp(T.posU[:, 56:70], f4, ["f4"], ["posF"])
+        mm([(P[7][:, 0:FP], T.Wo[:], OF)] + [(P[7][:, 0:FP], T.WN[:, 9 - 3 * j:137 - 3 * j], T.GF[:, FP * j:FP * j + FP]) for j in range(4)],
+           ["Wo", "WN", "OF"] + GFs, 7, 5 * FP)
+        ac(T.RF[:], P[7][:, 0:FP], ["P7", "WS"], ["RF"], bias=wcol(cEL), ns=cyc(FP), on="av")
+        cp(T.C[:].indirect(T.posU[:, 56:70]), T.RF[:], ["posF", "RF"], ["C"], ind(FP, SC))
+
+    def addresses(r, part):
+        a, b, c0, c1 = PARTS[part]
+        w, at = c1 - c0, (CF0, CB0)[part]
+        nc = 22 if r > 1 else 10
+        mm([(P[6][:, j:nc * w:w], T.C[:, at + j:at + 128 * w:w], WB[:, 0:nc]) for j in range(w)], ["C", "WB0", "WB"], 6, w * 64, start="each", stop="each")
+        ua, ub, uc = "UA%d" % part, "UB%d" % part, "UC%d" % part
+        cp(T.UA[:, 126 * part:126 * part + 9 * w], P[6][:, 0:9 * w], ["P6"], [ua], cyc(9 * w))
+        ts(T.UB[:, 70 * part:70 * part + 5 * w], P[6][:, 0:5 * w], 1.0, A.add, ["P6"], [ub], ns=cyc(5 * w))
+        tt(T.sm[:, 300 + c0:300 + c1], P[6][:, 9 * w:10 * w], T.MK[:, 8 + c0:8 + c1], A.min, ["P6", "TRX"], ["ez%d" % part])
+        ts(eU[:, c0:c1], T.sm[:, 300 + c0:300 + c1], BIG, A.add, ["ez%d" % part], ["eU%d" % part])
+        if r > 1:
+            ki, zz, mn = T.ki[:, 0:4 * w], T.sm[:, 0:8 * w], T.sm[:, 160:160 + 8 * w]
+            ts(ki, P[6][:, 5 * w:9 * w], 1.0 / 64, A.mult, ["P6"], ["ki"], 2 - ZC - 0.49, A.add)
+            tt(zz[:, 4 * w:8 * w], P[6][:, 18 * w:22 * w], T.KE[:, 56 * part:56 * part + 4 * w], A.add, ["P6", "KE%d" % part], ["za"])
+            tt(zz[:, 0:4 * w], P[6][:, w:5 * w], ki, A.add, ["P6", "ki"], ["zz"])
+            tt(mn, P[6][:, 10 * w:18 * w], zz, A.min, ["P6", "zz", "za"], ["mn"], cyc(8 * w))
+            cp(T.UC[:, 112 * part:112 * part + 8 * w], mn, ["mn"], [uc], cyc(8 * w))
+
+    def old_q(r, part):
+        a, b = PARTS[part][0:2]
+        ua, ub = "UA%d" % part, "UB%d" % part
+        win, names = upto(r - 1, 0), log(r - 1, 0)
+        cp(qe[:, 320 + a:320 + b], win.indirect(lists(part, "q1e")), names + [ub], ["q1e%d" % part], ind(b - a), "a")
+        cp(qe[:, a:b], win.indirect(lists(part, "q0e")), names + [ua], ["q0e%d" % part], ind(b - a), "a")
+        bank, o = OWN[part]
+        cp(P[bank][:, o:o + b - a], qe[:, a:b], ["q0e%d" % part], ["P%d" % bank], cyc(b - a), "a")
+
+    def old_fields(r, part):
+        a, b, c0, c1 = PARTS[part]
+        if (r, part) == (1, 1):
+            mm([(P[7][:, 0:CAP], W1(f), T.PT[0:1, 256 + CAP * k:256 + CAP * (k + 1)]) for k, f in enumerate((fJL, fJH, fP))], ["E1", "PJ0", "PJ1", "PJ2"], 7, 3 * CAP)
+            cp(T.JR[:], P[7][:, 0:CAP], ["P7"], ["JR"], cyc(CAP), "av")
+        if (r, part) == (1, 0):
+            mm([(P[6][:, 0:FP], ZI, aL), (P[6][:, 0:FP], Z128, aH), (P[6][:, 0:FP], Z128, aS2)], ["ZI0", "Z128", "aL", "aH", "aS2"], 6, 3 * FP)
+            cp(T.colU[:, FP:2 * FP], P[6][:, 0:FP], ["P6"], ["colL"], cyc(FP))
+        cp(T.GO[:, a:b], ST[:, 0:SL].indirect(eU[:, c0:c1]), STw + ["eU%d" % part], ["GO%d" % part], ind(b - a), "a")
+        mm([(P[7][:, 0:b - a], ZI, T.JR[:, a:b]), (P[7][:, 0:b - a], T.Wb[:], T.GO[:, a:b])], ["Wb", "GO%d" % part, "ZI0", "JR"], 7, 2 * (b - a))
+        ac(base[:, a:b], P[7][:, 0:b - a], ["P7", "BR%d" % r], ["base%d" % part], bias=T.BR[:, r:r + 1], ns=cyc(b - a))
+        cp(qe[:, 640 + a:640 + b], LI.indirect(lists(part, "case", 0, 1)), ["L3", "UA%d" % part], ["inv%d" % part], ind(b - a), "a")
 
     def flux(r, s, step):
-        ports = [s] if s < 4 else [2 * s - 4, 2 * s - 3]
         part = s // 4
+        k0, k1 = (s, s + 1) if s < 4 else (2 * s - 8, 2 * s - 6)
         a, b = PARTS[part][0:2]
-        lo, l0 = PORTS[ports[0]][0], PORTS[ports[0]][2]
-        wd = sum(PORTS[k][1] for k in ports)
-        l1, h, hb = l0 + wd // 16, (0, 1, 0, 1, 2, 3)[s], s % 2
+        lo, wd = PORTS[4 * part + k0][0], (k1 - k0) * (b - a)
+        h, hb = (0, 1, 0, 1, 2, 3)[s], s % 2
         at = (0, FP, 2 * FP, 2 * FP + 2 * NR)[h]
         q1n, c1, sg = cq[:, lo:lo + wd], T.cb[:, lo:lo + wd], T.cb[:, 1280 + lo:1280 + lo + wd]
         wn, un, we, ue, sq = [WK[:, 832 * j + at:832 * j + at + wd] for j in range(5)]
         nm = {x: "%s%d" % (x, h) for x in ("wn", "un", "we", "ue", "sq", "r", "x")}
-        bj, bs = 1 + hb, 3 + hb
-        pn, pj, ps, nj, ns_ = P[bj][:, 0:wd], P[bj][:, wd:2 * wd], P[bs][:, 0:wd], "P%d" % bj, "P%d" % bs
-        if step == "f":
+        bj, bs, os_ = 1 + hb, 3 + hb * (1 - part), wd * hb * part
+        pn, pj, ps, nj, ns_ = P[bj][:, 0:wd], P[bj][:, wd:2 * wd], P[bs][:, os_:os_ + wd], "P%d" % bj, "P%d" % bs
+        win, names = upto(r - 1, 1 - part), log(r - 1, 1 - part)
+        ua, ub, uc = "UA%d" % part, "UB%d" % part, "UC%d" % part
+        case = lists(part, "case", k0, k1)
+        if step == "g":
+            cp(c1, L1.indirect(case), ["L0", ua, "eF"], ["c1%d" % s], ind(wd), "a")
+            cp(q1n, win.indirect(lists(part, "q1n", k0, k1)), names + [ub], ["q1n%d" % s], ind(wd), "a")
+        elif step == "f":
             def each(f):
                 def fn(_):
-                    for k in ports:
-                        last = f(PORTS[k][0] - lo, PORTS[k][1], PORTS[k][2])
+                    for k in range(k0, k1):
+                        last = f((k - k0) * (b - a), b - a, k)
                     return last
                 return fn
-            cp(c1, L1.indirect(caseU[:, l0:l1]), ["L1", "L1n", "caseU"], ["c1%d" % s], ind(wd), "a")
-            cp(q1n, QB[:, 0:LO + QS * r].indirect(qnU[:, l0:l1]), qw("QB", r - 1) + ["qnU"], ["q1n%d" % s], ind(wd), "a")
-            op({"v": len(ports) * ind(b - a)},
-               each(lambda o, w_, c0: vec.tensor_tensor(we[:, o:o + w_], L2.indirect(caseU[:, c0:c0 + w_ // 16]), qe[:, 320 + a:320 + b], A.mult)),
-               ["L2", "L2n", "caseU", "q1e%d" % part], [nm["we"]])
-            tt(wn, L3.indirect(caseU[:, l0:l1]), q1n, A.mult, ["L3", "L3n", "caseU", "q1n%d" % s], [nm["wn"]], ind(wd))
-            tt(un, QA[:, 0:LO + QS * r].indirect(qnU[:, l0:l1]), c1, A.mult, qw("QA", r - 1) + ["qnU", "c1%d" % s], [nm["un"]], ind(wd))
+            bank, o0 = OWN[part]
+            op({"v": (k1 - k0) * ind(b - a)},
+               each(lambda o, w_, k: vec.tensor_tensor(we[:, o:o + w_], L2.indirect(lists(part, "case", k, k + 1)), qe[:, 320 + a:320 + b], A.mult)),
+               ["L1", ua, "q1e%d" % part], [nm["we"]])
+            tt(wn, L3.indirect(case), q1n, A.mult, ["L2", ua, "q1n%d" % s], [nm["wn"]], ind(wd))
+            tt(un, win.indirect(lists(part, "q0n", k0, k1)), c1, A.mult, names + [ua, "c1%d" % s], [nm["un"]], ind(wd))
             to, tn = (pj, nj) if s in JV else (ue, nm["ue"])
-            op({"v": cyc(wd)}, each(lambda o, w_, c0: vec.tensor_tensor(to[:, o:o + w_], P[0][:, a:b], c1[:, o:o + w_], A.mult)), ["P0", "c1%d" % s], [tn])
+            op({"v": (k1 - k0) * max(VMIN, (b - a) * CYC)},
+               each(lambda o, w_, k: vec.tensor_tensor(to[:, o:o + w_], P[bank][:, o0:o0 + w_], c1[:, o:o + w_], A.mult)), ["P%d" % bank, "c1%d" % s], [tn])
             if s in JV:
                 tt(pj, pj, we, A.add, [nj, nm["we"]], [nj], cyc(wd))
-            mm([(pn, ZF, wn), (pn, T.NI[:], un)], ["ZF", "NI", nm["wn"], nm["un"]], bj, 2 * wd, 4)
             if s not in JV:
-                mm([(pj, ZF, we), (pj, ZF, ue)], ["ZF", nm["we"], nm["ue"]], bj, 2 * wd, 4)
+                mm([(pj, ZF, we)], ["ZF", nm["we"]], bj, wd, 4, stop=False)
+                mm([(pj, ZF, ue)], ["ZF", nm["ue"]], bj, wd, 4, start=False)
+            mm([(pn, T.NI[:], wn)], ["NI", nm["wn"]], bj, wd, 4, stop=False)
+            mm([(pn, T.NI[:], un)], ["NI", nm["un"]], bj, wd, 4, start=False)
         elif step == "m":
             ac(rr[:, 2 * at:2 * at + 2 * wd], P[bj][:, 0:2 * wd], [nj], [nm["r"]], AF.Relu, ns=cyc(2 * wd))
             ac(sq, rr[:, 2 * at:2 * at + wd], [nm["r"]], [nm["sq"]], AF.Square, ns=cyc(wd))
             ac(ps, rr[:, 2 * at + wd:2 * at + 2 * wd], [nm["r"]], [ns_], AF.Square, ns=cyc(wd))
         else:
             f = FF[:, 8 + lo:8 + lo + wd]
-            if s in SGV:
-                ts(sg, c1, 0.0, A.is_lt, ["c1%d" % s], ["sg%d" % s], 0.5, A.subtract, cyc(wd // 2))
-            else:
-                cp(sg, LS.indirect(caseU[:, l0:l1]), ["LS", "caseU"], ["sg%d" % s], ind(wd), "a")
+            ts(sg, c1, 0.0, A.is_lt, ["c1%d" % s], ["sg%d" % s], 0.5, A.subtract, cyc(wd // 2))
             tt(ps, ps, sq, A.add, [ns_, nm["sq"]], [ns_], cyc(wd))
-            tt(f, ps, sg, A.mult, [ns_, "sg%d" % s], ["F%d" % s], cyc(wd))
             x, xn = f, "F%d" % s
             if r > 1:
                 x, xn = xx[:, at:at + wd], nm["x"]
-                tt(x, LG[:, 0:LO + BLKW * r].indirect(takeU[:, l0:l1]), f, A.add, lgw(r) + ["takeU", "F%d" % s], [xn], ind(wd))
-            pq, qf = P[5][:, a:b], QA[:, LO + QS * r + a:LO + QS * r + b]
-            if s == 0:
-                mm([(pq, ZF, qe[:, a:b])], ["ZF", "q0e0"], 5, wd, 4, stop=False)
-            if s < 3:
-                mm([(pq, ZF, x)], ["ZF", xn], 5, wd, 4, start=False, stop=s == 2)
-            elif s == 3:
-                tt(qf, pq, x, A.add, ["P5", xn], ["QA%d_0" % r], cyc(wd))
-            elif QV:
-                for j in range(2):
-                    last = s == 5 and j == 1
-                    tt(qf if last else pq, P[0][:, a:b] if s == 4 and j == 0 else pq, x[:, NR * j:NR * j + NR], A.add, ["P0", "P5", xn],
-                       ["QA%d_1" % r] if last else ["P5"], cyc(NR))
-            elif s == 4:
-                mm([(pq, ZF, qe[:, a:b]), (pq, ZF, x[:, 0:NR]), (pq, ZF, x[:, NR:2 * NR])], ["ZF", "q0e1", xn], 5, 3 * NR, 4, stop=False)
+            if (r, s) in APART:
+                take, keep = T.TK[:, lo:lo + wd], T.TK[:, 1280 + lo:1280 + lo + wd]
+                cp(take, upto(r - 1, 1 - part, ZC).indirect(lists(part, "take", k0, k1)), names + [uc], ["take%d" % s], ind(wd), "a")
+                cp(keep, upto(r - 1, 1 - part, ZC).indirect(lists(part, "keep", k0, k1)), names + [uc], ["keep%d" % s], ind(wd), "a")
+                tt(ps, ps, sg, A.mult, [ns_, "sg%d" % s], [ns_], cyc(wd))
+                tt(x, ps, take, A.add, [ns_, "take%d" % s], [xn], cyc(wd))
+                for k in range(k0, k1):
+                    o = (k - k0) * (b - a)
+                    tt(LG[:, BL * r + 6 * a + 2 + k:BL * r + 6 * b:6], keep[:, o:o + b - a], ps[:, o:o + b - a], A.subtract, [ns_, "keep%d" % s],
+                       ["LG%d_%d" % (r, 4 * part + k)], cyc(b - a))
             else:
-                mm([(pq, ZF, x[:, 0:NR])], ["ZF", xn], 5, NR, 4, start=False)
-                tt(qf, pq, x[:, NR:2 * NR], A.add, ["P5", xn], ["QA%d_1" % r], cyc(NR))
+                tt(f, ps, sg, A.mult, [ns_, "sg%d" % s], ["F%d" % s], cyc(wd))
+            if r > 1 and (r, s) not in APART:
+                tt(x, upto(r - 1, 1 - part, ZC).indirect(lists(part, "take", k0, k1)), f, A.add, names + [uc, "F%d" % s], [xn], ind(wd))
+            bank, o0 = ACC[part]
+            pq, qf = P[bank][:, o0:o0 + b - a], LG[:, BL * r + 6 * a:BL * r + 6 * b:6]
+            if s == 0:
+                mm([(pq, ZF, qe[:, a:b])], ["ZF", "q0e0"], bank, wd, 4, stop=False)
+            if s < 3:
+                mm([(pq, ZF, x)], ["ZF", xn], bank, wd, 4, start=False, stop=s == 2)
+            elif s == 3:
+                tt(qf, pq, x, A.add, ["P%d" % bank, xn], ["QA%d_0" % r], cyc(wd))
+            elif s == 4:
+                mm([(pq, ZF, qe[:, a:b]), (pq, ZF, x[:, 0:NR]), (pq, ZF, x[:, NR:2 * NR])], ["ZF", "q0e1", xn], bank, 3 * NR, 4, stop=False)
+            else:
+                mm([(pq, ZF, x[:, 0:NR])], ["ZF", xn], bank, NR, 4, start=False)
+                tt(qf, pq, x[:, NR:2 * NR], A.add, ["P%d" % bank, xn], ["QA%d_1" % r], cyc(NR))
 
     def sums(r, part):
         a, b = PARTS[part][0:2]
         for k in range(4):
-            lo, wd, l0 = PORTS[4 * part + k]
-            out, f, fn = LG[:, LO + BLKW * r + 320 * k + a:LO + BLKW * r + 320 * k + b], FF[:, 8 + lo:8 + lo + wd], "F%d" % (4 + k // 2 if part else k)
+            if (r, 4 + k // 2 if part else k) in APART:
+                continue
+            lo, wd = PORTS[4 * part + k]
+            out, f, fn = LG[:, BL * r + 6 * a + 2 + k:BL * r + 6 * b:6], FF[:, 8 + lo:8 + lo + wd], "F%d" % (4 + k // 2 if part else k)
             if r == 1:
                 ac(out, f, [fn], ["LG%d_%d" % (r, 4 * part + k)], scale=-1.0, ns=cyc(wd))
             else:
-                tt(out, LG[:, 0:LO + BLKW * r].indirect(keepU[:, l0:l0 + wd // 16]), f, A.subtract, lgw(r) + ["keepU", fn], ["LG%d_%d" % (r, 4 * part + k)], ind(wd))
+                tt(out, upto(r - 1, 1 - part, ZC).indirect(lists(part, "keep", k, k + 1)), f, A.subtract, log(r - 1, 1 - part) + ["UC%d" % part, fn],
+                   ["LG%d_%d" % (r, 4 * part + k)], ind(wd))
 
-    def new_fields(r, part):
+    def new_step(r, part):
         a, b, c0, c1 = PARTS[part]
-        g1, nn = [gb[:, 320 * k + a:320 * k + b] for k in range(2)]
-        size, qf, qn = po[:, a:b], QA[:, LO + QS * r + a:LO + QS * r + b], "QA%d_%d" % (r, part)
-        if part in ABS:
-            ac(size, qf, [qn], ["size%d" % part], AF.Abs, ns=cyc(b - a))
-            ts(g1, size, TH, A.is_gt, ["size%d" % part, "TH"], ["g%d" % part], ns=cyc(b - a))
-            mm([(P[7][:, 0:b - a], T.BK[:], g1)], ["BK", "g%d" % part], 7, b - a)
-        else:
-            g2 = gb[:, 960 + a:960 + b]
-            ts(g1, qf, TH, A.is_gt, [qn, "TH"], ["g%d" % part], ns=cyc(b - a))
-            ts(g2, qf, T.NT[:, 0:1], A.is_lt, [qn, "NTH"], ["h%d" % part], ns=cyc(b - a))
-            mm([(P[7][:, 0:b - a], T.BK[:], g1), (P[7][:, 0:b - a], T.BK[:], g2)], ["BK", "g%d" % part, "h%d" % part], 7, 2 * (b - a))
-        ts(nn, P[7][:, 0:b - a], wcol(20), A.is_ge, ["P7", "WS"], ["nn%d" % part], wcol(21), A.mult, cyc(b - a))
-        tt(ST[:, 0:TW].indirect(eU[:, c0:c1]), nn, base[:, a:b], A.add, ["nn%d" % part, "base", "eU"], STw, ind(b - a, SC))
+        g1, nn, g2 = [gb[:, o + a:o + b] for o in (0, 320, 960)]
+        qf, qn = LG[:, BL * r + 6 * a:BL * r + 6 * b:6], "QA%d_%d" % (r, part)
+        ts(g1, qf, TH, A.is_gt, [qn, "TH"], ["g%d" % part], ns=cyc(b - a))
+        ts(g2, qf, T.NT[:, 0:1], A.is_lt, [qn, "NTH"], ["h%d" % part], ns=cyc(b - a))
+        mm([(P[7][:, 0:b - a], T.BK[:], g1), (P[7][:, 0:b - a], T.BK[:], g2)], ["BK", "g%d" % part, "h%d" % part], 7, 2 * (b - a))
+        ts(nn, P[7][:, 0:b - a], wcol(cTH), A.is_ge, ["P7", "WS"], ["nn%d" % part], wcol(cNN), A.mult, cyc(b - a))
 
-    def tell(part):
-        a, b = PARTS[part][0:2]
-        for k in range(4):
-            l0 = PORTS[4 * part + k][2]
-            tt(T.G[:, 0:GW].indirect(faceU[:, l0:l0 + (b - a) // 16]), gb[:, 320 + a:320 + b], base[:, a:b], A.add,
-               ["nn%d" % part, "base", "faceU", "Gz"], Gs, ind(b - a, SC))
+    def new_fields(part):
+        a, b, c0, c1 = PARTS[part]
+        tt(ST[:, 0:SL].indirect(eU[:, c0:c1]), gb[:, 320 + a:320 + b], base[:, a:b], A.add, ["nn%d" % part, "base%d" % part, "eU%d" % part], STw, ind(b - a, SC))
 
     def new_q(r, part):
         a, b = PARTS[part][0:2]
-        o = LO + QS * r
-        tt(P[0][:, a:b], QA[:, o + a:o + b], P[0][:, a:b], A.subtract, ["QA%d_%d" % (r, part), "P0"], ["P0"], cyc(b - a))
-        tt(QB[:, o + a:o + b], P[0][:, a:b], qe[:, 640 + a:640 + b], A.mult, ["P0", "inv%d" % part], ["QB%d_%d" % (r, part)], cyc(b - a))
+        bank, o = OWN[part]
+        old = P[bank][:, o:o + b - a]
+        tt(old, LG[:, BL * r + 6 * a:BL * r + 6 * b:6], old, A.subtract, ["P%d" % bank, "QA%d_%d" % (r, part)], ["P%d" % bank], cyc(b - a))
+        tt(LG[:, BL * r + 6 * a + 1:BL * r + 6 * b:6], old, qe[:, 640 + a:640 + b], A.mult, ["P%d" % bank, "inv%d" % part], ["QB%d_%d" % (r, part)], cyc(b - a))
 
     def last_addresses():
-        cp(ST[:, 0:TW].indirect(eU), base, ["base", "eU"], STw, ind(CAP, SC))
-        cp(T.pk1[:], ST[:, 0:V].indirect(T.rimU[:, 0:14]), ["STl", "rimU"], ["pk1"], ind(FP), "a")
-        rim_address(7, T.rimK[:, 16:30], "rimL")
+        cp(ST[:, 0:SL].indirect(eU[:]), base, ["base0", "base1", "eU0", "eU1"], STw, ind(CAP, SC))
+        cp(T.pk1[:], ST[:, 0:V].indirect(T.rimU[:, 0:14]), STs + ["rimU"], ["pk1"], ind(FP), "a")
+        listed(7, 0, T.ZP, T.pk1, 14, ["pk1", "ZP"])
+        tt(T.ryF[:, 0:14], P[7][:, 0:14], T.rimK[:, 16:30], A.add, ["P7", "rimL"], ["ryF"])
+        cp(T.ryU[:, 0:14], T.ryF[:, 0:14], ["ryF"], ["ry0"])
         own_a, fa, fb = [T.PE[:, FP * k:FP * k + FP] for k in range(3)]
-        mm([(P[7][:, 0:FP], T.ZQ[:, 12 - 4 * m:140 - 4 * m], ST[:, m:V:4]) for m in range(4)], ["ZQ", "STl"], 7, 4 * FP)
-        ac(own_a, P[7][:, 0:FP], ["P7"], ["PE"], bias=float(LO), ns=cyc(FP))
-        mm([(P[7][:, 0:56], T.ZR[:, 15 - i:143 - i], ST[:, i:V:16]) for i in range(16)], ["ZR", "STl"], 7, 1024)
-        ts(qyU, P[7][:, 0:56], float(LO), A.add, ["P7"], ["qyU"])
-        neighbours()
-        mm([(P[6][:, 0:FP], ZF, T.KN[:])], ["ZF", "KN"], 6, FP, 4, stop=False)
-        by_slot(6, T.ZP, "ZP")
-        tt(fa, P[6][:, 0:FP], own_a, A.is_gt, ["P6", "PE"], ["fa"], cyc(FP))
-        tt(fb, P[6][:, 0:FP], fa, A.mult, ["P6", "fa"], ["fb"], cyc(FP))
-        cp(T.adU[:], fb, ["fb"], ["adU"], cyc(FP))
-
-    late, marks = [], {}
-    for r in range(1, RO + 1):
-        who_acts(r)
-        if r == RO:
-            last_addresses()
-        for step in ORDER.split():
-            if step != "out":
-                flux(r, int(step[1]), step[0])
-                continue
-            if r == RO:
-                pack_y(7, r, FF[:, 0:8 + 4 * FP], ["FF0", "F0", "F1", "F2", "F3"], -1.0)
-            new_fields(r, 0)
-            if r < RO:
-                message1(r)
-                neighbours()
-        new_fields(r, 1)
-        if r < RO:
-            tell(1)
-        new_q(r, 0)
-        if r < RO:
-            pack_q(r)
-            rim_address(6, T.rimK[:, 0:14], "rimK")
-        new_q(r, 1)
-        first = len(nodes)
-        sums(r, 0)
-        sums(r, 1)
-        late.append((first, len(nodes), r + 1))
-        if r < RO:
-            pack_y(6, r, LG[:, 0:LO + BLKW * r + 1280], lgw(r) + ["LG%d_%d" % (r, j) for j in range(8)], 1.0)
-
-    for W, nm, y, to, names in ((QA, "QA", T.y0, qe, ["q0e0", "q0e1", "q1e0", "q1e1", "inv0", "inv1"]), (QB, "QB", T.y1, cq, ["q1n%d" % s for s in range(6)])):
-        op({"x": 1.0}, None, [], names + [nm + "y0", nm + "y1"], 1.0, None)
+        mm([(P[7][:, 0:FP], T.ZQ[:, 12 - 4 * m:140 - 4 * m], ST[:, m:V:4]) for m in range(4)], ["ZQ"] + STs, 7, 4 * FP)
+        ac(own_a, P[7][:, 0:FP], ["P7"], ["PE"], bias=4.0, ns=cyc(FP))
+        listed(7, 0, T.ZX, ST, 56, ["ZX"] + STs)
         for k in range(2):
-            cp(to[:, 448 * k:448 * k + 448], W[:, 0:LO + QS * RO + CAP].indirect(qyU[:, 28 * k:28 * k + 28]),
-               qw(nm, RO - 1) + ["%s%d_%d" % (nm, RO, j) for j in range(2)] + ["qyU"], [nm + "y%d" % k], ind(448), "av")
-        store("s", y[:], to[:, 0:V], [nm + "y0", nm + "y1"])
+            ts(T.qyU[:, 56 * k:56 * k + 56], P[7][:, 0:56], float(k), A.add, ["P7"], ["qyU%d" % k])
+        neighbours(True, True)
+        far = P[6][:, 14:FP + 14]
+        mm([(far, NBI, aK), (far, NBI, aF2)], ["Z64", "aK", "aF2"], 6, 2 * FP, stop=False)
+        by_slot(6, T.ZX, "ZX")
+        tt(fa, far, own_a, A.is_gt, ["P6", "PE"], ["fa"], cyc(FP))
+        tt(fb, far, fa, A.mult, ["P6", "fa"], ["fb"], cyc(FP))
+        ts(T.adU[:], fb, 2 - ZC + 6.0 / 64, A.add, ["fb"], ["adU"], ns=cyc(FP))
+
+    for r in range(1, RO + 1):
+        marks["round", r] = len(nodes)
+        own_control(r)
+        for step in ORDER.split():
+            if step[0] in "gfmb":
+                flux(r, int(step[1]), step[0])
+            elif step[0] == "e":
+                old_q(r, int(step[1]))
+            elif step[0] == "a":
+                addresses(r, int(step[1]))
+            elif step == "x":
+                far_control(r)
+            elif step[0] == "o":
+                old_fields(r, int(step[1]))
+            elif step == "q":
+                new_q(r, 1)
+            elif step == "s":
+                new_step(r, 1)
+            elif step == "n":
+                if r == RO:
+                    last_addresses()
+                new_fields(1)
+            else:
+                sums(r, 1)
+        if r == RO:
+            ac(T.pk2[:, 0:FP], FF[:, 0:8 + 4 * FP].indirect(T.ryU[:, 0:14]), ["FF0", "F0", "F1", "F2", "F3", "ry0"], ["pk2_0"], scale=-1.0, ns=ind(FP))
+            shift(7, 0, T.pk2, 0, T.ZF, ["pk2_0", "ZF"], 4)
+            cp(T.snd3[:], P[7][:, 0:FP], ["P7"], ["snd3"], cyc(FP), "a")
+            send(3, r, ["snd3"], "lnd3")
+        new_step(r, 0)
+        marks["step", r] = wr["nn0"]
+        new_fields(0)
+        nodes[-1]["ends"] = r
+        if r < RO:
+            message1(r)
+        behind(("G", r + 1), new_q, r, 0)
+        behind(("G", r + 1), sums, r, 0)
+
+    full = log(RO, 0)
+    for j, (y, to, names) in enumerate(((T.y0, qe, ["q0e0", "q0e1", "q1e0", "q1e1", "inv0", "inv1"]), (T.y1, cq, ["q1n%d" % s for s in range(6)]))):
+        op({"x": 1.0}, None, [], names + ["y%d0" % j, "y%d1" % j], 1.0, None)
+        for k in range(2):
+            cp(to[:, 448 * k:448 * k + 448], upto(RO, 0).indirect(T.qyU[:, 56 * j + 28 * k:56 * j + 28 * k + 28]), full + ["qyU%d" % j], ["y%d%d" % (j, k)], ind(448), "av")
+        store("s", y[:], to[:, 0:V], ["y%d0" % j, "y%d1" % j])
     op({"x": 1.0}, None, [], ["r%d" % h for h in range(4)] + ["YT0", "YT1"], 1.0, None)
     for k, (a, b) in enumerate(halves):
-        mm([(P[1 + k][0:16, 0:b - a], T.Wy[:, 0:16], ST[:, a:b])], ["Wy0", "Wy1", "STl"], 1 + k, b - a)
+        mm([(P[1 + k][0:16, 0:b - a], T.Wy[:, 0:16], ST[:, a:b])], ["Wy0", "Wy1"] + STs, 1 + k, b - a)
         cp(rr[0:16, a:b], P[1 + k][0:16, 0:b - a], ["P%d" % (1 + k)], ["YT%d" % k], cyc(b - a), "a")
     for j in range(2):
         store("s", T.yt[:, V * j:V * j + V], rr[8 * j:8 * j + 8, 0:V], ["YT0", "YT1"])
     M = WK
     used = [x + h for x in ("wn", "un", "we", "ue", "sq") for h in "0123"]
     Ms = ["M%d" % k for k in range(NG)]
-    full = lgw(RO) + ["LG%d_%d" % (RO, j) for j in range(8)] + ["adU"]
     op({"x": 1.0}, None, [], used + Ms, 1.0, None)
-    op({"x": 1.0}, None, [], ["size0", "size1"] + ["YM%d" % k for k in range(4)], 1.0, None)
     for k in range(NG):
         w_ = FP // NG
-        cp(M[:, 16 * w_ * k:16 * w_ * (k + 1)], LG[:, 0:LO + BLKW * RO + 1280].indirect(T.adU[:, w_ * k:w_ * (k + 1)]), full, [Ms[k]], ind(16 * w_), "av")
-    Mr = T.pk2[:, 0:FP]
-    cp(Mr, M[:, 0:4 * V].indirect(T.rimS[:, 0:14]), Ms + ["rimS"], ["pk2_0"], ind(FP), "av")
-    tt(M[:, 0:4 * V].indirect(T.rimS[:, 0:14]), Mr, LG[:, LO + BLKW * RO + 1280:LO + BLKW * (RO + 1)], A.add, ["pk2_0", "LGh%d" % RO, "rimS"], Ms, ind(FP, SC))
+        cp(M[:, 16 * w_ * k:16 * w_ * (k + 1)], upto(RO, 0, ZC).indirect(T.adU[:, w_ * k:w_ * (k + 1)]), full + ["adU"], [Ms[k]], ind(16 * w_), "av")
+    Mr = T.pk2[:, FP:2 * FP]
+    cp(Mr, M[:, 0:4 * V].indirect(T.rimS[:, 0:14]), Ms + ["rimS"], ["pk2_1"], ind(FP), "av")
+    tt(M[:, 0:4 * V].indirect(T.rimS[:, 0:14]), Mr, T.lnd3[:], A.add, ["pk2_1", "lnd3", "rimS"], Ms, ind(FP, SC))
     for k in range(4):
         a, pb, nm, ms_ = V * k, P[3 + k % 2][:, 0:FP], "P%d" % (3 + k % 2), Ms[2 * k:2 * k + 2]
         if k == 3:
@@ -829,9 +1046,12 @@ def rank_program(g, core, T, topo):
             tt(po[:, FP * k:FP * k + FP], pb, M[:, a + 3:a + V:4], A.add, ms_ + [nm], ["YM%d" % k], cyc(FP))
         store("sa"[k % 2], T.ym[:, FP * k:FP * (k + 1)], po[:, FP * k:FP * (k + 1)], ["YM%d" % k])
 
-    for a, b, r in late:
+    for a, b, mark in soft:
         for nd in nodes[a:b]:
-            nd["soft"] = marks.get(r, set())
+            nd["key"] = marks[mark] + 0.5 + 1e-5 * nd["key"] if mark in marks else nd["key"]
+    for k, nd in enumerate(nodes):
+        size = marks["round", 3] - marks["round", 2]
+        nd["twin"] = divmod(k - marks["round", 2], size) if marks["round", 2] <= k < marks["round", RO] else None
     seen = {e: {} for e in Q}
 
     def need(e, toks):

@@ -3,32 +3,47 @@ from concourse.bass import DstId, RemoteDMATransfer
 from concourse.mybir import AluOpType as A, ActivationFunctionType as AF
 
 V, FP, CAP, RO = 896, 224, 320, 5
-NR = CAP - FP
+W = CAP // 16
 F, H, I, U = "float32", "bfloat16", "int32", "uint16"
-fS, fEL, fEH, fT, fM, fD, fR, fJL, fJH, fP, fQ = 0, 4, 5, 6, 7, 8, 9, 10, 11, 12, 13
-BL, LND, ZC = 2688, 1920, 2592
+fS, fK, fEL, fEH, fT, fM, fD, fJL, fJH, fQ = 0, 4, 8, 9, 10, 11, 12, 13, 14, 15
+PAD = 4
+FW = 10 * FP + 24
 SL = V + CAP
-CF0, CB0 = V, V + 8 * FP
-BIG, B2 = 4096.0, 8192.0
-NW = 77
-cWO, cWN, cWF = 22, 38, 54
-cS, cX, cZJ, cTH, cNN, cKP, cD, cB4, cR, cT, cEL, cPL, cQ4, cXR = range(63, NW)
+BIG = 4096.0
+R16, R32, R8192 = 1.5 * 2 ** 27, 1.5 * 2 ** 28, 1.5 * 2 ** 36
+NA, NB = 25, 22
+cWO, cWN = 48, 64
+cS, cX, cZJ, cTH, cNN, cKP, cD, cB4, cR, cT, cEL, cI1, cI2, cV, cVN, cSG = range(80, 96)
+NW = cSG + 4
+SCALES = (0.5, 1.5, 2.5, 3.5, 2.25, 3.75)
+CASES = [(1.0, y - 0.5, [(y, 1, 1.0)]) for y in range(1, 5)] + [(1.0, 1.0, [(2, 2, 2.0)]), (0.5, 1.0, [(3, 2, 4.0), (4, 4, 8.0)]), (0.5, 1.5, [(4, 2, 4.0)]),
+                                                                (1.5, 2.25, [(3, 3, 2.0)]), (1.5, 3.75, [(4, 3, 2.0)])]
 MSG = [(1, m_) for m_ in range(RO)] + [(2, m_) for m_ in range(RO)] + [(3, RO)]
 MSG.sort(key=lambda x: (x[1], x[0]))
 CYC, PCYC, GA, SC, LAT, DMA, HOP = 0.83, 0.42, 1.5, 3.6, 100.0, 2000.0, 4800.0
-MARGIN, TURNS, WAIT, SLACK, AHEAD = 1500.0, 3, 100.0, 3.0, 0.0
-JV = (1, 3, 5)
-GV = 34
-CUT = (4, 4)
+MARGIN, TURNS, WAIT, SLACK, SHAKE, TWINS = 1500.0, 40, 100.0, 3.0, 300.0, True
+WAYS = ("bbaaaaaaa", "bbbbcccaa")
+TBANK = (5, 6, 0)
+GV = 28
+SPLIT = 2
 VADD, VMIN, AADD, PFIX, CROSS = 0.0, 53.0, 66.0, 20.0, 120.0
-URGE = 1500.0
 WIDE, FIRST, T2, T3, ONCE = 4000.0, 1.4, 1.5, 2.0, 3000.0
-MOVES = ((None, 1, 26000), (1, 3, 36000), (4, None, 15000))
-STEP, HEAT, SEED = (0.0, 300.0, 600.0, 2500.0), 120.0, 1
-GFQ = "av"
-ORDER = "a1 e1 g4 g5 x a0 f4 f5 g0 e0 g1 m4 g2 m5 g3 f0 f1 b4 o1 b5 m0 q f2 m1 f3 b0 m2 b1 m3 s o0 b2 n b3 l"
-SNQ = "av"
-SA = (2, 3, 4, 5)
+MOVES = ((1, 3, 45000), (None, 2, 45000), (3, None, 35000))
+STEP, HEAT, SEED, MEAN, ASIDE, BEYOND = (0.0, 300.0, 600.0, 2500.0), 50.0, 3, 0.3, 0.4, 8000.0
+ORDER = "f a e o g0 g1 m0 g2 m1 b0 g3 m2 b1 m3 n b2 b3"
+LS = 2
+SLOT = (0, 1, 2, 0)
+
+
+def base(r):
+    return V + (CAP + PAD) * (r - 1) + PAD
+
+
+def place_of(y, m):
+    return y + min(6 * m, 19)
+
+
+NREC = base(RO) + CAP
 
 
 def sb(n, t):
@@ -36,27 +51,26 @@ def sb(n, t):
 
 
 SCRATCH = {
-    "ST": sb(SL + RO * FP, H), "C": sb(3456, H), "TK": sb(2560, F), "G": sb(FP + 4 * V, H), "GF": sb(V + 2 * FP, H), "GO": sb(CAP, H),
-    "RR": sb(V, H), "RF": sb(FP, H), "FT": sb(V, H), "LG": sb(RO * BL + LND, F),
-    "snd1": sb(5 * FP, H), "snd2": sb(5 * 3 * FP, F), "snd3": sb(FP, F), "lnd3": sb(FP, F),
-    "qa": sb(V, H), "qb": sb(V, H), "TD": sb(V, I), "TB": sb(V, H), "TH": sb(8, F),
-    "PI": sb(FP, I), "RI": sb(32, I), "RJ": sb(32, I), "rimU": sb(16, U), "rimS": sb(16, U), "rimK": sb(32, F), "ryF": sb(16, F), "ryU": sb(48, U),
-    "s0": sb(6 * FP, I), "SI": sb(FP, F), "colU": sb(2 * FP, U), "KN": sb(FP, F), "AB": sb(8 * FP + 16, H), "PE": sb(3 * FP, F), "adU": sb(FP, U),
-    "Pi": sb(8, I), "CI": sb(8, I), "CF": sb(32, F), "MK": sb(32, F), "BR": sb(8, F), "RW": sb(16 * NW, H), "E1": sb(144 + 256, H),
-    "WS": sb(80, F), "WB": sb(80, H), "X": sb(256, F), "XB": sb(256, H), "XQ": sb(144, F), "X16": sb(128, F), "CR": sb(512, H), "PT": sb(256 + 3 * CAP, H),
-    "HI": sb(V + 64, H), "Wt": sb(128, H), "Wo": sb(128, H), "WN": sb(144, H), "ZJ": sb(240, H), "ZI": sb(256, H), "ZF": sb(240, F), "NI": sb(128, F),
-    "ZE0": sb(144, H), "ZO0": sb(144, H), "ZA0": sb(144, H), "ZE": sb(144, H), "ZX": sb(144, H), "ZP": sb(144, H), "ZO": sb(144, H), "ZQ": sb(144, H),
-    "Z2": sb(144, H), "ZA": sb(4 * 144, H), "BK": sb(128, H), "TR": sb(13 * 128, H), "Wb": sb(128, H), "Wy": sb(16, H), "CH": sb(FP, H), "JR": sb(CAP, H),
-    "TRE": sb(56, F), "ONE": sb(56, F), "SX": sb(240, F), "LT": sb(4 * 256, F), "LW": sb(7 * 64, F), "KE": sb(80, F),
-    "bit": sb(FP, H), "can": sb(112, H), "THR": sb(56, F), "v1": sb(4 * 56, F), "posU": sb(72, U), "MF": sb(FP, H), "NB": sb(FP, H),
-    "FN": sb(5 * 56 + 32, U), "FW": sb(2 * 56, F), "FI": sb(32, I), "THF": sb(84, H), "bf": sb(70, F),
-    "UA": sb(180, U), "UB": sb(100, U), "UC": sb(160, U), "eU": sb(20, U), "qyU": sb(112, U), "ki": sb(80, I), "sm": sb(320, F),
-    "qe": sb(960, F), "cq": sb(1280, F), "cb": sb(2688, H), "WK": sb(5 * 832, F), "r": sb(2 * 832, F), "FF": sb(1288, F), "xx": sb(832, F),
-    "po": sb(V, F), "gb": sb(4 * 320, H), "NT": sb(8, F), "pk1": sb(FP, H), "pk2": sb(3 * FP, F),
+    "ST": sb(SL + RO * FP, H), "C": sb(V + 8 * CAP, H), "G": sb(4 * V + FP, H), "GO": sb(CAP, H),
+    "RR": sb(V, H), "TAB": sb(10 * base(RO) + FW, F), "Q0": sb(NREC, F), "Q1": sb(NREC, F), "OUT": sb(4 * (NREC - V), F),
+    "snd1": sb(5 * FP, H), "snd2": sb(3 * FP, F), "lnd2": sb(LS * 3 * FP, F), "MEM": sb(FP + 8, F),
+    "TD": sb(V, I), "TH": sb(8, F),
+    "PI": sb(FP, I), "RI": sb(32, I), "RJ": sb(48, I), "rimU": sb(32, U), "rimS": sb(16, U), "rimK": sb(48, F), "ryF": sb(128, F), "ryU": sb(80, U),
+    "colU": sb(FP, U), "AB": sb(5 * FP + 16, H), "adU": sb(FP, U),
+    "Pi": sb(8, I), "CI": sb(8, I), "CF": sb(32, F), "MK": sb(32, F), "BR": sb(16, F), "E1": sb(4 * 144, H),
+    "WS": sb(104, F), "WB": sb(104, H), "CR": sb(512, H), "KR": sb(128, H),
+    "Wt": sb(128, H), "Wo": sb(128, H), "WN": sb(144, H), "ZJ": sb(240, H), "ZI": sb(256, H), "ZF": sb(240, F), "ZS": sb(6 * 128, F), "ZB": sb(6 * 128, H),
+    "ZE0": sb(144, H), "ZO0": sb(144, H), "ZA0": sb(144, H), "ZE": sb(144, H), "ZX": sb(144, H), "ZO": sb(144, H), "ZQ": sb(144, H),
+    "Z2": sb(144, H), "ZA": sb(4 * 144, H), "BK": sb(128, H), "TR": sb(11 * 128, H), "Wb": sb(128, H), "Wy": sb(16, H), "CH": sb(FP, H), "JR": sb(CAP, H),
+    "TRE": sb(56, F), "ONE": sb(56, F), "LT": sb(128, F), "KE": sb(8 * W, F),
+    "bit": sb(FP, H), "can": sb(56, H), "v1": sb(4 * 56, F), "posU": sb(56, U),
+    "UA": sb(8 * W, U), "UC": sb(8 * W, U), "UQ": sb(W, U), "eU": sb(W, U), "qyU": sb(56, U), "sm": sb(34 * W, F),
+    "qe": sb(CAP, F), "r": sb(3 * 2 * CAP, F), "sq": sb(3 * CAP, F), "FF": sb(8 + 4 * CAP, F), "xx": sb(2 * CAP, F),
+    "gb": sb(4 * CAP, H), "NT": sb(8, F), "pk1": sb(2 * FP, H), "pk2": sb(3 * FP, F),
 }
 for _k in range(8):
     SCRATCH["P%d" % _k] = ("psum", [128, 512], F)
-SEMAPHORES = (["v", "a", "p", "g", "loc", "out"] + ["in%d" % k for k in range(8)]
+SEMAPHORES = (["v", "a", "p", "g", "loc", "out"] + ["in%d" % k for k in range(8)] + ["ls%d" % k for k in range(RO)]
               + ["ar%d" % k for k in range(len(MSG))] + ["hs%d" % k for k in range(len(MSG))])
 
 
@@ -91,13 +105,15 @@ def shares(engs, n):
 def piece(T, kind, which, m, a, n):
     w = 96 if which == 2 else 32
     if kind == "lnd":
-        buf, at = ((T.ST, SL + FP * m), (T.LG, BL * m + LND), (T.lnd3, 0))[which - 1]
+        buf, at = (T.ST, SL + FP * m) if which == 1 else (T.lnd2, 3 * FP * (m % LS))
+    elif kind == "hb":
+        buf, at = T.C if which == 1 else T.TAB, m * 3 * FP
     else:
-        buf, at = T["snd%d" % which], (m % RO) * 7 * w
+        buf, at = (T.snd1, m * FP) if which == 1 else (T.snd2, 0)
     return buf[:, at + w * a:at + w * (a + n)]
 
 
-def forward(g, T, topo, src, r, blocks, kind, first, which, m):
+def forward(g, T, topo, src, r, blocks, kind, first, which, m, left):
     n = len(T.cores)
     sh = shares(topo.engines(src, T.cores[(r + blocks[0] + 1) % n]), len(blocks))
     tr = []
@@ -105,11 +121,11 @@ def forward(g, T, topo, src, r, blocks, kind, first, which, m):
         rid, pid = topo.addr(T.cores[(r + b + 1) % n], src)
         tr.append(RemoteDMATransfer(dst_ids=[DstId(rid=rid, pnc=pid)], dma_engine_mask=mask, remote_sem=T.sem["ar%d" % MSG.index((which, m))],
                                     src=piece(T, kind, which, m, first + j, 1), dst=piece(T, "lnd", which, m, n - 2 - b, 1)))
-    g.remote_dma_fused(tr, local_sem=T.sem.loc)
+    g.remote_dma_fused(tr, local_sem=left)
     return sum(s for _, s in sh)
 
 
-def place(nodes, rank, before, after, urge=0.0):
+def place(nodes, rank, before, after):
     left, at = [len(x) for x in before], {}
     pool, free, due = {e: [] for e in "vapgsx"}, {e: 0.0 for e in "vapgsx"}, {e: [0.0] * len(nodes) for e in "vapgsx"}
     for k, nd in enumerate(nodes):
@@ -121,10 +137,6 @@ def place(nodes, rank, before, after, urge=0.0):
         row = sorted(pool[e], key=lambda k: ((MARGIN if e == "v" and len(nodes[k]["ns"]) > 1 else 0) - rank[k], k))
         k = None
         soon = [(j, ready[j]) for j in row if ready[j] > t]
-        for e2 in "vapg" if e != "x" else "":
-            for j in pool[e2] if e2 != e else ():
-                end = max(free[e2], due[e2][j], t) + nodes[j]["ns"][e2]
-                soon += [(i, max(ready[i], end + lat + CROSS)) for i, lat in after[j] if left[i] == 1 and e in nodes[i]["ns"] and end < t + AHEAD]
         for j in row:
             if ready[j] <= t and (e == "x" or all(t + nodes[j]["ns"][e] <= w + WAIT or rank[i] - rank[j] < SLACK * (w - t + nodes[i]["ns"][e]) for i, w in soon)):
                 k = j
@@ -132,7 +144,7 @@ def place(nodes, rank, before, after, urge=0.0):
         if k is None:
             free[e] = t + 50.0
             continue
-        at[k] = (e, t, t + nodes[k]["ns"][e] + (urge if nodes[k]["out"][0:1] and nodes[k]["out"][0][0:4] == "lnd1" else 0.0))
+        at[k] = (e, t, t + nodes[k]["ns"][e])
         if e != "x":
             free[e] = at[k][2]
         for e2 in nodes[k]["ns"]:
@@ -158,7 +170,7 @@ def polish(nodes, pre, post, at):
         kin.setdefault(nd["twin"][1] if nd["twin"] else -1 - k, []).append(k)
     alike = [kin[nd["twin"][1] if nd["twin"] else -1 - k] for k, nd in enumerate(nodes)]
     key, on = [at[k][1] for k in range(n)], [at[k][0] for k in range(n)]
-    length = (key[kin[0][2]] - key[kin[0][0]]) / 2
+    length = (key[ends[4]] - key[ends[2]]) / 2
     for row in kin.values():
         for i, k in enumerate(row):
             key[k], on[k] = at[row[len(row) // 2]][1] + (i - len(row) // 2) * length, at[row[len(row) // 2]][0]
@@ -179,40 +191,53 @@ def polish(nodes, pre, post, at):
         if late >= 0:
             move(k, late + 0.01, [], n * n)
 
+    order, ns, tail = list(range(n)), [nd["ns"] for nd in nodes], [nd["lat"] for nd in nodes]
+    edges = [[(j, lat, CROSS if lat == LAT else 0.0) for j, lat in row] for row in pre]
+
     def times(first, end, why, goal):
-        order = sorted(range(n), key=lambda k: key[k])
-        last, span, who = {}, 0.0, 0
+        order.sort(key=lambda k: key[k])
+        last, span, who, stop = {}, 0.0, 0, 1e30 if goal is None else key[goal] + BEYOND
         for k in order:
-            if goal is not None and key[k] > key[goal]:
-                return end[goal], end, why, goal
             e = on[k]
             if key[k] >= first:
+                if key[k] > stop:
+                    break
                 t, w = 0.0, None
-                for j, lat in pre[k]:
-                    x = end[j] + lat + (CROSS if lat == LAT and on[j] != e else 0.0)
+                for j, lat, cross in edges[k]:
+                    x = end[j] + lat if on[j] == e else end[j] + lat + cross
                     if x > t:
-                        t, w = x, (j, False)
+                        t, w = x, j
                 j = last.get(e)
                 if j is not None and end[j] >= t and e != "x":
-                    t, w = end[j], (j, True)
-                end[k], why[k] = t + nodes[k]["ns"][e], w
-                if end[k] + nodes[k]["lat"] > span:
-                    span, who = end[k] + nodes[k]["lat"], k
+                    t, why[k] = end[j], (j, True)
+                else:
+                    why[k] = None if w is None else (w, False)
+                t += ns[k][e]
+                end[k] = t
+                if t + tail[k] > span:
+                    span, who = t + tail[k], k
             last[e] = k
-        return span, end, why, who
+        mean = MEAN * sum([end[k] for k in inside]) / len(inside)
+        return (span + mean, end, why, who) if goal is None else (end[goal] + mean, end, why, goal)
 
+    inside = []
     for start, goal, moves in MOVES:
         start, goal = ends.get(start), ends.get(goal)
+        inside[:] = [k for k in range(n) if (start is None or key[k] > key[start]) and (goal is None or key[k] <= key[goal])]
         now = times(-1e30, [0.0] * n, [None] * n, goal)
         best = (now[0], list(key), list(on))
         for turn in range(moves):
             span, end, why, k = now
+            if draw() < ASIDE:
+                k = inside[int(draw() * len(inside))]
             links = []
             while why[k] and (start is None or key[k] > key[start]):
                 if why[k][1]:
                     links.append((why[k][0], k))
                 k = why[k][0]
-            u, v = links[int(draw() * len(links))]
+            if not links:
+                continue
+            u, v = links[int(draw() ** 2 * len(links)) if k != now[3] else int(draw() * len(links))]
             z, undo, both = draw(), [], [k for k in (u, v) if len(nodes[k]["ns"]) > 1]
             turned = both[int(draw() * len(both))] if both and z < 0.15 else None
             if turned is not None:
@@ -251,14 +276,19 @@ def arrange(nodes):
                 lat = 0.0 if nd["tok"] is False or list(nd["ns"]) == list(nodes[j]["ns"]) == ["p"] else nodes[j]["lat"]
                 pre[k].append((j, lat))
                 post[j].append((k, lat))
-        rank, best = [-nd["key"] for nd in nodes], None
+        rank, best, now, seed = [-k for k in range(n)], None, None, SEED
         for turn in range(TURNS):
             at = place(nodes, rank, pre, post)
             span = max(at[k][2] + nodes[k]["lat"] for k in range(n))
             if best is None or span < best[0]:
                 best = (span, at)
-            back = place(nodes, [at[k][2] for k in range(n)], post, pre)
-            rank = [back[k][2] for k in range(n)]
+            if turn < 8 or span < now[0] + SHAKE:
+                now = (span, at)
+            back = place(nodes, [now[1][k][2] for k in range(n)], post, pre)
+            rank = []
+            for k in range(n):
+                seed = (seed * 1103515245 + 12345) % 2147483648
+                rank.append(back[k][2] + (SHAKE * (seed % 2001 / 1000 - 1) if turn > 6 and seed // 4096 % 3 == 0 else 0.0))
         PLACED[n] = polish(nodes, pre, post, best[1])
     span, key, on = PLACED[n]
     for k, nd in enumerate(nodes):
@@ -279,7 +309,7 @@ def rank_program(g, core, T, topo):
                 sent = 0
                 for j, (which, m) in enumerate(MSG):
                     g.wait_ge(T.sem["hs%d" % j], hs[k][1])
-                    sent += forward(g, T, topo, core, r, blocks, "hb", 0, which, m)
+                    sent += forward(g, T, topo, core, r, blocks, "hb", 0, which, m, T.sem.loc)
                 g.wait_ge(T.sem.loc, sent)
         return
     arrive = 0
@@ -287,10 +317,13 @@ def rank_program(g, core, T, topo):
         for src, blocks in [(T.cores[r], plan[r][0])] + plan[r][1]:
             sh = shares(topo.engines(src, T.cores[(r + blocks[0] + 1) % n]), len(blocks))
             arrive += sum(s for b, (_, s) in zip(blocks, sh) if (r + b + 1) % n == rank)
+    hs = shares(topo.engines(core, plan[rank][1][0][0]), 2)
+    leave = sum(s for _, s in hs + shares(topo.engines(core, T.cores[(rank + plan[rank][0][0] + 1) % n]), len(plan[rank][0])))
 
     lay = plan[rank][1][0][1] + plan[rank][1][1][1] + plan[rank][0]
     Q = {"v": g.vector, "a": g.scalar, "p": g.tensor, "g": g, "s": g.sync}
     cnt = {"v": 0, "a": 0, "p": 0, "g": 0, "loc": 0, "out": 0}
+    cnt.update({"ls%d" % k: leave for k in range(RO)})
     nodes, wr, rd = [], {}, {}
 
     def op(ns, fn, reads, writes, lat=LAT, tok=True):
@@ -305,20 +338,17 @@ def rank_program(g, core, T, topo):
             if x in wr:
                 pre.add(wr[x])
             pre.update(rd.get(x, []))
-        nodes.append({"ns": ns, "fn": fn, "pre": pre, "lat": lat, "tok": tok, "out": writes, "soft": set(), "key": k})
+        nodes.append({"ns": ns, "fn": fn, "pre": pre, "lat": lat, "tok": tok, "out": writes})
         for x in reads:
             rd.setdefault(x, []).append(k)
         for x in writes:
             wr[x] = k
             rd[x] = []
 
-    soft, marks = [], {}
+    def meet(names):
+        op({"x": 1.0}, None, [], names, 1.0, None)
 
-    def behind(mark, fn, *args):
-        first = len(nodes)
-        fn(*args)
-        soft.append((first, len(nodes), mark))
-
+    marks = {}
     vec, act, pe = g.vector, g.scalar, g.tensor
     either = [""]
 
@@ -344,9 +374,11 @@ def rank_program(g, core, T, topo):
         op({"v": ns}, lambda e: vec.memset(out, c), [], writes)
 
     def ac(out, a, reads, writes, func=AF.Identity, bias=0.0, scale=1.0, ns=cyc(0), on="a", narrow=False):
-        narrow = narrow or writes[0][0:2] in ("aF", "aS", "SG", "ZA", "ZO", "ZE", "BQ", "ZJ", "ZX", "Wb", "tm", "ZP", "ZQ")
         op({e: ns / 2 if narrow and e == "v" else ns for e in (either[0] or on)},
            lambda e: act.activation(out, a, func, bias=bias, scale=scale) if e == "a" else vec.tensor_scalar(out, a, scale, bias, A.mult, A.add), reads, writes)
+
+    def cut(out, a, scale, reads, writes, ns):
+        op({e: ns for e in "av"}, lambda e: act.activation(out, a, AF.Relu, scale=scale) if e == "a" else vec.tensor_scalar(out, a, scale, 0.0, A.mult, A.max), reads, writes)
 
     def fills(on, parts, reads, writes):
         def fn(e):
@@ -362,17 +394,17 @@ def rank_program(g, core, T, topo):
             return last
         op({"p": cols * wide * PCYC + PFIX * (calls or len(parts))}, fn, reads, ["P%d" % bank])
 
-    def scan(out, first, bank, o, w, reads, writes):
-        op({"v": cyc(w)}, lambda e: vec.tensor_tensor_scan(out, T.ONE[:, 0:w], P[bank][:, o:o + w], first, A.mult, A.add), reads + ["ONE", "P%d" % bank], writes)
-
-    def iota(out, pat, base, cm, writes, exact=False, c=64, reads=()):
+    def iota(out, pat, base_, cm, writes, exact=False, c=64, reads=()):
         if exact:
-            op({"g": 130 + 2 * c * CYC}, lambda e: g.iota(out, pat, base, cm), list(reads), writes)
+            op({"g": 130 + 2 * c * CYC}, lambda e: g.iota(out, pat, base_, cm), list(reads), writes)
         else:
-            op({"g": 130 + 2 * c * CYC}, lambda e: g.iota(out, pat, base, cm, allow_small_or_imprecise_dtypes=True), list(reads), writes)
+            op({"g": 130 + 2 * c * CYC}, lambda e: g.iota(out, pat, base_, cm, allow_small_or_imprecise_dtypes=True), list(reads), writes)
 
-    def sel(out, a, cmp, fill, base, cm, reads, writes, step=1):
-        op({"g": 170 + 256 * CYC}, lambda e: g.affine_select(out, a, [[step, 128]], cmp, fill, base, cm), reads, writes)
+    def zero(buf, a, b, writes, reads=()):
+        iota(buf[:, a:b], [[0, b - a]], 0, 0, writes, c=b - a, reads=reads)
+
+    def sel(out, a, cmp, fill, base_, cm, reads, writes, step=1):
+        op({"g": 170 + 256 * CYC}, lambda e: g.affine_select(out, a, [[step, 128]], cmp, fill, base_, cm), reads, writes)
 
     def load(e, k, out, src, name, turn=1):
         def fn(_):
@@ -387,654 +419,599 @@ def rank_program(g, core, T, topo):
         op({e: 60.0}, fn, reads, [], DMA, None)
 
     def send(which, m, reads, lands):
+        left = "ls%d" % m if which == 2 else "loc"
+
         def fn(_):
-            hs = shares(topo.engines(core, plan[rank][1][0][0]), 2)
             tr = []
             for (h, blocks), (mask, s) in zip(plan[rank][1], hs):
                 rid, pid = topo.addr(h, core)
                 tr.append(RemoteDMATransfer(dst_ids=[DstId(rid=rid, pnc=pid)], dma_engine_mask=mask, remote_sem=T.sem["hs%d" % MSG.index((which, m))],
                                             src=piece(T, "snd", which, m, lay.index(blocks[0]), len(blocks)), dst=piece(T, "hb", which, m, 0, len(blocks))))
-                cnt["loc"] += s
-            g.remote_dma_fused(tr, local_sem=T.sem.loc)
-            cnt["loc"] += forward(g, T, topo, core, rank, plan[rank][0], "snd", lay.index(plan[rank][0][0]), which, m)
+            g.remote_dma_fused(tr, local_sem=T.sem[left])
+            forward(g, T, topo, core, rank, plan[rank][0], "snd", lay.index(plan[rank][0][0]), which, m, T.sem[left])
+            cnt["loc"] += leave * (left == "loc")
         op({"g": ONCE if (which, m) == (1, 0) else 1000.0}, fn, reads, ["sent"], 1.0, None)
         op({"x": HOP * (FIRST if m == 0 else 1) - 1000.0 + (WIDE if which == 2 else 0.0)}, None, ["sent"], [lands], 1.0, ("ar%d" % MSG.index((which, m)), arrive))
+        if which == 2:
+            op({"x": HOP}, None, ["sent"], ["snd2"], 1.0, (left, leave))
         rd["sent"] = []
 
     P = [T["P%d" % k] for k in range(8)]
-    ST, LG, WS, WB, CF = T.ST, T.LG, T.WS, T.WB, T.CF
+    ST, TAB, OUT, WS, WB, CF = T.ST, T.TAB, T.OUT, T.WS, T.WB, T.CF
+    QQ = (T.Q0, T.Q1)
+    NT = sum(len(c_[2]) for c_ in CASES)
 
-    def log(r, landed):
-        return (["T0a", "T0b", "TZ"] + ["TZ%d" % k for k in range(r)] + ["%s%d_%d" % (x, k, j) for k in range(1, r + 1) for x, c_ in (("QA", 2), ("QB", 2), ("LG", 8)) for j in range(c_)]
-                + ["lnd2_%d" % k for k in range(r + landed)])
+    def qlog(j, r):
+        return QQ[j][:, 0:base(r + 1) - PAD], ["Q%d_%d" % (j, k) for k in range(r + 1)]
 
-    def upto(r, landed, first=0):
-        return LG[:, first:BL * r + (ZC if landed else LND)]
+    def olog(r, far):
+        return (OUT[:, 0:4 * (base(r + 1) - V + (FP if far else -PAD))],
+                ["OZ1"] + ["O%d_%d" % (k, j) for k in range(1, r + 1) for j in range(4)] + ["MF%d" % (r + 1)] * far)
+
+    def tlog(r):
+        return TAB[:, 0:10 * base(r + 1) + FW], ["TZ0"] + ["T%d_%d" % (k, j) for k in range(r + 1) for j in range(NT * (1 if k else 2))] + ["TF%d" % (r + 1)]
+
+    def record(j, r):
+        return QQ[j][:, base(r):base(r) + CAP], "Q%d_%d" % (j, r)
 
     def wcol(k):
         return WS[:, k:k + 1]
 
-    def W1(f):
-        return T.E1[0:1, 15 - f:143 - f]
+    def W1(f, k=0):
+        return T.E1[0:1, 144 * k + 15 - f:144 * k + 143 - f]
 
-    cI, cG, cQ, cK, cP, cM, cE, nE, cO, n16, cF1, cF2, c12, c8, c2, cA, nS, c16, cF3, cF4, cF5 = [CF[:, k:k + 1] for k in range(21)]
-    s0, s1, s2, s3, s4, s5 = [T.s0[:, FP * k:FP * k + FP] for k in range(6)]
-    TRs, TRg, Na, nNa, Pa, nPa, Ka, Kb, NBK, NBI, BQ, tmp, Z128 = [T.TR[:, 128 * k:128 * k + 128] for k in range(13)]
+    def scaled(c, wide_):
+        return ((T.ZF if wide_ else T.ZI)[:, 0:128] if c == 1.0 else (T.ZS if wide_ else T.ZB)[:, 128 * SCALES.index(c):128 * SCALES.index(c) + 128],
+                ("ZF" if wide_ else "ZI0") if c == 1.0 else "%s%d" % ("ZS" if wide_ else "ZB", SCALES.index(c)))
+
+    cI, cG, cQ, cK, cP, cM, cE, nE, cO, n16, c12, c8, c2, cA, nS, cF0, cF1 = [CF[:, k:k + 1] for k in range(17)]
+    s0, s1, s2, s3 = [T.TD[:, FP * k:FP * k + FP] for k in range(4)]
+    TRs, Pa, nPa, Z8, tmp, Wi1, Wi2, Wv, Wvn = [T.TR[:, 128 * k:128 * k + 128] for k in range(9)]
+    SGM = [T.TR[:, 128 * k:128 * k + 128] for k in (9, 10)] + [T.ZA[:, 144 * k:144 * k + 128] for k in (0, 1)]
     ZF, ZI = T.ZF[:, 0:128], T.ZI[:, 0:128]
-    EA, EB = T.E1[0:1, 144:272], T.E1[0:1, 272:400]
     halves, wide = ((0, V // 2), (V // 2, V)), ((0, 512), (512, V))
+    spare = 10 * base(4) + 64
+    X, XQ, X16, SI, LW = [TAB[:, spare + a:spare + b] for a, b in ((0, 256), (256, 400), (400, 528), (528, 752), (752, 1008))]
+    early = ["X", "XQ", "X16", "SI", "ty", "td", "th_", "tb"]
+    RW, HI, PT, XB = T.G[0:1, 0:16 * NW], T.G[0:1, 1920:1920 + V + 64], T.G[0:1, 2880:2880 + 128], T.G[0:1, 3008:3008 + 256]
+    PJ, TB = T.C[0:1, 0:768], T.RR
+    qa, qb = T.gb[:, 0:V], T.snd1[:, FP:FP + V]
 
     load("s", 6, T.PI[:], T.port[:], "PI", T2)
     load("a", 1, T.TD[8:16, :], T.d0[:], "TD1")
     load("s", 0, T.TD[0:8, :], T.t0[:], "TD0")
     load("a", 3, T.RI[:, 0:14], T.rim[:], "RI")
     load("s", 2, T.TD[16:24, :], T.d0[:], "TD2")
-    load("s", 4, T.qa[:], T.q0[:], "qa", T3)
-    load("s", 5, T.qb[:], T.q1[:], "qb", T3)
+    load("s", 4, qa, T.q0[:], "qa", T3)
+    load("s", 5, qb, T.q1[:], "qb", T3)
     load("s", 7, T.TH[:, 0:1], T.th[:], "TH", T3)
 
     ms(T.Wt[0:24, :], 0.0, ["Wt"])
-    ms(T.RW[0:1, :], 0.0, ["RW0"], cyc(8 * NW))
-    ms(T.E1[0:1, :], 0.0, ["E1"], cyc(200))
+    ms(RW, 0.0, ["RW0"], cyc(8 * NW))
+    ms(T.E1[0:1, :], 0.0, ["E1"], cyc(288))
     iota(cP, [[0, 1]], 0, 1, ["cP"], c=1)
-    for base, fill in ((-fT, 1.0), (128 - fD, -1.0), (256 - fD, 1.0), (256 - fM, 1.0)):
-        sel(T.Wt[0:24, :], T.Wt[0:24, :], A.not_equal, fill, base, -16, ["Wt"], ["Wt"])
-    iota(T.X[:], [[1, 256]], 0, 0, ["X"], c=256)
-    iota(T.PT[0:1, 0:128], [[-96, 4], [3, 32]], 64, 0, ["PT0"], c=128)
+    for base_, fill in ((-fT, 1.0), (128 - fD, -1.0), (256 - fD, 1.0), (256 - fM, 1.0)):
+        sel(T.Wt[0:24, :], T.Wt[0:24, :], A.not_equal, fill, base_, -16, ["Wt"], ["Wt"])
+    iota(X, [[1, 256]], 0, 0, ["X"], c=256)
+    iota(PT, [[-32, 4], [1, 32]], 64 + PAD, 0, ["PT"], c=128)
     iota(T.Pi[:, 0:1], [[0, 1]], 0, 1, ["Pi"], True, 1)
-    iota(T.XQ[:], [[1, 36], [0, 4]], 0, 0, ["XQ"], c=144)
-    iota(T.X16[:], [[1, 8], [0, 16]], 0, 0, ["X16"], c=128)
-    iota(T.SI[:], [[16, FP]], 15, 1, ["SI"], c=FP)
+    iota(XQ, [[1, 36], [0, 4]], 0, 0, ["XQ"], c=144)
+    iota(X16, [[1, 8], [0, 16]], 0, 0, ["X16"], c=128)
+    iota(SI, [[16, FP]], 15, 1, ["SI"], c=FP)
     iota(T.TRE[:], [[16, 56]], 0, 1, ["TRE"])
-    iota(T.PT[0:1, 128:256], [[0, 8], [1, 16]], 0, 0, ["PT1"], c=128)
-    fills("v", [(T.E1[0:1, 15:144:16], None, 1), (EA[:, fEL:128:16], None, 1), (EA[:, fJL:128:16], None, 2),
-                (EB[:, fEH:128:16], None, 1), (EB[:, fJH:128:16], None, 2)], [], ["E1"])
+    fills("v", [(T.E1[0:1, 144 * k + 15:144 * k + 144:16], None, k / 32 if k else 1) for k in range(4)], [], ["E1"])
     ts(cM, cP, 16.0, A.is_ge, ["cP"], ["cM"], 2.0, A.mult)
-    fills("v", [(T.HI[0:1, V:V + 32], None, 19), (T.HI[0:1, V + 32:V + 64], None, 16)], [], ["HJ"])
-    ts(T.TB[0:24, :], T.TD[0:24, :], CF[0:24, 5:6], A.max, ["TD0", "TD1", "TD2", "cM"], ["TB"], ns=cyc(V))
+    fills("v", [(HI[:, V:V + 32], None, V // 128 + 1), (HI[:, V + 32:V + 64], None, V // 128)], [], ["HJ"])
+    ts(TB[0:24, :], T.TD[0:24, :], CF[0:24, 5:6], A.max, ["TD0", "TD1", "TD2", "cM"], ["TB"], ns=cyc(V))
+
     def relay(e):
         for j, b in enumerate(lay):
             last = vec.tensor_copy(T.RI[:, 16 + 2 * j:18 + 2 * j], T.RI[:, 2 * b:2 * b + 2])
         return last
     op({"v": 7 * VMIN}, relay, ["RI"], ["RP"])
     ts(T.RJ[:, 0:14], T.RI[:, 16:30], 2, A.arith_shift_right, ["RP"], ["RJ0"])
-    ts(T.ZI[:, 0:128], T.X[:, 0:128], cP, A.is_equal, ["X", "cP"], ["ZI0"], ns=cyc(128))
-    ts(T.ZI[:, 128:256], T.X[:, 0:128], cP, A.is_equal, ["X", "cP"], ["ZI"], ns=cyc(128))
-    cp(T.rimU[:, 0:14], T.RJ[:, 0:14], ["RJ0"], ["rimU"])
+    ts(T.ZI[:, 0:128], X[:, 0:128], cP, A.is_equal, ["X", "cP"], ["ZI0"], ns=cyc(128))
+    ts(T.ZI[:, 128:256], X[:, 0:128], cP, A.is_equal, ["X", "cP"], ["ZI"], ns=cyc(128))
+    rimU, rimN, rimS = T.rimU[:, 0:14], T.rimU[:, 16:30], T.rimS[:, 0:14]
+    cp(rimU, T.RJ[:, 0:14], ["RJ0"], ["rimU"])
+    ts(T.RJ[:, 32:46], T.RI[:, 0:14], 2, A.arith_shift_right, ["RI"], ["RJ2"])
+    cp(rimN, T.RJ[:, 32:46], ["RJ2"], ["rimN"])
+    cp(rimS, T.RI[:, 0:14], ["RI"], ["rimS"])
     for k, (a, b) in enumerate(wide):
-        mm([(P[k][:, 0:b - a], T.Wt[0:24, :], T.TB[0:24, a:b])], ["Wt", "TB"], k, b - a)
+        mm([(P[k][:, 0:b - a], T.Wt[0:24, :], TB[0:24, a:b])], ["Wt", "TB"], k, b - a)
         cp(ST[:, a:b], P[k][:, 0:b - a], ["P%d" % k], ["ST%d" % k], cyc(b - a), "av"[k])
     for j, b in enumerate(lay):
-        mm([(P[4][:, 32 * j:32 * j + 32], W1(fJL), T.PT[0:1, 32 * (b % 4):32 * (b % 4) + 32]),
-            (P[4][:, 32 * j:32 * j + 32], W1(fJH), T.HI[0:1, V + 32 * (b // 4):V + 32 * (b // 4) + 32])], ["E1", "PT0", "HJ"], 4, 128)
+        mm([(P[4][:, 32 * j:32 * j + 32], W1(fJL), PT[:, 32 * (b % 4):32 * (b % 4) + 32]),
+            (P[4][:, 32 * j:32 * j + 32], W1(fJH), HI[:, V + 32 * (b // 4):V + 32 * (b // 4) + 32])], ["E1", "PT", "HJ"], 4, 128)
     cp(T.CH[:], P[4][:, 0:FP], ["P4"], ["CH"], cyc(FP), "a")
     up, runs = 32 * (n - 1 - rank), []
     for j, b in enumerate(lay):
         o = 112 if 32 * b < up else 16
         runs = runs[:-1] + [(runs[-1][0], 32 * j + 32, o)] if runs and runs[-1][2] == o else runs + [(32 * j, 32 * j + 32, o)]
     STs = ["ST0", "ST1"]
+    pkL, pkN = T.pk1[:, 0:FP], T.pk1[:, FP:2 * FP]
 
-    def shift(bank, o_, src, a, Z, reads, wide, fresh=True):
-        mm([(P[bank][:, o_ + lo:o_ + hi], Z[:, o:o + 128], src[:, a + lo:a + hi]) for lo, hi, o in runs],
-           reads, bank, FP + 32, wide, "each" if fresh else False, "each" if fresh else True, 3)
+    def shift(bank, src, Z, reads, wide, fresh=True):
+        mm([(P[bank][:, lo:hi], Z[:, o:o + 128], src[:, lo:hi]) for lo, hi, o in runs], reads, bank, FP + 32, wide, "each" if fresh else False, "each" if fresh else True, 3)
+
+    def rim_fields():
+        cp(pkL, ST[:, 0:V].indirect(rimU), STs + ["rimU"], ["pkL"], ind(FP), "av")
+        cp(pkN, ST[:, 0:V].indirect(rimN), STs + ["rimN"], ["pkN"], ind(FP), "av")
 
     def message1(m):
-        cp(T.pk1[:], ST[:, 0:V].indirect(T.rimU[:, 0:14]), STs + ["rimU"], ["pk1"], ind(FP), "a")
         if m == 0:
-            shift(7, 0, T.pk1, 0, T.ZI, ["pk1", "ZI", "ZI0"], 1)
+            rim_fields()
+            shift(7, T.pk1, T.ZI, ["pkL", "ZI", "ZI0"], 1)
             tt(T.snd1[:, 0:FP], P[7][:, 0:FP], T.CH[:], A.add, ["P7", "CH"], ["snd1_0"], cyc(FP))
         else:
-            mm([(P[7][:, 0:FP], ZI, T.CH[:])], ["ZI0", "CH"], 7, FP, stop=False)
-            shift(7, 0, T.pk1, 0, T.ZJ, ["pk1", "ZJ"], 1, False)
-            cp(T.snd1[:, m * FP:(m + 1) * FP], P[7][:, 0:FP], ["P7"], ["snd1_%d" % m], cyc(FP), "a")
-        send(1, m, ["snd1_%d" % m, "Pa", "TRg", "nNa"], "lnd1_%d" % m)
+            mm([(P[3][:, 0:FP], ZI, T.CH[:])], ["ZI0", "CH"], 3, FP, stop=False)
+            rim_fields()
+            shift(3, T.pk1, T.ZJ, ["pkL", "ZJ"], 1, False)
+            ac(T.snd1[:, m * FP:(m + 1) * FP], P[3][:, 0:FP], ["P3", "BJ%d" % m], ["snd1_%d" % m], bias=T.BR[:, 8 + m:9 + m], ns=cyc(FP), on="av")
+        send(1, m, ["snd1_%d" % m], "lnd1_%d" % m)
 
-    def listed(bank, o, Z, src, w, reads, start=True, stop=True):
-        if start:
-            mm([(P[bank][:, o:o + w], Z[:, 15 - i:143 - i], src[:, i:16 * w:16]) for i in range(16)], reads, bank, 16 * max(w, 64), stop=stop)
+    def listed(bank, o, Z, src, w, reads, start=True):
+        mm([(P[bank][:, o:o + w], Z[:, 15 - i:143 - i], src[:, i:16 * w:16]) for i in range(16)], reads, bank, 16 * max(w, 64), start=start)
+
+    ry = [T.ryU[:, 16 * k:16 * k + 14] for k in range(5)]
+    rf = [T.ryF[:, 16 * k:16 * k + 14] for k in range(8)]
+
+    def rim_lists(m):
+        bank = 7 if m < RO else 4
+        listed(bank, 448, T.ZX, T.pk1, 28, ["pkL", "pkN", "ZX"])
+        sent_, kept, nb = P[bank][:, 448:462], P[bank][:, 462:476], "P%d" % bank
+        if m < RO:
+            cp(ry[0], sent_, [nb], ["ry0"])
+            ts(rf[0], sent_, 4.0, A.mult, [nb], ["rf0"], 16.0 - 4 * base(m), A.add)
+            tt(rf[0], rf[0], T.rimK[:, 0:14], A.add, ["rf0", "rimK"], ["rf0"])
         else:
-            mm([(P[bank][:, o:o + w], Z[:, 15 - i:143 - i], src[:, i:16 * w:16]) for i in range(16)], reads, bank, 16 * max(w, 64), start=False, stop=stop)
+            ts(rf[1], sent_, 0.5 - base(m), A.add, [nb], ["rf1"], BIG, A.mult)
+            tt(rf[0], sent_, T.rimK[:, 16:30], A.add, [nb, "rimL"], ["rf0"])
+            tt(rf[0], rf[0], rf[1], A.min, ["rf0", "rf1"], ["rf0"])
+        cp(ry[1], rf[0], ["rf0"], ["ry1"])
+        ts(rf[2], kept, 0.5 - base(m), A.add, [nb], ["rf2"], BIG, A.mult)
+        tt(rf[2], rf[2], T.TRE[:, 0:14], A.max, ["rf2", "TRE"], ["rf2"])
+        ts(ry[2], rf[2], float(FP), A.min, ["rf2"], ["ry2"])
 
     def message2(m):
-        ry = [T.ryU[:, 16 * k:16 * k + 14] for k in range(3)]
-        if m == 0:
-            for k in range(2):
-                ts(ry[k], T.RJ[:, 0:14], 2.0, A.mult, ["RJ0"], ["ry%d" % k], float(k), A.add)
-        else:
-            for k in range(2):
-                ts(ry[k], P[3][:, 0:14], float(k), A.add, ["P3"], ["ry%d" % k])
-            tt(T.ryF[:, 0:14], P[3][:, 0:14], T.rimK[:, 0:14], A.add, ["P3", "rimK"], ["ryF"])
-            cp(ry[2], T.ryF[:, 0:14], ["ryF"], ["ry2"])
         for k in range(3):
-            j = k if m else k % 2
-            if j == k:
-                cp(T.pk2[:, k * FP:(k + 1) * FP], upto(m, 0).indirect(ry[k]), log(m, 0) + ["ry%d" % k], ["pk2_%d" % k], ind(FP), "a")
-            bank, o = (5, 5, 6)[k], (0, FP, 0)[k]
-            shift(bank, o, T.pk2, j * FP, T.ZF, ["pk2_%d" % j, "ZF"], 4)
-        for k in range(3):
-            bank, o = (5, 5, 6)[k], (0, FP, 0)[k]
-            cp(T.snd2[:, 3 * FP * m + k:3 * FP * (m + 1):3], P[bank][:, o:o + FP], ["P%d" % bank], ["snd2_%d_%d" % (m, k)], cyc(FP), SNQ)
-        send(2, m, ["snd2_%d_%d" % (m, k) for k in range(3)], "lnd2_%d" % m)
+            out, bank = T.pk2[:, FP * k:FP * (k + 1)], (2, 4, 0 if m else 2)[k]
+            if k < 2:
+                win, names = qlog(k, m) if m else ((qa, ["qa"]), (qb, ["qb"]))[k]
+                cp(out, win.indirect(ry[0] if m else rimU), names + ["ry0" if m else "rimU"], ["pk2_%d" % k], ind(FP), "av")
+            elif m:
+                o = 4 * (base(m) - V)
+                cp(out, OUT[:, o - 16:o + 4 * CAP].indirect(ry[1]), ["O%d_%d" % (m, j) for j in range(4)] + ["ry1", "OZ%d" % m], ["pk2_2"], ind(FP), "av")
+            if k < 2 or m:
+                shift(bank, out, T.ZF, ["pk2_%d" % k, "ZF"], 4)
+            cp(T.snd2[:, k:3 * FP:3], P[bank][:, 0:FP], ["P%d" % bank, "snd2"], ["snd2_%d" % k], cyc(FP), "av")
+        send(2, m, ["snd2_%d" % k for k in range(3)], "lnd2_%d" % m)
+
+    def table(r):
+        j = 0
+        for a, b in (halves if r == 0 else ((base(r), base(r) + CAP),)):
+            w, made = b - a, {}
+            x0, x1 = (QQ[0][:, a:b], QQ[1][:, a:b]) if r else (qa[:, a:b], qb[:, a:b])
+            n0, n1 = ("Q0_%d" % r, "Q1_%d" % r) if r else ("qa", "qb")
+            for i, ((c0, c1, outs), way) in enumerate(zip(CASES, WAYS[r > 0])):
+                bank = TBANK[i % len(TBANK)]
+                pb, nb = P[bank][:, 0:w], "P%d" % bank
+                (z0, m0_), (z1, m1_) = scaled(c0, r), scaled(c1, r)
+                up0 = outs[0][2]
+                if way == "a":
+                    mm([(pb, z0, x0)], [m0_, n0], bank, w, 4 if r else 1, stop=False)
+                if way != "c":
+                    mm([(pb, z1, x1)], [m1_, n1], bank, w, 4 if r else 1, start=way == "b")
+                else:
+                    ac(pb, x1, [n1], [nb], scale=c1 * up0, ns=cyc(w))
+                u, nu = x0, n0
+                if way != "a" and c0 * up0 != 1.0:
+                    if c0 * up0 not in made:
+                        h = len(made)
+                        made[c0 * up0] = (T.r[:, 2 * CAP * h:2 * CAP * h + w], "rl%d" % h)
+                        ac(made[c0 * up0][0], x0, [n0], ["rl%d" % h, "rr%d" % h], scale=c0 * up0, ns=cyc(w), on="av")
+                    u, nu = made[c0 * up0]
+                first = None
+                for y, m, up_ in outs:
+                    out = TAB[:, 10 * a + place_of(y, m):10 * (b - 1) + place_of(y, m) + 1:10]
+                    if way == "a":
+                        ac(out, pb, [nb, "TF%d" % r], ["T%d_%d" % (r, j)], scale=up_, ns=cyc(w), on="av")
+                    elif first is None:
+                        tt(out, pb, u, A.add, [nb, nu, "TF%d" % r], ["T%d_%d" % (r, j)], cyc(w))
+                        first = out
+                    else:
+                        ac(out, first, ["T%d_%d" % (r, j - 1)], ["T%d_%d" % (r, j)], scale=up_ / up0, ns=cyc(w), on="av")
+                    j += 1
 
     ts(T.CI[:, 0:1], T.Pi[:, 0:1], 15, A.bitwise_and, ["Pi"], ["CI0"])
     ts(T.CI[:, 1:2], T.Pi[:, 0:1], 4, A.arith_shift_right, ["Pi"], ["CI1"])
     ts(T.CI[:, 2:3], T.Pi[:, 0:1], 2, A.arith_shift_right, ["Pi"], ["CI2"], 3, A.bitwise_and)
     ts(T.CI[:, 3:4], T.Pi[:, 0:1], 3, A.bitwise_and, ["Pi"], ["CI3"])
     cp(CF[:, 0:4], T.CI[:, 0:4], ["CI0", "CI1", "CI2", "CI3"], ["CF"])
-    ts(T.BK[:], T.X16[:], cG, A.is_equal, ["X16", "CF"], ["BK"], ns=cyc(128))
+    ts(T.BK[:], X16, cG, A.is_equal, ["X16", "CF"], ["BK"], ns=cyc(128))
     sel(TRs, T.BK[:], A.is_gt, 0.0, 0, -1, ["BK"], ["TRs"])
     sel(Pa, TRs, A.not_equal, BIG, 0, -1, ["TRs"], ["Pa"])
-    sel(TRg, T.BK[:], A.is_ge, 0.0, 0, 1, ["BK"], ["TRg"], -1)
-    sel(nNa, TRs, A.not_equal, -BIG, 0, -1, ["TRs"], ["nNa"])
     message1(0)
-    iota(T.C[:, CF0:3456], [[0, 2560]], 0, 0, ["C", "late"], c=2560, reads=["sent"])
+    zero(TAB, 0, 4, ["TZ0", "late"], ["sent"])
 
-    d3 = 3 * NW + 1
-    terms = [(12, 0, 1, 2, 2 * NW + 9), (13, 0, 128, 2, 2 * NW + 9), (0, 1, 1, 4, d3), (1, 1, 128, 4, d3), (2, 5, 1, 4, d3),
-             (0, 10, 256, 4, d3), (1, 10, 32768, 4, d3), (12, 10, -256, 4, 1), (13, 10, -32768, 4, 1), (12, 18, 1, 4, 1), (13, 18, 128, 4, 1),
-             (fJL, cWO + 12, 1, 2, NW + 1), (fR, cWO + 13, 21, 2, 4), (fEL, cWO + 14, 1, 2, NW + 1), (fS, cWO + 2, 1, 4, NW + 3),
-             (fT, cWO + 2, 1, 4, 3), (fM, cWO + 2, 9, 4, 3), (fD, cWO + 2, -9, 4, 3), (fJL, cWN, 1, 2, NW + 1), (fT, cWN + 2, -1, 1, 1),
-             (0, cWF, 1, 4, NW + 1), (4, cWF, 128, 4, NW + 1), (8, cWF + 4, 1, 4, NW + 1), (12, cWF + 4, BIG, 4, 1), (14, cWF + 8, 1, 1, 1), (15, cWF + 8, 128, 1, 1),
-             (fT, cS, 2, 2, NW), (fD, cS, -2, 1, 1), (fR, cX, BL, 1, 1), (fJL, cX, 1, 1, 1), (fJH, cX, 128, 1, 1), (fT, cZJ, 1, 4, NW),
-             (fM, cTH, 3.5, 1, 1), (fD, cTH, 8.5, 1, 1), (fM, cNN, -2, 1, 1), (fD, cNN, 1, 1, 1), (0, cKP, 1, 7, NW), (fM, cD, 1, 1, 1), (fD, cD, -1, 1, 1),
-             (fM, cB4, 4, 1, 1), (fR, cR, 1, 1, 1), (fT, cT, 1, 1, 1), (15, cEL, -BIG / 128, 1, 1),
-             (fP, cPL, 1, 2, NW + 1), (fR, cPL, BIG, 1, 1), (fT, cXR, 0.5, 1, 1), (fM, cXR, 64, 1, 1)]
-    places = [T.RW[0:1, NW * f + col:NW * f + col + (count - 1) * step + 1:step] for f, col, c, count, step in terms]
+    d3, o = 3 * NW + 1, 24
+    terms = [(1, 0, 1, 4, d3), (2, 4, 65536, 4, d3), (2, 16, 6, 4, d3), (15, 20, 6, 4, 1),
+             (0, o, 10, 4, d3), (1, o, 1280, 4, d3), (2, o, 1, 4, d3), (12, o + 4, 10, 4, 1), (13, o + 4, 1280, 4, 1), (15, o + 4, 1, 4, 1),
+             (2, o + 8, -32, 4, d3), (12, o + 12, 4, 4, 1), (13, o + 12, 512, 4, 1), (0, o + 16, 4, 4, d3), (1, o + 16, 512, 4, d3), (2, o + 16, 32, 4, d3),
+             (12, o + 20, 1, 2, 2 * NW + 1), (13, o + 20, 128, 1, 1), (15, o + 21, 8192, 1, 1), (15, o + 22, -8192, 1, 1),
+             (fJL, cWO + 12, 1, 2, NW + 1), (fEL, cWO + 14, 1, 2, NW + 1), (fM, cWO + 15, 1, 1, 1), (fD, cWO + 15, -1, 1, 1), (fS, cWO + 1, -32, 4, NW + 3),
+             (fK, cWO + 2, 1, 4, NW + 3), (fT, cWO + 2, 1, 4, 3), (fM, cWO + 2, 1, 4, 3), (fD, cWO + 2, -1, 4, 3), (fJL, cWN, 1, 2, NW + 1), (fT, cWN + 2, -1, 1, 1),
+             (fT, cS, 2, 2, NW), (fD, cS, -2, 1, 1), (fJL, cX, 1, 1, 1), (fJH, cX, 128, 1, 1), (fT, cZJ, 1, 3, NW),
+             (fM, cTH, 3.5, 1, 1), (fD, cTH, 8.5, 1, 1), (fM, cNN, -2, 1, 1), (fD, cNN, 1, 1, 1), (0, cKP, 1, 11, NW), (fM, cD, 1, 1, 1), (fD, cD, -1, 1, 1),
+             (fM, cB4, 4, 1, 1), (fJL, cR, PAD, 1, 1), (fJH, cR, CAP / 128, 1, 1), (fT, cT, 1, 1, 1), (1, cEL, 16, 4, 3 * NW),
+             (fM, cI1, -0.125, 1, 1), (fD, cI1, 0.5, 1, 1), (fQ, cI2, 0.75, 1, 1), (fT, cV, 0.5, 1, 1), (fM, cV, 8.5, 1, 1), (fD, cV, -8.5, 1, 1),
+             (fT, cVN, -0.5, 1, 1), (fS, cSG, 1, 4, NW + 1)]
+    places = [RW[:, NW * f + col:NW * f + col + (count - 1) * step + 1:step] for f, col, c, count, step in terms]
     fills("a", [(x, x, t[2]) for x, t in zip(places[1::2], terms[1::2])], ["RW0"], ["RWa"])
     fills("v", [(x, x, t[2]) for x, t in zip(places[0::2], terms[0::2])], ["RW0"], ["RWv"])
-    mm([(P[5][:, 0:NW], W1(f), T.RW[0:1, NW * f:NW * f + NW]) for f in range(16)], ["E1", "RWa", "RWv"], 5, 16 * NW)
+    mm([(P[5][:, 0:NW], W1(f), RW[:, NW * f:NW * f + NW]) for f in range(16)], ["E1", "RWa", "RWv"], 5, 16 * NW)
     either[0] = "av"
     cp(WS[:, 0:NW], P[5][:, 0:NW], ["P5"], ["WS"], cyc(NW), "a")
-    cp(WB[:, 0:NW], WS[:, 0:NW], ["WS"], ["WB0"], cyc(NW), "a")
-    ac(WB[:, 14:18], WS[:, 10:14], ["WS", "WB0"], ["WB"], scale=-1.0)
+    cp(WB[:, cWO:cS], WS[:, cWO:cS], ["WS"], ["WB0"], cyc(32), "a")
+    tt(T.sm[:, 0:4], WS[:, o + 4:o + 8], WS[:, o:o + 4], A.subtract, ["WS"], ["WD"])
+    ac(WS[:, 8:12], T.sm[:, 0:4], ["WD"], ["WS1"], scale=-1.0 / 16384)
+    ac(WS[:, 12:16], T.sm[:, 0:4], ["WD"], ["WS2"], scale=1.0 / 16384)
+    WLs = ["WL%d" % k for k in range(5)]
+    for k in range(4):
+        cp(WB[:, NA * (k // 2) + k % 2:NA * (k // 2) + NB:2], WS[:, k:2 * NB:4], ["WS", "WS1", "WS2"], [WLs[k]], on="a")
+    cp(WB[:, NB:NA], WS[:, 2 * NB:NA + NB], ["WS"], [WLs[4]], on="a")
     for x, sc, bi, nm in ((cE, 16, 15, "cE"), (nE, -16, -15, "nE"), (cO, 4, 3, "cO"), (c12, 16, 12, "c12"), (c8, 16, 8, "c8"), (n16, -16, 0, "n16"),
-                          (cF1, FP, CF0 + CAP - NR - 0.5, "cF1"), (cF2, NR - FP, 7 * FP, "cF2"), (c16, 16, CF0, "c16"),
-                          (cF3, FP, CF0 + CAP - 210.5, "cF3"), (cF4, FP, CF0 + CAP - 1 - BIG, "cF4"), (cF5, FP, CF0 - BIG, "cF5")):
+                          (cF0, CAP, V - BIG, "cF0"), (cF1, CAP, V + CAP - 0.5, "cF1")):
         ac(x, cG, ["CF"], [nm], bias=float(bi), scale=float(sc))
-    ac(T.SI[:], T.SI[:], ["SI", "nE"], ["SI"], bias=nE, ns=cyc(FP))
+    ac(SI, SI, ["SI", "nE"], ["SI"], bias=nE, ns=cyc(FP))
     ac(c2, cQ, ["CF", "c12"], ["c2"], bias=c12)
     ac(cA, cK, ["CF", "c8"], ["cA"], bias=c8)
     ac(nS, wcol(cS), ["WS"], ["nS"], scale=-1.0)
-    cp(T.XB[0:1, :], T.X[0:1, :], ["X"], ["XB"], cyc(256), "a")
-    cp(LG[:, 0:2 * V:2], T.qa[:], ["qa"], ["T0a"], cyc(V), "a")
-    cp(LG[:, 1:2 * V:2], T.qb[:], ["qb"], ["T0b"], cyc(V), "a")
-    iota(LG[:, 2 * V:LND], [[0, LND - 2 * V]], 0, 0, ["TZ"], c=LND - 2 * V)
-    for k in range(RO):
-        iota(LG[:, BL * k + ZC:BL * (k + 1)], [[0, BL - ZC]], 0, 0, ["TZ%d" % k], c=BL - ZC, reads=["late"])
+    cp(XB, X[0:1, :], ["X"], ["XB"], cyc(256), "a")
+    cp(T.Q0[:, 0:V], qa, ["qa"], ["Q0_0"], cyc(V), "a")
+    cp(T.Q1[:, 0:V], qb, ["qb"], ["Q1_0"], cyc(V), "a")
     cp(T.ZF[:], T.ZI[:, 0:240], ["ZI", "ZI0"], ["ZF"], cyc(240), "a")
+    for k, c_ in enumerate(SCALES):
+        ac(T.ZB[:, 128 * k:128 * k + 128], ZI, ["ZI0"], ["ZB%d" % k], scale=c_, ns=cyc(128), narrow=True)
+    for r in range(1, RO + 1):
+        zero(OUT, 4 * (base(r) - PAD - V), 4 * (base(r) - V), ["OZ%d" % r], ["late"])
 
     c = T.PI[:]
-    aL, aH, aF, aS, aK, aS2, aF2 = [T.AB[:, FP * k:FP * k + FP] for k in range(7)]
-    SG = T.AB[:, 7 * FP + 14:8 * FP + 14]
-    ms(T.AB[:, 7 * FP:7 * FP + 14], 0.0, ["SGz"])
+    aS, aK, aS2, aF, SG = [T.AB[:, FP * k:FP * k + FP] for k in range(5)]
+    meet(["TD0", "TD1", "TD2", "s0", "s1", "s2", "s3"])
     ts(s1, c, 4.0, A.mult, ["PI"], ["s1"], -10749.0, A.add, cyc(FP))
     ts(s3, c, float(4 * V + up), A.is_ge, ["PI"], ["s3"], ns=cyc(FP))
-    ts(T.bit[:], c, float(4 * V), A.is_ge, ["PI"], ["bit"], ns=cyc(FP))
+    ts(aF, c, float(4 * V), A.is_ge, ["PI"], ["aF"], -3.0 / 32, A.mult, cyc(FP))
     tt(s0, s1, c, A.max, ["s1", "PI"], ["s0"], cyc(2 * FP))
-    tt(s2, T.SI[:], c, A.is_lt, ["SI", "PI"], ["s2"], cyc(2 * FP))
-    ts(T.colU[:, 0:FP], s0, 0.25, A.mult, ["s0"], ["colU"], -0.375, A.add, cyc(FP))
+    tt(s2, SI, c, A.is_lt, ["SI", "PI"], ["s2"], cyc(2 * FP))
+    ts(T.colU[:], s0, 0.25, A.mult, ["s0"], ["colU"], -0.375, A.add, cyc(FP))
     tt(aS, s2, s3, A.subtract, ["s2", "s3"], ["aS"], cyc(2 * FP))
     ts(s1, s0, 3, A.bitwise_and, ["s0"], ["s1"], ns=cyc(FP))
-    ts(s4, s0, 2, A.arith_shift_right, ["s0"], ["s4"], 127, A.bitwise_and, cyc(FP))
-    ts(s5, s0, 9, A.arith_shift_right, ["s0"], ["s5"], ns=cyc(FP))
-    ts(aK, s1, 64.0, A.mult, ["s1"], ["aK"], -6.0, A.add, cyc(FP))
-    cp(aL, s4, ["s4"], ["aL"], cyc(FP))
-    cp(aH, s5, ["s5"], ["aH"], cyc(FP))
-    ac(aF, T.bit[:], ["bit"], ["aF"], scale=2.5, ns=cyc(FP))
-    ac(aF2, T.bit[:], ["bit"], ["aF2"], scale=-192.0, ns=cyc(FP))
-    ac(aS2, aS, ["aS"], ["aS2"], scale=32.0, ns=cyc(FP))
-    ac(SG, aS, ["aS"], ["SG"], bias=-0.5, ns=cyc(FP))
-    ts(T.MK[:, 0:4], T.X[:, 0:4], cQ, A.is_equal, ["X", "CF"], ["MK"])
-    ts(T.ZA0[:], T.X[:, 0:144], cA, A.is_equal, ["X", "cA"], ["ZA0"], ns=cyc(144))
-    ts(T.ZO0[:], T.XQ[:], cO, A.is_equal, ["XQ", "cO"], ["ZO0"], ns=cyc(144))
-    ts(T.ZE0[:], T.X[:, 0:144], cE, A.is_equal, ["X", "cE"], ["ZE0"], ns=cyc(144))
+    ts(aK, s1, 1.0 / 32, A.mult, ["s1"], ["aK"], ns=cyc(FP))
+    ac(aS2, aS, ["aS"], ["aS2"], bias=0.5, scale=-1.0, ns=cyc(FP), narrow=True)
+    ac(SG, aS, ["aS"], ["SG"], bias=-0.5, ns=cyc(FP), narrow=True)
+    ts(T.MK[:, 0:4], X[:, 0:4], cQ, A.is_equal, ["X", "CF"], ["MK"])
+    ts(T.ZA0[:], X[:, 0:144], cA, A.is_equal, ["X", "cA"], ["ZA0"], ns=cyc(144))
+    ts(T.ZO0[:], XQ, cO, A.is_equal, ["XQ", "cO"], ["ZO0"], ns=cyc(144))
+    ts(T.ZE0[:], X[:, 0:144], cE, A.is_equal, ["X", "cE"], ["ZE0"], ns=cyc(144))
     for m in range(4):
-        ac(T.ZA[:, 144 * m:144 * m + 144], T.ZA0[:], ["ZA0", "MK"], ["ZA%d" % m], scale=T.MK[:, m:m + 1], ns=cyc(144))
+        ac(T.ZA[:, 144 * m:144 * m + 144], T.ZA0[:], ["ZA0", "MK"], ["ZA%d" % m], scale=T.MK[:, m:m + 1], ns=cyc(144), narrow=True)
     ZAs = ["ZA%d" % m for m in range(4)]
-    ac(T.ZO[:], T.ZO0[:], ["ZO0", "nS"], ["ZO"], scale=nS, ns=cyc(144))
-    ac(T.ZE[:], T.ZE0[:], ["ZE0", "WS"], ["ZE"], scale=wcol(cS), ns=cyc(144))
+    ac(T.ZO[:], T.ZO0[:], ["ZO0", "nS"], ["ZO"], scale=nS, ns=cyc(144), narrow=True)
+    ac(T.ZE[:], T.ZE0[:], ["ZE0", "WS"], ["ZE"], scale=wcol(cS), ns=cyc(144), narrow=True)
     ac(T.TRE[:], T.TRE[:], ["TRE", "n16"], ["TRE"], bias=n16)
-    ts(T.Z2[:], T.X[:, 0:144], c2, A.is_equal, ["X", "c2"], ["Z2"], ns=cyc(144))
-    iota(T.HI[0:1, 0:V], [[1, 7], [0, 128]], 0, 0, ["HI"], c=V)
+    ts(T.Z2[:], X[:, 0:144], c2, A.is_equal, ["X", "c2"], ["Z2"], ns=cyc(144))
+    fills("v", [(HI[:, 128 * k:128 * k + 128], None, k) for k in range(V // 128)], [], ["HI"])
+    ms(T.CR[:], 0.0, ["CR"], cyc(256))
     ms(T.CR[0:1, :], 1.0, ["CR"], cyc(256))
-
-    def by_port(k, a, b, lists):
-        return [(P[k][:, m:b - a:4], T.ZA[:, 144 * m + 8 - f:144 * m + 136 - f], x[:, a // 4:b // 4]) for f, x in lists for m in range(4)]
-
     for k, (a, b) in enumerate(wide):
-        parts = [(P[k][:, 0:b - a], ZI, ST[:, a:b]), (P[k][:, 0:b - a], EB, T.HI[0:1, a:b])]
-        parts += [(P[k][:, c_ - a:c_ - a + 128], l_, r_) for c_ in range(a, b, 128) for l_, r_ in ((EA, T.XB[0:1, 0:128]), (W1(fQ), T.PT[0:1, 128:256]))]
-        mm(parts, ["ZI0", "E1", "HI", "XB", "PT1", STs[k]], k, 4 * (b - a), stop=False)
-        mm(by_port(k, a, b, ((0, aK), (0, aS2), (0, aF2))), ["aK", "aS2", "aF2"] + ZAs, k, 3 * (b - a), start=False)
+        parts = [(P[k][:, 0:b - a], ZI, ST[:, a:b]), (P[k][:, 0:b - a], W1(fJH), HI[:, a:b])]
+        parts += [(P[k][:, c_ - a:c_ - a + 128], W1(fJL), XB[:, 0:128]) for c_ in range(a, b, 128)]
+        for c_ in range(a, b, 256):
+            w_ = min(256, b - c_)
+            parts += [(P[k][:, c_ - a:c_ - a + w_], W1(fEL), XB[:, 0:w_])] + [(P[k][:, c_ - a:c_ - a + w_], W1(fEH, c_ // 256), T.CR[0:1, 0:w_])] * (c_ > 0)
+        mm(parts, ["ZI0", "E1", "HI", "XB", "CR", STs[k]], k, 5 * (b - a), stop=False)
+        mm([(P[k][:, m:b - a:4], T.ZA[:, 144 * m + 8 - f:144 * m + 136 - f], x[:, a // 4:b // 4]) for f, x in ((fS, aS2), (fK, aK), (fK, aF)) for m in range(4)],
+           ["aK", "aS2", "aF"] + ZAs, k, 3 * (b - a), start=False)
         cp(ST[:, a:b], P[k][:, 0:b - a], ["P%d" % k], [STs[k]], cyc(b - a), "a")
-    iota(ST[:, V:SL], [[0, CAP]], 0, 0, ["STz"], c=CAP)
+    zero(ST, V, SL, ["STz"], ["late"])
     STw = STs + ["STz"]
-    for k, (a, b) in enumerate(wide):
-        parts = [(P[2 + k][:, 0:b - a], W1(15), T.HI[0:1, a:b]), (P[2 + k][:, 0:b - a], W1(12), T.CR[0:1, 0:b - a])]
-        parts += [(P[2 + k][:, c_ - a:c_ - a + 128], W1(14), T.XB[0:1, 0:128]) for c_ in range(a, b, 128)]
-        mm(parts, ["E1", "HI", "XB", "CR"], 2 + k, 3 * (b - a), stop=False)
-        mm(by_port(2 + k, a, b, ((0, aL), (4, aH), (4, aF), (8, aS))), ["aL", "aH", "aF", "aS"] + ZAs, 2 + k, 4 * (b - a), start=False)
-        cp(T.FT[:, a:b], P[2 + k][:, 0:b - a], ["P%d" % (2 + k)], ["FT%d" % k], cyc(b - a), "a")
-    for x, y, sc, nm, src in ((nPa, Pa, -1.0, "nPa", "Pa"), (Na, nNa, -1.0, "Na", "nNa"), (Ka, TRs, -B2, "Ka", "TRs"), (Kb, TRg, -B2, "Kb", "TRg"),
-                              (NBK, T.BK[:], -1.0, "NBK", "BK"), (T.NI[:], ZI, -1.0, "NI", "ZI0")):
-        ac(x, y, [src], [nm], scale=sc, ns=cyc(128), narrow=nm != "NI")
+    ac(nPa, Pa, ["Pa"], ["nPa"], scale=-1.0, ns=cyc(128), narrow=True)
     ms(T.ONE[:], 1.0, ["ONE"])
-    mm([(P[4][:, 0:56], T.Z2[:, 12 - 4 * h:140 - 4 * h], T.bit[:, h:FP:4]) for h in range(4)], ["Z2", "bit"], 4, 256)
-    isf = T.can[:, 56:112]
-    ts(isf, P[4][:, 0:56], 0.5, A.is_ge, ["P4"], ["isf"])
-    ac(T.THR[:], isf, ["isf"], ["THR"], bias=3.5, scale=64.0)
-    mm([(P[5][:, 0:56], Pa, isf), (P[5][:, 1:56], T.BK[:], isf[:, 0:55]), (P[5][:, 1:56], nPa, isf[:, 0:55])], ["Pa", "nPa", "BK", "isf"], 5, 3 * 64)
-    m0, m1, m2, m3 = [T.v1[:, 56 * k:56 * k + 56] for k in range(4)]
-    scan(m0, -BIG, 5, 0, 56, [], ["m0"])
-    ts(T.ki[:, 0:56], m0, 0.0625, A.mult, ["m0"], ["ki"], -0.47, A.add)
-    ts(m1, T.ki[:, 0:56], 112.0, A.mult, ["ki", "c16"], ["m1"], c16, A.add)
-    tt(m2, m0, m1, A.add, ["m0", "m1"], ["m2"], cyc(112))
-    tt(m3, m2, T.TRE[:], A.max, ["m2", "TRE"], ["m3"], cyc(112))
-    cp(T.posU[:, 0:56], m3, ["m3"], ["posU"])
-    ms(T.cb[:, CF0:CB0], 0.0, ["FZ"], cyc(4 * FP))
-    cp(T.cb[:, 0:CB0].indirect(T.posU[:, 0:56]), T.FT[:], ["posU", "FT0", "FT1"], ["FZ"], ind(V, SC))
-    mm([(P[6][:, b:126:14], T.cb[:, CF0 + 128 * b:CF0 + 128 * b + 128], WB[:, cWF:cWF + 9]) for b in range(14)], ["FZ", "WB0"], 6, 14 * 64, start="each", stop="each")
-    eF, cF = T.FN[:, 280:294], T.FN[:, 296:310]
-    cp(T.FN[:, 0:56], P[6][:, 0:56], ["P6"], ["FN0"])
-    cp(eF, P[6][:, 112:126], ["P6"], ["eF"])
-    ts(T.THF[:, 0:56], P[6][:, 56:112], -0.5 - BIG, A.add, ["P6"], ["THF"])
-    ms(T.THF[:, 56:84], 0.0, ["THz"])
-    ts(cF, P[6][:, 112:126], 0.0625, A.mult, ["P6"], ["cF"], -0.47, A.add)
-    ts(T.FW[:, 0:56], P[6][:, 0:56], SL - 0.5, A.is_ge, ["P6"], ["FW0"], float(FP), A.mult)
-    cp(T.FW[:, 56:112], P[6][:, 0:56], ["P6"], ["FW1"])
-    for r in range(1, RO):
-        tt(T.FW[:, 56:112], T.FW[:, 56:112], T.FW[:, 0:56], A.add, ["FW0", "FW1"], ["FW1"], cyc(112))
-        cp(T.FN[:, 56 * r:56 * r + 56], T.FW[:, 56:112], ["FW1"], ["FN%d" % r])
     message2(0)
-    ac(BQ, T.BK[:], ["BK", "WS"], ["BQ"], scale=wcol(cQ4), ns=cyc(128))
-    ac(T.MK[:, 8:28], T.TRE[:, 0:20], ["TRE"], ["TRX"], bias=V - BIG)
+    ac(T.MK[:, 8:8 + W], T.TRE[:, 0:W], ["TRE"], ["TRX"], bias=float(V))
+    ac(T.rimK[:, 32:46], T.TRE[:, 0:14], ["TRE"], ["J10"], scale=10.0, bias=-27.0)
     mm([(P[4][:, 16 * (8 * h + j):16 * (8 * h + j) + 16], T.ZI[0:16, 128 - 16 * j:256 - 16 * j], WB[0:16, cWO + 16 * h:cWO + 16 * h + 16]) for h in range(2) for j in range(8)],
        ["ZI", "ZI0", "WB0"], 4, 16 * 64, start="each", stop="each")
     ms(T.WN[:, 0:16], 0.0, ["WN0"])
     cp(T.Wo[:], P[4][:, 0:128], ["P4"], ["Wo"], cyc(128), "a")
     cp(T.WN[:, 9:137], P[4][:, 128:256], ["P4", "WN0"], ["WN"], cyc(128), "a")
-    ac(T.ZJ[:], T.ZI[:, 0:240], ["ZI", "ZI0", "WS"], ["ZJ"], scale=wcol(cZJ), ns=cyc(240))
-    ac(T.ZX[:], T.ZE0[:], ["ZE0", "WS"], ["ZX"], scale=wcol(cX), ns=cyc(144))
+    ac(T.ZJ[:], T.ZI[:, 0:240], ["ZI", "ZI0", "WS"], ["ZJ"], scale=wcol(cZJ), ns=cyc(240), narrow=True)
+    ac(T.ZX[:], T.ZE0[:], ["ZE0", "WS"], ["ZX"], scale=wcol(cX), ns=cyc(144), narrow=True)
     ms(T.FF[:, 0:8], 0.0, ["FF0"])
+    ms(T.AB[:, 5 * FP:5 * FP + 14], -3.0, ["SGx"])
+    ms(T.MEM[:], 0.0, ["MEM"], cyc(FP))
     ts(T.NT[:, 0:1], T.TH[:, 0:1], -1.0, A.mult, ["TH"], ["NTH"])
-    iota(T.KE[:, 0:56], [[1, 4], [0, 14]], 2 - ZC, 0, ["KE0"], c=56, reads=["late"])
-    iota(T.KE[:, 56:80], [[1, 4], [0, 6]], 2 - ZC, 0, ["KE1"], c=24, reads=["late"])
+    iota(T.KE[:], [[2, 2], [1, 4], [0, W]], -4 * V, 0, ["KE0", "KE1"], c=8 * W, reads=["late"])
+    ms(T.KR[:], 0.0, ["KR"], cyc(64))
+    fills("v", [(T.KR[32:33, :], None, 1), (T.CR[32:33, 6 * W:8 * W], None, 2.5)], ["CR"], ["KR"])
     ts(T.RJ[:, 16:30], T.RI[:, 16:30], 3, A.bitwise_and, ["RP"], ["RJ1"])
-    ts(T.rimK[:, 0:14], T.RJ[:, 16:30], 2.0, A.add, ["RJ1"], ["rimK"])
-    ts(T.rimK[:, 16:30], T.RJ[:, 16:30], float(FP), A.mult, ["RJ1"], ["rimL"], 8.0 + 160 - BIG * RO, A.add)
-    ty, td, tg, tm, th_, ta, tb = [T.LW[:, 64 * k:64 * k + 64] for k in range(7)]
-    L1, L2, L3, LI = [T.LT[:, 256 * k:256 * k + 256] for k in range(4)]
-    iota(ty, [[0, 8], [1, 8]], -2, 0, ["ty"], reads=["late"])
-    iota(td, [[0, 2], [1, 4], [0, 8]], 1, 0, ["td"], reads=["late"])
-    iota(tg, [[2, 2], [0, 32]], -1, 0, ["tg"], reads=["late"])
-    ts(tm, ty, 0.0, A.max, ["ty"], ["tm"])
-    tt(tm, tm, td, A.min, ["tm", "td"], ["tm"], cyc(128))
-    ac(tg, tg, ["tg"], ["tg"], scale=1.0 / 32, ns=cyc(64))
-    ac(th_, tm, ["tm"], ["th_"], scale=-0.5, ns=cyc(64))
-    tt(L1[:, 0:64], tm, tg, A.mult, ["tm", "tg"], ["L0a"], cyc(128))
-    tt(ta, th_, td, A.add, ["th_", "td"], ["ta"], cyc(128))
+    cp(T.rimK[:, 0:14], T.RJ[:, 16:30], ["RJ1"], ["rimK"])
+    ts(T.rimK[:, 16:30], T.RJ[:, 16:30], float(CAP), A.mult, ["RJ1"], ["rimL"], 8.0 - base(RO), A.add)
+    ty, td, th_, tb = [LW[:, 64 * k:64 * k + 64] for k in range(4)]
+    L1, L3 = T.LT[:, 0:64], T.LT[:, 64:128]
+    iota(ty, [[0, 4], [1, 16]], -2, 0, ["ty"], reads=["late"])
+    iota(td, [[1, 4], [0, 16]], 1, 0, ["td"], reads=["late"])
+    ts(L1, ty, 0.0, A.max, ["ty"], ["L1"])
+    tt(L1, L1, td, A.min, ["L1", "td"], ["L1"], cyc(128))
+    ac(th_, L1, ["L1"], ["th_"], scale=-0.5, ns=cyc(64))
     tt(tb, th_, ty, A.add, ["th_", "ty"], ["tb"], cyc(128))
-    tt(L2[:, 0:64], L1[:, 0:64], ta, A.mult, ["L0a", "ta"], ["L1a"], cyc(128))
-    tt(L3[:, 0:64], L1[:, 0:64], tb, A.mult, ["L0a", "tb"], ["L2a"], cyc(128))
-    fills("av", [(LI[:, a:b], T.X[:, 0:b - a], val) for o in (0, 32) for a, b, val in ((o, o + 8, 1.0), (o + 8, o + 16, 0.5), (o + 16, o + 32, 0.25))], ["X"], ["L3a"])
-    for k, x in enumerate((L1, L2, L3, LI)):
-        cp(x[:, 64:128], x[:, 0:64], ["L%da" % k], ["L%db" % k], cyc(64), "a")
-        cp(x[:, 128:256], x[:, 0:128], ["L%da" % k, "L%db" % k], ["L%d" % k], cyc(128), "a")
-    ac(T.Wb[:], T.ZE0[:, 15 - fT:143 - fT], ["ZE0", "WS"], ["Wb"], scale=wcol(cD), ns=cyc(128))
-    ac(tmp, ZI, ["ZI0", "WS"], ["tmp"], scale=wcol(cKP), ns=cyc(128))
+    tt(L3, L1, tb, A.mult, ["L1", "tb"], ["L3"], cyc(128))
+    to_t = T.ZE0[:, 15 - fT:143 - fT]
+    ac(T.Wb[:], to_t, ["ZE0", "WS"], ["Wb"], scale=wcol(cD), ns=cyc(128), narrow=True)
+    ac(tmp, ZI, ["ZI0", "WS"], ["tmp"], scale=wcol(cKP), ns=cyc(128), narrow=True)
     tt(T.Wb[:], T.Wb[:], tmp, A.add, ["Wb", "tmp"], ["Wb"], cyc(256))
+    for x, y, col, nm, src in ((Wv, to_t, cV, "Wv", "ZE0"), (Wvn, to_t, cVN, "Wvn", "ZE0"), (Wi1, T.BK[:], cI1, "Wi1", "BK"), (Wi2, T.BK[:], cI2, "Wi2", "BK")):
+        ac(x, y, [src, "WS"], [nm], scale=wcol(col), ns=cyc(128), narrow=True)
+    for k in range(4):
+        ac(SGM[k], T.BK[:], ["BK", "WS"], ["SGM%d" % k] + ["ZA%d" % (k - 2)] * (k > 1), scale=wcol(cSG + k), ns=cyc(128), narrow=True)
     for r in range(1, RO + 1):
-        ac(T.BR[:, r:r + 1], wcol(cR), ["WS"], ["BR%d" % r], bias=wcol(cB4), scale=float(r))
-    for k, (pat, base) in enumerate((([[-16, 8], [6, 40]], 0), ([[2, 8], [0, 40]], 0), ([[1, CAP]], -160))):
-        iota(T.PT[0:1, 256 + CAP * k:256 + CAP * (k + 1)], pat, base, 0, ["PJ%d" % k], c=CAP, reads=["late"])
-    ac(T.ZP[:], T.ZE0[:], ["ZE0", "WS"], ["ZP"], scale=wcol(cPL), ns=cyc(144))
-    ac(T.ZQ[:], T.ZO0[:], ["ZO0", "WS"], ["ZQ"], scale=wcol(cX), ns=cyc(144))
+        ac(T.BR[:, r:r + 1], wcol(cR), ["WS"], ["BR%d" % r], bias=wcol(cB4), scale=float(r - 1))
+        if r < RO:
+            ac(T.BR[:, 8 + r:9 + r], wcol(cR), ["WS"], ["BJ%d" % r], scale=float(r))
+    ac(T.ZQ[:], T.ZO0[:], ["ZO0", "WS"], ["ZQ"], scale=wcol(cX), ns=cyc(144), narrow=True)
     ac(T.Wy[:, 0:8], T.BK[:, 0:128:16], ["BK", "WS"], ["Wy0"], scale=wcol(cT))
     ac(T.Wy[:, 8:16], T.BK[:, 0:128:16], ["BK", "WS"], ["Wy1"], scale=wcol(cD))
-    ac(Z128, ZI, ["ZI0"], ["Z128"], scale=128.0, ns=cyc(128), narrow=True)
-    ac(NBI, ZI, ["ZI0"], ["Z64"], scale=1.0 / 64, ns=cyc(128), narrow=True)
-    ac(aS2, aF, ["aF"], ["aS2"], scale=(SL + (RO - 1) * FP - V) / 320.0, ns=cyc(FP), narrow=True)
+    ac(Z8, ZI, ["ZI0"], ["Z8"], scale=8.0, ns=cyc(128), narrow=True)
+    for k, (pat, base_) in enumerate((([[0, 3], [1, 128]], PAD), ([[1, 3], [0, 128]], V // 128))):
+        iota(PJ[:, 384 * k:384 * (k + 1)], pat, base_, 0, ["PJ%d" % k], c=384, reads=["late"])
+    mm([(P[2][:, 0:CAP], W1(f), x[:, 0:CAP]) for f, x in ((fJL, PJ), (fJH, PJ[:, 384:768]), (fQ, T.CR[0:1, :]))], ["E1", "PJ0", "PJ1", "CR"], 2, 3 * CAP)
+    cp(T.JR[:], P[2][:, 0:CAP], ["P2"], ["JR"], cyc(CAP), "a")
+    table(0)
+    for k, c_ in enumerate(SCALES):
+        ac(T.ZS[:, 128 * k:128 * k + 128], ZI, ["ZI0"], ["ZS%d" % k], scale=c_, ns=cyc(128))
 
     either[0] = ""
-    cp(T.rimS[:, 0:14], T.RI[:, 0:14], ["RI"], ["rimS"])
     NG = 8
     Gs = ["G%d" % k for k in range(NG)]
+    meet(["RW0", "RWa", "RWv", "HI", "HJ", "PT", "XB"] + Gs)
+    meet(["PJ0", "PJ1", "CJ"])
+    meet(["TB", "RR0", "RR1"])
+    meet(["qa", "g", "h", "nn", "base"])
+    meet(["qb"] + ["snd1_%d" % k for k in range(1, RO)])
     edge = [56 * (k // 2) + GV * (k % 2) for k in range(NG + 1)]
-    OF = T.GF[:, V + FP:V + 2 * FP]
+    qe, FF, gb, eU, sm = T.qe, T.FF, T.gb, T.eU, T.sm
+    TH, fresh = T.TH[:, 0:1], gb[:, 2 * CAP:3 * CAP]
 
-    def neighbours(last, free):
-        o = FP * last
-        win, reads = (ST[:], STw + ["colL"] + ["lnd1_%d" % m for m in range(RO)]) if last else (ST[:, 0:SL], STw + ["colU"])
+    def neighbours(free):
         for k in range(NG):
             a, b = edge[k], edge[k + 1]
-            cp(T.G[:, FP + 16 * a:FP + 16 * b], win.indirect(T.colU[:, o + a:o + b]), reads, [Gs[k]], ind(16 * (b - a)), "av" if free else "va"[k % 2])
+            cp(T.G[:, 16 * a:16 * b], ST[:, 0:SL].indirect(T.colU[:, a:b]), STw + ["colU"], [Gs[k]], ind(16 * (b - a)), "av" if free else "va"[k % 2])
 
-    def by_slot(bank, Z, zn, more=False):
-        at = 0
-        for j, k in enumerate(CUT):
-            a, b = 14 + edge[at] - (14 if more and j == 0 else 0), 14 + edge[at + k]
-            mm([(P[bank][:, a:b], Z[:, 15 - i:143 - i], T.G[:, 16 * a + i:16 * b:16]) for i in range(16)], Gs[at:at + k] + [zn] + ["XR"] * (a == 0), bank,
-               16 * max(b - a, 64), start=False, stop=j == len(CUT) - 1)
-            at += k
-
-    qe, cq, WK, rr, FF, xx, po, gb, eU = T.qe, T.cq, T.WK, T.r, T.FF, T.xx, T.po, T.gb, T.eU
-    TH, base = T.TH[:, 0:1], gb[:, 640:960]
-    PARTS = ((0, FP, 0, 14), (FP, CAP, 14, 20))
-    PORTS = [(FP * k, FP) for k in range(4)] + [(4 * FP + NR * k, NR) for k in range(4)]
-    APART = [(r, s) for r in range(2, RO + 1) for s in SA if r < RO or s > 3]
-    OWN, ACC = ((0, 0), (4, 0)), ((5, 0), (4, NR))
-
-    def lists(part, what, k0=0, k1=4):
-        w = (14, 6)[part]
-        if what in ("q0e", "q1e"):
-            k0, k1 = -1, 0
-        buf, o = {"q0e": (T.UA, 9), "q0n": (T.UA, 9), "case": (T.UA, 9), "q1e": (T.UB, 5), "q1n": (T.UB, 5), "take": (T.UC, 8), "keep": (T.UC, 8)}[what]
-        at = 14 * o * part + w * {"case": 5, "take": 0, "keep": 4}.get(what, 1)
-        return buf[:, at + w * k0:at + w * k1]
-
-    def own_control(r):
-        if r > 1:
-            iota(T.C[:, CF0:3456], [[0, 2560]], 0, 0, ["C"], c=2560)
-        mm([(P[3][:, 0:FP + 14], ZI, T.AB[:, 7 * FP:8 * FP + 14])] + [(P[3][:, 14:FP + 14], T.ZO[:, 12 - 4 * m:140 - 4 * m], ST[:, m:V:4]) for m in range(4)],
-           ["ZI0", "SG", "SGz", "ZO"] + STs, 3, 5 * FP, stop=False)
-        if r > 1:
-            mm([(P[6][:, 0:FP], T.WN[:, 9 - fT:137 - fT], T.pk1[:])], ["WN", "pk1"], 6, FP)
-            ac(T.G[:, 0:FP], P[6][:, 0:FP], ["P6", "WS"], ["XR"], scale=wcol(cXR), ns=cyc(FP), on="av")
-        neighbours(False, r == 1)
-        marks["G", r] = len(nodes) - 1
-        by_slot(3, T.ZE, "ZE", r > 1)
-        ts(T.bit[:], P[3][:, 14:FP + 14], 0.0, A.is_gt, ["P3"], ["bit"], ns=cyc(FP))
-        if r > 1:
-            message2(r - 1)
+    def control(r):
+        for k in range(2):
+            zero(T.C, V + 4 * CAP * k, V + 4 * CAP * (k + 1), ["C%d" % k], ["late"])
+        meet(early * (r == 4) + ["TF%d" % r])
+        mm([(P[1][:, 0:FP + 14], ZI, T.AB[:, 4 * FP:5 * FP + 14])] + [(P[1][:, 0:FP], T.ZO[:, 12 - 4 * m:140 - 4 * m], ST[:, m:V:4]) for m in range(4)], ["ZI0", "SG", "SGx", "ZO"] + STs, 1, 5 * FP, stop=False)
+        for k, (a, b) in enumerate(halves):
+            mm([(P[3 + 4 * k][:, 0:b - a], T.Wo[:], ST[:, a:b])], ["Wo"] + STs, 3 + 4 * k, b - a, stop=False)
+        neighbours(r == 1)
+        landed, ln = piece(T, "lnd", 1, r - 1, 0, n - 1), "lnd1_%d" % (r - 1)
+        cp(T.G[:, 0:4 * V].indirect(rimS), landed, [ln, "rimS"], Gs, ind(FP, SC))
+        mm([(P[2][:, 0:FP], Wv, pkN), (P[2][:, 0:FP], Wvn, landed)], ["Wv", "Wvn", "pkN", ln], 2, 2 * FP)
+        cp(T.G[:, 4 * V:4 * V + FP], P[2][:, 0:FP], ["P2"], ["XF"], cyc(FP), "av")
+        listed(1, 0, T.ZE, T.G, FP + 14, Gs + ["ZE", "XF"], False)
+        ts(T.bit[:], P[1][:, 0:FP], 0.0, A.is_gt, ["P1"], ["bit"], ns=cyc(FP))
         mm([(P[4][:, 0:56], T.Z2[:, 12 - 4 * h:140 - 4 * h], T.bit[:, h:FP:4]) for h in range(4)], ["Z2", "bit"], 4, 256)
-        cn, cb_ = T.can[:, 0:56], T.can[:, 0:55]
-        tt(cn, P[4][:, 0:56], T.THR[:], A.is_ge, ["P4", "THR"], ["cn"])
-        mm([(P[0][:, 0:56], Na, cn), (P[0][:, 1:56], NBK, cb_), (P[0][:, 1:56], nNa, cb_)], ["Na", "NBK", "nNa", "cn"], 0, 3 * 64)
-        mm([(P[0][:, 56:112], Ka, cn), (P[0][:, 57:112], Kb, cb_)], ["Ka", "Kb", "cn"], 0, 2 * 64)
-        mm([(P[4][:, 0:56], TRs, cn), (P[4][:, 1:56], TRg, cb_)], ["TRs", "TRg", "cn"], 4, 2 * 64)
-        scan(T.SX[:, 0:56], cF4, 0, 0, 56, ["cF4"], ["SX0"])
-        scan(T.SX[:, 56:112], B2 * (CAP - 0.5), 0, 56, 56, [], ["SX1"])
-        scan(T.SX[:, 112:168], -210.0, 4, 0, 56, [], ["SX"])
-        tt(m0, T.SX[:, 0:56], T.SX[:, 56:112], A.min, ["SX0", "SX1"], ["m0"], cyc(112))
-        ts(m1, T.SX[:, 0:56], cF1, A.is_ge, ["SX0", "cF1", "cF2"], ["m1"], cF2, A.mult)
-        tt(m2, m0, T.TRE[:], A.max, ["m0", "TRE"], ["m2"], cyc(112))
-        tt(m3, m1, m2, A.add, ["m1", "m2"], ["m3"], cyc(112))
-        cp(T.posU[:, 0:56], m3, ["m3"], ["posU"])
+        cn, cb_ = T.can[:], T.can[:, 0:55]
+        ts(cn, P[4][:, 0:56], 3.5, A.is_ge, ["P4"], ["cn"])
+        mm([(P[4][:, 56:112], Pa, cn), (P[4][:, 57:112], T.BK[:], cb_), (P[4][:, 57:112], nPa, cb_)], ["Pa", "BK", "nPa", "cn"], 4, 3 * 64)
+        m0, m1, m2, m3 = [T.v1[:, 56 * k:56 * k + 56] for k in range(4)]
+        op({"v": cyc(56)}, lambda e: vec.tensor_tensor_scan(m0, T.ONE[:], P[4][:, 56:112], cF0, A.mult, A.add), ["ONE", "P4", "cF0"], ["m0"])
+        ts(m1, m0, cF1, A.is_ge, ["m0", "cF1"], ["m1"], -BIG, A.mult)
+        tt(m2, m0, m1, A.add, ["m0", "m1"], ["m2"], cyc(112))
+        tt(m3, m2, T.TRE[:], A.max, ["m2", "TRE"], ["m3"], cyc(112))
+        cp(T.posU[:], m3, ["m3"], ["posU"])
         for k, (a, b) in enumerate(halves):
             for j in range(4):
-                if j == 0:
-                    mm([(P[1 + k][:, 0:b - a], T.Wo[:], ST[:, a:b])], ["Wo"] + STs, 1 + k, b - a, stop=False)
-                mm([(P[1 + k][:, 0:b - a], T.WN[:, 9 - 3 * j:137 - 3 * j], T.G[:, FP + 4 * a + j:FP + 4 * b:4])], ["WN"] + Gs[4 * k:4 * k + 4], 1 + k, b - a, 1, False, j == 3)
-            ac(T.RR[:, a:b], P[1 + k][:, 0:b - a], ["P%d" % (1 + k), "WS"], ["RR%d" % k], bias=wcol(cEL), ns=cyc(b - a), on="av")
-            marks["rows%d" % k, r] = len(nodes) - 1
-        cp(OF, ST[:, 0:V].indirect(eF), STs + ["eF"], ["OF"], ind(FP), "a")
-        if r == 1:
-            mm([(P[7][:, 0:FP], BQ, OF)], ["BQ", "OF"], 7, FP)
-            ts(T.MF[:], P[7][:, 0:FP], cI, A.is_equal, ["P7", "CF"], ["MF"], ns=cyc(FP))
-        mm([(P[0][:, 0:84], ZI, T.THF[:])], ["ZI0", "THF", "THz"], 0, 84, stop=False)
-        tt(T.NB[:], T.SX[:, 112:168].indirect(cF), T.MF[:], A.mult, ["SX", "cF", "MF"], ["NB"], ind(FP))
-        for k, (a, b) in enumerate(halves):
-            cp(T.C[:].indirect(T.posU[:, a // 16:b // 16]), T.RR[:, a:b], ["posU", "RR%d" % k], ["C"], ind(b - a, SC))
-        mm([(P[7][:, 0:FP], T.ZE0[:, 15 - fT:143 - fT], T.NB[:])], ["ZE0", "NB"], 7, FP)
-        ac(T.GF[:, V:V + FP], P[7][:, 0:FP], ["P7"], ["GF4"], scale=0.5, ns=cyc(FP))
+                mm([(P[3 + 4 * k][:, 0:b - a], T.WN[:, 9 - 3 * j:137 - 3 * j], T.G[:, 4 * a + j:4 * b:4])], ["WN"] + Gs, 3 + 4 * k, b - a, 1, False, j == 3)
+            ac(T.RR[:, a:b], P[3 + 4 * k][:, 0:b - a], ["P%d" % (3 + 4 * k), "WS"], ["RR%d" % k], bias=wcol(cEL), ns=cyc(b - a), on="av")
+        for k in range(SPLIT):
+            a, b = V // SPLIT * k, V // SPLIT * (k + 1)
+            cp(T.C[:].indirect(T.posU[:, a // 16:b // 16]), T.RR[:, a:b], ["posU", "RR%d" % (2 * k // SPLIT)], ["C0", "C1", "CJ"], ind(b - a, SC))
 
-    def far_control(r):
-        for k in range(4):
-            cp(T.GF[:, FP * k:FP * k + FP], ST[:, 0:SL + FP * r].indirect(T.FN[:, 56 * (r - 1) + 14 * k:56 * (r - 1) + 14 * k + 14]),
-               STw + ["FN%d" % (r - 1)] + ["lnd1_%d" % m for m in range(r)], ["GF%d" % k], ind(FP), GFQ)
-        GFs = ["GF%d" % k for k in range(4)]
-        listed(0, 0, T.ZE, T.GF, 84, ["ZE", "GF4", "OF"] + GFs, start=False)
-        f0, f1, f2, f3, f4 = [T.SX[:, 168 + 14 * k:182 + 14 * k] for k in range(5)]
-        cp(T.bf[:, 0:28], P[0][:, 0:28], ["P0"], ["bf0"])
-        ts(f1, P[0][:, 56:70], -1.0, A.mult, ["P0", "cF3"], ["f1"], cF3, A.add)
-        tt(T.bf[:, 28:56], P[0][:, 28:56], T.bf[:, 0:28], A.min, ["P0", "bf0"], ["bf1"])
-        tt(T.bf[:, 56:70], T.bf[:, 28:42], T.bf[:, 42:56], A.min, ["bf1"], ["bf2"])
-        cf, cb_ = T.can[:, 56:70], T.can[:, 56:69]
-        tt(cf, P[0][:, 70:84], T.bf[:, 56:70], A.is_lt, ["P0", "bf2", "THR"], ["cf", "isf"])
-        mm([(P[5][:, 0:14], Pa, cf), (P[5][:, 1:14], T.BK[:], cb_), (P[5][:, 1:14], nPa, cb_)], ["Pa", "BK", "nPa", "cf"], 5, 3 * 64)
-        scan(f0, cF5, 5, 0, 14, ["cF5"], ["f0"])
-        tt(f2, f0, f1, A.is_lt, ["f0", "f1"], ["f2"])
-        tt(f3, f0, f2, A.mult, ["f0", "f2"], ["f3"])
-        tt(f4, f3, T.TRE[:, 0:14], A.max, ["f3", "TRE"], ["f4"])
-        cp(T.posU[:, 56:70], f4, ["f4"], ["posF"])
-        mm([(P[7][:, 0:FP], T.Wo[:], OF)] + [(P[7][:, 0:FP], T.WN[:, 9 - 3 * j:137 - 3 * j], T.GF[:, FP * j:FP * j + FP]) for j in range(4)],
-           ["Wo", "WN", "OF"] + GFs, 7, 5 * FP)
-        ac(T.RF[:], P[7][:, 0:FP], ["P7", "WS"], ["RF"], bias=wcol(cEL), ns=cyc(FP), on="av")
-        cp(T.C[:].indirect(T.posU[:, 56:70]), T.RF[:], ["posF", "RF"], ["C"], ind(FP, SC))
-
-    def addresses(r, part):
-        a, b, c0, c1 = PARTS[part]
-        w, at = c1 - c0, (CF0, CB0)[part]
-        nc = 22 if r > 1 else 10
-        mm([(P[6][:, j:nc * w:w], T.C[:, at + j:at + 128 * w:w], WB[:, 0:nc]) for j in range(w)], ["C", "WB0", "WB"], 6, w * 64, start="each", stop="each")
-        ua, ub, uc = "UA%d" % part, "UB%d" % part, "UC%d" % part
-        cp(T.UA[:, 126 * part:126 * part + 9 * w], P[6][:, 0:9 * w], ["P6"], [ua], cyc(9 * w))
-        ts(T.UB[:, 70 * part:70 * part + 5 * w], P[6][:, 0:5 * w], 1.0, A.add, ["P6"], [ub], ns=cyc(5 * w))
-        tt(T.sm[:, 300 + c0:300 + c1], P[6][:, 9 * w:10 * w], T.MK[:, 8 + c0:8 + c1], A.min, ["P6", "TRX"], ["ez%d" % part])
-        ts(eU[:, c0:c1], T.sm[:, 300 + c0:300 + c1], BIG, A.add, ["ez%d" % part], ["eU%d" % part])
+    def far_records(r):
+        v_ = P[1][:, FP:FP + 14]
+        d16, yy, y6, h_, s_ = rf[3:8]
+        ts(ry[3], v_, -11.0, A.add, ["P1"], ["ry3"])
+        ts(d16, v_, R16, A.add, ["P1"], ["d16"], R16 + 48, A.subtract)
+        tt(yy, v_, d16, A.subtract, ["P1", "d16"], ["yy"])
+        ts(h_, d16, 0.375, A.mult, ["d16"], ["h_"], 1.0, A.min)
+        ts(yy, yy, 46.0, A.max, ["yy"], ["yy"], 49.0, A.min)
+        ts(y6, yy, 6.0, A.mult, ["yy"], ["y6"], -288.0, A.add)
+        tt(s_, yy, T.rimK[:, 32:46], A.add, ["yy", "J10"], ["s_"])
+        tt(y6, y6, h_, A.min, ["y6", "h_"], ["y6"])
+        tt(s_, s_, y6, A.add, ["s_", "y6"], ["s_"])
+        cp(ry[4], s_, ["s_"], ["ry4"])
+        at, ln = 3 * FP * ((r - 1) % LS), "lnd2_%d" % (r - 1)
+        for k, (L, nm) in enumerate(((L1, "L1"), (L3, "L3"))):
+            tt(T.pk2[:, FP * k:FP * k + FP], L.indirect(ry[3]), T.lnd2[:, at + k:at + 3 * FP:3], A.mult, [nm, "ry3", ln], ["pk2_%d" % k], ind(FP))
+        tt(TAB[:, 10 * base(r):10 * base(r) + FW].indirect(ry[4]), T.pk2[:, 0:FP], T.pk2[:, FP:2 * FP], A.add, ["pk2_0", "pk2_1", "ry4"], ["TF%d" % r], ind(FP, SC))
         if r > 1:
-            ki, zz, mn = T.ki[:, 0:4 * w], T.sm[:, 0:8 * w], T.sm[:, 160:160 + 8 * w]
-            ts(ki, P[6][:, 5 * w:9 * w], 1.0 / 64, A.mult, ["P6"], ["ki"], 2 - ZC - 0.49, A.add)
-            tt(zz[:, 4 * w:8 * w], P[6][:, 18 * w:22 * w], T.KE[:, 56 * part:56 * part + 4 * w], A.add, ["P6", "KE%d" % part], ["za"])
-            tt(zz[:, 0:4 * w], P[6][:, w:5 * w], ki, A.add, ["P6", "ki"], ["zz"])
-            tt(mn, P[6][:, 10 * w:18 * w], zz, A.min, ["P6", "zz", "za"], ["mn"], cyc(8 * w))
-            cp(T.UC[:, 112 * part:112 * part + 8 * w], mn, ["mn"], [uc], cyc(8 * w))
+            o = 4 * (base(r) - V)
+            tt(OUT[:, o:o + 4 * FP:4], T.MEM[:].indirect(ry[2]), T.lnd2[:, at + 2:at + 3 * FP:3], A.add, ["MEM", "ry2", ln], ["MF%d" % r], ind(FP))
+            cp(T.MEM[:, 0:FP], OUT[:, o:o + 4 * FP:4], ["MF%d" % r], ["MEM"], cyc(FP), "a")
 
-    def old_q(r, part):
-        a, b = PARTS[part][0:2]
-        ua, ub = "UA%d" % part, "UB%d" % part
-        win, names = upto(r - 1, 0), log(r - 1, 0)
-        cp(qe[:, 320 + a:320 + b], win.indirect(lists(part, "q1e")), names + [ub], ["q1e%d" % part], ind(b - a), "a")
-        cp(qe[:, a:b], win.indirect(lists(part, "q0e")), names + [ua], ["q0e%d" % part], ind(b - a), "a")
-        bank, o = OWN[part]
-        cp(P[bank][:, o:o + b - a], qe[:, a:b], ["q0e%d" % part], ["P%d" % bank], cyc(b - a), "a")
+    def addresses(r):
+        for h, (bank, a, b) in enumerate(((6, 0, NA), (0, NA, NA + NB))):
+            mm([(P[bank][:, 0:(b - a) * W], T.KR[:], T.CR[:, 0:(b - a) * W])], ["CR", "KR"], bank, (b - a) * W, stop=False)
+            mm([(P[bank][:, j:(b - a) * W:W], T.C[:, V + j:V + 128 * W:W], WB[:, a:b]) for j in range(W)], ["C0", "C1"] + WLs, bank, W * 64, start=False)
+        for h, bank in enumerate((6, 0)):
+            def pa(a, b):
+                return P[bank][:, 2 * W * a:2 * W * b]
+            nb, o = "P%d" % bank, 16 * W * h
+            sd, u_, t_, zz, gt = [sm[:, o + W * a:o + W * b] for a, b in ((0, 2), (2, 4), (4, 8), (8, 12), (12, 16))]
+            ns_, nu, nt, nz, ng, ke = [x + str(h) for x in ("sd", "u_", "t_", "zz", "gt", "KE")]
+            side = [t_[:, 2 * W * k:2 * W * (k + 1)] for k in range(2)]
+            ts(sd, pa(0, 1), 31.5, A.is_ge, [nb, "WD"], [ns_], -16384.0, A.mult)
+            ts(u_, pa(1, 2), -32768.0, A.add, [nb], [nu], 19.0, A.min)
+            for k in range(2):
+                tt(side[k], pa(2 + k, 3 + k), sd, A.mult, [nb, ns_], [nt + "ab"[k]])
+                tt(u_, pa(4 + k, 5 + k), u_, A.min, [nb, nu], [nu])
+            tt(t_, pa(6, 8), t_, A.add, [nb, nt + "a", nt + "b"], [nt + "a", nt + "b"], cyc(4 * W))
+            for k in range(2):
+                tt(side[k], side[k], u_, A.add, [nt + "ab"[k], nu], [nt + "ab"[k]], cyc(4 * W))
+            ts(T.UA[:, 4 * W * h:4 * W * (h + 1)], t_, -0.33, A.add, [nt + "a", nt + "b"], ["UA%d" % h], ns=cyc(4 * W))
+            if h == 0:
+                e0, e1, own, raw, step = sm[:, 32 * W:33 * W], sm[:, 33 * W:34 * W], *[P[bank][:, W * k:W * (k + 1)] for k in range(NB, NA)]
+                cp(T.UQ[:], own, [nb], ["UQ"])
+                ts(e0, step, R8192, A.add, [nb], ["e0"], R8192, A.subtract)
+                tt(e1, step, T.MK[:, 8:8 + W], A.add, [nb, "TRX"], ["e1"])
+                tt(e0, raw, e0, A.add, [nb, "e0"], ["e0"])
+                tt(e0, e0, e1, A.max, ["e0", "e1"], ["e0"])
+                cp(eU[:], e0, ["e0"], ["eU"])
+            if r > 1:
+                fl, own, far = T.KE[:, W * (4 * h + 2):W * (4 * h + 4)], zz[:, 0:2 * W], zz[:, 2 * W:4 * W]
+                ts(fl, pa(8, 9), R32, A.add, [nb], [ke], R32 + 4 * V, A.subtract)
+                tt(fl, fl, sd, A.add, [ke, ns_], [ke], cyc(4 * W))
+                tt(zz, pa(9, 11), T.KE[:, 4 * W * h:4 * W * (h + 1)], A.add, [nb, ke], [nz], cyc(4 * W))
+                for k, (x, y) in enumerate(((far, own), (own, far))):
+                    z = gt[:, 2 * W * k:2 * W * (k + 1)]
+                    tt(z, x, y, A.is_gt, [nz], [ng + "ab"[k]], cyc(4 * W))
+                    tt(z, z, x, A.mult, [nz, ng + "ab"[k]], [ng + "ab"[k]], cyc(4 * W))
+                cp(T.UC[:, 4 * W * h:4 * W * (h + 1)], gt, [ng + "a", ng + "b"], ["UC%d" % h], cyc(4 * W))
 
-    def old_fields(r, part):
-        a, b, c0, c1 = PARTS[part]
-        if (r, part) == (1, 1):
-            mm([(P[7][:, 0:CAP], W1(f), T.PT[0:1, 256 + CAP * k:256 + CAP * (k + 1)]) for k, f in enumerate((fJL, fJH, fP))], ["E1", "PJ0", "PJ1", "PJ2"], 7, 3 * CAP)
-            cp(T.JR[:], P[7][:, 0:CAP], ["P7"], ["JR"], cyc(CAP), "av")
-        if (r, part) == (1, 0):
-            mm([(P[6][:, 0:FP], ZI, aL), (P[6][:, 0:FP], Z128, aH), (P[6][:, 0:FP], Z128, aS2)], ["ZI0", "Z128", "aL", "aH", "aS2"], 6, 3 * FP)
-            cp(T.colU[:, FP:2 * FP], P[6][:, 0:FP], ["P6"], ["colL"], cyc(FP))
-        cp(T.GO[:, a:b], ST[:, 0:SL].indirect(eU[:, c0:c1]), STw + ["eU%d" % part], ["GO%d" % part], ind(b - a), "a")
-        mm([(P[7][:, 0:b - a], ZI, T.JR[:, a:b]), (P[7][:, 0:b - a], T.Wb[:], T.GO[:, a:b])], ["Wb", "GO%d" % part, "ZI0", "JR"], 7, 2 * (b - a))
-        ac(base[:, a:b], P[7][:, 0:b - a], ["P7", "BR%d" % r], ["base%d" % part], bias=T.BR[:, r:r + 1], ns=cyc(b - a))
-        cp(qe[:, 640 + a:640 + b], LI.indirect(lists(part, "case", 0, 1)), ["L3", "UA%d" % part], ["inv%d" % part], ind(b - a), "a")
+    def port_list(buf, k, second):
+        a = W * (4 * (k // 2) + 2 * second + k % 2)
+        return buf[:, a:a + W]
+
+    def old_q(r):
+        win, names = qlog(0, r - 1)
+        cp(qe[:], win.indirect(T.UQ[:]), names + ["UQ"], ["qe"], ind(CAP), "av")
+        mm([(P[4][:, 0:CAP], ZF, qe[:])], ["ZF", "qe"], 4, CAP, 4)
+        mm([(P[5][:, 0:CAP], ZF, qe[:])], ["ZF", "qe"], 5, CAP, 4, stop=False)
+
+    def old_fields(r):
+        cp(T.GO[:], ST[:, 0:SL].indirect(eU[:]), STw + ["eU"], ["GO"], ind(CAP), "av")
+        mm([(P[0][:, 0:CAP], ZI, T.JR[:]), (P[0][:, 0:CAP], T.Wb[:], T.GO[:])], ["Wb", "GO", "ZI0", "JR"], 0, 2 * CAP)
+        ac(fresh, P[0][:, 0:CAP], ["P0", "BR%d" % r], ["base"], bias=T.BR[:, r:r + 1], ns=cyc(CAP), on="av")
 
     def flux(r, s, step):
-        part = s // 4
-        k0, k1 = (s, s + 1) if s < 4 else (2 * s - 8, 2 * s - 6)
-        a, b = PARTS[part][0:2]
-        lo, wd = PORTS[4 * part + k0][0], (k1 - k0) * (b - a)
-        h, hb = (0, 1, 0, 1, 2, 3)[s], s % 2
-        at = (0, FP, 2 * FP, 2 * FP + 2 * NR)[h]
-        q1n, c1, sg = cq[:, lo:lo + wd], T.cb[:, lo:lo + wd], T.cb[:, 1280 + lo:1280 + lo + wd]
-        wn, un, we, ue, sq = [WK[:, 832 * j + at:832 * j + at + wd] for j in range(5)]
-        nm = {x: "%s%d" % (x, h) for x in ("wn", "un", "we", "ue", "sq", "r", "x")}
-        bj, bs, os_ = 1 + hb, 3 + hb * (1 - part), wd * hb * part
-        pn, pj, ps, nj, ns_ = P[bj][:, 0:wd], P[bj][:, wd:2 * wd], P[bs][:, os_:os_ + wd], "P%d" % bj, "P%d" % bs
-        win, names = upto(r - 1, 1 - part), log(r - 1, 1 - part)
-        ua, ub, uc = "UA%d" % part, "UB%d" % part, "UC%d" % part
-        case = lists(part, "case", k0, k1)
+        h, bj, bs = SLOT[s], 1 + s % 2, 3 + 4 * (s % 2)
+        rl, rr, sq = T.r[:, 2 * CAP * h:2 * CAP * h + CAP], T.r[:, 2 * CAP * h + CAP:2 * CAP * (h + 1)], T.sq[:, CAP * h:CAP * (h + 1)]
+        sg, ps, nj, ng = P[bs][:, 0:CAP], P[bj][:, 0:CAP], "P%d" % bj, "P%d" % bs
         if step == "g":
-            cp(c1, L1.indirect(case), ["L0", ua, "eF"], ["c1%d" % s], ind(wd), "a")
-            cp(q1n, win.indirect(lists(part, "q1n", k0, k1)), names + [ub], ["q1n%d" % s], ind(wd), "a")
-        elif step == "f":
-            def each(f):
-                def fn(_):
-                    for k in range(k0, k1):
-                        last = f((k - k0) * (b - a), b - a, k)
-                    return last
-                return fn
-            bank, o0 = OWN[part]
-            op({"v": (k1 - k0) * ind(b - a)},
-               each(lambda o, w_, k: vec.tensor_tensor(we[:, o:o + w_], L2.indirect(lists(part, "case", k, k + 1)), qe[:, 320 + a:320 + b], A.mult)),
-               ["L1", ua, "q1e%d" % part], [nm["we"]])
-            tt(wn, L3.indirect(case), q1n, A.mult, ["L2", ua, "q1n%d" % s], [nm["wn"]], ind(wd))
-            tt(un, win.indirect(lists(part, "q0n", k0, k1)), c1, A.mult, names + [ua, "c1%d" % s], [nm["un"]], ind(wd))
-            to, tn = (pj, nj) if s in JV else (ue, nm["ue"])
-            op({"v": (k1 - k0) * max(VMIN, (b - a) * CYC)},
-               each(lambda o, w_, k: vec.tensor_tensor(to[:, o:o + w_], P[bank][:, o0:o0 + w_], c1[:, o:o + w_], A.mult)), ["P%d" % bank, "c1%d" % s], [tn])
-            if s in JV:
-                tt(pj, pj, we, A.add, [nj, nm["we"]], [nj], cyc(wd))
-            if s not in JV:
-                mm([(pj, ZF, we)], ["ZF", nm["we"]], bj, wd, 4, stop=False)
-                mm([(pj, ZF, ue)], ["ZF", nm["ue"]], bj, wd, 4, start=False)
-            mm([(pn, T.NI[:], wn)], ["NI", nm["wn"]], bj, wd, 4, stop=False)
-            mm([(pn, T.NI[:], un)], ["NI", nm["un"]], bj, wd, 4, start=False)
+            win, names = tlog(r - 1)
+            cut(rl, win.indirect(port_list(T.UA, s, 0)), 1.0 / 32, names + ["UA%d" % (s // 2)], ["rl%d" % h], ind(CAP))
+            cut(rr, win.indirect(port_list(T.UA, s, 1)), -1.0 / 32, names + ["UA%d" % (s // 2)], ["rr%d" % h], ind(CAP))
         elif step == "m":
-            ac(rr[:, 2 * at:2 * at + 2 * wd], P[bj][:, 0:2 * wd], [nj], [nm["r"]], AF.Relu, ns=cyc(2 * wd))
-            ac(sq, rr[:, 2 * at:2 * at + wd], [nm["r"]], [nm["sq"]], AF.Square, ns=cyc(wd))
-            ac(ps, rr[:, 2 * at + wd:2 * at + 2 * wd], [nm["r"]], [ns_], AF.Square, ns=cyc(wd))
+            mm([(sg, SGM[s], T.GO[:])], ["SGM%d" % s, "GO"], bs, CAP)
+            ac(sq, rl, ["rl%d" % h], ["sq%d" % h], AF.Square, ns=cyc(CAP))
+            ac(ps, rr, ["rr%d" % h], [nj], AF.Square, ns=cyc(CAP))
         else:
-            f = FF[:, 8 + lo:8 + lo + wd]
-            ts(sg, c1, 0.0, A.is_lt, ["c1%d" % s], ["sg%d" % s], 0.5, A.subtract, cyc(wd // 2))
-            tt(ps, ps, sq, A.add, [ns_, nm["sq"]], [ns_], cyc(wd))
+            f = FF[:, 8 + CAP * s:8 + CAP * (s + 1)]
+            tt(sq, ps, sq, A.add, [nj, "sq%d" % h], ["sq%d" % h], cyc(CAP))
+            tt(f, sg, sq, A.mult, [ng, "sq%d" % h], ["F%d" % s], cyc(CAP))
             x, xn = f, "F%d" % s
             if r > 1:
-                x, xn = xx[:, at:at + wd], nm["x"]
-            if (r, s) in APART:
-                take, keep = T.TK[:, lo:lo + wd], T.TK[:, 1280 + lo:1280 + lo + wd]
-                cp(take, upto(r - 1, 1 - part, ZC).indirect(lists(part, "take", k0, k1)), names + [uc], ["take%d" % s], ind(wd), "a")
-                cp(keep, upto(r - 1, 1 - part, ZC).indirect(lists(part, "keep", k0, k1)), names + [uc], ["keep%d" % s], ind(wd), "a")
-                tt(ps, ps, sg, A.mult, [ns_, "sg%d" % s], [ns_], cyc(wd))
-                tt(x, ps, take, A.add, [ns_, "take%d" % s], [xn], cyc(wd))
-                for k in range(k0, k1):
-                    o = (k - k0) * (b - a)
-                    tt(LG[:, BL * r + 6 * a + 2 + k:BL * r + 6 * b:6], keep[:, o:o + b - a], ps[:, o:o + b - a], A.subtract, [ns_, "keep%d" % s],
-                       ["LG%d_%d" % (r, 4 * part + k)], cyc(b - a))
-            else:
-                tt(f, ps, sg, A.mult, [ns_, "sg%d" % s], ["F%d" % s], cyc(wd))
-            if r > 1 and (r, s) not in APART:
-                tt(x, upto(r - 1, 1 - part, ZC).indirect(lists(part, "take", k0, k1)), f, A.add, names + [uc, "F%d" % s], [xn], ind(wd))
-            bank, o0 = ACC[part]
-            pq, qf = P[bank][:, o0:o0 + b - a], LG[:, BL * r + 6 * a:BL * r + 6 * b:6]
-            if s == 0:
-                mm([(pq, ZF, qe[:, a:b])], ["ZF", "q0e0"], bank, wd, 4, stop=False)
+                win, names = olog(r - 1, 1)
+                x, xn = T.xx[:, CAP * (s % 2):CAP * (s % 2 + 1)], "x%d" % (s % 2)
+                tt(x, win.indirect(port_list(T.UC, s, 0)), f, A.add, names + ["UC%d" % (s // 2), "F%d" % s], [xn], ind(CAP))
             if s < 3:
-                mm([(pq, ZF, x)], ["ZF", xn], bank, wd, 4, start=False, stop=s == 2)
-            elif s == 3:
-                tt(qf, pq, x, A.add, ["P%d" % bank, xn], ["QA%d_0" % r], cyc(wd))
-            elif s == 4:
-                mm([(pq, ZF, qe[:, a:b]), (pq, ZF, x[:, 0:NR]), (pq, ZF, x[:, NR:2 * NR])], ["ZF", "q0e1", xn], bank, 3 * NR, 4, stop=False)
+                mm([(P[5][:, 0:CAP], ZF, x)], ["ZF", xn], 5, CAP, 4, start=False, stop=s == 2)
             else:
-                mm([(pq, ZF, x[:, 0:NR])], ["ZF", xn], bank, NR, 4, start=False)
-                tt(qf, pq, x[:, NR:2 * NR], A.add, ["P%d" % bank, xn], ["QA%d_1" % r], cyc(NR))
+                tt(record(0, r)[0], P[5][:, 0:CAP], x, A.add, ["P5", xn], [record(0, r)[1]], cyc(CAP))
 
-    def sums(r, part):
-        a, b = PARTS[part][0:2]
+    def sums(r):
+        meet(["MF%d" % r])
+        win, names = olog(r - 1, 0)
         for k in range(4):
-            if (r, 4 + k // 2 if part else k) in APART:
-                continue
-            lo, wd = PORTS[4 * part + k]
-            out, f, fn = LG[:, BL * r + 6 * a + 2 + k:BL * r + 6 * b:6], FF[:, 8 + lo:8 + lo + wd], "F%d" % (4 + k // 2 if part else k)
+            o = 4 * (base(r) - V)
+            out, on_, f = OUT[:, o + k:o + 4 * CAP:4], "O%d_%d" % (r, k), FF[:, 8 + CAP * k:8 + CAP * (k + 1)]
             if r == 1:
-                ac(out, f, [fn], ["LG%d_%d" % (r, 4 * part + k)], scale=-1.0, ns=cyc(wd))
+                ac(out, f, ["F%d" % k], [on_], scale=-1.0, ns=cyc(CAP), on="av")
             else:
-                tt(out, upto(r - 1, 1 - part, ZC).indirect(lists(part, "keep", k, k + 1)), f, A.subtract, log(r - 1, 1 - part) + ["UC%d" % part, fn],
-                   ["LG%d_%d" % (r, 4 * part + k)], ind(wd))
+                tt(out, win.indirect(port_list(T.UC, k, 1)), f, A.subtract, names + ["UC%d" % (k // 2), "F%d" % k, "MF%d" % r], [on_], ind(CAP))
 
-    def new_step(r, part):
-        a, b, c0, c1 = PARTS[part]
-        g1, nn, g2 = [gb[:, o + a:o + b] for o in (0, 320, 960)]
-        qf, qn = LG[:, BL * r + 6 * a:BL * r + 6 * b:6], "QA%d_%d" % (r, part)
-        ts(g1, qf, TH, A.is_gt, [qn, "TH"], ["g%d" % part], ns=cyc(b - a))
-        ts(g2, qf, T.NT[:, 0:1], A.is_lt, [qn, "NTH"], ["h%d" % part], ns=cyc(b - a))
-        mm([(P[7][:, 0:b - a], T.BK[:], g1), (P[7][:, 0:b - a], T.BK[:], g2)], ["BK", "g%d" % part, "h%d" % part], 7, 2 * (b - a))
-        ts(nn, P[7][:, 0:b - a], wcol(cTH), A.is_ge, ["P7", "WS"], ["nn%d" % part], wcol(cNN), A.mult, cyc(b - a))
+    def new_fields(r):
+        g1, nn, g2 = [gb[:, CAP * k:CAP * (k + 1)] for k in (0, 1, 3)]
+        qf, qn = record(0, r)
+        ts(g1, qf, TH, A.is_gt, [qn, "TH"], ["g"], ns=cyc(CAP))
+        ts(g2, qf, T.NT[:, 0:1], A.is_lt, [qn, "NTH"], ["h"], ns=cyc(CAP))
+        mm([(P[1][:, 0:CAP], T.BK[:], g1)], ["BK", "g"], 1, CAP, stop=False)
+        mm([(P[1][:, 0:CAP], T.BK[:], g2)], ["BK", "h"], 1, CAP, start=False)
+        ts(nn, P[1][:, 0:CAP], wcol(cTH), A.is_ge, ["P1", "WS"], ["nn"], wcol(cNN), A.mult, cyc(CAP))
+        tt(ST[:, 0:SL].indirect(eU[:]), nn, fresh, A.add, ["nn", "base", "eU"], STw, ind(CAP, SC))
 
-    def new_fields(part):
-        a, b, c0, c1 = PARTS[part]
-        tt(ST[:, 0:SL].indirect(eU[:, c0:c1]), gb[:, 320 + a:320 + b], base[:, a:b], A.add, ["nn%d" % part, "base%d" % part, "eU%d" % part], STw, ind(b - a, SC))
-
-    def new_q(r, part):
-        a, b = PARTS[part][0:2]
-        bank, o = OWN[part]
-        old = P[bank][:, o:o + b - a]
-        tt(old, LG[:, BL * r + 6 * a:BL * r + 6 * b:6], old, A.subtract, ["P%d" % bank, "QA%d_%d" % (r, part)], ["P%d" % bank], cyc(b - a))
-        tt(LG[:, BL * r + 6 * a + 1:BL * r + 6 * b:6], old, qe[:, 640 + a:640 + b], A.mult, ["P%d" % bank, "inv%d" % part], ["QB%d_%d" % (r, part)], cyc(b - a))
+    def new_q(r):
+        d, dn = T.sq[:, CAP * SLOT[1]:CAP * (SLOT[1] + 1)], "sq%d" % SLOT[1]
+        mm([(P[6][:, 0:CAP], Wi1, T.GO[:]), (P[6][:, 0:CAP], Wi2, T.JR[:])], ["Wi1", "Wi2", "GO", "JR"], 6, 2 * CAP)
+        tt(d, record(0, r)[0], P[4][:, 0:CAP], A.subtract, ["P4", record(0, r)[1]], [dn], cyc(CAP))
+        tt(record(1, r)[0], P[6][:, 0:CAP], d, A.mult, ["P6", dn], [record(1, r)[1]], cyc(CAP))
 
     def last_addresses():
-        cp(ST[:, 0:SL].indirect(eU[:]), base, ["base0", "base1", "eU0", "eU1"], STw, ind(CAP, SC))
-        cp(T.pk1[:], ST[:, 0:V].indirect(T.rimU[:, 0:14]), STs + ["rimU"], ["pk1"], ind(FP), "a")
-        listed(7, 0, T.ZP, T.pk1, 14, ["pk1", "ZP"])
-        tt(T.ryF[:, 0:14], P[7][:, 0:14], T.rimK[:, 16:30], A.add, ["P7", "rimL"], ["ryF"])
-        cp(T.ryU[:, 0:14], T.ryF[:, 0:14], ["ryF"], ["ry0"])
-        own_a, fa, fb = [T.PE[:, FP * k:FP * k + FP] for k in range(3)]
-        mm([(P[7][:, 0:FP], T.ZQ[:, 12 - 4 * m:140 - 4 * m], ST[:, m:V:4]) for m in range(4)], ["ZQ"] + STs, 7, 4 * FP)
-        ac(own_a, P[7][:, 0:FP], ["P7"], ["PE"], bias=4.0, ns=cyc(FP))
-        listed(7, 0, T.ZX, ST, 56, ["ZX"] + STs)
-        for k in range(2):
-            ts(T.qyU[:, 56 * k:56 * k + 56], P[7][:, 0:56], float(k), A.add, ["P7"], ["qyU%d" % k])
-        neighbours(True, True)
-        far = P[6][:, 14:FP + 14]
-        mm([(far, NBI, aK), (far, NBI, aF2)], ["Z64", "aK", "aF2"], 6, 2 * FP, stop=False)
-        by_slot(6, T.ZX, "ZX")
-        tt(fa, far, own_a, A.is_gt, ["P6", "PE"], ["fa"], cyc(FP))
-        tt(fb, far, fa, A.mult, ["P6", "fa"], ["fb"], cyc(FP))
-        ts(T.adU[:], fb, 2 - ZC + 6.0 / 64, A.add, ["fb"], ["adU"], ns=cyc(FP))
+        cp(ST[:, 0:SL].indirect(eU[:]), fresh, ["base", "eU"], STw, ind(CAP, SC))
+        rim_fields()
+        rim_lists(RO)
+        cp(T.pk2[:, FP:2 * FP], T.MEM[:].indirect(ry[2]), ["MEM", "ry2"], ["pk2_1"], ind(FP), "av")
+        own_a, fa = T.snd2[:, FP:2 * FP], T.snd2[:, 2 * FP:3 * FP]
+        meet(["snd2", "own", "fa", "snd3"])
+        mm([(P[0][:, 0:FP], T.ZQ[:, 12 - 4 * m:140 - 4 * m], ST[:, m:V:4]) for m in range(4)], ["ZQ"] + STs, 0, 4 * FP)
+        ac(own_a, P[0][:, 0:FP], ["P0"], ["own"], bias=0.875, ns=cyc(FP), on="av")
+        listed(0, 0, T.ZX, ST, 56, ["ZX"] + STs)
+        cp(T.qyU[:], P[0][:, 0:56], ["P0"], ["qyU"])
+        neighbours(True)
+        far = P[6][:, 0:FP]
+        mm([(far, Z8, aK), (far, Z8, aF)], ["Z8", "aK", "aF"], 6, 2 * FP, stop=False)
+        listed(6, 0, T.ZX, T.G, FP, Gs + ["ZX"], False)
+        tt(fa, far, own_a, A.is_gt, ["P6", "own"], ["fa"], cyc(FP))
+        tt(fa, far, fa, A.mult, ["P6", "fa"], ["fa"], cyc(FP))
+        ts(T.adU[:], fa, 4.0, A.mult, ["fa"], ["adU"], -4.0 * V, A.add, cyc(FP))
 
     for r in range(1, RO + 1):
-        marks["round", r] = len(nodes)
-        own_control(r)
+        marks[r] = len(nodes)
+        control(r)
         for step in ORDER.split():
-            if step[0] in "gfmb":
+            if step[0] in "gmb":
                 flux(r, int(step[1]), step[0])
-            elif step[0] == "e":
-                old_q(r, int(step[1]))
-            elif step[0] == "a":
-                addresses(r, int(step[1]))
-            elif step == "x":
-                far_control(r)
-            elif step[0] == "o":
-                old_fields(r, int(step[1]))
-            elif step == "q":
-                new_q(r, 1)
-            elif step == "s":
-                new_step(r, 1)
-            elif step == "n":
-                if r == RO:
-                    last_addresses()
-                new_fields(1)
-            else:
-                sums(r, 1)
+            elif step != "n":
+                {"f": far_records, "a": addresses, "e": old_q, "o": old_fields}[step](r)
+            elif r == RO:
+                last_addresses()
         if r == RO:
-            ac(T.pk2[:, 0:FP], FF[:, 0:8 + 4 * FP].indirect(T.ryU[:, 0:14]), ["FF0", "F0", "F1", "F2", "F3", "ry0"], ["pk2_0"], scale=-1.0, ns=ind(FP))
-            shift(7, 0, T.pk2, 0, T.ZF, ["pk2_0", "ZF"], 4)
-            cp(T.snd3[:], P[7][:, 0:FP], ["P7"], ["snd3"], cyc(FP), "a")
+            ac(T.pk2[:, 0:FP], FF[:].indirect(ry[1]), ["FF0", "F0", "F1", "F2", "F3", "ry1"], ["pk2_0"], scale=-1.0, ns=ind(FP))
+            shift(0, T.pk2, T.ZF, ["pk2_0", "ZF"], 4)
+            cp(T.snd2[:, 0:FP], P[0][:, 0:FP], ["P0"], ["snd3"], cyc(FP), "av")
             send(3, r, ["snd3"], "lnd3")
-        new_step(r, 0)
-        marks["step", r] = wr["nn0"]
-        new_fields(0)
+        new_fields(r)
         nodes[-1]["ends"] = r
         if r < RO:
             message1(r)
-        behind(("G", r + 1), new_q, r, 0)
-        behind(("G", r + 1), sums, r, 0)
+        new_q(r)
+        sums(r)
+        if r < RO:
+            rim_lists(r)
+            message2(r)
+            table(r)
 
-    full = log(RO, 0)
-    for j, (y, to, names) in enumerate(((T.y0, qe, ["q0e0", "q0e1", "q1e0", "q1e1", "inv0", "inv1"]), (T.y1, cq, ["q1n%d" % s for s in range(6)]))):
-        op({"x": 1.0}, None, [], names + ["y%d0" % j, "y%d1" % j], 1.0, None)
+    M, po, ya, yb, yc = TAB[:, 0:4 * V], TAB[:, 4 * V:5 * V], TAB[:, 5 * V:6 * V], TAB[:, 6 * V:7 * V], TAB[0:16, 7 * V:8 * V]
+    Ms = ["M%d" % k for k in range(NG)]
+    meet(tlog(RO - 1)[1] + Ms + ["y00", "y01", "y10", "y11", "YT0", "YT1"] + ["YM%d" % k for k in range(4)])
+    for j, (y, to) in enumerate(((T.y0, ya), (T.y1, yb))):
+        win, names = qlog(j, RO)
         for k in range(2):
-            cp(to[:, 448 * k:448 * k + 448], upto(RO, 0).indirect(T.qyU[:, 56 * j + 28 * k:56 * j + 28 * k + 28]), full + ["qyU%d" % j], ["y%d%d" % (j, k)], ind(448), "av")
-        store("s", y[:], to[:, 0:V], ["y%d0" % j, "y%d1" % j])
-    op({"x": 1.0}, None, [], ["r%d" % h for h in range(4)] + ["YT0", "YT1"], 1.0, None)
+            cp(to[:, 448 * k:448 * k + 448], win.indirect(T.qyU[:, 28 * k:28 * k + 28]), names + ["qyU"], ["y%d%d" % (j, k)], ind(448), "av")
+        store("s", y[:], to, ["y%d0" % j, "y%d1" % j])
     for k, (a, b) in enumerate(halves):
         mm([(P[1 + k][0:16, 0:b - a], T.Wy[:, 0:16], ST[:, a:b])], ["Wy0", "Wy1"] + STs, 1 + k, b - a)
-        cp(rr[0:16, a:b], P[1 + k][0:16, 0:b - a], ["P%d" % (1 + k)], ["YT%d" % k], cyc(b - a), "a")
+        cp(yc[:, a:b], P[1 + k][0:16, 0:b - a], ["P%d" % (1 + k)], ["YT%d" % k], cyc(b - a), "av")
     for j in range(2):
-        store("s", T.yt[:, V * j:V * j + V], rr[8 * j:8 * j + 8, 0:V], ["YT0", "YT1"])
-    M = WK
-    used = [x + h for x in ("wn", "un", "we", "ue", "sq") for h in "0123"]
-    Ms = ["M%d" % k for k in range(NG)]
-    op({"x": 1.0}, None, [], used + Ms, 1.0, None)
+        store("s", T.yt[:, V * j:V * j + V], yc[8 * j:8 * j + 8, :], ["YT0", "YT1"])
+    win, names = olog(RO, 0)
     for k in range(NG):
         w_ = FP // NG
-        cp(M[:, 16 * w_ * k:16 * w_ * (k + 1)], upto(RO, 0, ZC).indirect(T.adU[:, w_ * k:w_ * (k + 1)]), full + ["adU"], [Ms[k]], ind(16 * w_), "av")
-    Mr = T.pk2[:, FP:2 * FP]
-    cp(Mr, M[:, 0:4 * V].indirect(T.rimS[:, 0:14]), Ms + ["rimS"], ["pk2_1"], ind(FP), "av")
-    tt(M[:, 0:4 * V].indirect(T.rimS[:, 0:14]), Mr, T.lnd3[:], A.add, ["pk2_1", "lnd3", "rimS"], Ms, ind(FP, SC))
+        cp(M[:, 16 * w_ * k:16 * w_ * (k + 1)], win.indirect(T.adU[:, w_ * k:w_ * (k + 1)]), names + ["adU"], [Ms[k]], ind(16 * w_), "av")
+    tt(M.indirect(rimS), T.pk2[:, FP:2 * FP], piece(T, "lnd", 3, RO, 0, n - 1), A.add, ["pk2_1", "lnd3", "rimS"], Ms, ind(FP, SC))
     for k in range(4):
         a, pb, nm, ms_ = V * k, P[3 + k % 2][:, 0:FP], "P%d" % (3 + k % 2), Ms[2 * k:2 * k + 2]
         if k == 3:
@@ -1046,12 +1023,8 @@ def rank_program(g, core, T, topo):
             tt(po[:, FP * k:FP * k + FP], pb, M[:, a + 3:a + V:4], A.add, ms_ + [nm], ["YM%d" % k], cyc(FP))
         store("sa"[k % 2], T.ym[:, FP * k:FP * (k + 1)], po[:, FP * k:FP * (k + 1)], ["YM%d" % k])
 
-    for a, b, mark in soft:
-        for nd in nodes[a:b]:
-            nd["key"] = marks[mark] + 0.5 + 1e-5 * nd["key"] if mark in marks else nd["key"]
     for k, nd in enumerate(nodes):
-        size = marks["round", 3] - marks["round", 2]
-        nd["twin"] = divmod(k - marks["round", 2], size) if marks["round", 2] <= k < marks["round", RO] else None
+        nd["twin"] = divmod(k - marks[2], marks[3] - marks[2]) if TWINS and marks[2] <= k < marks[RO] else None
     seen = {e: {} for e in Q}
 
     def need(e, toks):

@@ -4,6 +4,7 @@ from concourse.mybir import AluOpType as A, ActivationFunctionType as AF
 
 V, FP, CAP, RO = 896, 224, 320, 5
 W = CAP // 16
+HF = FP // 2
 F, H, I, U = "float32", "bfloat16", "int32", "uint16"
 fS, fK, fEL, fEH, fT, fM, fD, fJL, fJH, fQ = 0, 4, 8, 9, 10, 11, 12, 13, 14, 15
 PAD = 4
@@ -13,24 +14,35 @@ BIG = 4096.0
 R16, R32, R8192 = 1.5 * 2 ** 27, 1.5 * 2 ** 28, 1.5 * 2 ** 36
 NA, NB = 25, 22
 cWO, cWN = 48, 64
-cS, cX, cZJ, cTH, cNN, cKP, cD, cB4, cR, cT, cEL, cI1, cI2, cV, cVN, cSG = range(80, 96)
+cS, cX, cZJ, cTH, cNN, cKP, cD, cB4, cR, cT, cEL, cI1, cI2, cV, cVN, cEN, cSG = range(80, 97)
 NW = cSG + 4
 SCALES = (0.5, 1.5, 2.5, 3.5, 2.25, 3.75)
 CASES = [(1.0, y - 0.5, [(y, 1, 1.0)]) for y in range(1, 5)] + [(1.0, 1.0, [(2, 2, 2.0)]), (0.5, 1.0, [(3, 2, 4.0), (4, 4, 8.0)]), (0.5, 1.5, [(4, 2, 4.0)]),
                                                                 (1.5, 2.25, [(3, 3, 2.0)]), (1.5, 3.75, [(4, 3, 2.0)])]
-MSG = [(1, m_) for m_ in range(RO)] + [(2, m_) for m_ in range(RO)] + [(3, RO)]
+MSG = [(1, m_) for m_ in range(RO)] + [(2, m_) for m_ in range(RO)] + [(3, m_) for m_ in range(1, RO + 1)]
 MSG.sort(key=lambda x: (x[1], x[0]))
 CYC, PCYC, GA, SC, LAT, DMA, HOP = 0.83, 0.42, 1.5, 3.6, 100.0, 2000.0, 4800.0
-MARGIN, TURNS, WAIT, SLACK, SHAKE, TWINS = 1500.0, 40, 100.0, 3.0, 300.0, True
-WAYS = ("bbaaaaaaa", "bbbbcccaa")
-TBANK = (5, 6, 0)
-GV = 28
+MARGIN, TURNS, WAIT, SLACK, SHAKE, URGE = 500.0, 100, 100.0, 3.0, 300.0, (("sent", 8000.0), ("posU", 3000.0))
+WAYS = ("bbbbaaaaa", "bbbbcccaa")
+TBANK = ("375375375", "605605252", "560560460")
+GV = 22
 SPLIT = 2
 VADD, VMIN, AADD, PFIX, CROSS = 0.0, 53.0, 66.0, 20.0, 120.0
-WIDE, FIRST, T2, T3, ONCE = 4000.0, 1.4, 1.5, 2.0, 3000.0
-MOVES = ((1, 3, 45000), (None, 2, 45000), (3, None, 35000))
-STEP, HEAT, SEED, MEAN, ASIDE, BEYOND = (0.0, 300.0, 600.0, 2500.0), 50.0, 3, 0.3, 0.4, 8000.0
+WIDE, FIRST, T2, T3, ONCE = (0.0, 3300.0, 2000.0), 1.4, 1.5, 2.0, 3000.0
+MOVES = ((None, 1, 2, 95000), (4, None, None, 85000))
+STEP, HEAT, SEED, MEAN, ASIDE, BEYOND = (0.0, 300.0, 600.0, 2500.0), 120.0, 6, 0.0, 0.0, 3000.0
 ORDER = "f a e o g0 g1 m0 g2 m1 b0 g3 m2 b1 m3 n b2 b3"
+ROUND = {
+    "v": "pkL G0.0 snd1_ G2 T_1 ry0 rf0.0 O_2 rf0.1 G6 ry1 pk2_1.0 G4 O_3 rf2.0 snd2_0 T_0 O_0 O_1 T_2 T_7 bit LZ0 LZ1 G0.1 T_3 cn T_5 rf2.1 T_4 m0 m1 m2 ry2 m3 "
+         "posU C0.1 d16 ry3 yy.0 h_ yy.1 C0.2 y6.0 s_.0 y6.1 pk2_1.1 s_.1 pk2_0.1 ry4 TF sd0 u_0.0 UQ t_0a.0 u_0.1 t_0b.0 u_0.2 t_0a.1 t_0b.1 t_0a.2 UA0 e0.0 e1 "
+         "KE0.0 e0.1 rl0.1 e0.2 u_1.0 sd1 KE0.1 KE1.0 t_1b.0 u_1.1 t_1a.0 KE1.1 zz0 t_1a.1 eU u_1.2 rr1 t_1b.1 gt0b.0 gt0a.0 t_1a.2 gt0b.1 zz1 UA1 gt0a.1 gt1a.0 "
+         "gt1b.0 gt1b.1 gt1a.1 UC0 sq1.1 sq0.1 MF.1 F0 F1 x0.0 sq2.1 UC1 F2 x1.0 x0.1 sq0.3 F3 x1.1 Q0_ g h sq1.2 Q1_ nn ST0",
+    "a": "pkN G3 G1 pk2_0.0 G5 G7 rl0.0 snd2_1 P4.1 P6.1 P0.1 XF pk2_2 RR0 snd3_0 RR1 T_8 T_6 T_9 qe rr0.0 rl1 sq0.0 P1.5 sq1.0 P2.4 GO rr2 rl2 P1.6 "
+         "sq2.0 rr0.1 rl0.2 P2.5 sq0.2 base MEM",
+    "p": "P5.0 P0.0 P6.0 P3.0 P7.0 P1.0 P1.1 P2.0 P4.0 P1.2 P5.1 P2.1 P2.2 P3.1 P7.1 P1.3 P4.2 P4.3 P4.4 P3.2 P3.3 P3.4 P4.5 P3.5 P7.2 P1.4 P7.3 P7.4 P7.5 P2.3 "
+         "P6.2 P6.3 P0.2 P0.3 P6.4 P6.5 P0.4 P0.5 P4.6 P5.2 P3.6 P7.6 P3.7 P0.6 P5.3 P7.7 P6.6 P5.4 P5.5 P3.8 P1.7 P1.8",
+    "g": "C0.0 C1 sent.0 sent.1 sent.2",
+}
 LS = 2
 SLOT = (0, 1, 2, 0)
 
@@ -51,17 +63,17 @@ def sb(n, t):
 
 
 SCRATCH = {
-    "ST": sb(SL + RO * FP, H), "C": sb(V + 8 * CAP, H), "G": sb(4 * V + FP, H), "GO": sb(CAP, H),
+    "ST": sb(SL + RO * FP, H), "C": sb(V + 8 * CAP, H), "G": sb(4 * V, H), "GO": sb(CAP, H),
     "RR": sb(V, H), "TAB": sb(10 * base(RO) + FW, F), "Q0": sb(NREC, F), "Q1": sb(NREC, F), "OUT": sb(4 * (NREC - V), F),
-    "snd1": sb(5 * FP, H), "snd2": sb(3 * FP, F), "lnd2": sb(LS * 3 * FP, F), "MEM": sb(FP + 8, F),
+    "snd1": sb(5 * FP, H), "snd2": sb(2 * FP, F), "lnd2": sb(LS * 2 * FP, F), "snd3": sb(FP, F), "lnd3": sb(LS * FP, F), "MEM": sb(FP + 8, F),
     "TD": sb(V, I), "TH": sb(8, F),
     "PI": sb(FP, I), "RI": sb(32, I), "RJ": sb(48, I), "rimU": sb(32, U), "rimS": sb(16, U), "rimK": sb(48, F), "ryF": sb(128, F), "ryU": sb(80, U),
-    "colU": sb(FP, U), "AB": sb(5 * FP + 16, H), "adU": sb(FP, U),
+    "colU": sb(FP, U), "AB": sb(5 * FP, H), "XF": sb(FP, H), "PKS": sb(FP, H), "LZ": sb(512, H), "THR": sb(512, H), "CO": sb(V, H), "adU": sb(FP, U),
     "Pi": sb(8, I), "CI": sb(8, I), "CF": sb(32, F), "MK": sb(32, F), "BR": sb(16, F), "E1": sb(4 * 144, H),
     "WS": sb(104, F), "WB": sb(104, H), "CR": sb(512, H), "KR": sb(128, H),
     "Wt": sb(128, H), "Wo": sb(128, H), "WN": sb(144, H), "ZJ": sb(240, H), "ZI": sb(256, H), "ZF": sb(240, F), "ZS": sb(6 * 128, F), "ZB": sb(6 * 128, H),
     "ZE0": sb(144, H), "ZO0": sb(144, H), "ZA0": sb(144, H), "ZE": sb(144, H), "ZX": sb(144, H), "ZO": sb(144, H), "ZQ": sb(144, H),
-    "Z2": sb(144, H), "ZA": sb(4 * 144, H), "BK": sb(128, H), "TR": sb(11 * 128, H), "Wb": sb(128, H), "Wy": sb(16, H), "CH": sb(FP, H), "JR": sb(CAP, H),
+    "Z2": sb(144, H), "ZA": sb(4 * 144, H), "BK": sb(128, H), "TR": sb(14 * 128, H), "Wb": sb(128, H), "Wy": sb(16, H), "CH": sb(FP, H), "JR": sb(CAP, H),
     "TRE": sb(56, F), "ONE": sb(56, F), "LT": sb(128, F), "KE": sb(8 * W, F),
     "bit": sb(FP, H), "can": sb(56, H), "v1": sb(4 * 56, F), "posU": sb(56, U),
     "UA": sb(8 * W, U), "UC": sb(8 * W, U), "UQ": sb(W, U), "eU": sb(W, U), "qyU": sb(56, U), "sm": sb(34 * W, F),
@@ -70,8 +82,8 @@ SCRATCH = {
 }
 for _k in range(8):
     SCRATCH["P%d" % _k] = ("psum", [128, 512], F)
-SEMAPHORES = (["v", "a", "p", "g", "loc", "out"] + ["in%d" % k for k in range(8)] + ["ls%d" % k for k in range(RO)]
-              + ["ar%d" % k for k in range(len(MSG))] + ["hs%d" % k for k in range(len(MSG))])
+SEMAPHORES = (["v", "a", "p", "g", "loc", "out"] + ["in%d" % k for k in range(10)]
+              + [x + str(k) for x in ("ar", "hs", "ls") for k in range(len(MSG))])
 
 
 def routes(T, topo):
@@ -103,13 +115,13 @@ def shares(engs, n):
 
 
 def piece(T, kind, which, m, a, n):
-    w = 96 if which == 2 else 32
+    w = 64 if which == 2 else 32
     if kind == "lnd":
-        buf, at = (T.ST, SL + FP * m) if which == 1 else (T.lnd2, 3 * FP * (m % LS))
+        buf, at = (T.ST, SL + FP * m) if which == 1 else (T["lnd%d" % which], 7 * w * (m % LS))
     elif kind == "hb":
-        buf, at = T.C if which == 1 else T.TAB, m * 3 * FP
+        buf, at = T.C if which == 1 else T.TAB, 128 * MSG.index((which, m))
     else:
-        buf, at = (T.snd1, m * FP) if which == 1 else (T.snd2, 0)
+        buf, at = T["snd%d" % which], m * FP if which == 1 else 0
     return buf[:, at + w * a:at + w * (a + n)]
 
 
@@ -158,6 +170,22 @@ def place(nodes, rank, before, after):
     return at
 
 
+def steady(nodes, pre):
+    one = {nd["step"][1]: k for k, nd in enumerate(nodes) if nd["step"] and nd["step"][0] == 3}
+    where = {s: e for e, row in ROUND.items() for s in row.split()}
+    where.update({s: "x" for s in one if s not in where})
+    rows = [[(f, s) for f in range(4) for s in row] for row in [x.split() for x in ROUND.values()] + [[s] for s in one if where[s] == "x"]]
+    waits = {s: [(nodes[j]["step"][0] - 3, nodes[j]["step"][1], lat) for j, lat in pre[k] if nodes[j]["step"]] for s, k in one.items()}
+    start, end, free = {}, {}, [0.0] * len(rows)
+    while any(rows):
+        for i, row in enumerate(rows):
+            while row and all(f_ + row[0][0] < 0 or (f_ + row[0][0], j) in end for f_, j, lat in waits[row[0][1]]):
+                f, s = row.pop(0)
+                start[f, s] = max([free[i]] + [end[f + f_, j] + lat + (CROSS if lat == LAT and where[j] != where[s] else 0.0) for f_, j, lat in waits[s] if f + f_ >= 0])
+                end[f, s] = free[i] = start[f, s] + nodes[one[s]]["ns"][where[s]]
+    return {s: start[3, s] - end[2, "ST0"] for s in one}, where, end[3, "ST0"] - end[2, "ST0"]
+
+
 def polish(nodes, pre, post, at):
     n, seed = len(nodes), [SEED]
 
@@ -165,25 +193,22 @@ def polish(nodes, pre, post, at):
         seed[0] = (seed[0] * 1103515245 + 12345) % 2147483648
         return (seed[0] + 0.5) / 2147483648
 
-    kin, ends = {}, {nd["ends"]: k for k, nd in enumerate(nodes) if "ends" in nd}
-    for k, nd in enumerate(nodes):
-        kin.setdefault(nd["twin"][1] if nd["twin"] else -1 - k, []).append(k)
-    alike = [kin[nd["twin"][1] if nd["twin"] else -1 - k] for k, nd in enumerate(nodes)]
+    ends = {nd["ends"]: k for k, nd in enumerate(nodes) if "ends" in nd}
+    when, where, length = steady(nodes, pre)
     key, on = [at[k][1] for k in range(n)], [at[k][0] for k in range(n)]
-    length = (key[ends[4]] - key[ends[2]]) / 2
-    for row in kin.values():
-        for i, k in enumerate(row):
-            key[k], on[k] = at[row[len(row) // 2]][1] + (i - len(row) // 2) * length, at[row[len(row) // 2]][0]
+    for k, nd in enumerate(nodes):
+        if nd["step"]:
+            key[k], on[k] = at[ends[1]][2] + (nd["step"][0] - 1) * length + when[nd["step"][1]], where[nd["step"][1]]
+        elif k > ends[2]:
+            key[k] += at[ends[1]][2] + 3 * length - at[ends[4]][2]
 
     def move(k, d, undo, most):
         todo = [(k, d)]
         while todo and len(undo) <= most:
-            a, d = todo.pop()
-            for i in alike[a]:
-                undo.append((i, key[i]))
-                key[i] += d
-            for i in alike[a]:
-                todo += [(j, key[i] - key[j] + math.copysign(0.01, d)) for j, lat in (post if d > 0 else pre)[i] if (key[i] - key[j]) * d >= 0]
+            i, d = todo.pop()
+            undo.append((i, key[i]))
+            key[i] += d
+            todo += [(j, key[i] - key[j] + math.copysign(0.01 + 0.01 * draw(), d)) for j, lat in (post if d > 0 else pre)[i] if (key[i] - key[j]) * d >= 0]
         return not todo
 
     for k in range(n):
@@ -221,9 +246,9 @@ def polish(nodes, pre, post, at):
         return (span + mean, end, why, who) if goal is None else (end[goal] + mean, end, why, goal)
 
     inside = []
-    for start, goal, moves in MOVES:
-        start, goal = ends.get(start), ends.get(goal)
-        inside[:] = [k for k in range(n) if (start is None or key[k] > key[start]) and (goal is None or key[k] <= key[goal])]
+    for start, stop, goal, moves in MOVES:
+        start, stop, goal = ends.get(start), ends.get(stop), ends.get(goal)
+        inside[:] = [k for k in range(n) if (start is None or key[k] > key[start]) and (stop is None or key[k] <= key[stop])]
         now = times(-1e30, [0.0] * n, [None] * n, goal)
         best = (now[0], list(key), list(on))
         for turn in range(moves):
@@ -232,7 +257,7 @@ def polish(nodes, pre, post, at):
                 k = inside[int(draw() * len(inside))]
             links = []
             while why[k] and (start is None or key[k] > key[start]):
-                if why[k][1]:
+                if why[k][1] and (stop is None or key[k] < key[stop] + BEYOND):
                     links.append((why[k][0], k))
                 k = why[k][0]
             if not links:
@@ -242,14 +267,13 @@ def polish(nodes, pre, post, at):
             turned = both[int(draw() * len(both))] if both and z < 0.15 else None
             if turned is not None:
                 was = on[turned]
-                for i in alike[turned]:
-                    undo.append((i, key[i]))
-                    on[i] = "v" if was == "a" else "a"
+                undo.append((turned, key[turned]))
+                on[turned] = "v" if was == "a" else "a"
                 ok = True
             elif z < 0.55:
-                ok = move(v, key[u] - key[v] - 0.01 + STEP[int(draw() * len(STEP))] * math.log(draw()), undo, 60)
+                ok = move(v, key[u] - key[v] - 0.01 * (1 + z) + STEP[int(draw() * len(STEP))] * math.log(draw()), undo, 60)
             else:
-                ok = move(u, key[v] - key[u] + 0.01 - STEP[int(draw() * len(STEP))] * math.log(draw()), undo, 60)
+                ok = move(u, key[v] - key[u] + 0.01 * (1 + z) - STEP[int(draw() * len(STEP))] * math.log(draw()), undo, 60)
             new = times(min(min(x, key[i]) for i, x in undo), list(end), list(why), goal) if ok else None
             if ok and new[0] - span <= -math.log(draw()) * (HEAT * (1 - turn / moves) + 2):
                 now = new
@@ -276,10 +300,18 @@ def arrange(nodes):
                 lat = 0.0 if nd["tok"] is False or list(nd["ns"]) == list(nodes[j]["ns"]) == ["p"] else nodes[j]["lat"]
                 pre[k].append((j, lat))
                 post[j].append((k, lat))
+        urge = [0.0] * n
+        for name, more in URGE:
+            urgent = {[nd["out"][0:1] for nd in nodes].index([name])}
+            for k in range(n - 1, -1, -1):
+                if k in urgent:
+                    urgent.update(nodes[k]["pre"])
+                    urge[k] += more
         rank, best, now, seed = [-k for k in range(n)], None, None, SEED
         for turn in range(TURNS):
             at = place(nodes, rank, pre, post)
-            span = max(at[k][2] + nodes[k]["lat"] for k in range(n))
+            ends = [at[k][2] for k, nd in enumerate(nodes) if "ends" in nd]
+            span = max(at[k][2] + nodes[k]["lat"] for k in range(n)) - (ends[3] - ends[0]) * 0.8
             if best is None or span < best[0]:
                 best = (span, at)
             if turn < 8 or span < now[0] + SHAKE:
@@ -288,7 +320,7 @@ def arrange(nodes):
             rank = []
             for k in range(n):
                 seed = (seed * 1103515245 + 12345) % 2147483648
-                rank.append(back[k][2] + (SHAKE * (seed % 2001 / 1000 - 1) if turn > 6 and seed // 4096 % 3 == 0 else 0.0))
+                rank.append(back[k][2] + urge[k] + (SHAKE * (seed % 2001 / 1000 - 1) if turn > 6 and seed // 4096 % 3 == 0 else 0.0))
         PLACED[n] = polish(nodes, pre, post, best[1])
     span, key, on = PLACED[n]
     for k, nd in enumerate(nodes):
@@ -322,8 +354,8 @@ def rank_program(g, core, T, topo):
 
     lay = plan[rank][1][0][1] + plan[rank][1][1][1] + plan[rank][0]
     Q = {"v": g.vector, "a": g.scalar, "p": g.tensor, "g": g, "s": g.sync}
-    cnt = {"v": 0, "a": 0, "p": 0, "g": 0, "loc": 0, "out": 0}
-    cnt.update({"ls%d" % k: leave for k in range(RO)})
+    cnt = {"v": 0, "a": 0, "p": 0, "g": 0, "out": 0}
+    cnt.update({"ls%d" % k: leave for k in range(len(MSG))})
     nodes, wr, rd = [], {}, {}
 
     def op(ns, fn, reads, writes, lat=LAT, tok=True):
@@ -406,10 +438,10 @@ def rank_program(g, core, T, topo):
     def sel(out, a, cmp, fill, base_, cm, reads, writes, step=1):
         op({"g": 170 + 256 * CYC}, lambda e: g.affine_select(out, a, [[step, 128]], cmp, fill, base_, cm), reads, writes)
 
-    def load(e, k, out, src, name, turn=1):
+    def load(e, k, out, src, name, turn=1, reads=(), ns=60.0):
         def fn(_):
             Q[e].dma_start(out, src).then_inc(T.sem["in%d" % k], 16)
-        op({e: 60.0}, fn, ["issued"], [name], DMA * turn, ("in%d" % k, 16))
+        op({e: ns}, fn, ["issued"] + list(reads), [name], DMA * turn, ("in%d" % k, 16))
         op({"x": 1.0}, None, [], ["issued"], 1.0, False)
 
     def store(e, out, src, reads):
@@ -419,7 +451,7 @@ def rank_program(g, core, T, topo):
         op({e: 60.0}, fn, reads, [], DMA, None)
 
     def send(which, m, reads, lands):
-        left = "ls%d" % m if which == 2 else "loc"
+        left = "ls%d" % MSG.index((which, m))
 
         def fn(_):
             tr = []
@@ -429,11 +461,10 @@ def rank_program(g, core, T, topo):
                                             src=piece(T, "snd", which, m, lay.index(blocks[0]), len(blocks)), dst=piece(T, "hb", which, m, 0, len(blocks))))
             g.remote_dma_fused(tr, local_sem=T.sem[left])
             forward(g, T, topo, core, rank, plan[rank][0], "snd", lay.index(plan[rank][0][0]), which, m, T.sem[left])
-            cnt["loc"] += leave * (left == "loc")
         op({"g": ONCE if (which, m) == (1, 0) else 1000.0}, fn, reads, ["sent"], 1.0, None)
-        op({"x": HOP * (FIRST if m == 0 else 1) - 1000.0 + (WIDE if which == 2 else 0.0)}, None, ["sent"], [lands], 1.0, ("ar%d" % MSG.index((which, m)), arrive))
-        if which == 2:
-            op({"x": HOP}, None, ["sent"], ["snd2"], 1.0, (left, leave))
+        op({"x": HOP * (FIRST if m == 0 else 1) - 1000.0 + WIDE[which - 1]}, None, ["sent"], [lands], 1.0, ("ar%d" % MSG.index((which, m)), arrive))
+        if which > 1:
+            op({"x": HOP}, None, ["sent"], ["snd%d" % which], 1.0, (left, leave))
         rd["sent"] = []
 
     P = [T["P%d" % k] for k in range(8)]
@@ -467,6 +498,8 @@ def rank_program(g, core, T, topo):
     cI, cG, cQ, cK, cP, cM, cE, nE, cO, n16, c12, c8, c2, cA, nS, cF0, cF1 = [CF[:, k:k + 1] for k in range(17)]
     s0, s1, s2, s3 = [T.TD[:, FP * k:FP * k + FP] for k in range(4)]
     TRs, Pa, nPa, Z8, tmp, Wi1, Wi2, Wv, Wvn = [T.TR[:, 128 * k:128 * k + 128] for k in range(9)]
+    KB, nKB, EB = [T.TR[:, 128 * k:128 * k + 128] for k in range(11, 14)]
+    cH = [CF[:, k:k + 1] for k in (17, 18)]
     SGM = [T.TR[:, 128 * k:128 * k + 128] for k in (9, 10)] + [T.ZA[:, 144 * k:144 * k + 128] for k in (0, 1)]
     ZF, ZI = T.ZF[:, 0:128], T.ZI[:, 0:128]
     halves, wide = ((0, V // 2), (V // 2, V)), ((0, 512), (512, V))
@@ -544,7 +577,6 @@ def rank_program(g, core, T, topo):
             shift(7, T.pk1, T.ZI, ["pkL", "ZI", "ZI0"], 1)
             tt(T.snd1[:, 0:FP], P[7][:, 0:FP], T.CH[:], A.add, ["P7", "CH"], ["snd1_0"], cyc(FP))
         else:
-            mm([(P[3][:, 0:FP], ZI, T.CH[:])], ["ZI0", "CH"], 3, FP, stop=False)
             rim_fields()
             shift(3, T.pk1, T.ZJ, ["pkL", "ZJ"], 1, False)
             ac(T.snd1[:, m * FP:(m + 1) * FP], P[3][:, 0:FP], ["P3", "BJ%d" % m], ["snd1_%d" % m], bias=T.BR[:, 8 + m:9 + m], ns=cyc(FP), on="av")
@@ -574,18 +606,25 @@ def rank_program(g, core, T, topo):
         ts(ry[2], rf[2], float(FP), A.min, ["rf2"], ["ry2"])
 
     def message2(m):
-        for k in range(3):
-            out, bank = T.pk2[:, FP * k:FP * (k + 1)], (2, 4, 0 if m else 2)[k]
-            if k < 2:
-                win, names = qlog(k, m) if m else ((qa, ["qa"]), (qb, ["qb"]))[k]
-                cp(out, win.indirect(ry[0] if m else rimU), names + ["ry0" if m else "rimU"], ["pk2_%d" % k], ind(FP), "av")
-            elif m:
-                o = 4 * (base(m) - V)
-                cp(out, OUT[:, o - 16:o + 4 * CAP].indirect(ry[1]), ["O%d_%d" % (m, j) for j in range(4)] + ["ry1", "OZ%d" % m], ["pk2_2"], ind(FP), "av")
-            if k < 2 or m:
-                shift(bank, out, T.ZF, ["pk2_%d" % k, "ZF"], 4)
-            cp(T.snd2[:, k:3 * FP:3], P[bank][:, 0:FP], ["P%d" % bank, "snd2"], ["snd2_%d" % k], cyc(FP), "av")
-        send(2, m, ["snd2_%d" % k for k in range(3)], "lnd2_%d" % m)
+        for k in range(2):
+            out, bank = T.pk2[:, FP * k:FP * (k + 1)], (2, 4)[k]
+            win, names = qlog(k, m) if m else ((qa, ["qa"]), (qb, ["qb"]))[k]
+            cp(out, win.indirect(ry[0] if m else rimU), names + ["ry0" if m else "rimU"], ["pk2_%d" % k], ind(FP), "av")
+            shift(bank, out, T.ZF, ["pk2_%d" % k, "ZF"], 4)
+            cp(T.snd2[:, k:2 * FP:2], P[bank][:, 0:FP], ["P%d" % bank, "snd2"], ["snd2_%d" % k], cyc(FP), "av")
+        send(2, m, ["snd2_0", "snd2_1"], "lnd2_%d" % m)
+
+    def message3(m):
+        out = T.pk2[:, 2 * FP:3 * FP]
+        if m < RO:
+            o = 4 * (base(m) - V)
+            cp(out, OUT[:, o - 16:o + 4 * CAP].indirect(ry[1]), ["O%d_%d" % (m, j) for j in range(4)] + ["ry1", "OZ%d" % m], ["pk2_2"], ind(FP), "av")
+        else:
+            ac(out, T.FF[:].indirect(ry[1]), ["FF0", "F0", "F1", "F2", "F3", "ry1"], ["pk2_2"], scale=-1.0, ns=ind(FP))
+        bank = 1 if m < RO else 0
+        shift(bank, out, T.ZF, ["pk2_2", "ZF"], 4)
+        cp(T.snd3[:], P[bank][:, 0:FP], ["P%d" % bank, "snd3"], ["snd3_0"], cyc(FP), "av")
+        send(3, m, ["snd3_0"], "lnd3_%d" % m)
 
     def table(r):
         j = 0
@@ -594,7 +633,7 @@ def rank_program(g, core, T, topo):
             x0, x1 = (QQ[0][:, a:b], QQ[1][:, a:b]) if r else (qa[:, a:b], qb[:, a:b])
             n0, n1 = ("Q0_%d" % r, "Q1_%d" % r) if r else ("qa", "qb")
             for i, ((c0, c1, outs), way) in enumerate(zip(CASES, WAYS[r > 0])):
-                bank = TBANK[i % len(TBANK)]
+                bank = int(TBANK[2 if r else a > 0][i])
                 pb, nb = P[bank][:, 0:w], "P%d" % bank
                 (z0, m0_), (z1, m1_) = scaled(c0, r), scaled(c1, r)
                 up0 = outs[0][2]
@@ -645,11 +684,12 @@ def rank_program(g, core, T, topo):
              (fM, cTH, 3.5, 1, 1), (fD, cTH, 8.5, 1, 1), (fM, cNN, -2, 1, 1), (fD, cNN, 1, 1, 1), (0, cKP, 1, 11, NW), (fM, cD, 1, 1, 1), (fD, cD, -1, 1, 1),
              (fM, cB4, 4, 1, 1), (fJL, cR, PAD, 1, 1), (fJH, cR, CAP / 128, 1, 1), (fT, cT, 1, 1, 1), (1, cEL, 16, 4, 3 * NW),
              (fM, cI1, -0.125, 1, 1), (fD, cI1, 0.5, 1, 1), (fQ, cI2, 0.75, 1, 1), (fT, cV, 0.5, 1, 1), (fM, cV, 8.5, 1, 1), (fD, cV, -8.5, 1, 1),
-             (fT, cVN, -0.5, 1, 1), (fS, cSG, 1, 4, NW + 1)]
+             (fT, cVN, -0.5, 1, 1), (fEL, cEN, 1, 1, 1), (fEH, cEN, 8192, 1, 1), (fS, cSG, 1, 4, NW + 1)]
     places = [RW[:, NW * f + col:NW * f + col + (count - 1) * step + 1:step] for f, col, c, count, step in terms]
-    fills("a", [(x, x, t[2]) for x, t in zip(places[1::2], terms[1::2])], ["RW0"], ["RWa"])
-    fills("v", [(x, x, t[2]) for x, t in zip(places[0::2], terms[0::2])], ["RW0"], ["RWv"])
-    mm([(P[5][:, 0:NW], W1(f), RW[:, NW * f:NW * f + NW]) for f in range(16)], ["E1", "RWa", "RWv"], 5, 16 * NW)
+    RWs = ["RW%d" % k for k in range(1, 9)]
+    for k in range(8):
+        fills("av", [(x, x, t[2]) for x, t in zip(places[k::8], terms[k::8])], ["RW0"], [RWs[k]])
+    mm([(P[5][:, 0:NW], W1(f), RW[:, NW * f:NW * f + NW]) for f in range(16)], ["E1"] + RWs, 5, 16 * NW)
     either[0] = "av"
     cp(WS[:, 0:NW], P[5][:, 0:NW], ["P5"], ["WS"], cyc(NW), "a")
     cp(WB[:, cWO:cS], WS[:, cWO:cS], ["WS"], ["WB0"], cyc(32), "a")
@@ -668,8 +708,6 @@ def rank_program(g, core, T, topo):
     ac(cA, cK, ["CF", "c8"], ["cA"], bias=c8)
     ac(nS, wcol(cS), ["WS"], ["nS"], scale=-1.0)
     cp(XB, X[0:1, :], ["X"], ["XB"], cyc(256), "a")
-    cp(T.Q0[:, 0:V], qa, ["qa"], ["Q0_0"], cyc(V), "a")
-    cp(T.Q1[:, 0:V], qb, ["qb"], ["Q1_0"], cyc(V), "a")
     cp(T.ZF[:], T.ZI[:, 0:240], ["ZI", "ZI0"], ["ZF"], cyc(240), "a")
     for k, c_ in enumerate(SCALES):
         ac(T.ZB[:, 128 * k:128 * k + 128], ZI, ["ZI0"], ["ZB%d" % k], scale=c_, ns=cyc(128), narrow=True)
@@ -719,6 +757,8 @@ def rank_program(g, core, T, topo):
     ac(nPa, Pa, ["Pa"], ["nPa"], scale=-1.0, ns=cyc(128), narrow=True)
     ms(T.ONE[:], 1.0, ["ONE"])
     message2(0)
+    for k, x in enumerate((T.q0, T.q1)):
+        load("g", 8 + k, QQ[k][:, 0:V], x[:], "Q%d_0" % k, T3, ["sent"], 1000.0)
     ac(T.MK[:, 8:8 + W], T.TRE[:, 0:W], ["TRE"], ["TRX"], bias=float(V))
     ac(T.rimK[:, 32:46], T.TRE[:, 0:14], ["TRE"], ["J10"], scale=10.0, bias=-27.0)
     mm([(P[4][:, 16 * (8 * h + j):16 * (8 * h + j) + 16], T.ZI[0:16, 128 - 16 * j:256 - 16 * j], WB[0:16, cWO + 16 * h:cWO + 16 * h + 16]) for h in range(2) for j in range(8)],
@@ -729,7 +769,6 @@ def rank_program(g, core, T, topo):
     ac(T.ZJ[:], T.ZI[:, 0:240], ["ZI", "ZI0", "WS"], ["ZJ"], scale=wcol(cZJ), ns=cyc(240), narrow=True)
     ac(T.ZX[:], T.ZE0[:], ["ZE0", "WS"], ["ZX"], scale=wcol(cX), ns=cyc(144), narrow=True)
     ms(T.FF[:, 0:8], 0.0, ["FF0"])
-    ms(T.AB[:, 5 * FP:5 * FP + 14], -3.0, ["SGx"])
     ms(T.MEM[:], 0.0, ["MEM"], cyc(FP))
     ts(T.NT[:, 0:1], T.TH[:, 0:1], -1.0, A.mult, ["TH"], ["NTH"])
     iota(T.KE[:], [[2, 2], [1, 4], [0, W]], -4 * V, 0, ["KE0", "KE1"], c=8 * W, reads=["late"])
@@ -763,18 +802,23 @@ def rank_program(g, core, T, topo):
     ac(T.Wy[:, 0:8], T.BK[:, 0:128:16], ["BK", "WS"], ["Wy0"], scale=wcol(cT))
     ac(T.Wy[:, 8:16], T.BK[:, 0:128:16], ["BK", "WS"], ["Wy1"], scale=wcol(cD))
     ac(Z8, ZI, ["ZI0"], ["Z8"], scale=8.0, ns=cyc(128), narrow=True)
+    for x, col, nm, src in ((KB, wcol(cS), "KB", "WS"), (nKB, nS, "nKB", "nS"), (EB, wcol(cEN), "EB", "WS")):
+        ac(x, T.BK[:], ["BK", src], [nm], scale=col, ns=cyc(128), narrow=True)
+    for h in range(2):
+        ts(cH[h], cP, up - HF * h - 0.5, A.is_ge, ["cP"], ["cH%d" % h], 255.5, A.add)
+    THRs, COs = ["THR%d" % k for k in range(4)], ["CO%d" % k for k in range(16)]
     for k, (pat, base_) in enumerate((([[0, 3], [1, 128]], PAD), ([[1, 3], [0, 128]], V // 128))):
         iota(PJ[:, 384 * k:384 * (k + 1)], pat, base_, 0, ["PJ%d" % k], c=384, reads=["late"])
     mm([(P[2][:, 0:CAP], W1(f), x[:, 0:CAP]) for f, x in ((fJL, PJ), (fJH, PJ[:, 384:768]), (fQ, T.CR[0:1, :]))], ["E1", "PJ0", "PJ1", "CR"], 2, 3 * CAP)
     cp(T.JR[:], P[2][:, 0:CAP], ["P2"], ["JR"], cyc(CAP), "a")
     table(0)
     for k, c_ in enumerate(SCALES):
-        ac(T.ZS[:, 128 * k:128 * k + 128], ZI, ["ZI0"], ["ZS%d" % k], scale=c_, ns=cyc(128))
+        sel(T.ZS[:, 128 * k:128 * k + 128], ZF, A.not_equal, c_, 0, -1, ["ZF", "late"], ["ZS%d" % k])
 
     either[0] = ""
     NG = 8
     Gs = ["G%d" % k for k in range(NG)]
-    meet(["RW0", "RWa", "RWv", "HI", "HJ", "PT", "XB"] + Gs)
+    meet(["RW0", "HI", "HJ", "PT", "XB"] + RWs + Gs)
     meet(["PJ0", "PJ1", "CJ"])
     meet(["TB", "RR0", "RR1"])
     meet(["qa", "g", "h", "nn", "base"])
@@ -788,21 +832,40 @@ def rank_program(g, core, T, topo):
             a, b = edge[k], edge[k + 1]
             cp(T.G[:, 16 * a:16 * b], ST[:, 0:SL].indirect(T.colU[:, a:b]), STw + ["colU"], [Gs[k]], ind(16 * (b - a)), "av" if free else "va"[k % 2])
 
+    def by_slot(bank, Z, zn, pieces):
+        for j in range(pieces):
+            a, b = FP // pieces * j, FP // pieces * (j + 1)
+            mm([(P[bank][:, a:b], Z[:, 15 - i:143 - i], T.G[:, 16 * a + i:16 * b:16]) for i in range(16)], Gs[NG // pieces * j:NG // pieces * (j + 1)] + [zn], bank,
+               16 * (b - a), start=False, stop=j == pieces - 1)
+
     def control(r):
         for k in range(2):
             zero(T.C, V + 4 * CAP * k, V + 4 * CAP * (k + 1), ["C%d" % k], ["late"])
-        meet(early * (r == 4) + ["TF%d" % r])
-        mm([(P[1][:, 0:FP + 14], ZI, T.AB[:, 4 * FP:5 * FP + 14])] + [(P[1][:, 0:FP], T.ZO[:, 12 - 4 * m:140 - 4 * m], ST[:, m:V:4]) for m in range(4)], ["ZI0", "SG", "SGx", "ZO"] + STs, 1, 5 * FP, stop=False)
+        meet(["room", "TF%d" % r] + early * (r == 4))
+        mm([(P[1][:, 0:FP], ZI, SG)] + [(P[1][:, 0:FP], T.ZO[:, 12 - 4 * m:140 - 4 * m], ST[:, m:V:4]) for m in range(4)], ["ZI0", "SG", "ZO"] + STs, 1, 5 * FP, stop=False)
         for k, (a, b) in enumerate(halves):
             mm([(P[3 + 4 * k][:, 0:b - a], T.Wo[:], ST[:, a:b])], ["Wo"] + STs, 3 + 4 * k, b - a, stop=False)
         neighbours(r == 1)
         landed, ln = piece(T, "lnd", 1, r - 1, 0, n - 1), "lnd1_%d" % (r - 1)
-        cp(T.G[:, 0:4 * V].indirect(rimS), landed, [ln, "rimS"], Gs, ind(FP, SC))
-        mm([(P[2][:, 0:FP], Wv, pkN), (P[2][:, 0:FP], Wvn, landed)], ["Wv", "Wvn", "pkN", ln], 2, 2 * FP)
-        cp(T.G[:, 4 * V:4 * V + FP], P[2][:, 0:FP], ["P2"], ["XF"], cyc(FP), "av")
-        listed(1, 0, T.ZE, T.G, FP + 14, Gs + ["ZE", "XF"], False)
+        if r == 1:
+            cp(T.G[:].indirect(rimS), landed, [ln, "rimS"], Gs, ind(FP, SC))
+        by_slot(1, T.ZE, "ZE", 1 if r == 1 else 2)
         ts(T.bit[:], P[1][:, 0:FP], 0.0, A.is_gt, ["P1"], ["bit"], ns=cyc(FP))
-        mm([(P[4][:, 0:56], T.Z2[:, 12 - 4 * h:140 - 4 * h], T.bit[:, h:FP:4]) for h in range(4)], ["Z2", "bit"], 4, 256)
+        if r > 1:
+            for k, (x, z, names) in enumerate(((pkN, nKB, ["pkN", "nKB"]), (landed, KB, [ln, "KB"]))):
+                mm([(P[2][0:HF, 128 * h:128 * h + 128], x[:, HF * h:HF * (h + 1)], z) for h in range(2)], names, 2, 256, start=k == 0, stop=k == 1)
+            for k in range(2):
+                tt(T.LZ[0:HF, 256 * k:256 * k + 256], P[2][0:HF, 0:256], T.THR[0:HF, 256 * k:256 * k + 256], A.is_lt, ["P2"] + THRs, ["LZ%d" % k], cyc(256))
+                mm([(P[4][:, 0:56], T.KR[:], T.CR[:, 0:56])] * (k == 0)
+                   + [(P[4][32 * q:32 * q + 32, 0:56], T.LZ[0:HF, 256 * k + 128 * h + 32 * q:256 * k + 128 * h + 32 * q + 32],
+                       T.CO[0:HF, 56 * (8 * h + 2 * q + k):56 * (8 * h + 2 * q + k + 1)]) for q in range(4) for h in range(2)],
+                   ["LZ%d" % k, "KR", "CR"] + COs, 4, (9 - k) * 56, start=k == 0, stop=False)
+            cp(T.G[:].indirect(rimS), landed, [ln, "rimS"], Gs, ind(FP, SC))
+        mm([(P[4][:, 0:56], T.Z2[:, 12 - 4 * h:140 - 4 * h], T.bit[:, h:FP:4]) for h in range(4)], ["Z2", "bit"], 4, 256, start=r == 1)
+        mm([(P[1][:, 0:FP], Wv, pkN), (P[1][:, 0:FP], Wvn, landed)], ["Wv", "Wvn", "pkN", ln], 1, 2 * FP)
+        ac(T.XF[:], P[1][:, 0:FP], ["P1"], ["XF"], bias=-1.5, ns=cyc(FP), on="av")
+        if r > 1:
+            message3(r - 1)
         cn, cb_ = T.can[:], T.can[:, 0:55]
         ts(cn, P[4][:, 0:56], 3.5, A.is_ge, ["P4"], ["cn"])
         mm([(P[4][:, 56:112], Pa, cn), (P[4][:, 57:112], T.BK[:], cb_), (P[4][:, 57:112], nPa, cb_)], ["Pa", "BK", "nPa", "cn"], 4, 3 * 64)
@@ -820,12 +883,35 @@ def rank_program(g, core, T, topo):
             a, b = V // SPLIT * k, V // SPLIT * (k + 1)
             cp(T.C[:].indirect(T.posU[:, a // 16:b // 16]), T.RR[:, a:b], ["posU", "RR%d" % (2 * k // SPLIT)], ["C0", "C1", "CJ"], ind(b - a, SC))
 
+    def far_places():
+        ex, ci = P[4][0:HF, 0:256], T.TD[0:HF, 0:256]
+        c16, i56 = T.xx[0:HF, 0:256], T.xx[0:HF, CAP:CAP + 56]
+        one = [T.LZ[0:HF, 256 * k:256 * k + 256] for k in range(2)]
+        meet(["s0", "s1", "ci"])
+        ts(SG, aF, -1024.0, A.mult, ["aF", "aS"], ["SG"], ns=cyc(FP // 2))
+        tt(SG, SG, aS2, A.subtract, ["SG", "aS2"], ["SG"], cyc(2 * FP))
+        cp(T.PKS[:], ST[:, 0:V].indirect(rimN), STs + ["rimN"], ["PKS"], ind(FP), "av")
+        iota(i56, [[-16, 56]], 0, 0, ["x1"], reads=["late"])
+        mm([(ex[:, 128 * h:128 * h + 128], T.PKS[:, HF * h:HF * (h + 1)], EB) for h in range(2)], ["PKS", "EB"], 4, 256, start="each", stop="each")
+        ts(ci, ex, 0.0625, A.mult, ["P4"], ["ci"], -0.47, A.add, cyc(256))
+        ac(c16, ci, ["ci"], ["x0"], scale=-16.0, ns=cyc(256), on="v")
+        tt(ex, ex, c16, A.add, ["P4", "x0"], ["P4"], cyc(256))
+        for k in range(2):
+            iota(one[k], [[0, 8], [1, 32]], -16 * k, 0, ["LZ%d" % k], c=256, reads=["late"])
+            tt(one[k], ex, one[k], A.is_equal, ["P4", "LZ%d" % k], ["LZ%d" % k], cyc(256))
+            for h in range(2):
+                a = 256 * k + 128 * h
+                ac(T.THR[0:HF, a:a + 128], T.LZ[0:HF, a:a + 128], ["LZ%d" % k, "cH%d" % h], [THRs[2 * k + h]], scale=cH[h][0:HF], bias=-256.0, ns=cyc(128), on="av", narrow=True)
+        for j in range(16):
+            ts(T.CO[0:HF, 56 * j:56 * j + 56], i56, c16[:, 16 * j:16 * j + 1], A.is_equal, ["x0", "x1"], [COs[j]], -8.0, A.mult)
+
     def far_records(r):
-        v_ = P[1][:, FP:FP + 14]
+        listed(2, 0, T.ZE, T.XF, 14, ["ZE", "XF"])
+        v_ = P[2][:, 0:14]
         d16, yy, y6, h_, s_ = rf[3:8]
-        ts(ry[3], v_, -11.0, A.add, ["P1"], ["ry3"])
-        ts(d16, v_, R16, A.add, ["P1"], ["d16"], R16 + 48, A.subtract)
-        tt(yy, v_, d16, A.subtract, ["P1", "d16"], ["yy"])
+        ts(ry[3], v_, -11.0, A.add, ["P2"], ["ry3"])
+        ts(d16, v_, R16, A.add, ["P2"], ["d16"], R16 + 48, A.subtract)
+        tt(yy, v_, d16, A.subtract, ["P2", "d16"], ["yy"])
         ts(h_, d16, 0.375, A.mult, ["d16"], ["h_"], 1.0, A.min)
         ts(yy, yy, 46.0, A.max, ["yy"], ["yy"], 49.0, A.min)
         ts(y6, yy, 6.0, A.mult, ["yy"], ["y6"], -288.0, A.add)
@@ -833,13 +919,12 @@ def rank_program(g, core, T, topo):
         tt(y6, y6, h_, A.min, ["y6", "h_"], ["y6"])
         tt(s_, s_, y6, A.add, ["s_", "y6"], ["s_"])
         cp(ry[4], s_, ["s_"], ["ry4"])
-        at, ln = 3 * FP * ((r - 1) % LS), "lnd2_%d" % (r - 1)
         for k, (L, nm) in enumerate(((L1, "L1"), (L3, "L3"))):
-            tt(T.pk2[:, FP * k:FP * k + FP], L.indirect(ry[3]), T.lnd2[:, at + k:at + 3 * FP:3], A.mult, [nm, "ry3", ln], ["pk2_%d" % k], ind(FP))
+            tt(T.pk2[:, FP * k:FP * k + FP], L.indirect(ry[3]), piece(T, "lnd", 2, r - 1, 0, n - 1)[:, k::2], A.mult, [nm, "ry3", "lnd2_%d" % (r - 1)], ["pk2_%d" % k], ind(FP))
         tt(TAB[:, 10 * base(r):10 * base(r) + FW].indirect(ry[4]), T.pk2[:, 0:FP], T.pk2[:, FP:2 * FP], A.add, ["pk2_0", "pk2_1", "ry4"], ["TF%d" % r], ind(FP, SC))
         if r > 1:
             o = 4 * (base(r) - V)
-            tt(OUT[:, o:o + 4 * FP:4], T.MEM[:].indirect(ry[2]), T.lnd2[:, at + 2:at + 3 * FP:3], A.add, ["MEM", "ry2", ln], ["MF%d" % r], ind(FP))
+            tt(OUT[:, o:o + 4 * FP:4], T.MEM[:].indirect(ry[2]), piece(T, "lnd", 3, r - 1, 0, n - 1), A.add, ["MEM", "ry2", "lnd3_%d" % (r - 1)], ["MF%d" % r], ind(FP))
             cp(T.MEM[:, 0:FP], OUT[:, o:o + 4 * FP:4], ["MF%d" % r], ["MEM"], cyc(FP), "a")
 
     def addresses(r):
@@ -949,13 +1034,19 @@ def rank_program(g, core, T, topo):
         tt(d, record(0, r)[0], P[4][:, 0:CAP], A.subtract, ["P4", record(0, r)[1]], [dn], cyc(CAP))
         tt(record(1, r)[0], P[6][:, 0:CAP], d, A.mult, ["P6", dn], [record(1, r)[1]], cyc(CAP))
 
+    def once(fn, *args):
+        first = len(nodes)
+        fn(*args)
+        for nd in nodes[first:]:
+            nd["once"] = True
+
     def last_addresses():
         cp(ST[:, 0:SL].indirect(eU[:]), fresh, ["base", "eU"], STw, ind(CAP, SC))
         rim_fields()
         rim_lists(RO)
         cp(T.pk2[:, FP:2 * FP], T.MEM[:].indirect(ry[2]), ["MEM", "ry2"], ["pk2_1"], ind(FP), "av")
-        own_a, fa = T.snd2[:, FP:2 * FP], T.snd2[:, 2 * FP:3 * FP]
-        meet(["snd2", "own", "fa", "snd3"])
+        own_a, fa = T.snd2[:, 0:FP], T.snd2[:, FP:2 * FP]
+        meet(["snd2", "own", "fa"])
         mm([(P[0][:, 0:FP], T.ZQ[:, 12 - 4 * m:140 - 4 * m], ST[:, m:V:4]) for m in range(4)], ["ZQ"] + STs, 0, 4 * FP)
         ac(own_a, P[0][:, 0:FP], ["P0"], ["own"], bias=0.875, ns=cyc(FP), on="av")
         listed(0, 0, T.ZX, ST, 56, ["ZX"] + STs)
@@ -963,31 +1054,32 @@ def rank_program(g, core, T, topo):
         neighbours(True)
         far = P[6][:, 0:FP]
         mm([(far, Z8, aK), (far, Z8, aF)], ["Z8", "aK", "aF"], 6, 2 * FP, stop=False)
-        listed(6, 0, T.ZX, T.G, FP, Gs + ["ZX"], False)
+        by_slot(6, T.ZX, "ZX", 2)
         tt(fa, far, own_a, A.is_gt, ["P6", "own"], ["fa"], cyc(FP))
         tt(fa, far, fa, A.mult, ["P6", "fa"], ["fa"], cyc(FP))
         ts(T.adU[:], fa, 4.0, A.mult, ["fa"], ["adU"], -4.0 * V, A.add, cyc(FP))
 
     for r in range(1, RO + 1):
-        marks[r] = len(nodes)
         control(r)
+        if r == 1:
+            far_places()
         for step in ORDER.split():
             if step[0] in "gmb":
                 flux(r, int(step[1]), step[0])
             elif step != "n":
                 {"f": far_records, "a": addresses, "e": old_q, "o": old_fields}[step](r)
             elif r == RO:
-                last_addresses()
+                once(last_addresses)
         if r == RO:
-            ac(T.pk2[:, 0:FP], FF[:].indirect(ry[1]), ["FF0", "F0", "F1", "F2", "F3", "ry1"], ["pk2_0"], scale=-1.0, ns=ind(FP))
-            shift(0, T.pk2, T.ZF, ["pk2_0", "ZF"], 4)
-            cp(T.snd2[:, 0:FP], P[0][:, 0:FP], ["P0"], ["snd3"], cyc(FP), "av")
-            send(3, r, ["snd3"], "lnd3")
+            once(message3, r)
+        else:
+            mm([(P[3][:, 0:FP], ZI, T.CH[:])], ["ZI0", "CH"], 3, FP, stop=False)
+        new_q(r)
         new_fields(r)
         nodes[-1]["ends"] = r
+        marks[r] = len(nodes)
         if r < RO:
             message1(r)
-        new_q(r)
         sums(r)
         if r < RO:
             rim_lists(r)
@@ -1011,7 +1103,7 @@ def rank_program(g, core, T, topo):
     for k in range(NG):
         w_ = FP // NG
         cp(M[:, 16 * w_ * k:16 * w_ * (k + 1)], win.indirect(T.adU[:, w_ * k:w_ * (k + 1)]), names + ["adU"], [Ms[k]], ind(16 * w_), "av")
-    tt(M.indirect(rimS), T.pk2[:, FP:2 * FP], piece(T, "lnd", 3, RO, 0, n - 1), A.add, ["pk2_1", "lnd3", "rimS"], Ms, ind(FP, SC))
+    tt(M.indirect(rimS), T.pk2[:, FP:2 * FP], piece(T, "lnd", 3, RO, 0, n - 1), A.add, ["pk2_1", "lnd3_%d" % RO, "rimS"], Ms, ind(FP, SC))
     for k in range(4):
         a, pb, nm, ms_ = V * k, P[3 + k % 2][:, 0:FP], "P%d" % (3 + k % 2), Ms[2 * k:2 * k + 2]
         if k == 3:
@@ -1023,8 +1115,16 @@ def rank_program(g, core, T, topo):
             tt(po[:, FP * k:FP * k + FP], pb, M[:, a + 3:a + V:4], A.add, ms_ + [nm], ["YM%d" % k], cyc(FP))
         store("sa"[k % 2], T.ym[:, FP * k:FP * (k + 1)], po[:, FP * k:FP * (k + 1)], ["YM%d" % k])
 
-    for k, nd in enumerate(nodes):
-        nd["twin"] = divmod(k - marks[2], marks[3] - marks[2]) if TWINS and marks[2] <= k < marks[RO] else None
+    for nd in nodes:
+        nd["step"] = None
+    for r in range(1, RO):
+        row = [nd for nd in nodes[marks[r]:marks[r + 1]] if not nd.get("once")]
+        names = [nd["out"][0] for nd in row]
+        names = [x.rstrip("12345") if x[0:2] in ("Q0", "Q1", "MF", "TF", "ln") or x[0:4] == "snd1" else x.replace("%d_" % r, "_") if x[0] in "OT" else x for x in names]
+        if r == 1:
+            many = {x for x in names if names.count(x) > 1}
+        for j, (nd, x) in enumerate(zip(row, names)):
+            nd["step"] = (r, x + ".%d" % names[:j].count(x) if x in many else x)
     seen = {e: {} for e in Q}
 
     def need(e, toks):

import math
from concourse.bass import DstId, RemoteDMATransfer
from concourse.mybir import AluOpType as A, ActivationFunctionType as AF

V, FP, CAP, RO = 896, 224, 320, 5
W = CAP // 16
HF = FP // 2
F, H, I, U = "float32", "bfloat16", "int32", "uint16"
fS, fK, fEL, fEH, fT, fM, fD, fJL, fJH, fQ = 0, 4, 8, 9, 10, 11, 12, 13, 14, 15
PAD = 4
FW = 10 * FP + 24
SL = V + CAP
BIG = 4096.0
R16, R32, R8192 = 1.5 * 2 ** 27, 1.5 * 2 ** 28, 1.5 * 2 ** 36
NA, NB = 25, 22
cWO, cWN = 48, 64
cS, cX, cZJ, cTH, cNN, cKP, cD, cB4, cR, cT, cEL, cI1, cI2, cV, cVN, cEN, cSG = range(80, 97)
NW = cSG + 4
SCALES = (0.5, 1.5, 2.5, 3.5, 2.25, 3.75)
CASES = [(1.0, y - 0.5, [(y, 1, 1.0)]) for y in range(1, 5)] + [(1.0, 1.0, [(2, 2, 2.0)]), (0.5, 1.0, [(3, 2, 4.0), (4, 4, 8.0)]), (0.5, 1.5, [(4, 2, 4.0)]),
                                                                (1.5, 2.25, [(3, 3, 2.0)]), (1.5, 3.75, [(4, 3, 2.0)])]
MSG = [(1, m_) for m_ in range(RO)] + [(2, m_) for m_ in range(RO)] + [(3, m_) for m_ in range(1, RO + 1)]
MSG.sort(key=lambda x: (x[1], x[0]))
CYC, PCYC, GA, SC, LAT, DMA, HOP = 0.83, 0.42, 1.5, 3.6, 100.0, 2000.0, 4800.0
MARGIN, TURNS, WAIT, SLACK, SHAKE, URGE = 500.0, 100, 100.0, 3.0, 300.0, (("sent", 8000.0), ("posU", 3000.0))
WAYS = ("bbbbaaaaa", "bbbbcccaa")
TBANK = ("375375375", "605605252", "560560460")
GV = 22
SPLIT = 2
VADD, VMIN, AADD, PFIX, CROSS = 0.0, 53.0, 66.0, 20.0, 120.0
WIDE, FIRST, T2, T3, ONCE = (0.0, 3300.0, 2000.0), 1.4, 1.5, 2.0, 3000.0
MOVES = ((None, 1, 2, 95000), (4, None, None, 85000))
STEP, HEAT, SEED, MEAN, ASIDE, BEYOND = (0.0, 300.0, 600.0, 2500.0), 120.0, 6, 0.0, 0.0, 3000.0
ORDER = "f a e o g0 g1 m0 g2 m1 b0 g3 m2 b1 m3 n b2 b3"
ROUND = {
    "v": "pkL G0.0 snd1_ G2 T_1 ry0 rf0.0 O_2 rf0.1 G6 ry1 pk2_1.0 G4 O_3 rf2.0 snd2_0 T_0 O_0 O_1 T_2 T_7 bit LZ0 LZ1 G0.1 T_3 cn T_5 rf2.1 T_4 m0 m1 m2 ry2 m3 "
         "posU C0.1 d16 ry3 yy.0 h_ yy.1 C0.2 y6.0 s_.0 y6.1 pk2_1.1 s_.1 pk2_0.1 ry4 TF sd0 u_0.0 UQ t_0a.0 u_0.1 t_0b.0 u_0.2 t_0a.1 t_0b.1 t_0a.2 UA0 e0.0 e1 "
         "KE0.0 e0.1 rl0.1 e0.2 u_1.0 sd1 KE0.1 KE1.0 t_1b.0 u_1.1 t_1a.0 KE1.1 zz0 t_1a.1 eU u_1.2 rr1 t_1b.1 gt0b.0 gt0a.0 t_1a.2 gt0b.1 zz1 UA1 gt0a.1 gt1a.0 "
         "gt1b.0 gt1b.1 gt1a.1 UC0 sq1.1 sq0.1 MF.1 F0 F1 x0.0 sq2.1 UC1 F2 x1.0 x0.1 sq0.3 F3 x1.1 Q0_ g h sq1.2 Q1_ nn ST0",
    "a": "pkN G3 G1 pk2_0.0 G5 G7 rl0.0 snd2_1 P4.1 P6.1 P0.1 XF pk2_2 RR0 snd3_0 RR1 T_8 T_6 T_9 qe rr0.0 rl1 sq0.0 P1.5 sq1.0 P2.4 GO rr2 rl2 P1.6 "
         "sq2.0 rr0.1 rl0.2 P2.5 sq0.2 base MEM",
    "p": "P5.0 P0.0 P6.0 P3.0 P7.0 P1.0 P1.1 P2.0 P4.0 P1.2 P5.1 P2.1 P2.2 P3.1 P7.1 P1.3 P4.2 P4.3 P4.4 P3.2 P3.3 P3.4 P4.5 P3.5 P7.2 P1.4 P7.3 P7.4 P7.5 P2.3 "
         "P6.2 P6.3 P0.2 P0.3 P6.4 P6.5 P0.4 P0.5 P4.6 P5.2 P3.6 P7.6 P3.7 P0.6 P5.3 P7.7 P6.6 P5.4 P5.5 P3.8 P1.7 P1.8",
    "g": "C0.0 C1 sent.0 sent.1 sent.2",
}
LS = 2
SLOT = (0, 1, 2, 0)


def base(r):
    return V + (CAP + PAD) * (r - 1) + PAD


def place_of(y, m):
    return y + min(6 * m, 19)


NREC = base(RO) + CAP


def sb(n, t):
    return ("sbuf", [128, n], t)


SCRATCH = {
    "ST": sb(SL + RO * FP, H), "C": sb(V + 8 * CAP, H), "G": sb(4 * V, H), "GO": sb(CAP, H),
    "RR": sb(V, H), "TAB": sb(10 * base(RO) + FW, F), "Q0": sb(NREC, F), "Q1": sb(NREC, F), "OUT": sb(4 * (NREC - V), F),
    "snd1": sb(5 * FP, H), "snd2": sb(2 * FP, F), "lnd2": sb(LS * 2 * FP, F), "snd3": sb(FP, F), "lnd3": sb(LS * FP, F), "MEM": sb(FP + 8, F),
    "TD": sb(V, I), "TH": sb(8, F),
    "PI": sb(FP, I), "RI": sb(32, I), "RJ": sb(48, I), "rimU": sb(32, U), "rimS": sb(16, U), "rimK": sb(48, F), "ryF": sb(128, F), "ryU": sb(80, U),
    "colU": sb(FP, U), "AB": sb(5 * FP, H), "XF": sb(FP, H), "PKS": sb(FP, H), "LZ": sb(512, H), "THR": sb(512, H), "CO": sb(V, H), "adU": sb(FP, U),
    "Pi": sb(8, I), "CI": sb(8, I), "CF": sb(32, F), "MK": sb(32, F), "BR": sb(16, F), "E1": sb(4 * 144, H),
    "WS": sb(104, F), "WB": sb(104, H), "CR": sb(512, H), "KR": sb(128, H),
    "Wt": sb(128, H), "Wo": sb(128, H), "WN": sb(144, H), "ZJ": sb(240, H), "ZI": sb(256, H), "ZF": sb(240, F), "ZS": sb(6 * 128, F), "ZB": sb(6 * 128, H),
    "ZE0": sb(144, H), "ZO0": sb(144, H), "ZA0": sb(144, H), "ZE": sb(144, H), "ZX": sb(144, H), "ZO": sb(144, H), "ZQ": sb(144, H),
    "Z2": sb(144, H), "ZA": sb(4 * 144, H), "BK": sb(128, H), "TR": sb(14 * 128, H), "Wb": sb(128, H), "Wy": sb(16, H), "CH": sb(FP, H), "JR": sb(CAP, H),
    "TRE": sb(56, F), "ONE": sb(56, F), "LT": sb(128, F), "KE": sb(8 * W, F),
    "bit": sb(FP, H), "can": sb(56, H), "v1": sb(4 * 56, F), "posU": sb(56, U),
    "UA": sb(8 * W, U), "UC": sb(8 * W, U), "UQ": sb(W, U), "eU": sb(W, U), "qyU": sb(56, U), "sm": sb(34 * W, F),
    "qe": sb(CAP, F), "r": sb(3 * 2 * CAP, F), "sq": sb(3 * CAP, F), "FF": sb(8 + 4 * CAP, F), "xx": sb(2 * CAP, F),
    "gb": sb(4 * CAP, H), "NT": sb(8, F), "pk1": sb(2 * FP, H), "pk2": sb(3 * FP, F),
}
for _k in range(8):
    SCRATCH["P%d" % _k] = ("psum", [128, 512], F)
SEMAPHORES = (["v", "a", "p", "g", "loc", "out"] + ["in%d" % k for k in range(10)]
              + [x + str(k) for x in ("ar", "hs", "ls") for k in range(len(MSG))])


def routes(T, topo):
    plan = []
    n = len(T.cores)
    for r, c in enumerate(T.cores):
        direct = [d - 1 for d in range(1, n) if topo.may_write(c, T.cores[(r + d) % n])]
        far = [d - 1 for d in range(1, n) if d - 1 not in direct]
        able = [h for h in topo.cores_of(c) if T.rank_of(h) is None
                and all(topo.may_write(h, T.cores[(r + b + 1) % n]) for b in far)]
        able.sort(key=lambda h: topo.die(h) != topo.die(c))
        half = len(far) // 2
        plan.append((direct[::-1], [(able[0], far[:half]), (able[1], far[half:])]))
    return plan


def shares(engs, n):
    size = [1] * n
    while True:
        k = size.index(min(size))
        if sum(size) + size[k] > len(engs):
            break
        size[k] *= 2
    out, at = [], 0
    for s in size:
        out.append((sum(1 << e for e in engs[at:at + s]), s))
        at += s
    return out


def piece(T, kind, which, m, a, n):
    w = 64 if which == 2 else 32
    if kind == "lnd":
        buf, at = (T.ST, SL + FP * m) if which == 1 else (T["lnd%d" % which], 7 * w * (m % LS))
    elif kind == "hb":
        buf, at = T.C if which == 1 else T.TAB, 128 * MSG.index((which, m))
    else:
        buf, at = T["snd%d" % which], m * FP if which == 1 else 0
    return buf[:, at + w * a:at + w * (a + n)]


def forward(g, T, topo, src, r, blocks, kind, first, which, m, left):
    n = len(T.cores)
    sh = shares(topo.engines(src, T.cores[(r + blocks[0] + 1) % n]), len(blocks))
    tr = []
    for j, (b, (mask, _)) in enumerate(zip(blocks, sh)):
        rid, pid = topo.addr(T.cores[(r + b + 1) % n], src)
        tr.append(RemoteDMATransfer(dst_ids=[DstId(rid=rid, pnc=pid)], dma_engine_mask=mask, remote_sem=T.sem["ar%d" % MSG.index((which, m))],
                                    src=piece(T, kind, which, m, first + j, 1), dst=piece(T, "lnd", which, m, n - 2 - b, 1)))
    g.remote_dma_fused(tr, local_sem=left)
    return sum(s for _, s in sh)


def place(nodes, rank, before, after):
    left, at = [len(x) for x in before], {}
    pool, free, due = {e: [] for e in "vapgsx"}, {e: 0.0 for e in "vapgsx"}, {e: [0.0] * len(nodes) for e in "vapgsx"}
    for k, nd in enumerate(nodes):
        for e in nd["ns"] if not left[k] else ():
            pool[e].append(k)
    while len(at) < len(nodes):
        t, e = min((max(free[e], min(due[e][k] for k in row)), e) for e, row in pool.items() if row)
        ready = due[e]
        row = sorted(pool[e], key=lambda k: ((MARGIN if e == "v" and len(nodes[k]["ns"]) > 1 else 0) - rank[k], k))
        k = None
        soon = [(j, ready[j]) for j in row if ready[j] > t]
        for j in row:
            if ready[j] <= t and (e == "x" or all(t + nodes[j]["ns"][e] <= w + WAIT or rank[i] - rank[j] < SLACK * (w - t + nodes[i]["ns"][e]) for i, w in soon)):
                k = j
                break
        if k is None:
            free[e] = t + 50.0
            continue
        at[k] = (e, t, t + nodes[k]["ns"][e])
        if e != "x":
            free[e] = at[k][2]
        for e2 in nodes[k]["ns"]:
            pool[e2].remove(k)
        for j, lat in after[k]:
            for e2 in nodes[j]["ns"]:
                due[e2][j] = max(due[e2][j], at[k][2] + lat + (CROSS if lat == LAT and e2 != e else 0.0))
            left[j] -= 1
            for e2 in nodes[j]["ns"] if not left[j] else ():
                pool[e2].append(j)
    return at


def steady(nodes, pre):
    one = {nd["step"][1]: k for k, nd in enumerate(nodes) if nd["step"] and nd["step"][0] == 3}
    where = {s: e for e, row in ROUND.items() for s in row.split()}
    where.update({s: "x" for s in one if s not in where})
    rows = [[(f, s) for f in range(4) for s in row] for row in [x.split() for x in ROUND.values()] + [[s] for s in one if where[s] == "x"]]
    waits = {s: [(nodes[j]["step"][0] - 3, nodes[j]["step"][1], lat) for j, lat in pre[k] if nodes[j]["step"]] for s, k in one.items()}
    start, end, free = {}, {}, [0.0] * len(rows)
    while any(rows):
        for i, row in enumerate(rows):
            while row and all(f_ + row[0][0] < 0 or (f_ + row[0][0], j) in end for f_, j, lat in waits[row[0][1]]):
                f, s = row.pop(0)
                start[f, s] = max([free[i]] + [end[f + f_, j] + lat + (CROSS if lat == LAT and where[j] != where[s] else 0.0) for f_, j, lat in waits[s] if f + f_ >= 0])
                end[f, s] = free[i] = start[f, s] + nodes[one[s]]["ns"][where[s]]
    return {s: start[3, s] - end[2, "ST0"] for s in one}, where, end[3, "ST0"] - end[2, "ST0"]


def polish(nodes, pre, post, at):
    n, seed = len(nodes), [SEED]

    def draw():
        seed[0] = (seed[0] * 1103515245 + 12345) % 2147483648
        return (seed[0] + 0.5) / 2147483648

    ends = {nd["ends"]: k for k, nd in enumerate(nodes) if "ends" in nd}
    when, where, length = steady(nodes, pre)
    key, on = [at[k][1] for k in range(n)], [at[k][0] for k in range(n)]
    for k, nd in enumerate(nodes):
        if nd["step"]:
            key[k], on[k] = at[ends[1]][2] + (nd["step"][0] - 1) * length + when[nd["step"][1]], where[nd["step"][1]]
        elif k > ends[2]:
            key[k] += at[ends[1]][2] + 3 * length - at[ends[4]][2]

    def move(k, d, undo, most):
        todo = [(k, d)]
        while todo and len(undo) <= most:
            i, d = todo.pop()
            undo.append((i, key[i]))
            key[i] += d
            todo += [(j, key[i] - key[j] + math.copysign(0.01 + 0.01 * draw(), d)) for j, lat in (post if d > 0 else pre)[i] if (key[i] - key[j]) * d >= 0]
        return not todo

    for k in range(n):
        late = max([key[j] - key[k] for j, lat in pre[k]] + [-1.0])
        if late >= 0:
            move(k, late + 0.01, [], n * n)

    order, ns, tail = list(range(n)), [nd["ns"] for nd in nodes], [nd["lat"] for nd in nodes]
    edges = [[(j, lat, CROSS if lat == LAT else 0.0) for j, lat in row] for row in pre]

    def times(first, end, why, goal):
        order.sort(key=lambda k: key[k])
        last, span, who, stop = {}, 0.0, 0, 1e30 if goal is None else key[goal] + BEYOND
        for k in order:
            e = on[k]
            if key[k] >= first:
                if key[k] > stop:
                    break
                t, w = 0.0, None
                for j, lat, cross in edges[k]:
                    x = end[j] + lat if on[j] == e else end[j] + lat + cross
                    if x > t:
                        t, w = x, j
                j = last.get(e)
                if j is not None and end[j] >= t and e != "x":
                    t, why[k] = end[j], (j, True)
                else:
                    why[k] = None if w is None else (w, False)
                t += ns[k][e]
                end[k] = t
                if t + tail[k] > span:
                    span, who = t + tail[k], k
            last[e] = k
        mean = MEAN * sum([end[k] for k in inside]) / len(inside)
        return (span + mean, end, why, who) if goal is None else (end[goal] + mean, end, why, goal)

    inside = []
    for start, stop, goal, moves in MOVES:
        start, stop, goal = ends.get(start), ends.get(stop), ends.get(goal)
        inside[:] = [k for k in range(n) if (start is None or key[k] > key[start]) and (stop is None or key[k] <= key[stop])]
        now = times(-1e30, [0.0] * n, [None] * n, goal)
        best = (now[0], list(key), list(on))
        for turn in range(moves):
            span, end, why, k = now
            if draw() < ASIDE:
                k = inside[int(draw() * len(inside))]
            links = []
            while why[k] and (start is None or key[k] > key[start]):
                if why[k][1] and (stop is None or key[k] < key[stop] + BEYOND):
                    links.append((why[k][0], k))
                k = why[k][0]
            if not links:
                continue
            u, v = links[int(draw() ** 2 * len(links)) if k != now[3] else int(draw() * len(links))]
            z, undo, both = draw(), [], [k for k in (u, v) if len(nodes[k]["ns"]) > 1]
            turned = both[int(draw() * len(both))] if both and z < 0.15 else None
            if turned is not None:
                was = on[turned]
                undo.append((turned, key[turned]))
                on[turned] = "v" if was == "a" else "a"
                ok = True
            elif z < 0.55:
                ok = move(v, key[u] - key[v] - 0.01 * (1 + z) + STEP[int(draw() * len(STEP))] * math.log(draw()), undo, 60)
            else:
                ok = move(u, key[v] - key[u] + 0.01 * (1 + z) - STEP[int(draw() * len(STEP))] * math.log(draw()), undo, 60)
            new = times(min(min(x, key[i]) for i, x in undo), list(end), list(why), goal) if ok else None
            if ok and new[0] - span <= -math.log(draw()) * (HEAT * (1 - turn / moves) + 2):
                now = new
                if new[0] < best[0]:
                    best = (new[0], list(key), list(on))
            else:
                for i, x in reversed(undo):
                    key[i] = x
                    if turned is not None:
                        on[i] = was
        key[:], on[:] = best[1], best[2]
    return best


PLACED = {}


def arrange(nodes):
    n = len(nodes)
    if n not in PLACED:
        pre, post = [[] for nd in nodes], [[] for nd in nodes]
        for k, nd in enumerate(nodes):
            for j in sorted(nd["pre"]):
                lat = 0.0 if nd["tok"] is False or list(nd["ns"]) == list(nodes[j]["ns"]) == ["p"] else nodes[j]["lat"]
                pre[k].append((j, lat))
                post[j].append((k, lat))
        urge = [0.0] * n
        for name, more in URGE:
            urgent = {[nd["out"][0:1] for nd in nodes].index([name])}
            for k in range(n - 1, -1, -1):
                if k in urgent:
                    urgent.update(nodes[k]["pre"])
                    urge[k] += more
        rank, best, now, seed = [-k for k in range(n)], None, None, SEED
        for turn in range(TURNS):
            at = place(nodes, rank, pre, post)
            ends = [at[k][2] for k, nd in enumerate(nodes) if "ends" in nd]
            span = max(at[k][2] + nodes[k]["lat"] for k in range(n)) - (ends[3] - ends[0]) * 0.8
            if best is None or span < best[0]:
                best = (span, at)
            if turn < 8 or span < now[0] + SHAKE:
                now = (span, at)
            back = place(nodes, [now[1][k][2] for k in range(n)], post, pre)
            rank = []
            for k in range(n):
                seed = (seed * 1103515245 + 12345) % 2147483648
                rank.append(back[k][2] + urge[k] + (SHAKE * (seed % 2001 / 1000 - 1) if turn > 6 and seed // 4096 % 3 == 0 else 0.0))
        PLACED[n] = polish(nodes, pre, post, best[1])
    span, key, on = PLACED[n]
    for k, nd in enumerate(nodes):
        nd["e"] = on[k]
    return sorted(range(n), key=lambda k: key[k])


def rank_program(g, core, T, topo):
    plan = routes(T, topo)
    n = len(T.cores)
    rank = T.rank_of(core)
    if rank is None:
        for r in range(n):
            hs = shares(topo.engines(T.cores[r], plan[r][1][0][0]), 2)
            for k, (h, blocks) in enumerate(plan[r][1]):
                if h != core:
                    continue
                sent = 0
                for j, (which, m) in enumerate(MSG):
                    g.wait_ge(T.sem["hs%d" % j], hs[k][1])
                    sent += forward(g, T, topo, core, r, blocks, "hb", 0, which, m, T.sem.loc)
                g.wait_ge(T.sem.loc, sent)
        return
    arrive = 0
    for r in range(n):
        for src, blocks in [(T.cores[r], plan[r][0])] + plan[r][1]:
            sh = shares(topo.engines(src, T.cores[(r + blocks[0] + 1) % n]), len(blocks))
            arrive += sum(s for b, (_, s) in zip(blocks, sh) if (r + b + 1) % n == rank)
    hs = shares(topo.engines(core, plan[rank][1][0][0]), 2)
    leave = sum(s for _, s in hs + shares(topo.engines(core, T.cores[(rank + plan[rank][0][0] + 1) % n]), len(plan[rank][0])))

    lay = plan[rank][1][0][1] + plan[rank][1][1][1] + plan[rank][0]
    Q = {"v": g.vector, "a": g.scalar, "p": g.tensor, "g": g, "s": g.sync}
    cnt = {"v": 0, "a": 0, "p": 0, "g": 0, "out": 0}
    cnt.update({"ls%d" % k: leave for k in range(len(MSG))})
    nodes, wr, rd = [], {}, {}

    def op(ns, fn, reads, writes, lat=LAT, tok=True):
        k, pre = len(nodes), set()
        ns = {e: x if x > 0 else max(VADD - x, VMIN) if e == "v" else AADD - x for e, x in ns.items()}
        for x in reads:
            if x in wr:
                pre.add(wr[x])
            if x[0] == "P" and x[1:].isdigit():
                pre.update(j for j in rd.get(x, []) if len(ns) > 1 or list(nodes[j]["ns"]) != list(ns))
        for x in writes:
            if x in wr:
                pre.add(wr[x])
            pre.update(rd.get(x, []))
        nodes.append({"ns": ns, "fn": fn, "pre": pre, "lat": lat, "tok": tok, "out": writes})
        for x in reads:
            rd.setdefault(x, []).append(k)
        for x in writes:
            wr[x] = k
            rd[x] = []

    def meet(names):
        op({"x": 1.0}, None, [], names, 1.0, None)

    marks = {}
    vec, act, pe = g.vector, g.scalar, g.tensor
    either = [""]

    def cyc(c):
        return -1.0 - c * CYC

    def ind(c, rate=GA):
        return 60 + rate * c * CYC

    def tt(out, a, b, o, reads, writes, ns=cyc(0)):
        op({"v": ns}, lambda e: vec.tensor_tensor(out, a, b, o), reads, writes)

    def ts(out, a, s1, o1, reads, writes, s2=None, o2=None, ns=cyc(0)):
        if o2 is None:
            op({"v": ns}, lambda e: vec.tensor_scalar(out, a, s1, None, o1), reads, writes)
        else:
            op({"v": ns}, lambda e: vec.tensor_scalar(out, a, s1, s2, o1, o2), reads, writes)

    def cp(out, a, reads, writes, ns=cyc(0), on="v"):
        op({e: ns for e in (on if on == "v" else either[0] or on)}, lambda e: vec.tensor_copy(out, a) if e == "v" else act.activation(out, a, AF.Identity), reads, writes)

    def ms(out, c, writes, ns=cyc(0)):
        op({"v": ns}, lambda e: vec.memset(out, c), [], writes)

    def ac(out, a, reads, writes, func=AF.Identity, bias=0.0, scale=1.0, ns=cyc(0), on="a", narrow=False):
        op({e: ns / 2 if narrow and e == "v" else ns for e in (either[0] or on)},
           lambda e: act.activation(out, a, func, bias=bias, scale=scale) if e == "a" else vec.tensor_scalar(out, a, scale, bias, A.mult, A.add), reads, writes)

    def cut(out, a, scale, reads, writes, ns):
        op({e: ns for e in "av"}, lambda e: act.activation(out, a, AF.Relu, scale=scale) if e == "a" else vec.tensor_scalar(out, a, scale, 0.0, A.mult, A.max), reads, writes)

    def fills(on, parts, reads, writes):
        def fn(e):
            for out, src, val in parts:
                last = vec.memset(out, float(val)) if e == "v" else act.activation(out, src, AF.Identity, bias=float(val), scale=0.0)
            return last
        op({e: (VMIN if e == "v" else AADD + 10) * len(parts) for e in on}, fn, reads, writes)

    def mm(parts, reads, bank, cols, wide=1, start=True, stop=True, calls=None):
        def fn(_):
            for j, (out, l, r) in enumerate(parts):
                last = pe.matmul(out, l, r, start == "each" or (start and j == 0), stop == "each" or (stop and j == len(parts) - 1))
            return last
        op({"p": cols * wide * PCYC + PFIX * (calls or len(parts))}, fn, reads, ["P%d" % bank])

    def iota(out, pat, base_, cm, writes, exact=False, c=64, reads=()):
        if exact:
            op({"g": 130 + 2 * c * CYC}, lambda e: g.iota(out, pat, base_, cm), list(reads), writes)
        else:
            op({"g": 130 + 2 * c * CYC}, lambda e: g.iota(out, pat, base_, cm, allow_small_or_imprecise_dtypes=True), list(reads), writes)

    def zero(buf, a, b, writes, reads=()):
        iota(buf[:, a:b], [[0, b - a]], 0, 0, writes, c=b - a, reads=reads)

    def sel(out, a, cmp, fill, base_, cm, reads, writes, step=1):
        op({"g": 170 + 256 * CYC}, lambda e: g.affine_select(out, a, [[step, 128]], cmp, fill, base_, cm), reads, writes)

    def load(e, k, out, src, name, turn=1, reads=(), ns=60.0):
        def fn(_):
            Q[e].dma_start(out, src).then_inc(T.sem["in%d" % k], 16)
        op({e: ns}, fn, ["issued"] + list(reads), [name], DMA * turn, ("in%d" % k, 16))
        op({"x": 1.0}, None, [], ["issued"], 1.0, False)

    def store(e, out, src, reads):
        def fn(_):
            Q[e].dma_start(out, src).then_inc(T.sem.out, 16)
            cnt["out"] += 16
        op({e: 60.0}, fn, reads, [], DMA, None)

    def send(which, m, reads, lands):
        left = "ls%d" % MSG.index((which, m))

        def fn(_):
            tr = []
            for (h, blocks), (mask, s) in zip(plan[rank][1], hs):
                rid, pid = topo.addr(h, core)
                tr.append(RemoteDMATransfer(dst_ids=[DstId(rid=rid, pnc=pid)], dma_engine_mask=mask, remote_sem=T.sem["hs%d" % MSG.index((which, m))],
                                            src=piece(T, "snd", which, m, lay.index(blocks[0]), len(blocks)), dst=piece(T, "hb", which, m, 0, len(blocks))))
            g.remote_dma_fused(tr, local_sem=T.sem[left])
            forward(g, T, topo, core, rank, plan[rank][0], "snd", lay.index(plan[rank][0][0]), which, m, T.sem[left])
        op({"g": ONCE if (which, m) == (1, 0) else 1000.0}, fn, reads, ["sent"], 1.0, None)
        op({"x": HOP * (FIRST if m == 0 else 1) - 1000.0 + WIDE[which - 1]}, None, ["sent"], [lands], 1.0, ("ar%d" % MSG.index((which, m)), arrive))
        if which > 1:
            op({"x": HOP}, None, ["sent"], ["snd%d" % which], 1.0, (left, leave))
        rd["sent"] = []

    P = [T["P%d" % k] for k in range(8)]
    ST, TAB, OUT, WS, WB, CF = T.ST, T.TAB, T.OUT, T.WS, T.WB, T.CF
    QQ = (T.Q0, T.Q1)
    NT = sum(len(c_[2]) for c_ in CASES)

    def qlog(j, r):
        return QQ[j][:, 0:base(r + 1) - PAD], ["Q%d_%d" % (j, k) for k in range(r + 1)]

    def olog(r, far):
        return (OUT[:, 0:4 * (base(r + 1) - V + (FP if far else -PAD))],
                ["OZ1"] + ["O%d_%d" % (k, j) for k in range(1, r + 1) for j in range(4)] + ["MF%d" % (r + 1)] * far)

    def tlog(r):
        return TAB[:, 0:10 * base(r + 1) + FW], ["TZ0"] + ["T%d_%d" % (k, j) for k in range(r + 1) for j in range(NT * (1 if k else 2))] + ["TF%d" % (r + 1)]

    def record(j, r):
        return QQ[j][:, base(r):base(r) + CAP], "Q%d_%d" % (j, r)

    def wcol(k):
        return WS[:, k:k + 1]

    def W1(f, k=0):
        return T.E1[0:1, 144 * k + 15 - f:144 * k + 143 - f]

    def scaled(c, wide_):
        return ((T.ZF if wide_ else T.ZI)[:, 0:128] if c == 1.0 else (T.ZS if wide_ else T.ZB)[:, 128 * SCALES.index(c):128 * SCALES.index(c) + 128],
                ("ZF" if wide_ else "ZI0") if c == 1.0 else "%s%d" % ("ZS" if wide_ else "ZB", SCALES.index(c)))

    cI, cG, cQ, cK, cP, cM, cE, nE, cO, n16, c12, c8, c2, cA, nS, cF0, cF1 = [CF[:, k:k + 1] for k in range(17)]
    s0, s1, s2, s3 = [T.TD[:, FP * k:FP * k + FP] for k in range(4)]
    TRs, Pa, nPa, Z8, tmp, Wi1, Wi2, Wv, Wvn = [T.TR[:, 128 * k:128 * k + 128] for k in range(9)]
    KB, nKB, EB = [T.TR[:, 128 * k:128 * k + 128] for k in range(11, 14)]
    cH = [CF[:, k:k + 1] for k in (17, 18)]
    SGM = [T.TR[:, 128 * k:128 * k + 128] for k in (9, 10)] + [T.ZA[:, 144 * k:144 * k + 128] for k in (0, 1)]
    ZF, ZI = T.ZF[:, 0:128], T.ZI[:, 0:128]
    halves, wide = ((0, V // 2), (V // 2, V)), ((0, 512), (512, V))
    spare = 10 * base(4) + 64
    X, XQ, X16, SI, LW = [TAB[:, spare + a:spare + b] for a, b in ((0, 256), (256, 400), (400, 528), (528, 752), (752, 1008))]
    early = ["X", "XQ", "X16", "SI", "ty", "td", "th_", "tb"]
    RW, HI, PT, XB = T.G[0:1, 0:16 * NW], T.G[0:1, 1920:1920 + V + 64], T.G[0:1, 2880:2880 + 128], T.G[0:1, 3008:3008 + 256]
    PJ, TB = T.C[0:1, 0:768], T.RR
    qa, qb = T.gb[:, 0:V], T.snd1[:, FP:FP + V]

    load("s", 6, T.PI[:], T.port[:], "PI", T2)
    load("a", 1, T.TD[8:16, :], T.d0[:], "TD1")
    load("s", 0, T.TD[0:8, :], T.t0[:], "TD0")
    load("a", 3, T.RI[:, 0:14], T.rim[:], "RI")
    load("s", 2, T.TD[16:24, :], T.d0[:], "TD2")
    load("s", 4, qa, T.q0[:], "qa", T3)
    load("s", 5, qb, T.q1[:], "qb", T3)
    load("s", 7, T.TH[:, 0:1], T.th[:], "TH", T3)

    ms(T.Wt[0:24, :], 0.0, ["Wt"])
    ms(RW, 0.0, ["RW0"], cyc(8 * NW))
    ms(T.E1[0:1, :], 0.0, ["E1"], cyc(288))
    iota(cP, [[0, 1]], 0, 1, ["cP"], c=1)
    for base_, fill in ((-fT, 1.0), (128 - fD, -1.0), (256 - fD, 1.0), (256 - fM, 1.0)):
        sel(T.Wt[0:24, :], T.Wt[0:24, :], A.not_equal, fill, base_, -16, ["Wt"], ["Wt"])
    iota(X, [[1, 256]], 0, 0, ["X"], c=256)
    iota(PT, [[-32, 4], [1, 32]], 64 + PAD, 0, ["PT"], c=128)
    iota(T.Pi[:, 0:1], [[0, 1]], 0, 1, ["Pi"], True, 1)
    iota(XQ, [[1, 36], [0, 4]], 0, 0, ["XQ"], c=144)
    iota(X16, [[1, 8], [0, 16]], 0, 0, ["X16"], c=128)
    iota(SI, [[16, FP]], 15, 1, ["SI"], c=FP)
    iota(T.TRE[:], [[16, 56]], 0, 1, ["TRE"])
    fills("v", [(T.E1[0:1, 144 * k + 15:144 * k + 144:16], None, k / 32 if k else 1) for k in range(4)], [], ["E1"])
    ts(cM, cP, 16.0, A.is_ge, ["cP"], ["cM"], 2.0, A.mult)
    fills("v", [(HI[:, V:V + 32], None, V // 128 + 1), (HI[:, V + 32:V + 64], None, V // 128)], [], ["HJ"])
    ts(TB[0:24, :], T.TD[0:24, :], CF[0:24, 5:6], A.max, ["TD0", "TD1", "TD2", "cM"], ["TB"], ns=cyc(V))

    def relay(e):
        for j, b in enumerate(lay):
            last = vec.tensor_copy(T.RI[:, 16 + 2 * j:18 + 2 * j], T.RI[:, 2 * b:2 * b + 2])
        return last
    op({"v": 7 * VMIN}, relay, ["RI"], ["RP"])
    ts(T.RJ[:, 0:14], T.RI[:, 16:30], 2, A.arith_shift_right, ["RP"], ["RJ0"])
    ts(T.ZI[:, 0:128], X[:, 0:128], cP, A.is_equal, ["X", "cP"], ["ZI0"], ns=cyc(128))
    ts(T.ZI[:, 128:256], X[:, 0:128], cP, A.is_equal, ["X", "cP"], ["ZI"], ns=cyc(128))
    rimU, rimN, rimS = T.rimU[:, 0:14], T.rimU[:, 16:30], T.rimS[:, 0:14]
    cp(rimU, T.RJ[:, 0:14], ["RJ0"], ["rimU"])
    ts(T.RJ[:, 32:46], T.RI[:, 0:14], 2, A.arith_shift_right, ["RI"], ["RJ2"])
    cp(rimN, T.RJ[:, 32:46], ["RJ2"], ["rimN"])
    cp(rimS, T.RI[:, 0:14], ["RI"], ["rimS"])
    for k, (a, b) in enumerate(wide):
        mm([(P[k][:, 0:b - a], T.Wt[0:24, :], TB[0:24, a:b])], ["Wt", "TB"], k, b - a)
        cp(ST[:, a:b], P[k][:, 0:b - a], ["P%d" % k], ["ST%d" % k], cyc(b - a), "av"[k])
    for j, b in enumerate(lay):
        mm([(P[4][:, 32 * j:32 * j + 32], W1(fJL), PT[:, 32 * (b % 4):32 * (b % 4) + 32]),
            (P[4][:, 32 * j:32 * j + 32], W1(fJH), HI[:, V + 32 * (b // 4):V + 32 * (b // 4) + 32])], ["E1", "PT", "HJ"], 4, 128)
    cp(T.CH[:], P[4][:, 0:FP], ["P4"], ["CH"], cyc(FP), "a")
    up, runs = 32 * (n - 1 - rank), []
    for j, b in enumerate(lay):
        o = 112 if 32 * b < up else 16
        runs = runs[:-1] + [(runs[-1][0], 32 * j + 32, o)] if runs and runs[-1][2] == o else runs + [(32 * j, 32 * j + 32, o)]
    STs = ["ST0", "ST1"]
    pkL, pkN = T.pk1[:, 0:FP], T.pk1[:, FP:2 * FP]

    def shift(bank, src, Z, reads, wide, fresh=True):
        mm([(P[bank][:, lo:hi], Z[:, o:o + 128], src[:, lo:hi]) for lo, hi, o in runs], reads, bank, FP + 32, wide, "each" if fresh else False, "each" if fresh else True, 3)

    def rim_fields():
        cp(pkL, ST[:, 0:V].indirect(rimU), STs + ["rimU"], ["pkL"], ind(FP), "av")
        cp(pkN, ST[:, 0:V].indirect(rimN), STs + ["rimN"], ["pkN"], ind(FP), "av")

    def message1(m):
        if m == 0:
            rim_fields()
            shift(7, T.pk1, T.ZI, ["pkL", "ZI", "ZI0"], 1)
            tt(T.snd1[:, 0:FP], P[7][:, 0:FP], T.CH[:], A.add, ["P7", "CH"], ["snd1_0"], cyc(FP))
        else:
            rim_fields()
            shift(3, T.pk1, T.ZJ, ["pkL", "ZJ"], 1, False)
            ac(T.snd1[:, m * FP:(m + 1) * FP], P[3][:, 0:FP], ["P3", "BJ%d" % m], ["snd1_%d" % m], bias=T.BR[:, 8 + m:9 + m], ns=cyc(FP), on="av")
        send(1, m, ["snd1_%d" % m], "lnd1_%d" % m)

    def listed(bank, o, Z, src, w, reads, start=True):
        mm([(P[bank][:, o:o + w], Z[:, 15 - i:143 - i], src[:, i:16 * w:16]) for i in range(16)], reads, bank, 16 * max(w, 64), start=start)

    ry = [T.ryU[:, 16 * k:16 * k + 14] for k in range(5)]
    rf = [T.ryF[:, 16 * k:16 * k + 14] for k in range(8)]

    def rim_lists(m):
        bank = 7 if m < RO else 4
        listed(bank, 448, T.ZX, T.pk1, 28, ["pkL", "pkN", "ZX"])
        sent_, kept, nb = P[bank][:, 448:462], P[bank][:, 462:476], "P%d" % bank
        if m < RO:
            cp(ry[0], sent_, [nb], ["ry0"])
            ts(rf[0], sent_, 4.0, A.mult, [nb], ["rf0"], 16.0 - 4 * base(m), A.add)
            tt(rf[0], rf[0], T.rimK[:, 0:14], A.add, ["rf0", "rimK"], ["rf0"])
        else:
            ts(rf[1], sent_, 0.5 - base(m), A.add, [nb], ["rf1"], BIG, A.mult)
            tt(rf[0], sent_, T.rimK[:, 16:30], A.add, [nb, "rimL"], ["rf0"])
            tt(rf[0], rf[0], rf[1], A.min, ["rf0", "rf1"], ["rf0"])
        cp(ry[1], rf[0], ["rf0"], ["ry1"])
        ts(rf[2], kept, 0.5 - base(m), A.add, [nb], ["rf2"], BIG, A.mult)
        tt(rf[2], rf[2], T.TRE[:, 0:14], A.max, ["rf2", "TRE"], ["rf2"])
        ts(ry[2], rf[2], float(FP), A.min, ["rf2"], ["ry2"])

    def message2(m):
        for k in range(2):
            out, bank = T.pk2[:, FP * k:FP * (k + 1)], (2, 4)[k]
            win, names = qlog(k, m) if m else ((qa, ["qa"]), (qb, ["qb"]))[k]
            cp(out, win.indirect(ry[0] if m else rimU), names + ["ry0" if m else "rimU"], ["pk2_%d" % k], ind(FP), "av")
            shift(bank, out, T.ZF, ["pk2_%d" % k, "ZF"], 4)
            cp(T.snd2[:, k:2 * FP:2], P[bank][:, 0:FP], ["P%d" % bank, "snd2"], ["snd2_%d" % k], cyc(FP), "av")
        send(2, m, ["snd2_0", "snd2_1"], "lnd2_%d" % m)

    def message3(m):
        out = T.pk2[:, 2 * FP:3 * FP]
        if m < RO:
            o = 4 * (base(m) - V)
            cp(out, OUT[:, o - 16:o + 4 * CAP].indirect(ry[1]), ["O%d_%d" % (m, j) for j in range(4)] + ["ry1", "OZ%d" % m], ["pk2_2"], ind(FP), "av")
        else:
            ac(out, T.FF[:].indirect(ry[1]), ["FF0", "F0", "F1", "F2", "F3", "ry1"], ["pk2_2"], scale=-1.0, ns=ind(FP))
        bank = 1 if m < RO else 0
        shift(bank, out, T.ZF, ["pk2_2", "ZF"], 4)
        cp(T.snd3[:], P[bank][:, 0:FP], ["P%d" % bank, "snd3"], ["snd3_0"], cyc(FP), "av")
        send(3, m, ["snd3_0"], "lnd3_%d" % m)

    def table(r):
        j = 0
        for a, b in (halves if r == 0 else ((base(r), base(r) + CAP),)):
            w, made = b - a, {}
            x0, x1 = (QQ[0][:, a:b], QQ[1][:, a:b]) if r else (qa[:, a:b], qb[:, a:b])
            n0, n1 = ("Q0_%d" % r, "Q1_%d" % r) if r else ("qa", "qb")
            for i, ((c0, c1, outs), way) in enumerate(zip(CASES, WAYS[r > 0])):
                bank = int(TBANK[2 if r else a > 0][i])
                pb, nb = P[bank][:, 0:w], "P%d" % bank
                (z0, m0_), (z1, m1_) = scaled(c0, r), scaled(c1, r)
                up0 = outs[0][2]
                if way == "a":
                    mm([(pb, z0, x0)], [m0_, n0], bank, w, 4 if r else 1, stop=False)
                if way != "c":
                    mm([(pb, z1, x1)], [m1_, n1], bank, w, 4 if r else 1, start=way == "b")
                else:
                    ac(pb, x1, [n1], [nb], scale=c1 * up0, ns=cyc(w))
                u, nu = x0, n0
                if way != "a" and c0 * up0 != 1.0:
                    if c0 * up0 not in made:
                        h = len(made)
                        made[c0 * up0] = (T.r[:, 2 * CAP * h:2 * CAP * h + w], "rl%d" % h)
                        ac(made[c0 * up0][0], x0, [n0], ["rl%d" % h, "rr%d" % h], scale=c0 * up0, ns=cyc(w), on="av")
                    u, nu = made[c0 * up0]
                first = None
                for y, m, up_ in outs:
                    out = TAB[:, 10 * a + place_of(y, m):10 * (b - 1) + place_of(y, m) + 1:10]
                    if way == "a":
                        ac(out, pb, [nb, "TF%d" % r], ["T%d_%d" % (r, j)], scale=up_, ns=cyc(w), on="av")
                    elif first is None:
                        tt(out, pb, u, A.add, [nb, nu, "TF%d" % r], ["T%d_%d" % (r, j)], cyc(w))
                        first = out
                    else:
                        ac(out, first, ["T%d_%d" % (r, j - 1)], ["T%d_%d" % (r, j)], scale=up_ / up0, ns=cyc(w), on="av")
                    j += 1

    ts(T.CI[:, 0:1], T.Pi[:, 0:1], 15, A.bitwise_and, ["Pi"], ["CI0"])
    ts(T.CI[:, 1:2], T.Pi[:, 0:1], 4, A.arith_shift_right, ["Pi"], ["CI1"])
    ts(T.CI[:, 2:3], T.Pi[:, 0:1], 2, A.arith_shift_right, ["Pi"], ["CI2"], 3, A.bitwise_and)
    ts(T.CI[:, 3:4], T.Pi[:, 0:1], 3, A.bitwise_and, ["Pi"], ["CI3"])
    cp(CF[:, 0:4], T.CI[:, 0:4], ["CI0", "CI1", "CI2", "CI3"], ["CF"])
    ts(T.BK[:], X16, cG, A.is_equal, ["X16", "CF"], ["BK"], ns=cyc(128))
    sel(TRs, T.BK[:], A.is_gt, 0.0, 0, -1, ["BK"], ["TRs"])
    sel(Pa, TRs, A.not_equal, BIG, 0, -1, ["TRs"], ["Pa"])
    message1(0)
    zero(TAB, 0, 4, ["TZ0", "late"], ["sent"])

    d3, o = 3 * NW + 1, 24
    terms = [(1, 0, 1, 4, d3), (2, 4, 65536, 4, d3), (2, 16, 6, 4, d3), (15, 20, 6, 4, 1),
             (0, o, 10, 4, d3), (1, o, 1280, 4, d3), (2, o, 1, 4, d3), (12, o + 4, 10, 4, 1), (13, o + 4, 1280, 4, 1), (15, o + 4, 1, 4, 1),
             (2, o + 8, -32, 4, d3), (12, o + 12, 4, 4, 1), (13, o + 12, 512, 4, 1), (0, o + 16, 4, 4, d3), (1, o + 16, 512, 4, d3), (2, o + 16, 32, 4, d3),
             (12, o + 20, 1, 2, 2 * NW + 1), (13, o + 20, 128, 1, 1), (15, o + 21, 8192, 1, 1), (15, o + 22, -8192, 1, 1),
             (fJL, cWO + 12, 1, 2, NW + 1), (fEL, cWO + 14, 1, 2, NW + 1), (fM, cWO + 15, 1, 1, 1), (fD, cWO + 15, -1, 1, 1), (fS, cWO + 1, -32, 4, NW + 3),
             (fK, cWO + 2, 1, 4, NW + 3), (fT, cWO + 2, 1, 4, 3), (fM, cWO + 2, 1, 4, 3), (fD, cWO + 2, -1, 4, 3), (fJL, cWN, 1, 2, NW + 1), (fT, cWN + 2, -1, 1, 1),
             (fT, cS, 2, 2, NW), (fD, cS, -2, 1, 1), (fJL, cX, 1, 1, 1), (fJH, cX, 128, 1, 1), (fT, cZJ, 1, 3, NW),
             (fM, cTH, 3.5, 1, 1), (fD, cTH, 8.5, 1, 1), (fM, cNN, -2, 1, 1), (fD, cNN, 1, 1, 1), (0, cKP, 1, 11, NW), (fM, cD, 1, 1, 1), (fD, cD, -1, 1, 1),
             (fM, cB4, 4, 1, 1), (fJL, cR, PAD, 1, 1), (fJH, cR, CAP / 128, 1, 1), (fT, cT, 1, 1, 1), (1, cEL, 16, 4, 3 * NW),
             (fM, cI1, -0.125, 1, 1), (fD, cI1, 0.5, 1, 1), (fQ, cI2, 0.75, 1, 1), (fT, cV, 0.5, 1, 1), (fM, cV, 8.5, 1, 1), (fD, cV, -8.5, 1, 1),
             (fT, cVN, -0.5, 1, 1), (fEL, cEN, 1, 1, 1), (fEH, cEN, 8192, 1, 1), (fS, cSG, 1, 4, NW + 1)]
    places = [RW[:, NW * f + col:NW * f + col + (count - 1) * step + 1:step] for f, col, c, count, step in terms]
    RWs = ["RW%d" % k for k in range(1, 9)]
    for k in range(8):
        fills("av", [(x, x, t[2]) for x, t in zip(places[k::8], terms[k::8])], ["RW0"], [RWs[k]])
    mm([(P[5][:, 0:NW], W1(f), RW[:, NW * f:NW * f + NW]) for f in range(16)], ["E1"] + RWs, 5, 16 * NW)
    either[0] = "av"
    cp(WS[:, 0:NW], P[5][:, 0:NW], ["P5"], ["WS"], cyc(NW), "a")
    cp(WB[:, cWO:cS], WS[:, cWO:cS], ["WS"], ["WB0"], cyc(32), "a")
    tt(T.sm[:, 0:4], WS[:, o + 4:o + 8], WS[:, o:o + 4], A.subtract, ["WS"], ["WD"])
    ac(WS[:, 8:12], T.sm[:, 0:4], ["WD"], ["WS1"], scale=-1.0 / 16384)
    ac(WS[:, 12:16], T.sm[:, 0:4], ["WD"], ["WS2"], scale=1.0 / 16384)
    WLs = ["WL%d" % k for k in range(5)]
    for k in range(4):
        cp(WB[:, NA * (k // 2) + k % 2:NA * (k // 2) + NB:2], WS[:, k:2 * NB:4], ["WS", "WS1", "WS2"], [WLs[k]], on="a")
    cp(WB[:, NB:NA], WS[:, 2 * NB:NA + NB], ["WS"], [WLs[4]], on="a")
    for x, sc, bi, nm in ((cE, 16, 15, "cE"), (nE, -16, -15, "nE"), (cO, 4, 3, "cO"), (c12, 16, 12, "c12"), (c8, 16, 8, "c8"), (n16, -16, 0, "n16"),
                          (cF0, CAP, V - BIG, "cF0"), (cF1, CAP, V + CAP - 0.5, "cF1")):
        ac(x, cG, ["CF"], [nm], bias=float(bi), scale=float(sc))
    ac(SI, SI, ["SI", "nE"], ["SI"], bias=nE, ns=cyc(FP))
    ac(c2, cQ, ["CF", "c12"], ["c2"], bias=c12)
    ac(cA, cK, ["CF", "c8"], ["cA"], bias=c8)
    ac(nS, wcol(cS), ["WS"], ["nS"], scale=-1.0)
    cp(XB, X[0:1, :], ["X"], ["XB"], cyc(256), "a")
    cp(T.ZF[:], T.ZI[:, 0:240], ["ZI", "ZI0"], ["ZF"], cyc(240), "a")
    for k, c_ in enumerate(SCALES):
        ac(T.ZB[:, 128 * k:128 * k + 128], ZI, ["ZI0"], ["ZB%d" % k], scale=c_, ns=cyc(128), narrow=True)
    for r in range(1, RO + 1):
        zero(OUT, 4 * (base(r) - PAD - V), 4 * (base(r) - V), ["OZ%d" % r], ["late"])

    c = T.PI[:]
    aS, aK, aS2, aF, SG = [T.AB[:, FP * k:FP * k + FP] for k in range(5)]
    meet(["TD0", "TD1", "TD2", "s0", "s1", "s2", "s3"])
    ts(s1, c, 4.0, A.mult, ["PI"], ["s1"], -10749.0, A.add, cyc(FP))
    ts(s3, c, float(4 * V + up), A.is_ge, ["PI"], ["s3"], ns=cyc(FP))
    ts(aF, c, float(4 * V), A.is_ge, ["PI"], ["aF"], -3.0 / 32, A.mult, cyc(FP))
    tt(s0, s1, c, A.max, ["s1", "PI"], ["s0"], cyc(2 * FP))
    tt(s2, SI, c, A.is_lt, ["SI", "PI"], ["s2"], cyc(2 * FP))
    ts(T.colU[:], s0, 0.25, A.mult, ["s0"], ["colU"], -0.375, A.add, cyc(FP))
    tt(aS, s2, s3, A.subtract, ["s2", "s3"], ["aS"], cyc(2 * FP))
    ts(s1, s0, 3, A.bitwise_and, ["s0"], ["s1"], ns=cyc(FP))
    ts(aK, s1, 1.0 / 32, A.mult, ["s1"], ["aK"], ns=cyc(FP))
    ac(aS2, aS, ["aS"], ["aS2"], bias=0.5, scale=-1.0, ns=cyc(FP), narrow=True)
    ac(SG, aS, ["aS"], ["SG"], bias=-0.5, ns=cyc(FP), narrow=True)
    ts(T.MK[:, 0:4], X[:, 0:4], cQ, A.is_equal, ["X", "CF"], ["MK"])
    ts(T.ZA0[:], X[:, 0:144], cA, A.is_equal, ["X", "cA"], ["ZA0"], ns=cyc(144))
    ts(T.ZO0[:], XQ, cO, A.is_equal, ["XQ", "cO"], ["ZO0"], ns=cyc(144))
    ts(T.ZE0[:], X[:, 0:144], cE, A.is_equal, ["X", "cE"], ["ZE0"], ns=cyc(144))
    for m in range(4):
        ac(T.ZA[:, 144 * m:144 * m + 144], T.ZA0[:], ["ZA0", "MK"], ["ZA%d" % m], scale=T.MK[:, m:m + 1], ns=cyc(144), narrow=True)
    ZAs = ["ZA%d" % m for m in range(4)]
    ac(T.ZO[:], T.ZO0[:], ["ZO0", "nS"], ["ZO"], scale=nS, ns=cyc(144), narrow=True)
    ac(T.ZE[:], T.ZE0[:], ["ZE0", "WS"], ["ZE"], scale=wcol(cS), ns=cyc(144), narrow=True)
    ac(T.TRE[:], T.TRE[:], ["TRE", "n16"], ["TRE"], bias=n16)
    ts(T.Z2[:], X[:, 0:144], c2, A.is_equal, ["X", "c2"], ["Z2"], ns=cyc(144))
    fills("v", [(HI[:, 128 * k:128 * k + 128], None, k) for k in range(V // 128)], [], ["HI"])
    ms(T.CR[:], 0.0, ["CR"], cyc(256))
    ms(T.CR[0:1, :], 1.0, ["CR"], cyc(256))
    for k, (a, b) in enumerate(wide):
        parts = [(P[k][:, 0:b - a], ZI, ST[:, a:b]), (P[k][:, 0:b - a], W1(fJH), HI[:, a:b])]
        parts += [(P[k][:, c_ - a:c_ - a + 128], W1(fJL), XB[:, 0:128]) for c_ in range(a, b, 128)]
        for c_ in range(a, b, 256):
            w_ = min(256, b - c_)
            parts += [(P[k][:, c_ - a:c_ - a + w_], W1(fEL), XB[:, 0:w_])] + [(P[k][:, c_ - a:c_ - a + w_], W1(fEH, c_ // 256), T.CR[0:1, 0:w_])] * (c_ > 0)
        mm(parts, ["ZI0", "E1", "HI", "XB", "CR", STs[k]], k, 5 * (b - a), stop=False)
        mm([(P[k][:, m:b - a:4], T.ZA[:, 144 * m + 8 - f:144 * m + 136 - f], x[:, a // 4:b // 4]) for f, x in ((fS, aS2), (fK, aK), (fK, aF)) for m in range(4)],
           ["aK", "aS2", "aF"] + ZAs, k, 3 * (b - a), start=False)
        cp(ST[:, a:b], P[k][:, 0:b - a], ["P%d" % k], [STs[k]], cyc(b - a), "a")
    zero(ST, V, SL, ["STz"], ["late"])
    STw = STs + ["STz"]
    ac(nPa, Pa, ["Pa"], ["nPa"], scale=-1.0, ns=cyc(128), narrow=True)
    ms(T.ONE[:], 1.0, ["ONE"])
    message2(0)
    for k, x in enumerate((T.q0, T.q1)):
        load("g", 8 + k, QQ[k][:, 0:V], x[:], "Q%d_0" % k, T3, ["sent"], 1000.0)
    ac(T.MK[:, 8:8 + W], T.TRE[:, 0:W], ["TRE"], ["TRX"], bias=float(V))
    ac(T.rimK[:, 32:46], T.TRE[:, 0:14], ["TRE"], ["J10"], scale=10.0, bias=-27.0)
    mm([(P[4][:, 16 * (8 * h + j):16 * (8 * h + j) + 16], T.ZI[0:16, 128 - 16 * j:256 - 16 * j], WB[0:16, cWO + 16 * h:cWO + 16 * h + 16]) for h in range(2) for j in range(8)],
       ["ZI", "ZI0", "WB0"], 4, 16 * 64, start="each", stop="each")
    ms(T.WN[:, 0:16], 0.0, ["WN0"])
    cp(T.Wo[:], P[4][:, 0:128], ["P4"], ["Wo"], cyc(128), "a")
    cp(T.WN[:, 9:137], P[4][:, 128:256], ["P4", "WN0"], ["WN"], cyc(128), "a")
    ac(T.ZJ[:], T.ZI[:, 0:240], ["ZI", "ZI0", "WS"], ["ZJ"], scale=wcol(cZJ), ns=cyc(240), narrow=True)
    ac(T.ZX[:], T.ZE0[:], ["ZE0", "WS"], ["ZX"], scale=wcol(cX), ns=cyc(144), narrow=True)
    ms(T.FF[:, 0:8], 0.0, ["FF0"])
    ms(T.MEM[:], 0.0, ["MEM"], cyc(FP))
    ts(T.NT[:, 0:1], T.TH[:, 0:1], -1.0, A.mult, ["TH"], ["NTH"])
    iota(T.KE[:], [[2, 2], [1, 4], [0, W]], -4 * V, 0, ["KE0", "KE1"], c=8 * W, reads=["late"])
    ms(T.KR[:], 0.0, ["KR"], cyc(64))
    fills("v", [(T.KR[32:33, :], None, 1), (T.CR[32:33, 6 * W:8 * W], None, 2.5)], ["CR"], ["KR"])
    ts(T.RJ[:, 16:30], T.RI[:, 16:30], 3, A.bitwise_and, ["RP"], ["RJ1"])
    cp(T.rimK[:, 0:14], T.RJ[:, 16:30], ["RJ1"], ["rimK"])
    ts(T.rimK[:, 16:30], T.RJ[:, 16:30], float(CAP), A.mult, ["RJ1"], ["rimL"], 8.0 - base(RO), A.add)
    ty, td, th_, tb = [LW[:, 64 * k:64 * k + 64] for k in range(4)]
    L1, L3 = T.LT[:, 0:64], T.LT[:, 64:128]
    iota(ty, [[0, 4], [1, 16]], -2, 0, ["ty"], reads=["late"])
    iota(td, [[1, 4], [0, 16]], 1, 0, ["td"], reads=["late"])
    ts(L1, ty, 0.0, A.max, ["ty"], ["L1"])
    tt(L1, L1, td, A.min, ["L1", "td"], ["L1"], cyc(128))
    ac(th_, L1, ["L1"], ["th_"], scale=-0.5, ns=cyc(64))
    tt(tb, th_, ty, A.add, ["th_", "ty"], ["tb"], cyc(128))
    tt(L3, L1, tb, A.mult, ["L1", "tb"], ["L3"], cyc(128))
    to_t = T.ZE0[:, 15 - fT:143 - fT]
    ac(T.Wb[:], to_t, ["ZE0", "WS"], ["Wb"], scale=wcol(cD), ns=cyc(128), narrow=True)
    ac(tmp, ZI, ["ZI0", "WS"], ["tmp"], scale=wcol(cKP), ns=cyc(128), narrow=True)
    tt(T.Wb[:], T.Wb[:], tmp, A.add, ["Wb", "tmp"], ["Wb"], cyc(256))
    for x, y, col, nm, src in ((Wv, to_t, cV, "Wv", "ZE0"), (Wvn, to_t, cVN, "Wvn", "ZE0"), (Wi1, T.BK[:], cI1, "Wi1", "BK"), (Wi2, T.BK[:], cI2, "Wi2", "BK")):
        ac(x, y, [src, "WS"], [nm], scale=wcol(col), ns=cyc(128), narrow=True)
    for k in range(4):
        ac(SGM[k], T.BK[:], ["BK", "WS"], ["SGM%d" % k] + ["ZA%d" % (k - 2)] * (k > 1), scale=wcol(cSG + k), ns=cyc(128), narrow=True)
    for r in range(1, RO + 1):
        ac(T.BR[:, r:r + 1], wcol(cR), ["WS"], ["BR%d" % r], bias=wcol(cB4), scale=float(r - 1))
        if r < RO:
            ac(T.BR[:, 8 + r:9 + r], wcol(cR), ["WS"], ["BJ%d" % r], scale=float(r))
    ac(T.ZQ[:], T.ZO0[:], ["ZO0", "WS"], ["ZQ"], scale=wcol(cX), ns=cyc(144), narrow=True)
    ac(T.Wy[:, 0:8], T.BK[:, 0:128:16], ["BK", "WS"], ["Wy0"], scale=wcol(cT))
    ac(T.Wy[:, 8:16], T.BK[:, 0:128:16], ["BK", "WS"], ["Wy1"], scale=wcol(cD))
    ac(Z8, ZI, ["ZI0"], ["Z8"], scale=8.0, ns=cyc(128), narrow=True)
    for x, col, nm, src in ((KB, wcol(cS), "KB", "WS"), (nKB, nS, "nKB", "nS"), (EB, wcol(cEN), "EB", "WS")):
        ac(x, T.BK[:], ["BK", src], [nm], scale=col, ns=cyc(128), narrow=True)
    for h in range(2):
        ts(cH[h], cP, up - HF * h - 0.5, A.is_ge, ["cP"], ["cH%d" % h], 255.5, A.add)
    THRs, COs = ["THR%d" % k for k in range(4)], ["CO%d" % k for k in range(16)]
    for k, (pat, base_) in enumerate((([[0, 3], [1, 128]], PAD), ([[1, 3], [0, 128]], V // 128))):
        iota(PJ[:, 384 * k:384 * (k + 1)], pat, base_, 0, ["PJ%d" % k], c=384, reads=["late"])
    mm([(P[2][:, 0:CAP], W1(f), x[:, 0:CAP]) for f, x in ((fJL, PJ), (fJH, PJ[:, 384:768]), (fQ, T.CR[0:1, :]))], ["E1", "PJ0", "PJ1", "CR"], 2, 3 * CAP)
    cp(T.JR[:], P[2][:, 0:CAP], ["P2"], ["JR"], cyc(CAP), "a")
    table(0)
    for k, c_ in enumerate(SCALES):
        sel(T.ZS[:, 128 * k:128 * k + 128], ZF, A.not_equal, c_, 0, -1, ["ZF", "late"], ["ZS%d" % k])

    either[0] = ""
    NG = 8
    Gs = ["G%d" % k for k in range(NG)]
    meet(["RW0", "HI", "HJ", "PT", "XB"] + RWs + Gs)
    meet(["PJ0", "PJ1", "CJ"])
    meet(["TB", "RR0", "RR1"])
    meet(["qa", "g", "h", "nn", "base"])
    meet(["qb"] + ["snd1_%d" % k for k in range(1, RO)])
    edge = [56 * (k // 2) + GV * (k % 2) for k in range(NG + 1)]
    qe, FF, gb, eU, sm = T.qe, T.FF, T.gb, T.eU, T.sm
    TH, fresh = T.TH[:, 0:1], gb[:, 2 * CAP:3 * CAP]

    def neighbours(free):
        for k in range(NG):
            a, b = edge[k], edge[k + 1]
            cp(T.G[:, 16 * a:16 * b], ST[:, 0:SL].indirect(T.colU[:, a:b]), STw + ["colU"], [Gs[k]], ind(16 * (b - a)), "av" if free else "va"[k % 2])

    def by_slot(bank, Z, zn, pieces):
        for j in range(pieces):
            a, b = FP // pieces * j, FP // pieces * (j + 1)
            mm([(P[bank][:, a:b], Z[:, 15 - i:143 - i], T.G[:, 16 * a + i:16 * b:16]) for i in range(16)], Gs[NG // pieces * j:NG // pieces * (j + 1)] + [zn], bank,
               16 * (b - a), start=False, stop=j == pieces - 1)

    def control(r):
        for k in range(2):
            zero(T.C, V + 4 * CAP * k, V + 4 * CAP * (k + 1), ["C%d" % k], ["late"])
        meet(["room", "TF%d" % r] + early * (r == 4))
        mm([(P[1][:, 0:FP], ZI, SG)] + [(P[1][:, 0:FP], T.ZO[:, 12 - 4 * m:140 - 4 * m], ST[:, m:V:4]) for m in range(4)], ["ZI0", "SG", "ZO"] + STs, 1, 5 * FP, stop=False)
        for k, (a, b) in enumerate(halves):
            mm([(P[3 + 4 * k][:, 0:b - a], T.Wo[:], ST[:, a:b])], ["Wo"] + STs, 3 + 4 * k, b - a, stop=False)
        neighbours(r == 1)
        landed, ln = piece(T, "lnd", 1, r - 1, 0, n - 1), "lnd1_%d" % (r - 1)
        if r == 1:
            cp(T.G[:].indirect(rimS), landed, [ln, "rimS"], Gs, ind(FP, SC))
        by_slot(1, T.ZE, "ZE", 1 if r == 1 else 2)
        ts(T.bit[:], P[1][:, 0:FP], 0.0, A.is_gt, ["P1"], ["bit"], ns=cyc(FP))
        if r > 1:
            for k, (x, z, names) in enumerate(((pkN, nKB, ["pkN", "nKB"]), (landed, KB, [ln, "KB"]))):
                mm([(P[2][0:HF, 128 * h:128 * h + 128], x[:, HF * h:HF * (h + 1)], z) for h in range(2)], names, 2, 256, start=k == 0, stop=k == 1)
            for k in range(2):
                tt(T.LZ[0:HF, 256 * k:256 * k + 256], P[2][0:HF, 0:256], T.THR[0:HF, 256 * k:256 * k + 256], A.is_lt, ["P2"] + THRs, ["LZ%d" % k], cyc(256))
                mm([(P[4][:, 0:56], T.KR[:], T.CR[:, 0:56])] * (k == 0)
                   + [(P[4][32 * q:32 * q + 32, 0:56], T.LZ[0:HF, 256 * k + 128 * h + 32 * q:256 * k + 128 * h + 32 * q + 32],
                       T.CO[0:HF, 56 * (8 * h + 2 * q + k):56 * (8 * h + 2 * q + k + 1)]) for q in range(4) for h in range(2)],
                   ["LZ%d" % k, "KR", "CR"] + COs, 4, (9 - k) * 56, start=k == 0, stop=False)
            cp(T.G[:].indirect(rimS), landed, [ln, "rimS"], Gs, ind(FP, SC))
        mm([(P[4][:, 0:56], T.Z2[:, 12 - 4 * h:140 - 4 * h], T.bit[:, h:FP:4]) for h in range(4)], ["Z2", "bit"], 4, 256, start=r == 1)
        mm([(P[1][:, 0:FP], Wv, pkN), (P[1][:, 0:FP], Wvn, landed)], ["Wv", "Wvn", "pkN", ln], 1, 2 * FP)
        ac(T.XF[:], P[1][:, 0:FP], ["P1"], ["XF"], bias=-1.5, ns=cyc(FP), on="av")
        if r > 1:
            message3(r - 1)
        cn, cb_ = T.can[:], T.can[:, 0:55]
        ts(cn, P[4][:, 0:56], 3.5, A.is_ge, ["P4"], ["cn"])
        mm([(P[4][:, 56:112], Pa, cn), (P[4][:, 57:112], T.BK[:], cb_), (P[4][:, 57:112], nPa, cb_)], ["Pa", "BK", "nPa", "cn"], 4, 3 * 64)
        m0, m1, m2, m3 = [T.v1[:, 56 * k:56 * k + 56] for k in range(4)]
        op({"v": cyc(56)}, lambda e: vec.tensor_tensor_scan(m0, T.ONE[:], P[4][:, 56:112], cF0, A.mult, A.add), ["ONE", "P4", "cF0"], ["m0"])
        ts(m1, m0, cF1, A.is_ge, ["m0", "cF1"], ["m1"], -BIG, A.mult)
        tt(m2, m0, m1, A.add, ["m0", "m1"], ["m2"], cyc(112))
        tt(m3, m2, T.TRE[:], A.max, ["m2", "TRE"], ["m3"], cyc(112))
        cp(T.posU[:], m3, ["m3"], ["posU"])
        for k, (a, b) in enumerate(halves):
            for j in range(4):
                mm([(P[3 + 4 * k][:, 0:b - a], T.WN[:, 9 - 3 * j:137 - 3 * j], T.G[:, 4 * a + j:4 * b:4])], ["WN"] + Gs, 3 + 4 * k, b - a, 1, False, j == 3)
            ac(T.RR[:, a:b], P[3 + 4 * k][:, 0:b - a], ["P%d" % (3 + 4 * k), "WS"], ["RR%d" % k], bias=wcol(cEL), ns=cyc(b - a), on="av")
        for k in range(SPLIT):
            a, b = V // SPLIT * k, V // SPLIT * (k + 1)
            cp(T.C[:].indirect(T.posU[:, a // 16:b // 16]), T.RR[:, a:b], ["posU", "RR%d" % (2 * k // SPLIT)], ["C0", "C1", "CJ"], ind(b - a, SC))

    def far_places():
        ex, ci = P[4][0:HF, 0:256], T.TD[0:HF, 0:256]
        c16, i56 = T.xx[0:HF, 0:256], T.xx[0:HF, CAP:CAP + 56]
        one = [T.LZ[0:HF, 256 * k:256 * k + 256] for k in range(2)]
        meet(["s0", "s1", "ci"])
        ts(SG, aF, -1024.0, A.mult, ["aF", "aS"], ["SG"], ns=cyc(FP // 2))
        tt(SG, SG, aS2, A.subtract, ["SG", "aS2"], ["SG"], cyc(2 * FP))
        cp(T.PKS[:], ST[:, 0:V].indirect(rimN), STs + ["rimN"], ["PKS"], ind(FP), "av")
        iota(i56, [[-16, 56]], 0, 0, ["x1"], reads=["late"])
        mm([(ex[:, 128 * h:128 * h + 128], T.PKS[:, HF * h:HF * (h + 1)], EB) for h in range(2)], ["PKS", "EB"], 4, 256, start="each", stop="each")
        ts(ci, ex, 0.0625, A.mult, ["P4"], ["ci"], -0.47, A.add, cyc(256))
        ac(c16, ci, ["ci"], ["x0"], scale=-16.0, ns=cyc(256), on="v")
        tt(ex, ex, c16, A.add, ["P4", "x0"], ["P4"], cyc(256))
        for k in range(2):
            iota(one[k], [[0, 8], [1, 32]], -16 * k, 0, ["LZ%d" % k], c=256, reads=["late"])
            tt(one[k], ex, one[k], A.is_equal, ["P4", "LZ%d" % k], ["LZ%d" % k], cyc(256))
            for h in range(2):
                a = 256 * k + 128 * h
                ac(T.THR[0:HF, a:a + 128], T.LZ[0:HF, a:a + 128], ["LZ%d" % k, "cH%d" % h], [THRs[2 * k + h]], scale=cH[h][0:HF], bias=-256.0, ns=cyc(128), on="av", narrow=True)
        for j in range(16):
            ts(T.CO[0:HF, 56 * j:56 * j + 56], i56, c16[:, 16 * j:16 * j + 1], A.is_equal, ["x0", "x1"], [COs[j]], -8.0, A.mult)

    def far_records(r):
        listed(2, 0, T.ZE, T.XF, 14, ["ZE", "XF"])
        v_ = P[2][:, 0:14]
        d16, yy, y6, h_, s_ = rf[3:8]
        ts(ry[3], v_, -11.0, A.add, ["P2"], ["ry3"])
        ts(d16, v_, R16, A.add, ["P2"], ["d16"], R16 + 48, A.subtract)
        tt(yy, v_, d16, A.subtract, ["P2", "d16"], ["yy"])
        ts(h_, d16, 0.375, A.mult, ["d16"], ["h_"], 1.0, A.min)
        ts(yy, yy, 46.0, A.max, ["yy"], ["yy"], 49.0, A.min)
        ts(y6, yy, 6.0, A.mult, ["yy"], ["y6"], -288.0, A.add)
        tt(s_, yy, T.rimK[:, 32:46], A.add, ["yy", "J10"], ["s_"])
        tt(y6, y6, h_, A.min, ["y6", "h_"], ["y6"])
        tt(s_, s_, y6, A.add, ["s_", "y6"], ["s_"])
        cp(ry[4], s_, ["s_"], ["ry4"])
        for k, (L, nm) in enumerate(((L1, "L1"), (L3, "L3"))):
            tt(T.pk2[:, FP * k:FP * k + FP], L.indirect(ry[3]), piece(T, "lnd", 2, r - 1, 0, n - 1)[:, k::2], A.mult, [nm, "ry3", "lnd2_%d" % (r - 1)], ["pk2_%d" % k], ind(FP))
        tt(TAB[:, 10 * base(r):10 * base(r) + FW].indirect(ry[4]), T.pk2[:, 0:FP], T.pk2[:, FP:2 * FP], A.add, ["pk2_0", "pk2_1", "ry4"], ["TF%d" % r], ind(FP, SC))
        if r > 1:
            o = 4 * (base(r) - V)
            tt(OUT[:, o:o + 4 * FP:4], T.MEM[:].indirect(ry[2]), piece(T, "lnd", 3, r - 1, 0, n - 1), A.add, ["MEM", "ry2", "lnd3_%d" % (r - 1)], ["MF%d" % r], ind(FP))
            cp(T.MEM[:, 0:FP], OUT[:, o:o + 4 * FP:4], ["MF%d" % r], ["MEM"], cyc(FP), "a")

    def addresses(r):
        for h, (bank, a, b) in enumerate(((6, 0, NA), (0, NA, NA + NB))):
            mm([(P[bank][:, 0:(b - a) * W], T.KR[:], T.CR[:, 0:(b - a) * W])], ["CR", "KR"], bank, (b - a) * W, stop=False)
            mm([(P[bank][:, j:(b - a) * W:W], T.C[:, V + j:V + 128 * W:W], WB[:, a:b]) for j in range(W)], ["C0", "C1"] + WLs, bank, W * 64, start=False)
        for h, bank in enumerate((6, 0)):
            def pa(a, b):
                return P[bank][:, 2 * W * a:2 * W * b]
            nb, o = "P%d" % bank, 16 * W * h
            sd, u_, t_, zz, gt = [sm[:, o + W * a:o + W * b] for a, b in ((0, 2), (2, 4), (4, 8), (8, 12), (12, 16))]
            ns_, nu, nt, nz, ng, ke = [x + str(h) for x in ("sd", "u_", "t_", "zz", "gt", "KE")]
            side = [t_[:, 2 * W * k:2 * W * (k + 1)] for k in range(2)]
            ts(sd, pa(0, 1), 31.5, A.is_ge, [nb, "WD"], [ns_], -16384.0, A.mult)
            ts(u_, pa(1, 2), -32768.0, A.add, [nb], [nu], 19.0, A.min)
            for k in range(2):
                tt(side[k], pa(2 + k, 3 + k), sd, A.mult, [nb, ns_], [nt + "ab"[k]])
                tt(u_, pa(4 + k, 5 + k), u_, A.min, [nb, nu], [nu])
            tt(t_, pa(6, 8), t_, A.add, [nb, nt + "a", nt + "b"], [nt + "a", nt + "b"], cyc(4 * W))
            for k in range(2):
                tt(side[k], side[k], u_, A.add, [nt + "ab"[k], nu], [nt + "ab"[k]], cyc(4 * W))
            ts(T.UA[:, 4 * W * h:4 * W * (h + 1)], t_, -0.33, A.add, [nt + "a", nt + "b"], ["UA%d" % h], ns=cyc(4 * W))
            if h == 0:
                e0, e1, own, raw, step = sm[:, 32 * W:33 * W], sm[:, 33 * W:34 * W], *[P[bank][:, W * k:W * (k + 1)] for k in range(NB, NA)]
                cp(T.UQ[:], own, [nb], ["UQ"])
                ts(e0, step, R8192, A.add, [nb], ["e0"], R8192, A.subtract)
                tt(e1, step, T.MK[:, 8:8 + W], A.add, [nb, "TRX"], ["e1"])
                tt(e0, raw, e0, A.add, [nb, "e0"], ["e0"])
                tt(e0, e0, e1, A.max, ["e0", "e1"], ["e0"])
                cp(eU[:], e0, ["e0"], ["eU"])
            if r > 1:
                fl, own, far = T.KE[:, W * (4 * h + 2):W * (4 * h + 4)], zz[:, 0:2 * W], zz[:, 2 * W:4 * W]
                ts(fl, pa(8, 9), R32, A.add, [nb], [ke], R32 + 4 * V, A.subtract)
                tt(fl, fl, sd, A.add, [ke, ns_], [ke], cyc(4 * W))
                tt(zz, pa(9, 11), T.KE[:, 4 * W * h:4 * W * (h + 1)], A.add, [nb, ke], [nz], cyc(4 * W))
                for k, (x, y) in enumerate(((far, own), (own, far))):
                    z = gt[:, 2 * W * k:2 * W * (k + 1)]
                    tt(z, x, y, A.is_gt, [nz], [ng + "ab"[k]], cyc(4 * W))
                    tt(z, z, x, A.mult, [nz, ng + "ab"[k]], [ng + "ab"[k]], cyc(4 * W))
                cp(T.UC[:, 4 * W * h:4 * W * (h + 1)], gt, [ng + "a", ng + "b"], ["UC%d" % h], cyc(4 * W))

    def port_list(buf, k, second):
        a = W * (4 * (k // 2) + 2 * second + k % 2)
        return buf[:, a:a + W]

    def old_q(r):
        win, names = qlog(0, r - 1)
        cp(qe[:], win.indirect(T.UQ[:]), names + ["UQ"], ["qe"], ind(CAP), "av")
        mm([(P[4][:, 0:CAP], ZF, qe[:])], ["ZF", "qe"], 4, CAP, 4)
        mm([(P[5][:, 0:CAP], ZF, qe[:])], ["ZF", "qe"], 5, CAP, 4, stop=False)

    def old_fields(r):
        cp(T.GO[:], ST[:, 0:SL].indirect(eU[:]), STw + ["eU"], ["GO"], ind(CAP), "av")
        mm([(P[0][:, 0:CAP], ZI, T.JR[:]), (P[0][:, 0:CAP], T.Wb[:], T.GO[:])], ["Wb", "GO", "ZI0", "JR"], 0, 2 * CAP)
        ac(fresh, P[0][:, 0:CAP], ["P0", "BR%d" % r], ["base"], bias=T.BR[:, r:r + 1], ns=cyc(CAP), on="av")

    def flux(r, s, step):
        h, bj, bs = SLOT[s], 1 + s % 2, 3 + 4 * (s % 2)
        rl, rr, sq = T.r[:, 2 * CAP * h:2 * CAP * h + CAP], T.r[:, 2 * CAP * h + CAP:2 * CAP * (h + 1)], T.sq[:, CAP * h:CAP * (h + 1)]
        sg, ps, nj, ng = P[bs][:, 0:CAP], P[bj][:, 0:CAP], "P%d" % bj, "P%d" % bs
        if step == "g":
            win, names = tlog(r - 1)
            cut(rl, win.indirect(port_list(T.UA, s, 0)), 1.0 / 32, names + ["UA%d" % (s // 2)], ["rl%d" % h], ind(CAP))
            cut(rr, win.indirect(port_list(T.UA, s, 1)), -1.0 / 32, names + ["UA%d" % (s // 2)], ["rr%d" % h], ind(CAP))
        elif step == "m":
            mm([(sg, SGM[s], T.GO[:])], ["SGM%d" % s, "GO"], bs, CAP)
            ac(sq, rl, ["rl%d" % h], ["sq%d" % h], AF.Square, ns=cyc(CAP))
            ac(ps, rr, ["rr%d" % h], [nj], AF.Square, ns=cyc(CAP))
        else:
            f = FF[:, 8 + CAP * s:8 + CAP * (s + 1)]
            tt(sq, ps, sq, A.add, [nj, "sq%d" % h], ["sq%d" % h], cyc(CAP))
            tt(f, sg, sq, A.mult, [ng, "sq%d" % h], ["F%d" % s], cyc(CAP))
            x, xn = f, "F%d" % s
            if r > 1:
                win, names = olog(r - 1, 1)
                x, xn = T.xx[:, CAP * (s % 2):CAP * (s % 2 + 1)], "x%d" % (s % 2)
                tt(x, win.indirect(port_list(T.UC, s, 0)), f, A.add, names + ["UC%d" % (s // 2), "F%d" % s], [xn], ind(CAP))
            if s < 3:
                mm([(P[5][:, 0:CAP], ZF, x)], ["ZF", xn], 5, CAP, 4, start=False, stop=s == 2)
            else:
                tt(record(0, r)[0], P[5][:, 0:CAP], x, A.add, ["P5", xn], [record(0, r)[1]], cyc(CAP))

    def sums(r):
        meet(["MF%d" % r])
        win, names = olog(r - 1, 0)
        for k in range(4):
            o = 4 * (base(r) - V)
            out, on_, f = OUT[:, o + k:o + 4 * CAP:4], "O%d_%d" % (r, k), FF[:, 8 + CAP * k:8 + CAP * (k + 1)]
            if r == 1:
                ac(out, f, ["F%d" % k], [on_], scale=-1.0, ns=cyc(CAP), on="av")
            else:
                tt(out, win.indirect(port_list(T.UC, k, 1)), f, A.subtract, names + ["UC%d" % (k // 2), "F%d" % k, "MF%d" % r], [on_], ind(CAP))

    def new_fields(r):
        g1, nn, g2 = [gb[:, CAP * k:CAP * (k + 1)] for k in (0, 1, 3)]
        qf, qn = record(0, r)
        ts(g1, qf, TH, A.is_gt, [qn, "TH"], ["g"], ns=cyc(CAP))
        ts(g2, qf, T.NT[:, 0:1], A.is_lt, [qn, "NTH"], ["h"], ns=cyc(CAP))
        mm([(P[1][:, 0:CAP], T.BK[:], g1)], ["BK", "g"], 1, CAP, stop=False)
        mm([(P[1][:, 0:CAP], T.BK[:], g2)], ["BK", "h"], 1, CAP, start=False)
        ts(nn, P[1][:, 0:CAP], wcol(cTH), A.is_ge, ["P1", "WS"], ["nn"], wcol(cNN), A.mult, cyc(CAP))
        tt(ST[:, 0:SL].indirect(eU[:]), nn, fresh, A.add, ["nn", "base", "eU"], STw, ind(CAP, SC))

    def new_q(r):
        d, dn = T.sq[:, CAP * SLOT[1]:CAP * (SLOT[1] + 1)], "sq%d" % SLOT[1]
        mm([(P[6][:, 0:CAP], Wi1, T.GO[:]), (P[6][:, 0:CAP], Wi2, T.JR[:])], ["Wi1", "Wi2", "GO", "JR"], 6, 2 * CAP)
        tt(d, record(0, r)[0], P[4][:, 0:CAP], A.subtract, ["P4", record(0, r)[1]], [dn], cyc(CAP))
        tt(record(1, r)[0], P[6][:, 0:CAP], d, A.mult, ["P6", dn], [record(1, r)[1]], cyc(CAP))

    def once(fn, *args):
        first = len(nodes)
        fn(*args)
        for nd in nodes[first:]:
            nd["once"] = True

    def last_addresses():
        cp(ST[:, 0:SL].indirect(eU[:]), fresh, ["base", "eU"], STw, ind(CAP, SC))
        rim_fields()
        rim_lists(RO)
        cp(T.pk2[:, FP:2 * FP], T.MEM[:].indirect(ry[2]), ["MEM", "ry2"], ["pk2_1"], ind(FP), "av")
        own_a, fa = T.snd2[:, 0:FP], T.snd2[:, FP:2 * FP]
        meet(["snd2", "own", "fa"])
        mm([(P[0][:, 0:FP], T.ZQ[:, 12 - 4 * m:140 - 4 * m], ST[:, m:V:4]) for m in range(4)], ["ZQ"] + STs, 0, 4 * FP)
        ac(own_a, P[0][:, 0:FP], ["P0"], ["own"], bias=0.875, ns=cyc(FP), on="av")
        listed(0, 0, T.ZX, ST, 56, ["ZX"] + STs)
        cp(T.qyU[:], P[0][:, 0:56], ["P0"], ["qyU"])
        neighbours(True)
        far = P[6][:, 0:FP]
        mm([(far, Z8, aK), (far, Z8, aF)], ["Z8", "aK", "aF"], 6, 2 * FP, stop=False)
        by_slot(6, T.ZX, "ZX", 2)
        tt(fa, far, own_a, A.is_gt, ["P6", "own"], ["fa"], cyc(FP))
        tt(fa, far, fa, A.mult, ["P6", "fa"], ["fa"], cyc(FP))
        ts(T.adU[:], fa, 4.0, A.mult, ["fa"], ["adU"], -4.0 * V, A.add, cyc(FP))

    for r in range(1, RO + 1):
        control(r)
        if r == 1:
            far_places()
        for step in ORDER.split():
            if step[0] in "gmb":
                flux(r, int(step[1]), step[0])
            elif step != "n":
                {"f": far_records, "a": addresses, "e": old_q, "o": old_fields}[step](r)
            elif r == RO:
                once(last_addresses)
        if r == RO:
            once(message3, r)
        else:
            mm([(P[3][:, 0:FP], ZI, T.CH[:])], ["ZI0", "CH"], 3, FP, stop=False)
        new_q(r)
        new_fields(r)
        nodes[-1]["ends"] = r
        marks[r] = len(nodes)
        if r < RO:
            message1(r)
        sums(r)
        if r < RO:
            rim_lists(r)
            message2(r)
            table(r)

    M, po, ya, yb, yc = TAB[:, 0:4 * V], TAB[:, 4 * V:5 * V], TAB[:, 5 * V:6 * V], TAB[:, 6 * V:7 * V], TAB[0:16, 7 * V:8 * V]
    Ms = ["M%d" % k for k in range(NG)]
    meet(tlog(RO - 1)[1] + Ms + ["y00", "y01", "y10", "y11", "YT0", "YT1"] + ["YM%d" % k for k in range(4)])
    for j, (y, to) in enumerate(((T.y0, ya), (T.y1, yb))):
        win, names = qlog(j, RO)
        for k in range(2):
            cp(to[:, 448 * k:448 * k + 448], win.indirect(T.qyU[:, 28 * k:28 * k + 28]), names + ["qyU"], ["y%d%d" % (j, k)], ind(448), "av")
        store("s", y[:], to, ["y%d0" % j, "y%d1" % j])
    for k, (a, b) in enumerate(halves):
        mm([(P[1 + k][0:16, 0:b - a], T.Wy[:, 0:16], ST[:, a:b])], ["Wy0", "Wy1"] + STs, 1 + k, b - a)
        cp(yc[:, a:b], P[1 + k][0:16, 0:b - a], ["P%d" % (1 + k)], ["YT%d" % k], cyc(b - a), "av")
    for j in range(2):
        store("s", T.yt[:, V * j:V * j + V], yc[8 * j:8 * j + 8, :], ["YT0", "YT1"])
    win, names = olog(RO, 0)
    for k in range(NG):
        w_ = FP // NG
        cp(M[:, 16 * w_ * k:16 * w_ * (k + 1)], win.indirect(T.adU[:, w_ * k:w_ * (k + 1)]), names + ["adU"], [Ms[k]], ind(16 * w_), "av")
    tt(M.indirect(rimS), T.pk2[:, FP:2 * FP], piece(T, "lnd", 3, RO, 0, n - 1), A.add, ["pk2_1", "lnd3_%d" % RO, "rimS"], Ms, ind(FP, SC))
    for k in range(4):
        a, pb, nm, ms_ = V * k, P[3 + k % 2][:, 0:FP], "P%d" % (3 + k % 2), Ms[2 * k:2 * k + 2]
        if k == 3:
            mm([(P[5][:, 0:FP], ZF, M[:, a + j:a + V:4]) for j in range(4)], ["ZF"] + ms_, 5, V, 4)
            cp(po[:, FP * k:FP * k + FP], P[5][:, 0:FP], ["P5"], ["YM%d" % k], cyc(FP), "a")
        else:
            tt(pb, M[:, a:a + V:4], M[:, a + 1:a + V:4], A.add, ms_, [nm], cyc(2 * FP))
            tt(pb, pb, M[:, a + 2:a + V:4], A.add, ms_ + [nm], [nm], cyc(FP))
            tt(po[:, FP * k:FP * k + FP], pb, M[:, a + 3:a + V:4], A.add, ms_ + [nm], ["YM%d" % k], cyc(FP))
        store("sa"[k % 2], T.ym[:, FP * k:FP * (k + 1)], po[:, FP * k:FP * (k + 1)], ["YM%d" % k])

    for nd in nodes:
        nd["step"] = None
    for r in range(1, RO):
        row = [nd for nd in nodes[marks[r]:marks[r + 1]] if not nd.get("once")]
        names = [nd["out"][0] for nd in row]
        names = [x.rstrip("12345") if x[0:2] in ("Q0", "Q1", "MF", "TF", "ln") or x[0:4] == "snd1" else x.replace("%d_" % r, "_") if x[0] in "OT" else x for x in names]
        if r == 1:
            many = {x for x in names if names.count(x) > 1}
        for j, (nd, x) in enumerate(zip(row, names)):
            nd["step"] = (r, x + ".%d" % names[:j].count(x) if x in many else x)
    seen = {e: {} for e in Q}

    def need(e, toks):
        top = {}
        for s, val in toks:
            if not (e == "p" and s == "p"):
                top[s] = max(top.get(s, 0), val)
        for s, val in top.items():
            if seen[e].get(s, 0) < val:
                Q[e].wait_ge(T.sem[s], val)
                seen[e][s] = val

    for k in arrange(nodes):
        nd = nodes[k]
        toks = [t for j in nd["pre"] for t in nodes[j]["done"]]
        if nd["fn"] is None:
            nd["done"] = [nd["tok"]] if nd["tok"] else toks if nd["tok"] is None else []
            continue
        e = nd["e"]
        need(e, toks)
        last = nd["fn"](e)
        if nd["tok"] is True:
            last.then_inc(T.sem[e], 1)
            cnt[e] += 1
            nd["done"] = [(e, cnt[e])]
        else:
            nd["done"] = [nd["tok"]] if nd["tok"] else []
    need("g", [(s, c_) for s, c_ in cnt.items()])
